import numpy as np, ml_dtypes
CORES = [24,25,26,27,28,29,30,31]
N = 8
BF = ml_dtypes.bfloat16
def gentries(a):
    return np.ascontiguousarray(a.reshape(8, 16, -1).transpose(0, 2, 1)).reshape(8, -1)
def gtable(e):
    e = np.asarray(e); return np.ascontiguousarray(e.reshape(8, -1, 16).transpose(0, 2, 1)).reshape(128, -1).astype(np.int32)
V, C, S, RO = 4096, 512, 128, 3
Q, B = 32, 16
def parts(rng):
    X = rng.integers(0, 160, (N, 8, 16, V)) + 96 * rng.integers(0, 2, (N, 8, 1, V))
    p = rng.integers(0, 160, (N, 8, 16, S)) + 96 * rng.integers(0, 2, (N, 8, 1, S))
    return X, rng.integers(0, V, (N, 8, 16, C)), rng.integers(0, V, (N, 8, 16, S)), p, rng.integers(0, C, (N, 8, S))
def pack(X, K, M, p, c):
    return {"tx": np.ascontiguousarray(X.reshape(N, 128, V)).astype(BF), "kt": np.ascontiguousarray(K.reshape(N, 128, C)).astype(np.int32),
            "ms": np.ascontiguousarray(M.reshape(N, 128, S)).astype(np.int32), "z": np.ascontiguousarray(p.reshape(N, 128, S)).astype(BF), "cp": np.stack([gtable(a) for a in c])}
def setup_inputs(rng):
    return pack(*parts(rng))
def setup_inputs_spread(rng):
    X, K, M, p, c = parts(rng)
    X = np.minimum((np.exp2(8 * rng.random((N, 8, 1, V))) * rng.random((N, 8, 16, V))).astype(np.int64), 255)
    p = np.minimum((np.exp2(8 * rng.random((N, 8, 1, S))) * rng.random((N, 8, 16, S))).astype(np.int64), 255)
    K = np.minimum((V * rng.random((N, 8, 16, C)) ** 3).astype(np.int64), V - 1)
    M = np.minimum((V * rng.random((N, 8, 16, S)) ** 2).astype(np.int64), V - 1)
    c = np.minimum((C * rng.random((N, 8, S)) ** 2).astype(np.int64), C - 1)
    return pack(X, K, M, p, c)
def setup_inputs_ends(rng):
    half = (np.arange(16) >> 3)[:, None]
    X = 255 * rng.integers(0, 2, (N, 8, 16, V)); lo = 255 * rng.integers(0, 2, (N, 8, 1)); lo[:, 0] = 0; lo[:, 7] = 0
    for g in (0, 2, 4, 7):
        X[:, g, :, 0] = lo[:, g]; X[:, g, :, V - 1] = 255 - lo[:, g]
    p = 255 * rng.integers(0, 2, (N, 8, 16, S)); r = rng.integers(0, 4, (N, 8, 1, S)); p = np.where(r == 0, 0, np.where(r == 1, 255, p))
    K = rng.integers(0, 2, (N, 8, 16, C)); r = rng.integers(0, 5, (N, 8, 1, C))
    K = (V - 1) * np.where(r == 0, half, np.where(r == 1, 1 - half, np.where(r == 2, K[:, :, :1], K)))
    M = rng.integers(0, 2, (N, 8, 16, S)); r = rng.integers(0, 5, (N, 8, 1, S))
    M = (V - 1) * np.where(r == 0, half, np.where(r == 1, 1 - half, np.where(r == 2, M[:, :, :1], M)))
    c = np.where(rng.random((N, 8, S)) < 0.75, (C - 1) * rng.integers(0, 2, (N, 8, S)), rng.integers(0, C, (N, 8, S)))
    K[:, 7, :, C - 1] = V - 1; K[:, 0, :8, C - 1] = V - 1; K[:, 0, 8:, C - 1] = 0
    for g in (0, 7):
        for i in (0, 1, S - 1):
            p[:, g, :, i] = 0; c[:, g, i] = C - 1; M[:, g, :, i] = 0
        for i in (3, S - 5):
            p[:, g, :, i] = 0; c[:, g, i] = C - 1; M[:, g, :8, i] = 0; M[:, g, 8:, i] = V - 1
        for i in (2, S - 2):
            p[:, g, :, i] = 0; c[:, g, i] = C - 1; M[:, g, :, i] = V - 1
        for i in (4, S - 3):
            p[:, g, :, i] = 255; c[:, g, i] = C - 1; M[:, g, :, i] = 0
        for i in (5, S - 4):
            p[:, g, :, i] = 255; c[:, g, i] = C - 1; M[:, g, :8, i] = V - 1; M[:, g, 8:, i] = 0
    return pack(X, K, M, p, c)
def setup_inputs_corners(rng):
    X, K, M, p, c = parts(rng)
    c = rng.choice(np.array([0, 1, C // 2 - 1, C // 2, C - 2, C - 1]), (N, 8, S)); c[:, ::2] = (C - 1) * rng.integers(0, 2, (N, 4, S))
    X[:, 2] = rng.integers(0, 4, (N, 16, V)); p[:, 2] = rng.integers(0, 4, (N, 16, S))
    X[:, 5] = 8 * rng.integers(0, 32, (N, 16, V)); p[:, 5] = 8 * rng.integers(0, 32, (N, 16, S)); c[:, 5] = rng.integers(0, C, (N, S))
    K[:, 0] = rng.choice(np.array([0, 1, V - 1]), (N, 16, C)); M[:, 0, :, ::2] = 0; M[:, 0, :, 1::2] = V - 1
    M[:, 1] = Q * np.arange(S) + np.arange(16)[:, None] % Q
    M[:, 3] = np.take_along_axis(K[:, 3], c[:, 3][:, None, :], 2)
    K[:, 4] = K[:, 4, :1].copy(); M[:, 4, :, ::2] = M[:, 4, :1, ::2].copy()
    K[:, 6, 8:] = K[:, 6, :8].copy()
    kc = np.take_along_axis(K[:, 6, :1], c[:, 6][:, None, :], 2); near = np.take_along_axis(X[:, 6], kc, 2); p[:, 6, :, ::3] = near[:, :, ::3]
    p[:, 7] = np.take_along_axis(X[:, 7], M[:, 7, :1], 2)
    return pack(X, K, M, p, c)
def setup_inputs_crowd(rng):
    X, K, M, p, c = parts(rng); far1 = Q * B + 1
    for q in range(N):
        for g in range(7):
            o = rng.permutation(V)
            if g == 4:
                j = int(np.flatnonzero(o == far1)[0]); o[j] = o[B]; o[B] = far1
                X[q, g, :, far1] = 255 * (q & 1); X[q, g, 0, far1 + 1] = 0
                X[q, g, :, far1 + 2] = X[q, g, :, far1 + 1]; X[q, g, 0, far1 + 2] = S - 1
            own, far = o[:S], o[S:]
            M[q, g] = own[None, :]; p[q, g] = np.minimum(X[q, g][:, own] + rng.integers(0, 8, (16, S)), 255)
            two = rng.permutation(C)[:2]
            if g == 3: two = np.array([C - 1, C - 1])
            if g == 4:
                two = 1 + rng.permutation(C - 1)[:2]
                p[q, g, :, B] = X[q, g, :, far1]; K[q, g, :8, 0] = far1 + 1; K[q, g, 8:, 0] = far1 + 2
            if g in (2, 6):
                c[q, g] = two[rng.integers(0, 2, S)]; K[q, g, :, two[0]] = far[:16]; K[q, g, :, two[1]] = far[16:32]
            else:
                c[q, g] = two[0]; K[q, g, :, two[0]] = np.concatenate([far[:8], far[:8]])
            if g in (1, 5):
                i = 0 if g == 1 else S - 1
                M[q, g, :, i] = K[q, g, :, two[0]]
        full, near, home = [int(v) for v in rng.permutation(V)[:3]]
        X[q, 7, :, full] = 255; X[q, 7, :, near] = 255; X[q, 7, int(rng.integers(0, 16)), near] = 254; X[q, 7, :, home] = rng.integers(0, 8, 16)
        c[q, 7] = rng.integers(1, C // 2 - 1, S) + (C // 2) * rng.integers(0, 2, S)
        for i in (0, S - 2, S - 1): p[q, 7, :, i] = 0
        c[q, 7, 0] = 0; M[q, 7, :, 0] = home; K[q, 7, :8, 0] = full; K[q, 7, 8:, 0] = near
        c[q, 7, S - 1] = C - 1; M[q, 7, :, S - 1] = home; K[q, 7, :8, C - 1] = near; K[q, 7, 8:, C - 1] = full
        c[q, 7, S - 2] = C // 2; M[q, 7, :, S - 2] = near; M[q, 7, 0, S - 2] = full; K[q, 7, :, C // 2] = home
    return pack(X, K, M, p, c)
def check_inputs(d):
    bad = []
    for k, hi in (("tx", 255), ("kt", V - 1), ("ms", V - 1), ("z", 255), ("cp", C - 1)):
        v = np.asarray(d[k]).astype(np.float64)
        if not (np.min(v) >= 0 and np.max(v) <= hi): bad.append("range of " + k)
        elif np.any(v != np.floor(v)): bad.append("whole numbers of " + k)
    return bad
def mixed(p):
    return np.add.reduce(p * (2 * np.arange(16) + 1)[:, None], axis=-2)
def travel(v):
    w = v.reshape(v.shape[:-1] + (N, B)); o = np.empty_like(w)
    for h in range(N): o[..., (h + 1) % N, :] = np.roll(w[..., h, :], h, axis=0)
    return o.reshape(v.shape)
def reference(tx, kt, ms, z, cp):
    X = tx.astype(np.float32).astype(np.int64).reshape(N, 8, 16, V); K = kt.astype(np.int64).reshape(N, 8, 16, C); M = ms.astype(np.int64).reshape(N, 8, 16, S)
    p = z.astype(np.float32).astype(np.int64).reshape(N, 8, 16, S); c = np.stack([gentries(a) for a in cp]).astype(np.int64)
    A = np.zeros((N, 8), np.int64); row = np.arange(16)[:, None]; slot = np.arange(S)
    for rnd in range(RO):
        kc = np.take_along_axis(K, c[:, :, None, :], 3)
        x = np.take_along_axis(X, kc.reshape(N, 8, 1, 16 * S), 3).reshape(N, 8, 16, 16, S)
        m = np.take_along_axis(X, M.reshape(N, 8, 1, 16 * S), 3).reshape(N, 8, 16, 16, S)
        d = np.add.reduce(np.abs(x - p[:, :, :, None, :]), axis=2); dm = np.add.reduce(np.abs(m - p[:, :, :, None, :]), axis=2)
        s0, s1 = np.add.reduce(d[:, :, :8], axis=2), np.add.reduce(d[:, :, 8:], axis=2)
        t0, t1 = np.add.reduce(dm[:, :, :8], axis=2), np.add.reduce(dm[:, :, 8:], axis=2)
        b = (s1 < s0).astype(np.int64); e = np.argmin(dm, axis=2); a = np.argmax(d, axis=2)
        db = np.where(b[:, :, None, :] == 1, d[:, :, 8:], d[:, :, :8]); w = 8 * b + np.argmin(db, axis=2)
        trust = np.abs(s1 - s0) >= np.abs(t1 - t0) + 8 * A[:, :, None]
        contra = trust & (np.min(dm, axis=2) < np.min(db, axis=2)); agree = trust & ~contra
        me = np.take_along_axis(m, e[:, :, None, None, :], 3)[:, :, :, 0]; xw = np.take_along_axis(x, w[:, :, None, None, :], 3)[:, :, :, 0]
        name = np.take_along_axis(M, e[:, :, None, :], 2)[:, :, 0]; u = mixed(p)
        take = agree[:, :, None, :] & ((row >> 3) == b[:, :, None, :]) & (d < dm)
        fresh = ~trust[:, :, None, :] & (16 * dm > (t0 + t1)[:, :, None, :])
        M = np.where(take, kc, np.where(fresh, (kc + u[:, :, None, :] + 37 * row) & (V - 1), M))
        t = (2 * c + 1 - b) & (C - 1)
        for q in range(N):
            for g in range(8):
                i = np.flatnonzero(contra[q, g]); col, first = np.unique(t[q, g, i], return_index=True); i = i[first]
                K[q, g, a[q, g, i], col] = name[q, g, i]
        p = np.where(agree[:, :, None, :], (p + xw) >> 1, np.abs(p - me)); u = mixed(p)
        own = np.repeat((Q * slot + (u & (Q - 1)))[:, :, None, :], 16, axis=2)
        np.put_along_axis(X, own, (np.take_along_axis(X, own, 3) + p) >> 1, 3)
        if rnd < RO - 1:
            A = np.add.reduce(contra.astype(np.int64), axis=2)
            c = np.where(agree, (2 * c + b) & (C - 1), u & (C - 1))
            p = travel(p); M = travel(M); c = travel(c)
    return {"ytx": X.reshape(N, 128, V).astype(BF), "ykt": K.reshape(N, 128, C).astype(np.float32), "yms": M.reshape(N, 128, S).astype(np.float32), "yz": p.reshape(N, 128, S).astype(BF)}

@@ -1,0 +1,591 @@
+from concourse.bass import DstId, RemoteDMATransfer
+from concourse.mybir import AluOpType as ALU, ActivationFunctionType as ACT
+
+RO = 3
+ZW = 48
+BIG = float(2 ** 26)
+MAGIC = float(3 * 2 ** 22)
+MAGIC4 = float(3 * 2 ** 34)
+KBASE = -4081 * 4096
+OFF = 2047.5
+
+F, B, I, U = "float32", "bfloat16", "int32", "uint16"
+SCRATCH = {}
+
+
+def _sb(dtype, **kw):
+    for name, shape in kw.items():
+        SCRATCH[name] = ("sbuf", [128] + list(shape), dtype)
+
+
+_sb(B, X=[4096], xm=[4096], mn=[4096], E=[2048], UL=[2048], zb=[128], zT=[128], nzb=[128],
+    Ib=[128], I37=[128], Inh=[128], Inq=[128], Uw=[128], Kcol=[128], ones=[128], ZX=[512], ZM=[384],
+    WR=[4, 32], WN=[4, 32], masks=[256], eq=[16, 128], kap=[8], ny=[128], y2=[128], ohA=[128])
+_sb(F, Kw=[640], If=[128], nIf=[128], I16=[128], BD=[128], KCX=[128], KCM=[128], D0S=[256], D8=[128], D16=[128],
+    DA=[128], DM=[256], TRI=[128], tabA=[16], tabN=[640], pm=[8], SL=[8], S32=[8], D512=[8],
+    lz1=[8 * ZW], lz2=[8 * ZW], sz0=[8 * ZW], sz1=[8 * ZW],
+    Mf=[128], Mn=[128], kc=[128], DD=[256], cmpv=[256], mmin=[128], msum=[256], aTD=[8], thr=[8],
+    thrT=[16], A8=[8], rs=[256], xmin=[128], amax=[128], q=[16], qm=[8], rmin=[8], nrm=[8], PSI=[24], L1=[128],
+    L2=[256], Wm=[256], Wz=[256], ag=[8], lo=[8], s1=[8], cu=[8], yy=[128],
+    w=[8], nk=[8], tL=[8], old=[128], oM=[128], o1=[8], cnt=[32])
+_sb(I, kti=[512], msi=[128], tmpi=[256], tmpj=[256], ksi=[8], KS=[8], seli=[8],
+    bi=[8], c2m=[8], ci=[8], cj=[8], ui=[8], uj=[8], vi=[8], xa=[128], xb=[128], ai=[8], P2=[16])
+_sb(U, Mu=[128], kcu=[128], cu16=[8], EX=[16], EX3=[16], selu=[8],
+    szu=[8], eu=[8], au=[8], tu=[8], vu=[8], ou=[16])
+BANKS = ("ZE0", "ZE1", "ZE2", "ZE3", "PX", "PM", "PA", "PB")
+for _n in BANKS:
+    SCRATCH[_n] = ("psum", [128, 512], F)
+
+SEMAPHORES = ["cV", "cS", "cP", "cG", "ldX", "ldK", "ldM", "ldZ", "ldC", "stX", "stX2", "stK", "stM", "stZ",
+              "arZ0", "arZ1", "sent"]
+
+CH_M = [(0, 32), (32, 32), (64, 32), (96, 32)]
+CH_X = [(0, 32), (32, 32), (64, 32), (96, 16), (112, 16)]
+G_M = [[("V", 0, 32), ("S", 32, 32), ("S", 64, 32), ("S", 96, 32)]] * RO
+G_X = [[("S", 0, 32), ("S", 32, 32), ("S", 64, 32), ("S", 96, 16), ("S", 112, 16)]] * RO
+MM_X = [(0, 96), (96, 32)]
+CY, GAT, SCA, PEC, WAKE, FIX, T_DMA, BW = 1.04e-3, 1.56, 3.8, 0.53e-3, 0.06, 0.03, 2.2, 250e3
+T_REM, T_FIRST = 4.2, 1.5
+KC_ON, ZB_ON = "S", "S"
+BOOST = {"send": 6.0}
+SEED, TRIES, HEAT = 1, 2000, 0.0
+PLANS = {}
+
+
+def plan(ops):
+    n = len(ops)
+    pred = [set() for _ in ops]
+    soft = set()
+    writer, readers = {}, {}
+    for i, o in enumerate(ops):
+        for r in o["rd"] + o["wr"]:
+            if r in writer:
+                pred[i].add(writer[r])
+                if r[0] == "~":
+                    soft.add((writer[r], i))
+        for w in o["wr"]:
+            pred[i].update(readers.get(w, []))
+        for r in o["rd"]:
+            readers.setdefault(r, []).append(i)
+        for w in o["wr"]:
+            writer[w] = i
+            readers[w] = []
+        pred[i].discard(i)
+    succ = [[] for _ in ops]
+    for i in range(n):
+        for p in pred[i]:
+            succ[p].append(i)
+
+    def gap(p, i):
+        if (p, i) in soft:
+            return -ops[p]["lat"]
+        return 0.0 if ops[p]["e"] == "P" and ops[i]["e"] == "P" else WAKE
+    prio = [0.0] * n
+    for i in range(n - 1, -1, -1):
+        prio[i] = ops[i]["hold"] + ops[i]["lat"] + max([prio[s] + gap(i, s) for s in succ[i]] + [0.0])
+    eng = [o["e"] for o in ops]
+    hold = [o["hold"] for o in ops]
+    lat = [o["lat"] for o in ops]
+    rb = [[r for r in o["rd"] if r in BANKS] for o in ops]
+    ab = [[r for r in o["rd"] + o["wr"] if r in BANKS] for o in ops]
+    sg = [[(s, gap(i, s)) for s in succ[i]] for i in range(n)]
+
+    def schedule(prio):
+        left = [len(p) for p in pred]
+        ready = {e: [] for e in "VSPGY"}
+        for i in range(n):
+            if not left[i]:
+                ready[eng[i]].append(i)
+        at = [0.0] * n
+        free = {e: 0.0 for e in ready}
+        bank = {b: ("", 0.0) for b in BANKS}
+        out, end = [], 0.0
+        for _ in range(n):
+            t0, e0, st0 = 1e9, None, None
+            for e, rl in ready.items():
+                if not rl or free[e] >= t0:
+                    continue
+                st = []
+                for i in rl:
+                    t = at[i] if at[i] > free[e] else free[e]
+                    for r in rb[i]:
+                        if bank[r][0] != e and bank[r][1] + WAKE > t:
+                            t = bank[r][1] + WAKE
+                    st.append(t)
+                if min(st) < t0:
+                    t0, e0, st0 = min(st), e, st
+            rl = ready[e0]
+            top = max(range(len(rl)), key=lambda j: prio[rl[j]])
+            j = max((j for j in range(len(rl)) if st0[j] <= t0 + 0.02), key=lambda j: prio[rl[j]])
+            if j != top and st0[top] - st0[j] < 0.4 * hold[rl[j]]:
+                j = top
+            i = rl.pop(j)
+            free[e0] = st0[j] + hold[i]
+            fin = free[e0] + lat[i]
+            end = max(end, fin)
+            for r in ab[i]:
+                bank[r] = (e0, fin)
+            out.append(i)
+            for s, gp in sg[i]:
+                if fin + gp > at[s]:
+                    at[s] = fin + gp
+                left[s] -= 1
+                if not left[s]:
+                    ready[eng[s]].append(s)
+        return end, out
+
+    for kind, boost in BOOST.items():
+        todo = [i for i, o in enumerate(ops) if kind in o["wr"] or (kind == "send" and o["remote"])]
+        seen = set(todo)
+        while todo:
+            i = todo.pop()
+            for p in pred[i]:
+                if p not in seen and "rs" not in ops[i]["wr"] and ops[p]["round"] == ops[i]["round"] and ops[p]["tail"]:
+                    seen.add(p)
+                    todo.append(p)
+        for i in seen:
+            prio[i] += boost
+    best, out = schedule(prio)
+    seed = [SEED]
+
+    def rnd():
+        seed[0] = (seed[0] * 1103515245 + 12345) % 2 ** 31
+        return seed[0] / 2 ** 31
+    cur = best
+    movable = [i for i in range(n) if eng[i] != "P"]
+    for it in range(TRIES):
+        chain = {movable[int(rnd() * len(movable))]}
+        link = pred if rnd() < 0.7 else succ
+        for _d in range(int(rnd() * 10)):
+            chain |= {p for i in chain for p in link[i] if ops[p]["round"] == ops[i]["round"] and rnd() < 0.8}
+        d = (6 * rnd() - 3) * (1 if rnd() < 0.7 else 0.3)
+        trial = [p + d if i in chain else p for i, p in enumerate(prio)]
+        end, o2 = schedule(trial)
+        if end <= cur + HEAT * (1 - it / TRIES) * rnd() ** 3:
+            cur, prio = end, trial
+            if end < best:
+                best, out = end, o2
+    PLANS["t"] = best
+    return out
+
+
+def rank_program(g, core, T, topo):
+    rank = T.rank_of(core)
+    if rank is None:
+        return
+    N = len(T.cores)
+    Q = {"V": g.vector, "S": g.scalar, "P": g.tensor, "G": g, "Y": g.sync}
+    SEM = {"V": "cV", "S": "cS", "P": "cP", "G": "cG"}
+    V, S, P = g.vector, g.scalar, g.tensor
+    ops = []
+    where = [-1, False]
+
+    def op(e, fn, rd, wr, hold, lat=0.0, sem=None, inc=1, remote=False):
+        ops.append(dict(round=where[0], tail=where[1], e=e, fn=fn, rd=list(rd), wr=list(wr), hold=hold, lat=lat, sem=sem or SEM[e], inc=inc, remote=remote))
+
+    def cost(n, k):
+        if k == "g":
+            return 0.055 + n * GAT * CY
+        if k == "s":
+            return 0.05 + n * SCA * CY
+        return FIX + max(64, n * {"": 1, "h": 0.5, "2": 2}[k]) * CY
+
+    def dma(e, sem, out, in_, rd, wr, nbytes):
+        op(e, lambda: Q[e].dma_start(out, in_), rd, wr, 0.05, T_DMA + nbytes / BW, sem, 16)
+
+    def cp(out, in_, rd, wr, n=8, k=""):
+        op("V", lambda: V.tensor_copy(out, in_), rd, wr, cost(n, k))
+
+    def tt(out, a, b, o, rd, wr, n=8, k="2"):
+        op("V", lambda: V.tensor_tensor(out, a, b, o), rd, wr, cost(n, k))
+
+    def ts(out, a, s1, s2, o0, o1, rd, wr, n=8, k=""):
+        if s2 is None:
+            op("V", lambda: V.tensor_scalar(out, a, s1, None, o0), rd, wr, cost(n, k))
+        else:
+            op("V", lambda: V.tensor_scalar(out, a, s1, s2, o0, o1), rd, wr, cost(n, k))
+
+    def scan(out, d0, d1, o0, o1, rd, wr, n):
+        op("V", lambda: V.tensor_tensor_scan(out, d0, d1, 0.0, o0, o1), rd, wr, cost(n, ""))
+
+    def ms(out, val, wr, n=8, k=""):
+        op("V", lambda: V.memset(out, val), [], wr, cost(n, k))
+
+    def act(out, in_, rd, wr, n=8, k="", func=ACT.Identity, bias=0.0, scale=1.0):
+        op("S", lambda: S.activation(out, in_, func, bias=bias, scale=scale), rd, wr, cost(n, k))
+
+    def mm(out, l, r, st, sp, rd, wr, n=128, f32=False, m=128):
+        op("P", lambda: P.matmul(out, l, r, st, sp), rd, wr, max(min(64, m), n) * PEC * (4 if f32 else 1))
+
+    def iota(out, pat, base, cm, wr, n, fl=False):
+        if fl:
+            op("G", lambda: g.iota(out, pat, base, cm, allow_small_or_imprecise_dtypes=True), [], wr, 0.13 + 2 * n * CY)
+        else:
+            op("G", lambda: g.iota(out, pat, base, cm), [], wr, 0.13 + 2 * n * CY)
+
+    dma("S", "ldZ", T.zb[:], T.z[:], [], ["zb", "~S"], 2 ** 15)
+    dma("S", "ldM", T.msi[:], T.ms[:], [], ["msi", "~S"], 2 ** 16)
+    dma("S", "ldC", T.cj[:], T.cp[:], [], ["cj", "~S"], 2 ** 12)
+    dma("Y", "ldX", T.X[:], T.tx[:], ["~S"], ["X", "~Y"], 2 ** 20)
+    dma("Y", "ldK", T.kti[:], T.kt[:], [], ["kti", "~Y"], 2 ** 20 + 2 ** 18)
+
+    iota(T.tmpi[:, 0:128], [[-1, 128]], 0, 1, ["tmpi", "~G"], 128)
+    iota(T.tmpj[:, 0:128], [[-16, 8], [0, 16]], 0, 1, ["tmpj", "~G"], 128)
+    iota(T.ui[:, 0:1], [[0, 1]], 0, 1, ["ui", "~G"], 1)
+    iota(T.tmpj[:, 160:176], [[1, 16]], 0, 0, ["J16", "~G"], 16)
+    iota(T.tmpj[:, 128:144], [[-1, 16]], 30, 0, ["tmpj2", "~G"], 16)
+    iota(T.Wm[:], [[0, 16], [1, 16]], 0, 0, ["Wm", "~G"], 256, True)
+    iota(T.KCM[:], [[0, 8], [1, 16]], KBASE + 2048, 16, ["KCM", "~G"], 128, True)
+    iota(T.KCX[:], [[0, 8], [1, 16]], KBASE, 16, ["KCX", "~G"], 128, True)
+    iota(T.Kw[:, 512:640], [[0, 128]], 0, 0, ["Kwd", "~G"], 128, True)
+    iota(T.sz0[:], [[0, 8 * ZW]], 0, 0, ["sz0", "~G"], 8 * ZW, True)
+    iota(T.sz1[:], [[0, 8 * ZW]], 0, 0, ["sz1", "~G"], 8 * ZW, True)
+    iota(T.TRI[:], [[1, 128]], 0, 0, ["TRI", "~G"], 128, True)
+    iota(T.tabN[:], [[256, 640]], 0, 0, ["tabN", "~G"], 640, True)
+    ms(T.UL[:], 0.0, ["UL"], 2048, "h")
+    ms(T.D0S[:], 1.0, ["D0S"], 256)
+    ms(T.D8[:], 0.0, ["D8"], 128)
+    ms(T.D16[:], 0.0, ["D16"], 128)
+    ms(T.DA[:], 2.0, ["DA"], 128)
+    J16 = T.tmpj[:, 160:176]
+    ms(T.ZX[:, 128:384], 0.0, ["ZX0"], 256, "h")
+    ms(T.ZM[:, 128:256], 0.0, ["ZM0"], 128, "h")
+    ms(T.ones[:], 1.0, ["ones"], 128, "h")
+    ms(T.A8[:], 0.0, ["A8"])
+    ms(T.WR[:, 2:4, 24:32], 0.0, ["WR0"])
+    ms(T.D0S[:, 0:256:16], 0.0, ["D0S"])
+    ms(T.D8[:, 0:128:8], BIG, ["D8"])
+    ms(T.D16[:, 0:128:16], BIG, ["D16"])
+    ms(T.DA[:, 0:128:16], -BIG, ["DA"])
+    ts(T.Ib[:], T.tmpi[:, 0:128], 0.0, None, ALU.is_equal, None, ["tmpi"], ["Ib"], 128)
+    ts(T.tmpi[:, 128:256], T.tmpj[:, 0:128], 4, None, ALU.arith_shift_right, None, ["tmpj"], ["tmpi2"], 128)
+    ts(T.uj[:, 0:1], T.ui[:, 0:1], 15, None, ALU.bitwise_and, None, ["ui"], ["uj"])
+    ts(T.BD[:], T.tmpi[:, 128:256], 0.0, None, ALU.is_equal, None, ["tmpi2"], ["BD"], 128)
+    cp(T.pm[:, 0:1], T.uj[:, 0:1], ["uj"], ["pm"])
+    for k in range(16):
+        ts(T.E[:, k:2048:16], T.Ib[:], 0.5, None, ALU.mult, None, ["Ib"], ["E%d" % k], 128, "h")
+    Eall = ["E%d" % k for k in range(16)]
+    Ih = T.E[:, 0:2048:16]
+    G8 = T.BD[:, 0:128:16]
+    for name, sc in (("If", 1.0), ("nIf", -1.0), ("I16", 1.0 / 16), ("I37", 37.0), ("Inh", -0.5), ("Inq", -0.25)):
+        act(T[name][:], T.Ib[:], ["Ib"], [name], 128, scale=sc)
+    act(T.ZX[:, 0:128], T.BD[:], ["BD"], ["ZX1"], 128, scale=4096.0)
+    act(T.ZX[:, 384:512], T.BD[:], ["BD"], ["ZX2"], 128, scale=-1.0)
+    act(T.ZM[:, 0:128], T.BD[:], ["BD"], ["ZM1"], 128, scale=4096.0)
+    act(T.ZM[:, 256:384], T.BD[:], ["BD"], ["ZM2"], 128)
+    act(T.WR[:, 0, 0:8], G8, ["BD"], ["Wa"], scale=8192.0)
+    act(T.WR[:, 0, 8:24:2], G8, ["BD"], ["Wb"], scale=2 * BIG)
+    act(T.WR[:, 0, 9:24:2], G8, ["BD"], ["Wc"], scale=-2 * BIG)
+    act(T.WR[:, 0, 24:32], G8, ["BD"], ["Wd"], scale=-2.0)
+    act(T.WR[:, 1, :], T.WR[:, 0, :], ["Wa", "Wb", "Wc", "Wd"], ["We"])
+    act(T.WR[:, 1, 8:24], T.WR[:, 0, 8:24], ["Wb", "Wc"], ["We"], scale=-1.0)
+    act(T.WR[:, 2:4, 0:8], T.WR[:, 0:2, 0:8], ["Wa", "We"], ["Wf"])
+    act(T.WR[:, 2, 8:16], G8, ["BD"], ["Wg"], scale=-2.0)
+    act(T.WR[:, 3, 8:16], G8, ["BD"], ["Wh"], scale=2.0)
+    act(T.WR[:, 2:4, 16:24], T.WR[:, 0:2, 24:32], ["Wd", "We"], ["Wi"], scale=-1.0)
+    WRall = ["W" + x for x in "abcdefghi"] + ["WR0"]
+    act(T.WN[:], T.WR[:], WRall, ["WN"], 128, scale=-2.0)
+    pm, pm2, pm3 = T.pm[:, 0:1], T.pm[:, 1:2], T.pm[:, 2:3]
+    ts(T.DM[:], T.Wm[:], pm, None, ALU.is_equal, None, ["Wm", "pm"], ["DM"], 256)
+    ts(pm2, pm, 2.0, 1.0, ALU.mult, ALU.add, ["pm"], ["pm2"])
+    ts(pm3, pm, 8.0, None, ALU.is_ge, None, ["pm"], ["pm3"])
+    act(T.Kcol[:], T.ones[:], ["ones", "pm"], ["Kcol"], 128, scale=pm)
+    ts(T.SL[:], T.tmpj[:, 160:168], 16.0, pm, ALU.mult, ALU.add, ["J16", "pm"], ["SL"])
+    cp(T.EX[:], J16, ["J16"], ["EX"])
+    act(T.Uw[:], T.BD[:], ["BD", "pm2"], ["Uw"], 128, scale=pm2)
+    act(T.S32[:], T.SL[:], ["SL"], ["S32"], scale=32.0)
+    act(T.D512[:], T.SL[:], ["SL"], ["D512"], bias=512.0)
+    ts(T.EX3[:, 0:8], T.tmpj[:, 160:168], 2.0, pm3, ALU.mult, ALU.add, ["J16", "pm3"], ["EX3a"])
+    ts(T.EX3[:, 8:16], T.tmpj[:, 168:176], 8.0, None, ALU.add, None, ["J16"], ["EX3b"])
+    ts(T.tmpj[:, 144:160], T.tmpj[:, 128:144], 15, None, ALU.bitwise_and, None, ["tmpj2"], ["tmpj3"])
+    ts(T.tabA[:], T.tmpj[:, 144:160], pm, None, ALU.is_equal, None, ["tmpj3", "pm"], ["tabA"])
+    for gi in range(8):
+        act(T.UL[:, 16 * gi:16 * gi + 129 * 15 + 1:129], T.Uw[:, 16 * gi:16 * gi + 16], ["Uw", "UL"], ["UL%d" % gi])
+    ULall = ["UL%d" % gi for gi in range(8)]
+    cp(T.Mu[:], T.msi[:], ["msi"], ["Mu"], 128)
+    ts(T.Mf[:], T.msi[:], -OFF, None, ALU.add, None, ["msi"], ["Mf"], 128)
+    cp(T.Kw[:, 0:512], T.kti[:], ["kti", "Kwd"], ["Kw"], 512)
+
+    peers = []
+    for h in range(1, N):
+        dst = T.cores[(rank + h) % N]
+        rid, pid, _ = topo.addr(dst)
+        eng = topo.engines(core, dst)
+        per = len(eng) // N
+        peers.append((DstId(rid=rid, pnc=pid), sum(1 << e for e in eng[per * (h - 1):per * h]), per, h))
+    arrive = sum(p[2] for p in peers)
+
+    def send(src_of, dst_of, sem, rd, wr):
+        op("G", lambda: g.remote_dma_fused(
+            [RemoteDMATransfer(dst_ids=[d], dma_engine_mask=m, remote_sem=T.sem[sem], src=src_of(h),
+                               dst=dst_of((h + 1) % N)) for d, m, _, h in peers], local_sem=T.sem.sent),
+           rd, wr + ["~G"], 0.5 + (T_FIRST if sem == "arZ0" else 0), T_REM - 0.5,
+           sem, arrive, True)
+
+    def tags(t, s0, n):
+        return ["%s%d" % (t, b) for b in range(s0 // 16, (s0 + n) // 16)]
+
+    def gather(e, t, lst, lname, s0, n):
+        base = 2048 if t == "m" else 0
+        out = T.xm[:, base + 16 * s0:base + 16 * (s0 + n)]
+        src = T.X[:].indirect(lst[:, s0:s0 + n])
+        if e == "S":
+            act(out, src, ["X"] + lname, tags(t, s0, n) + ["~g"], 16 * n, "g", scale=0.5)
+        else:
+            ts(out, src, 0.5, None, ALU.mult, None, ["X"] + lname, tags(t, s0, n), 16 * n, "g")
+
+    def mins(t, s0, n):
+        base = 2048 if t == "m" else 0
+        bank = "ZE%d" % (s0 // 32)
+        o = 16 * (s0 % 32)
+        tt(T.mn[:, base + 16 * s0:base + 16 * (s0 + n)], T.xm[:, base + 16 * s0:base + 16 * (s0 + n)],
+           T[bank][:, o:o + 16 * n], ALU.min, tags(t, s0, n) + [bank], tags("n" + t, s0, n) + ["~n"], 16 * n, "")
+
+    XM, XX = tags("m", 0, 128), tags("x", 0, 128)
+
+    for r in range(RO):
+        last = r == RO - 1
+        where[0], where[1] = r, False
+        lz, sz = T["lz%d" % max(r, 1)], T["sz%d" % min(r, 1)]
+        nlz = ["lz%d" % r, "lz%dr" % r]
+        Mf, nMf = (lz[:, 0:384:3], nlz) if r else (T.Mf[:], ["Mf"])
+        if r:
+            ts(T.Mu[:], Mf, OFF, None, ALU.add, None, nMf, ["Mu"], 128)
+            if ZB_ON == "S":
+                act(T.zb[:], lz[:, 1:384:3], nlz, ["zb"], 128)
+            else:
+                cp(T.zb[:], lz[:, 1:384:3], nlz, ["zb"], 128)
+        for e, s0, n in G_M[r]:
+            gather(e, "m", T.Mu, ["Mu"], s0, n)
+        mm(T.PA[:, 0:128], T.zb[:], T.Ib[:], True, True, ["zb", "Ib"], ["PA"])
+        cp(T.zT[:], T.PA[:, 0:128], ["PA"], ["zT"], 128)
+        if r:
+            for il in range(16):
+                mm(T.PA[:, 384:392], T.UL[:, 128 * il:128 * il + 128], T.zb[:, il:128:16], il == 0, il == 15,
+                   ULall + ["zb"], ["PA"], 8)
+            tt(T.cu[:], T.PA[:, 384:392], lz[:, 5:384:ZW], ALU.mult, ["PA"] + nlz, ["cu"])
+            tt(T.ci[:], T.cu[:], lz[:, 2:384:ZW], ALU.add, ["cu"] + nlz, ["ci"])
+            ts(T.cj[:], T.ci[:], 511, None, ALU.bitwise_and, None, ["ci"], ["cj"])
+        for b4 in range(4):
+            mm(T["ZE%d" % b4][:], T.zT[:], T.E[:, 512 * b4:512 * b4 + 512], True, True, ["zT"] + Eall, ["ZE%d" % b4], 512)
+        cp(T.cu16[:], T.cj[:], ["cj"], ["cu16"])
+        if KC_ON == "S":
+            act(T.kc[:], T.Kw[:].indirect(T.cu16[:]), ["Kw", "cu16"], ["kc"], 128, "g", bias=-OFF)
+        else:
+            ts(T.kc[:], T.Kw[:].indirect(T.cu16[:]), -OFF, None, ALU.add, None, ["Kw", "cu16"], ["kc"], 128, "g")
+        ts(T.kcu[:], T.kc[:], OFF, None, ALU.add, None, ["kc"], ["kcu"], 128)
+        for e, s0, n in G_X[r]:
+            gather(e, "x", T.kcu, ["kcu"], s0, n)
+        ts(T.ci[:], T.cj[:], 2.0, None, ALU.mult, None, ["cj"], ["ci"])
+        ts(T.c2m[:], T.ci[:], 511, None, ALU.bitwise_and, None, ["ci"], ["c2m"])
+        for lo, hi in ((0, 128), (256, 384)):
+            mm(T.PA[:, lo:hi], T.Uw[:], T.zb[:], True, False, ["Uw", "zb"], ["PA"])
+            mm(T.PA[:, lo:hi], T.I37[:], T.Kcol[:], False, False, ["I37", "Kcol"], ["PA"])
+            mm(T.PA[:, lo:hi], T.If[:], T.kc[:], False, not lo, ["If", "kc"], ["PA"], 128, True)
+            if not lo:
+                act(T.yy[:], T.PA[:, 0:128], ["PA"], ["yy"], 128, bias=MAGIC4)
+                act(T.ny[:], T.yy[:], ["yy"], ["ny"], 128, bias=MAGIC4, scale=-1.0)
+                mm(T.PA[:, 128:256], T.If[:], T.kc[:], True, False, ["If", "kc"], ["PA"], 128, True)
+                mm(T.PA[:, 128:256], T.nIf[:], Mf, False, True, ["nIf"] + nMf, ["PA"], 128, True)
+        mm(T.PA[:, 256:384], T.nIf[:], Mf, False, False, ["nIf"] + nMf, ["PA"], 128, True)
+        mm(T.PA[:, 256:384], T.Ib[:], T.ny[:], False, True, ["Ib", "ny"], ["PA"])
+        act(T.DD[:], T.PA[:, 128:384], ["PA"], ["DD"], 256)
+        mm(T.PM[:, 0:384], T.zb[:], T.ZM[:], True, False, ["zb", "ZM0", "ZM1", "ZM2"], ["PM"], 384)
+        mm(T.PM[:, 0:128], T.If[:], T.KCM[:], False, False, ["If", "KCM"], ["PM"], 128, True)
+        for s0, n in CH_M:
+            mins("m", s0, n)
+        for k in range(16):
+            mm(T.PM[:, k:384:16], T.xm[:, 2048 + k:4096:16], T.WR[:, 2 + k // 8, 0:24], False, False, XM + WRall, ["PM"], 24)
+        for k in range(16):
+            mm(T.PM[:, k:384:16], T.mn[:, 2048 + k:4096:16], T.WN[:, 2 + k // 8, 0:24], False, k == 15,
+               ["n" + x for x in XM] + ["WN"], ["PM"], 24)
+        scan(T.msum[:], T.D0S[:], T.PM[:, 128:384], ALU.mult, ALU.add, ["D0S", "PM"], ["msum"], 256)
+        scan(T.mmin[:], T.D16[:], T.PM[:, 0:128], ALU.add, ALU.min, ["D16", "PM"], ["mmin"], 128)
+        act(T.cmpv[:, 128:256], T.PM[:, 256:384], ["PM"], ["cmpb"], 128, scale=16.0)
+        TD, TS, mk = T.msum[:, 15:128:16], T.msum[:, 143:256:16], T.mmin[:, 15:128:16]
+        act(T.aTD[:], TD, ["msum"], ["aTD"], func=ACT.Abs)
+        tt(T.thr[:], T.aTD[:], T.A8[:], ALU.add, ["aTD", "A8"], ["thr"])
+        act(T.thrT[:, 0:16:2], T.thr[:], ["thr"], ["thrTa"], bias=-0.5 * BIG, scale=BIG)
+        act(T.thrT[:, 1:16:2], T.thr[:], ["thr"], ["thrTb"], func=ACT.Relu, bias=-BIG, scale=BIG)
+        mm(T.PX[:], T.zb[:], T.ZX[:], True, False, ["zb", "ZX0", "ZX1", "ZX2"], ["PX"], 512)
+        mm(T.PX[:, 0:128], T.If[:], T.KCX[:], False, False, ["If", "KCX"], ["PX"], 128, True)
+        mm(T.PX[:, 384:512], T.I16[:], T.cmpv[:, 128:256], False, False, ["I16", "cmpb"], ["PX"], 128, True)
+        mm(T.PX[:, 128:384:16], T.If[:], T.thrT[:], False, False, ["If", "thrTa", "thrTb"], ["PX"], 16, True)
+        for s0, n in CH_X:
+            mins("x", s0, n)
+        for s0, n in MM_X:
+            for buf, wt, t, dep in ((T.xm, T.WR, "x", WRall), (T.mn, T.WN, "nx", ["WN"])):
+                for k in range(15 if t == "nx" else 16):
+                    mm(T.PX[s0:s0 + n, k:512:16], buf[:, 16 * s0 + k:16 * (s0 + n):16], wt[:, k // 8, :], False,
+                       False, tags(t, s0, n) + dep, ["PX"], 32, False, n)
+        mm(T.PX[:, 15:512:16], T.mn[:, 15:2048:16], T.WN[:, 1, :], False, True, tags("nx", 0, 128) + ["WN"], ["PX"], 32)
+        where[1] = True
+        scan(T.rs[:], T.D0S[:], T.PX[:, 128:384], ALU.mult, ALU.add, ["D0S", "PX"], ["rs"], 256)
+        scan(T.xmin[:], T.D8[:], T.PX[:, 0:128], ALU.add, ALU.min, ["D8", "PX"], ["xmin"], 128)
+        act(T.cmpv[:, 0:128], T.PX[:, 384:512], ["PX"], ["cmpa"], 128)
+        R, R0, R1 = T.rs[:, 15:256:16], T.rs[:, 15:256:32], T.rs[:, 31:256:32]
+        tt(T.q[:], T.xmin[:, 7:128:8], R, ALU.max, ["xmin", "rs"], ["q"], 16)
+        tt(T.qm[:], T.q[:, 0:16:2], T.q[:, 1:16:2], ALU.min, ["q"], ["qm"])
+        tt(T.ksi[:], T.qm[:], mk, ALU.min, ["qm", "mmin"], ["ksi"])
+        ts(T.KS[:], T.ksi[:], 4095, None, ALU.bitwise_and, None, ["ksi"], ["KS"])
+        tt(T.L1[:], T.KS[:].indirect(T.EX[:, 0:8]), T.DM[:, 0:128], ALU.mult, ["KS", "EX", "DM"], ["L1"], 128, "g")
+        mm(T.PB[:, 0:8], T.L1[:], G8, True, True, ["L1", "BD"], ["PB"], 8, True)
+        cp(T.selu[:], T.PB[:, 0:8], ["PB"], ["selu"])
+        ts(T.szu[:], T.PB[:, 0:8], 1.0 / 16, -15.0 / 32, ALU.mult, ALU.add, ["PB"], ["szu"])
+        cp(T.seli[:], T.PB[:, 0:8], ["PB"], ["seli"])
+        tt(T.rmin[:], R0, R1, ALU.min, ["rs"], ["rmin"])
+        act(T.PSI[:, 0:16], R, ["rs"], ["PSIa"], func=ACT.Relu, bias=BIG / 4)
+        act(T.nrm[:], T.rmin[:], ["rmin"], ["nrm"], func=ACT.Relu, scale=-1.0)
+        tt(T.PSI[:, 16:24], T.nrm[:], TS, ALU.max, ["nrm", "msum"], ["PSIb"])
+        tt(T.masks[:], T.PSI[:].indirect(T.EX3[:]), T.cmpv[:], ALU.is_lt,
+           ["PSIa", "PSIb", "EX3a", "EX3b", "cmpa", "cmpb"], ["masks"], 256, "g")
+        mm(T.ZE2[:, 0:128], T.masks[:, 0:128], T.Ib[:], True, True, ["masks", "Ib"], ["ZE2"])
+        mm(T.ZE2[:, 128:256], T.masks[:, 128:256], T.Ib[:], True, True, ["masks", "Ib"], ["ZE2"])
+        tt(T.Wm[:], T.ZE2[:, 0:256], T.DD[:], ALU.mult, ["ZE2", "DD"], ["Wm"], 256, "")
+        if last:
+            tt(T.Mn[:], T.Wm[:].indirect(T.szu[:]), Mf, ALU.add, ["Wm", "szu"] + nMf, ["Mn"], 128, "g")
+        else:
+            tt(sz[:, 0:384:3], T.Wm[:].indirect(T.szu[:]), Mf, ALU.add, ["Wm", "szu", "sz%d" % r] + nMf,
+               ["sz%dd" % r], 128, "g")
+        mm(T.ZE0[:, 0:128], Ih, T.zb[:], True, False, ["E0", "zb"], ["ZE0"])
+        mm(T.ZE0[:, 0:128], T.Inq[:], T.ones[:], False, False, ["Inq", "ones"], ["ZE0"])
+        mm(T.ZE1[:, 0:128], T.Inh[:], T.zb[:], True, False, ["Inh", "zb"], ["ZE1"])
+        act(T.y2[:], T.xm[:].indirect(T.selu[:]), XM + XX + ["selu"], ["y2"], 128, "g")
+        mm(T.ZE0[:, 0:128], T.Ib[:], T.y2[:], False, True, ["Ib", "y2"], ["ZE0"])
+        mm(T.ZE1[:, 0:128], T.Ib[:], T.y2[:], False, True, ["Ib", "y2"], ["ZE1"])
+        ts(T.Wz[:, 0:128], T.ZE0[:, 0:128], MAGIC, MAGIC, ALU.add, ALU.subtract, ["ZE0"], ["Wza"], 128)
+        act(T.Wz[:, 128:256], T.ZE1[:, 0:128], ["ZE1"], ["Wzb"], 128, func=ACT.Abs, scale=2.0)
+        act(T.nzb[:], T.Wz[:].indirect(T.szu[:]), ["Wza", "Wzb", "szu"], ["nzb"], 128, "g")
+        for il in range(16):
+            mm(T.PB[:, 8:16], T.UL[:, 128 * il:128 * il + 128], T.nzb[:, il:128:16], il == 0, il == 15,
+               ULall + ["nzb"], ["PB"], 8)
+        cp(T.ui[:], T.PB[:, 8:16], ["PB"], ["ui"])
+        if last:
+            act(T.yy[:], T.Mn[:], ["Mn"], ["yy"], 128, bias=OFF)
+            dma("Y", "stZ", T.yz[:], T.nzb[:], ["nzb"], [], 2 ** 15)
+            dma("Y", "stM", T.yms[:], T.yy[:], ["yy"], [], 2 ** 16)
+        else:
+            lz2 = T["lz%d" % (r + 1)]
+            act(sz[:, 1:384:3], T.Wz[:].indirect(T.szu[:]), ["Wza", "Wzb", "szu", "sz%d" % r], ["sz%da" % r], 128, "g")
+            ts(T.bi[:], T.seli[:], 3, 1, ALU.arith_shift_right, ALU.bitwise_and, ["seli"], ["bi"])
+            ts(T.ag[:], T.seli[:], 2048.0, None, ALU.is_lt, None, ["seli"], ["ag"])
+            ts(sz[:, 5:384:ZW], T.seli[:], 2048.0, None, ALU.is_ge, None, ["seli", "sz%d" % r], ["sz%dc" % r])
+            tt(T.s1[:], T.bi[:], T.c2m[:], ALU.add, ["bi", "c2m"], ["s1"])
+            tt(sz[:, 2:384:ZW], T.s1[:], T.ag[:], ALU.mult, ["s1", "ag", "sz%d" % r], ["sz%db" % r])
+            nsz = ["sz%d%s" % (r, x) for x in "abcd"]
+            send(lambda h, a=sz: a[:, ZW * h:ZW * h + ZW], lambda s, a=lz2: a[:, ZW * s:ZW * s + ZW], "arZ%d" % r, nsz,
+                 ["lz%dr" % (r + 1)])
+            act(lz2[:, ZW:2 * ZW], sz[:, 0:ZW], nsz, ["lz%d" % (r + 1)], ZW)
+        ts(T.uj[:], T.ui[:], 31, None, ALU.bitwise_and, None, ["ui"], ["uj"])
+        tt(T.vi[:], T.uj[:], T.S32[:], ALU.add, ["uj", "S32"], ["vi"])
+        cp(T.vu[:], T.vi[:], ["vi"], ["vu"])
+        tt(T.xa[:], T.X[:].indirect(T.vu[:]), T.nzb[:], ALU.add, ["X", "vu", "nzb"], ["xa"], 128, "g")
+        ts(T.xb[:], T.xa[:], 1, None, ALU.arith_shift_right, None, ["xa"], ["xb"], 128)
+        cp(T.X[:].indirect(T.vu[:]), T.xb[:], ["vu", "xb"], ["X"], 128, "s")
+        if last:
+            dma("Y", "stX", T.ytx[:, 0:2048], T.X[:, 0:2048], ["X"], [], 2 ** 20)
+            dma("Y", "stX2", T.ytx[:, 2048:4096], T.X[:, 2048:4096], ["X"], [], 2 ** 20)
+        scan(T.amax[:], T.DA[:], T.PX[:, 0:128], ALU.add, ALU.max, ["DA", "PX"], ["amax"], 128)
+        cp(T.ai[:], T.amax[:, 15:128:16], ["amax"], ["ai"])
+        ts(T.P2[:, 0:8], T.ai[:], 15, None, ALU.bitwise_and, None, ["ai"], ["P2a"])
+        tt(T.aTD[:], mk, T.qm[:], ALU.subtract, ["mmin", "qm"], ["aTD"])
+        tt(T.w[:], T.aTD[:], T.rmin[:], ALU.max, ["aTD", "rmin"], ["w"])
+        ts(T.nk[:], T.w[:], 0.0, 1024.0, ALU.is_ge, ALU.mult, ["w"], ["nk"])
+        ts(T.thr[:], R1, 0.0, None, ALU.is_ge, None, ["rs"], ["thr"])
+        tt(T.P2[:, 8:16], T.nk[:], T.thr[:], ALU.add, ["nk", "thr"], ["P2b"])
+        if not last:
+            act(T.kap[:], T.w[:], ["w"], ["kap"], func=ACT.Sign, bias=0.5)
+            mm(T.PB[:, 32:40], T.ones[:], T.kap[:], True, True, ["ones", "kap"], ["PB"], 8)
+            act(T.A8[:], T.PB[:, 32:40], ["PB"], ["A8"], bias=512.0, scale=-4.0)
+        ts(T.bi[:], T.seli[:], 15, None, ALU.bitwise_and, None, ["seli"], ["bi"])
+        cp(T.eu[:], T.bi[:], ["bi"], ["eu"])
+        tt(T.oM[:], T.DM[:, 0:16].indirect(T.eu[:]), Mf, ALU.mult, ["DM", "eu"] + nMf, ["oM"], 128, "g")
+        tt(T.L2[:, 128:256], T.P2[:, 8:16].indirect(T.EX[:, 0:8]), T.DM[:, 0:128], ALU.mult, ["P2b", "EX", "DM"],
+           ["L2b"], 128, "g")
+        mm(T.PM[:, 24:32], T.L2[:, 128:256], G8, True, True, ["L2b", "BD"], ["PM"], 8, True)
+        tt(T.o1[:], T.PM[:, 24:32], T.c2m[:], ALU.add, ["PM", "c2m"], ["o1"])
+        tt(T.L2[:, 0:128], T.P2[:, 0:8].indirect(T.EX[:, 0:8]), T.DM[:, 0:128], ALU.mult, ["P2a", "EX", "DM"],
+           ["L2a"], 128, "g")
+        mm(T.PB[:, 16:24], T.L2[:, 0:128], G8, True, True, ["L2a", "BD"], ["PB"], 8, True)
+        cp(T.au[:], T.PB[:, 16:24], ["PB"], ["au"])
+        tt(T.tL[:], T.o1[:], T.D512[:], ALU.min, ["o1", "D512"], ["tL"])
+        cp(T.tu[:], T.tL[:], ["tL"], ["tu"])
+        act(T.old[:], T.Kw[:].indirect(T.tu[:]), ["Kw", "tu"], ["old"], 128, "g", bias=-OFF)
+        act(T.ohA[:], T.tabA[:].indirect(T.au[:]), ["tabA", "au"], ["ohA"], 128, "g")
+        mm(T.PB[:, 128:256], T.BD[:], T.oM[:], True, False, ["BD", "oM"], ["PB"], 128, True)
+        mm(T.PB[:, 128:256], T.nIf[:], T.old[:], False, True, ["nIf", "old"], ["PB"], 128, True)
+        tt(T.oM[:], T.PB[:, 128:256], T.ohA[:], ALU.mult, ["PB", "ohA"], ["oM"], 128, "")
+        mm(T.PB[:, 256:384], T.If[:], T.old[:], True, False, ["If", "old"], ["PB"], 128, True)
+        mm(T.PB[:, 256:384], T.If[:], T.oM[:], False, True, ["If", "oM"], ["PB"], 128, True)
+        act(T.old[:], T.PB[:, 256:384], ["PB"], ["old"], 128, bias=OFF)
+        tt(T.L1[:], T.tabN[:].indirect(T.tu[:]), T.TRI[:], ALU.add, ["tabN", "tu", "TRI"], ["L1"], 128, "g")
+        act(T.nk[:], T.tL[:], ["tL"], ["nk"], bias=0.5, scale=-256.0)
+        tt(T.cnt[:, 16:24], T.nk[:], T.SL[:], ALU.subtract, ["nk", "SL"], ["b0"])
+        act(T.cnt[:, 24:32], T.cnt[:, 16:24], ["b0"], ["b1"], bias=128.0)
+        for h in range(8):
+            for j in range(2):
+                op("S", lambda h=h, j=j: S.activation(T.eq[:, 8 * j + h, 0:16 * h + 16], T.L1[:, 0:16 * h + 16], ACT.Sign,
+                                                      bias=T.cnt[:, 16 + 8 * j + h:17 + 8 * j + h], scale=1.0,
+                                                      accum_out=T.cnt[:, 8 * j + h:8 * j + h + 1]),
+                   ["L1", "b%d" % j], ["cnt%d" % (8 * j + h), "~g"], cost(16 * h + 16, "") + 0.02)
+        tt(T.o1[:], T.cnt[:, 0:8], T.cnt[:, 8:16], ALU.not_equal, ["cnt%d" % j for j in range(16)], ["o1"])
+        tt(T.ag[:], T.o1[:], T.D512[:], ALU.mult, ["o1", "D512"], ["ag"])
+        tt(T.lo[:], T.ag[:], T.tL[:], ALU.max, ["ag", "tL"], ["lo"])
+        cp(T.ou[:, 0:8], T.lo[:], ["lo"], ["ou"])
+        cp(T.Kw[:].indirect(T.ou[:, 0:8]), T.old[:], ["ou", "old"], ["Kw"], 128, "s")
+        if last:
+            dma("Y", "stK", T.ykt[:], T.Kw[:, 0:512], ["Kw"], [], 2 ** 18)
+
+    count = {}
+    clock = {e: {} for e in Q}
+    snap = {}
+    writer, readers = {}, {}
+
+    def wait(e, ev):
+        s, n = ev
+        if clock[e].get(s, 0) >= n:
+            return
+        Q[e].wait_ge(T.sem[s], n)
+        clock[e][s] = n
+        for k, v in snap.get(ev, {}).items():
+            if clock[e].get(k, 0) < v:
+                clock[e][k] = v
+
+    if "order" not in PLANS:
+        PLANS["order"] = plan(ops)
+    for i in PLANS["order"]:
+        o = ops[i]
+        e = o["e"]
+        o["rd"] = [r for r in o["rd"] if r[0] != "~"]
+        o["wr"] = [w for w in o["wr"] if w[0] != "~"]
+        evs = []
+        for r in o["rd"]:
+            if r in writer:
+                evs.append(writer[r])
+            if r in BANKS:
+                evs += [ev for ev in readers.get(r, []) if ev[0] != SEM[e]]
+        for w in o["wr"]:
+            if w in writer and not (e == "P" and writer[w][0] == "cP"):
+                evs.append(writer[w])
+            evs += readers.get(w, [])
+        best = {}
+        for s, n in evs:
+            best[s] = max(best.get(s, 0), n)
+        for s, n in best.items():
+            wait(e, (s, n))
+        ins = o["fn"]()
+        count[o["sem"]] = count.get(o["sem"], 0) + o["inc"]
+        ev = (o["sem"], count[o["sem"]])
+        if o["remote"]:
+            count["sent"] = count.get("sent", 0) + o["inc"]
+        else:
+            ins.then_inc(T.sem[o["sem"]], o["inc"])
+            snap[ev] = dict(clock[e])
+            for r in o["rd"]:
+                readers.setdefault(r, []).append(ev)
+        for w in o["wr"]:
+            writer[w] = ev
+            readers[w] = []
+
+    for s, n in count.items():
+        wait("G", (s, n))

@@ -20,14 +20,15 @@ def _sb(dtype, **kw):
 
 _sb(B, X=[4096], xm=[4096], mn=[4096], E=[2048], UL=[2048], zb=[128], zT=[128], nzb=[128],
     Ib=[128], I37=[128], Inh=[128], Inq=[128], Uw=[128], Kcol=[128], ones=[128], ZX=[512], ZM=[384],
-    WR=[4, 32], WN=[4, 32], masks=[256], eq=[16, 128], kap=[8], ny=[128], y2=[128], ohA=[128])
+    WR=[4, 32], WN=[4, 32], masks=[256], eq=[16, 128], kap=[8], ny=[128], y2=[128], ohA=[128], TRm=[128])
 _sb(F, Kw=[640], If=[128], nIf=[128], I16=[128], BD=[128], KCX=[128], KCM=[128], D0S=[256], D8=[128], D16=[128],
     DA=[128], DM=[256], TRI=[128], tabA=[16], tabN=[640], pm=[8], SL=[8], S32=[8], D512=[8],
     lz1=[8 * ZW], lz2=[8 * ZW], sz0=[8 * ZW], sz1=[8 * ZW],
     Mf=[128], Mn=[128], kc=[128], DD=[256], cmpv=[256], mmin=[128], msum=[256], aTD=[8], thr=[8],
     thrT=[16], A8=[8], rs=[256], xmin=[128], amax=[128], q=[16], qm=[8], rmin=[8], nrm=[8], PSI=[24], L1=[128],
     L2=[256], Wm=[256], Wz=[256], ag=[8], lo=[8], s1=[8], cu=[8], yy=[128],
-    w=[8], nk=[8], tL=[8], old=[128], oM=[128], o1=[8], cnt=[32])
+
+    w=[8], nk=[8], tL=[8], old=[128], oM=[128], o1=[8], cnt=[32], s2=[8], s3=[8], tq=[8], S32h=[8], sc=[32], lc=[32])
 _sb(I, kti=[512], msi=[128], tmpi=[256], tmpj=[256], ksi=[8], KS=[8], seli=[8],
     bi=[8], c2m=[8], ci=[8], cj=[8], ui=[8], uj=[8], vi=[8], xa=[128], xb=[128], ai=[8], P2=[16])
 _sb(U, Mu=[128], kcu=[128], cu16=[8], EX=[16], EX3=[16], selu=[8],
@@ -37,18 +38,18 @@ for _n in BANKS:
     SCRATCH[_n] = ("psum", [128, 512], F)
 
 SEMAPHORES = ["cV", "cS", "cP", "cG", "ldX", "ldK", "ldM", "ldZ", "ldC", "stX", "stX2", "stK", "stM", "stZ",
-              "arZ0", "arZ1", "sent"]
+              "arC", "arZ0", "arZ1", "sent"]
 
 CH_M = [(0, 32), (32, 32), (64, 32), (96, 32)]
 CH_X = [(0, 32), (32, 32), (64, 32), (96, 16), (112, 16)]
 G_M = [[("V", 0, 32), ("S", 32, 32), ("S", 64, 32), ("S", 96, 32)]] * RO
 G_X = [[("S", 0, 32), ("S", 32, 32), ("S", 64, 32), ("S", 96, 16), ("S", 112, 16)]] * RO
 MM_X = [(0, 96), (96, 32)]
-CY, GAT, SCA, PEC, WAKE, FIX, T_DMA, BW = 1.04e-3, 1.56, 3.8, 0.53e-3, 0.06, 0.03, 2.2, 250e3
+CY, GAT, SCA, PEC, WAKE, FIX, T_DMA, BW = 1.04e-3, 1.56, 3.8, 0.53e-3, 0.12, 0.03, 2.2, 250e3
 T_REM, T_FIRST = 4.2, 1.5
-KC_ON, ZB_ON = "S", "S"
-BOOST = {"send": 6.0}
-SEED, TRIES, HEAT = 1, 2000, 0.0
+KC_ON, ZB_ON, DEDUP = "S", "S", "VVS"
+BOOST = {"send": 6.0, "X0": 3.0}
+SEED, TRIES, HEAT = 3, 1500, 0.0
 PLANS = {}
 
 
@@ -191,7 +192,8 @@ def rank_program(g, core, T, topo):
         return FIX + max(64, n * {"": 1, "h": 0.5, "2": 2}[k]) * CY
 
     def dma(e, sem, out, in_, rd, wr, nbytes):
-        op(e, lambda: Q[e].dma_start(out, in_), rd, wr, 0.05, T_DMA + nbytes / BW, sem, 16)
+        flow = nbytes / BW + 0.15
+        op(e, lambda: Q[e].dma_start(out, in_), rd, wr, flow if e == "Y" else 0.05, T_DMA + (0 if e == "Y" else flow), sem, 16)
 
     def cp(out, in_, rd, wr, n=8, k=""):
         op("V", lambda: V.tensor_copy(out, in_), rd, wr, cost(n, k))
@@ -214,7 +216,18 @@ def rank_program(g, core, T, topo):
     def act(out, in_, rd, wr, n=8, k="", func=ACT.Identity, bias=0.0, scale=1.0):
         op("S", lambda: S.activation(out, in_, func, bias=bias, scale=scale), rd, wr, cost(n, k))
 
+    group = {}
+
     def mm(out, l, r, st, sp, rd, wr, n=128, f32=False, m=128):
+        bank = wr[0]
+        if st and not sp:
+            group[bank] = []
+            wr = wr + ["~" + bank]
+        elif not st and not sp:
+            group[bank].append("~%s_%d" % (bank, len(group[bank])))
+            rd, wr = rd + ["~" + bank], wr[1:] + group[bank][-1:]
+        elif not st:
+            rd = rd + group[bank]
         op("P", lambda: P.matmul(out, l, r, st, sp), rd, wr, max(min(64, m), n) * PEC * (4 if f32 else 1))
 
     def iota(out, pat, base, cm, wr, n, fl=False):
@@ -226,8 +239,8 @@ def rank_program(g, core, T, topo):
     dma("S", "ldZ", T.zb[:], T.z[:], [], ["zb", "~S"], 2 ** 15)
     dma("S", "ldM", T.msi[:], T.ms[:], [], ["msi", "~S"], 2 ** 16)
     dma("S", "ldC", T.cj[:], T.cp[:], [], ["cj", "~S"], 2 ** 12)
-    dma("Y", "ldX", T.X[:], T.tx[:], ["~S"], ["X", "~Y"], 2 ** 20)
-    dma("Y", "ldK", T.kti[:], T.kt[:], [], ["kti", "~Y"], 2 ** 20 + 2 ** 18)
+    dma("Y", "ldX", T.X[:], T.tx[:], ["~S"], ["X", "~Y"], 2 ** 20 + 2 ** 17)
+    dma("Y", "ldK", T.kti[:], T.kt[:], [], ["kti", "~Y"], 2 ** 18)
 
     iota(T.tmpi[:, 0:128], [[-1, 128]], 0, 1, ["tmpi", "~G"], 128)
     iota(T.tmpj[:, 0:128], [[-16, 8], [0, 16]], 0, 1, ["tmpj", "~G"], 128)
@@ -293,7 +306,11 @@ def rank_program(g, core, T, topo):
     ts(T.SL[:], T.tmpj[:, 160:168], 16.0, pm, ALU.mult, ALU.add, ["J16", "pm"], ["SL"])
     cp(T.EX[:], J16, ["J16"], ["EX"])
     act(T.Uw[:], T.BD[:], ["BD", "pm2"], ["Uw"], 128, scale=pm2)
+    if "V" in DEDUP:
+        ts(T.TRm[:], T.Wm[:, 0:128], pm, None, ALU.is_ge, None, ["Wm", "pm"], ["TRm"], 128)
     act(T.S32[:], T.SL[:], ["SL"], ["S32"], scale=32.0)
+    act(T.S32h[:, 0:4], T.SL[:, 0:4], ["SL"], ["S32h"], scale=32.0)
+    act(T.S32h[:, 4:8], T.SL[:, 0:4], ["SL"], ["S32g"], scale=32.0)
     act(T.D512[:], T.SL[:], ["SL"], ["D512"], bias=512.0)
     ts(T.EX3[:, 0:8], T.tmpj[:, 160:168], 2.0, pm3, ALU.mult, ALU.add, ["J16", "pm3"], ["EX3a"])
     ts(T.EX3[:, 8:16], T.tmpj[:, 168:176], 8.0, None, ALU.add, None, ["J16"], ["EX3b"])
@@ -307,23 +324,27 @@ def rank_program(g, core, T, topo):
     cp(T.Kw[:, 0:512], T.kti[:], ["kti", "Kwd"], ["Kw"], 512)
 
     peers = []
+    taken = {True: 0, False: 0}
     for h in range(1, N):
         dst = T.cores[(rank + h) % N]
         rid, pid, _ = topo.addr(dst)
         eng = topo.engines(core, dst)
         per = len(eng) // N
-        peers.append((DstId(rid=rid, pnc=pid), sum(1 << e for e in eng[per * (h - 1):per * h]), per, h))
+        far = topo.die(dst) != topo.die(core)
+        mine = eng[int(far)::2][per * taken[far]:per * taken[far] + per]
+        taken[far] += 1
+        peers.append((DstId(rid=rid, pnc=pid), sum(1 << e for e in mine), per, h))
     arrive = sum(p[2] for p in peers)
 
     def send(src_of, dst_of, sem, rd, wr):
         op("G", lambda: g.remote_dma_fused(
             [RemoteDMATransfer(dst_ids=[d], dma_engine_mask=m, remote_sem=T.sem[sem], src=src_of(h),
                                dst=dst_of((h + 1) % N)) for d, m, _, h in peers], local_sem=T.sem.sent),
-           rd, wr + ["~G"], 0.5 + (T_FIRST if sem == "arZ0" else 0), T_REM - 0.5,
+           rd, wr + ["~R"], 0.5 + (T_FIRST if sem == "arC" else 0), T_REM - 0.5,
            sem, arrive, True)
 
     def tags(t, s0, n):
-        return ["%s%d" % (t, b) for b in range(s0 // 16, (s0 + n) // 16)]
+        return ["%s%d" % (t, b) for b in range(s0 // 8, (s0 + n) // 8)]
 
     def gather(e, t, lst, lname, s0, n):
         base = 2048 if t == "m" else 0
@@ -363,13 +384,20 @@ def rank_program(g, core, T, topo):
             for il in range(16):
                 mm(T.PA[:, 384:392], T.UL[:, 128 * il:128 * il + 128], T.zb[:, il:128:16], il == 0, il == 15,
                    ULall + ["zb"], ["PA"], 8)
-            tt(T.cu[:], T.PA[:, 384:392], lz[:, 5:384:ZW], ALU.mult, ["PA"] + nlz, ["cu"])
-            tt(T.ci[:], T.cu[:], lz[:, 2:384:ZW], ALU.add, ["cu"] + nlz, ["ci"])
+            nxt, nn = lz[:, 2:384:ZW], nlz
+            if r == 1:
+                tt(T.s3[:], nxt, T.lc[:, 0:32:4], ALU.add, nlz + ["lc", "lcr"], ["s3"])
+                nxt, nn = T.s3[:], nlz + ["s3"]
+            tt(T.s2[:], T.PA[:, 384:392], nxt, ALU.subtract, ["PA"] + nn, ["s2"])
+            tt(T.cu[:], T.s2[:], lz[:, 5:384:ZW], ALU.mult, ["s2"] + nlz, ["cu"])
+            tt(T.ci[:], T.cu[:], nxt, ALU.add, ["cu"] + nn, ["ci"])
             ts(T.cj[:], T.ci[:], 511, None, ALU.bitwise_and, None, ["ci"], ["cj"])
         for b4 in range(4):
             mm(T["ZE%d" % b4][:], T.zT[:], T.E[:, 512 * b4:512 * b4 + 512], True, True, ["zT"] + Eall, ["ZE%d" % b4], 512)
         cp(T.cu16[:], T.cj[:], ["cj"], ["cu16"])
-        if KC_ON == "S":
+        if r == 0:
+            ts(T.kc[:], T.kti[:].indirect(T.cu16[:]), -OFF, None, ALU.add, None, ["kti", "cu16"], ["kc"], 128, "g")
+        elif KC_ON == "S":
             act(T.kc[:], T.Kw[:].indirect(T.cu16[:]), ["Kw", "cu16"], ["kc"], 128, "g", bias=-OFF)
         else:
             ts(T.kc[:], T.Kw[:].indirect(T.cu16[:]), -OFF, None, ALU.add, None, ["Kw", "cu16"], ["kc"], 128, "g")
@@ -378,6 +406,11 @@ def rank_program(g, core, T, topo):
             gather(e, "x", T.kcu, ["kcu"], s0, n)
         ts(T.ci[:], T.cj[:], 2.0, None, ALU.mult, None, ["cj"], ["ci"])
         ts(T.c2m[:], T.ci[:], 511, None, ALU.bitwise_and, None, ["ci"], ["c2m"])
+        if r == 0:
+            ms(T.sc[:], 0.0, ["sc"], 32)
+            cp(T.sc[:, 0:32:4], T.c2m[:], ["c2m"], ["sc"])
+            send(lambda h: T.sc[:, 4 * h:4 * h + 4], lambda s: T.lc[:, 4 * s:4 * s + 4], "arC", ["sc", "kti", "X"], ["lcr"])
+            act(T.lc[:, 4:8], T.sc[:, 0:4], ["sc"], ["lc"])
         for lo, hi in ((0, 128), (256, 384)):
             mm(T.PA[:, lo:hi], T.Uw[:], T.zb[:], True, False, ["Uw", "zb"], ["PA"])
             mm(T.PA[:, lo:hi], T.I37[:], T.Kcol[:], False, False, ["I37", "Kcol"], ["PA"])
@@ -395,10 +428,11 @@ def rank_program(g, core, T, topo):
         for s0, n in CH_M:
             mins("m", s0, n)
         for k in range(16):
-            mm(T.PM[:, k:384:16], T.xm[:, 2048 + k:4096:16], T.WR[:, 2 + k // 8, 0:24], False, False, XM + WRall, ["PM"], 24)
+            mm(T.PM[:, k:384:16], T.xm[:, 2048 + k:4096:16], T.WR[:, 2 + k // 8, 0:24], False, False, XM + WRall,
+               ["PM", "~rm%d" % k], 24)
         for k in range(16):
             mm(T.PM[:, k:384:16], T.mn[:, 2048 + k:4096:16], T.WN[:, 2 + k // 8, 0:24], False, k == 15,
-               ["n" + x for x in XM] + ["WN"], ["PM"], 24)
+               ["n" + x for x in XM] + ["WN", "~rm%d" % k], ["PM"], 24)
         scan(T.msum[:], T.D0S[:], T.PM[:, 128:384], ALU.mult, ALU.add, ["D0S", "PM"], ["msum"], 256)
         scan(T.mmin[:], T.D16[:], T.PM[:, 0:128], ALU.add, ALU.min, ["D16", "PM"], ["mmin"], 128)
         act(T.cmpv[:, 128:256], T.PM[:, 256:384], ["PM"], ["cmpb"], 128, scale=16.0)
@@ -417,7 +451,8 @@ def rank_program(g, core, T, topo):
             for buf, wt, t, dep in ((T.xm, T.WR, "x", WRall), (T.mn, T.WN, "nx", ["WN"])):
                 for k in range(15 if t == "nx" else 16):
                     mm(T.PX[s0:s0 + n, k:512:16], buf[:, 16 * s0 + k:16 * (s0 + n):16], wt[:, k // 8, :], False,
-                       False, tags(t, s0, n) + dep, ["PX"], 32, False, n)
+                       False, tags(t, s0, n) + dep + ["~rx%d_%d" % (s0, k)] * (t == "nx"),
+                       ["PX"] + ["~rx%d_%d" % (s0, k)] * (t == "x"), 32, False, n)
         mm(T.PX[:, 15:512:16], T.mn[:, 15:2048:16], T.WN[:, 1, :], False, True, tags("nx", 0, 128) + ["WN"], ["PX"], 32)
         where[1] = True
         scan(T.rs[:], T.D0S[:], T.PX[:, 128:384], ALU.mult, ALU.add, ["D0S", "PX"], ["rs"], 256)
@@ -457,9 +492,9 @@ def rank_program(g, core, T, topo):
         act(T.Wz[:, 128:256], T.ZE1[:, 0:128], ["ZE1"], ["Wzb"], 128, func=ACT.Abs, scale=2.0)
         act(T.nzb[:], T.Wz[:].indirect(T.szu[:]), ["Wza", "Wzb", "szu"], ["nzb"], 128, "g")
         for il in range(16):
-            mm(T.PB[:, 8:16], T.UL[:, 128 * il:128 * il + 128], T.nzb[:, il:128:16], il == 0, il == 15,
-               ULall + ["nzb"], ["PB"], 8)
-        cp(T.ui[:], T.PB[:, 8:16], ["PB"], ["ui"])
+            mm(T.ZE3[:, 128:136], T.UL[:, 128 * il:128 * il + 128], T.nzb[:, il:128:16], il == 0, il == 15,
+               ULall + ["nzb"], ["ZE3"], 8)
+        cp(T.ui[:], T.ZE3[:, 128:136], ["ZE3"], ["ui"])
         if last:
             act(T.yy[:], T.Mn[:], ["Mn"], ["yy"], 128, bias=OFF)
             dma("Y", "stZ", T.yz[:], T.nzb[:], ["nzb"], [], 2 ** 15)
@@ -468,31 +503,46 @@ def rank_program(g, core, T, topo):
             lz2 = T["lz%d" % (r + 1)]
             act(sz[:, 1:384:3], T.Wz[:].indirect(T.szu[:]), ["Wza", "Wzb", "szu", "sz%d" % r], ["sz%da" % r], 128, "g")
             ts(T.bi[:], T.seli[:], 3, 1, ALU.arith_shift_right, ALU.bitwise_and, ["seli"], ["bi"])
-            ts(T.ag[:], T.seli[:], 2048.0, None, ALU.is_lt, None, ["seli"], ["ag"])
-            ts(sz[:, 5:384:ZW], T.seli[:], 2048.0, None, ALU.is_ge, None, ["seli", "sz%d" % r], ["sz%dc" % r])
-            tt(T.s1[:], T.bi[:], T.c2m[:], ALU.add, ["bi", "c2m"], ["s1"])
-            tt(sz[:, 2:384:ZW], T.s1[:], T.ag[:], ALU.mult, ["s1", "ag", "sz%d" % r], ["sz%db" % r])
+            act(T.s1[:], T.PB[:, 0:8], ["PB"], ["s1"], func=ACT.Sign, bias=-OFF)
+            act(sz[:, 5:384:ZW], T.s1[:], ["s1", "sz%d" % r], ["sz%dc" % r], func=ACT.Relu)
+            if r:
+                tt(sz[:, 2:384:ZW], T.bi[:], T.c2m[:], ALU.add, ["bi", "c2m", "sz%d" % r], ["sz%db" % r])
+            else:
+                cp(sz[:, 2:384:ZW], T.bi[:], ["bi", "sz%d" % r], ["sz%db" % r])
             nsz = ["sz%d%s" % (r, x) for x in "abcd"]
             send(lambda h, a=sz: a[:, ZW * h:ZW * h + ZW], lambda s, a=lz2: a[:, ZW * s:ZW * s + ZW], "arZ%d" % r, nsz,
                  ["lz%dr" % (r + 1)])
             act(lz2[:, ZW:2 * ZW], sz[:, 0:ZW], nsz, ["lz%d" % (r + 1)], ZW)
         ts(T.uj[:], T.ui[:], 31, None, ALU.bitwise_and, None, ["ui"], ["uj"])
-        tt(T.vi[:], T.uj[:], T.S32[:], ALU.add, ["uj", "S32"], ["vi"])
-        cp(T.vu[:], T.vi[:], ["vi"], ["vu"])
-        tt(T.xa[:], T.X[:].indirect(T.vu[:]), T.nzb[:], ALU.add, ["X", "vu", "nzb"], ["xa"], 128, "g")
-        ts(T.xb[:], T.xa[:], 1, None, ALU.arith_shift_right, None, ["xa"], ["xb"], 128)
-        cp(T.X[:].indirect(T.vu[:]), T.xb[:], ["vu", "xb"], ["X"], 128, "s")
         if last:
-            dma("Y", "stX", T.ytx[:, 0:2048], T.X[:, 0:2048], ["X"], [], 2 ** 20)
-            dma("Y", "stX2", T.ytx[:, 2048:4096], T.X[:, 2048:4096], ["X"], [], 2 ** 20)
+            tt(T.vi[:], T.uj[:], T.S32h[:], ALU.add, ["uj", "S32h", "S32g"], ["vi"])
+            cp(T.vu[:], T.vi[:], ["vi"], ["vu"])
+            for j in range(2):
+                win, cols, xj = T.X[:, 2048 * j:2048 * j + 2048], slice(64 * j, 64 * j + 64), "X%d" % j
+                off = T.vu[:, 4 * j:4 * j + 4]
+                tt(T.xa[:, cols], win.indirect(off), T.nzb[:, cols], ALU.add, ["X", "vu", "nzb"], ["xa%d" % j], 64, "g")
+                ts(T.xb[:, cols], T.xa[:, cols], 1, None, ALU.arith_shift_right, None, ["xa%d" % j], ["xb%d" % j], 64)
+                cp(win.indirect(off), T.xb[:, cols], ["vu", "xb%d" % j], [xj, "~X"], 64, "s")
+                dma("Y", ("stX", "stX2")[j], T.ytx[:, 2048 * j:2048 * j + 2048], win, [xj], [], 2 ** 19)
+        else:
+            tt(T.vi[:], T.uj[:], T.S32[:], ALU.add, ["uj", "S32"], ["vi"])
+            cp(T.vu[:], T.vi[:], ["vi"], ["vu"])
+            mm(T.ZE3[:, 0:128], Ih, T.nzb[:], True, False, ["E0", "nzb"], ["ZE3"])
+            mm(T.ZE3[:, 0:128], T.Inq[:], T.ones[:], False, False, ["Inq", "ones"], ["ZE3"])
+            act(T.y2[:], T.X[:].indirect(T.vu[:]), ["X", "vu"], ["y2"], 128, "g", scale=0.5)
+            mm(T.ZE3[:, 0:128], T.Ib[:], T.y2[:], False, True, ["Ib", "y2"], ["ZE3"])
+            act(T.yy[:], T.ZE3[:, 0:128], ["ZE3"], ["yy"], 128, bias=MAGIC)
+            act(T.ny[:], T.yy[:], ["yy"], ["ny"], 128, bias=-MAGIC)
+            cp(T.X[:].indirect(T.vu[:]), T.ny[:], ["vu", "ny"], ["X"], 128, "s")
         scan(T.amax[:], T.DA[:], T.PX[:, 0:128], ALU.add, ALU.max, ["DA", "PX"], ["amax"], 128)
         cp(T.ai[:], T.amax[:, 15:128:16], ["amax"], ["ai"])
         ts(T.P2[:, 0:8], T.ai[:], 15, None, ALU.bitwise_and, None, ["ai"], ["P2a"])
         tt(T.aTD[:], mk, T.qm[:], ALU.subtract, ["mmin", "qm"], ["aTD"])
         tt(T.w[:], T.aTD[:], T.rmin[:], ALU.max, ["aTD", "rmin"], ["w"])
-        ts(T.nk[:], T.w[:], 0.0, 1024.0, ALU.is_ge, ALU.mult, ["w"], ["nk"])
-        ts(T.thr[:], R1, 0.0, None, ALU.is_ge, None, ["rs"], ["thr"])
-        tt(T.P2[:, 8:16], T.nk[:], T.thr[:], ALU.add, ["nk", "thr"], ["P2b"])
+        act(T.nk[:], T.w[:], ["w"], ["nk"], bias=1024.0, scale=1024.0)
+        act(T.o1[:], R1, ["rs"], ["o1"], func=ACT.Sign, bias=1.0)
+        act(T.thr[:], T.o1[:], ["o1"], ["thr"], func=ACT.Relu)
+        tt(T.tq[:], T.nk[:], T.thr[:], ALU.max, ["nk", "thr"], ["P2b"])
         if not last:
             act(T.kap[:], T.w[:], ["w"], ["kap"], func=ACT.Sign, bias=0.5)
             mm(T.PB[:, 32:40], T.ones[:], T.kap[:], True, True, ["ones", "kap"], ["PB"], 8)
@@ -500,7 +550,7 @@ def rank_program(g, core, T, topo):
         ts(T.bi[:], T.seli[:], 15, None, ALU.bitwise_and, None, ["seli"], ["bi"])
         cp(T.eu[:], T.bi[:], ["bi"], ["eu"])
         tt(T.oM[:], T.DM[:, 0:16].indirect(T.eu[:]), Mf, ALU.mult, ["DM", "eu"] + nMf, ["oM"], 128, "g")
-        tt(T.L2[:, 128:256], T.P2[:, 8:16].indirect(T.EX[:, 0:8]), T.DM[:, 0:128], ALU.mult, ["P2b", "EX", "DM"],
+        tt(T.L2[:, 128:256], T.tq[:].indirect(T.EX[:, 0:8]), T.DM[:, 0:128], ALU.mult, ["P2b", "EX", "DM"],
            ["L2b"], 128, "g")
         mm(T.PM[:, 24:32], T.L2[:, 128:256], G8, True, True, ["L2b", "BD"], ["PM"], 8, True)
         tt(T.o1[:], T.PM[:, 24:32], T.c2m[:], ALU.add, ["PM", "c2m"], ["o1"])
@@ -518,16 +568,30 @@ def rank_program(g, core, T, topo):
         mm(T.PB[:, 256:384], T.If[:], T.old[:], True, False, ["If", "old"], ["PB"], 128, True)
         mm(T.PB[:, 256:384], T.If[:], T.oM[:], False, True, ["If", "oM"], ["PB"], 128, True)
         act(T.old[:], T.PB[:, 256:384], ["PB"], ["old"], 128, bias=OFF)
+        if DEDUP[r] == "V":
+            tt(T.L1[:], T.tabN[:].indirect(T.tu[:]), T.TRm[:], ALU.add, ["tabN", "tu", "TRm"], ["L1"], 128, "g")
+            act(T.nk[:], T.tL[:], ["tL"], ["nk"], scale=256.0)
+            tt(T.eq[:, 0, :], T.nk[:].indirect(T.EX[:, 0:8]), T.L1[:], ALU.is_equal, ["nk", "EX", "L1"], ["eq"], 128, "g")
+            scan(T.amax[:], T.D0S[:, 0:128], T.eq[:, 0, :], ALU.mult, ALU.max, ["D0S", "eq"], ["amax"], 128)
+            tt(T.ag[:], T.amax[:, 15:128:16], T.D512[:], ALU.mult, ["amax", "D512"], ["ag"])
+            tt(T.lo[:], T.ag[:], T.tL[:], ALU.max, ["ag", "tL"], ["lo"])
+            cp(T.ou[:, 0:16:2], T.lo[:], ["lo"], ["ou"])
+            for h in range(7, -1, -1):
+                cp(T.Kw[:].indirect(T.ou[:, 2 * h:2 * h + 1]), T.old[:, 16 * h:16 * h + 16], ["ou", "old"], ["Kw"], 16, "s")
+            if last:
+                dma("Y", "stK", T.ykt[:], T.Kw[:, 0:512], ["Kw"], [], 2 ** 18)
+            continue
         tt(T.L1[:], T.tabN[:].indirect(T.tu[:]), T.TRI[:], ALU.add, ["tabN", "tu", "TRI"], ["L1"], 128, "g")
+        key, k0, nkey = T.L1, 0, "L1"
         act(T.nk[:], T.tL[:], ["tL"], ["nk"], bias=0.5, scale=-256.0)
         tt(T.cnt[:, 16:24], T.nk[:], T.SL[:], ALU.subtract, ["nk", "SL"], ["b0"])
         act(T.cnt[:, 24:32], T.cnt[:, 16:24], ["b0"], ["b1"], bias=128.0)
         for h in range(8):
             for j in range(2):
-                op("S", lambda h=h, j=j: S.activation(T.eq[:, 8 * j + h, 0:16 * h + 16], T.L1[:, 0:16 * h + 16], ACT.Sign,
+                op("S", lambda h=h, j=j: S.activation(T.eq[:, 8 * j + h, 0:16 * h + 16], key[:, k0:k0 + 16 * h + 16], ACT.Sign,
                                                       bias=T.cnt[:, 16 + 8 * j + h:17 + 8 * j + h], scale=1.0,
                                                       accum_out=T.cnt[:, 8 * j + h:8 * j + h + 1]),
-                   ["L1", "b%d" % j], ["cnt%d" % (8 * j + h), "~g"], cost(16 * h + 16, "") + 0.02)
+                   [nkey, "b%d" % j], ["cnt%d" % (8 * j + h), "~g"], cost(16 * h + 16, "") + 0.02)
         tt(T.o1[:], T.cnt[:, 0:8], T.cnt[:, 8:16], ALU.not_equal, ["cnt%d" % j for j in range(16)], ["o1"])
         tt(T.ag[:], T.o1[:], T.D512[:], ALU.mult, ["o1", "D512"], ["ag"])
         tt(T.lo[:], T.ag[:], T.tL[:], ALU.max, ["ag", "tL"], ["lo"])

@@ -37,16 +37,17 @@ BANKS = ("ZE0", "ZE1", "ZE2", "ZE3", "PX", "PM", "PA", "PB")
 for _n in BANKS:
     SCRATCH[_n] = ("psum", [128, 512], F)
 
-SEMAPHORES = ["cV", "cS", "cP", "cG", "ldX", "ldK", "ldM", "ldZ", "ldC", "stX", "stX2", "stK", "stM", "stZ",
+SEMAPHORES = ["cV", "cS", "cP", "cG", "ldX", "ldX2", "ldK", "ldM", "ldZ", "ldC", "stX", "stX2", "stK", "stM", "stZ",
               "arC", "arZ0", "arZ1", "sent"]
 
 CH_M = [(0, 32), (32, 32), (64, 32), (96, 32)]
 CH_X = [(0, 32), (32, 32), (64, 32), (96, 16), (112, 16)]
-G_M = [[("V", 0, 32), ("S", 32, 32), ("S", 64, 32), ("S", 96, 32)]] * RO
+_LATER = [("S", 16, 16), ("S", 0, 16), ("V", 32, 32), ("S", 64, 32), ("S", 96, 32)]
+G_M = [[("V", 0, 32), ("S", 32, 32), ("S", 64, 32), ("V", 96, 16), ("S", 112, 16)], _LATER, _LATER]
 G_X = [[("S", 0, 32), ("S", 32, 32), ("S", 64, 32), ("S", 96, 16), ("S", 112, 16)]] * RO
 MM_X = [(0, 96), (96, 32)]
 CY, GAT, SCA, PEC, WAKE, FIX, T_DMA, BW = 1.04e-3, 1.56, 3.8, 0.53e-3, 0.12, 0.03, 2.2, 250e3
-T_REM, T_FIRST = 4.2, 1.5
+T_REM, T_FIRST = 4.4, 1.5
 KC_ON, ZB_ON, DEDUP = "S", "S", "VVS"
 BOOST = {"send": 6.0, "X0": 3.0}
 SEED, TRIES, HEAT = 3, 1500, 0.0
@@ -236,11 +237,12 @@ def rank_program(g, core, T, topo):
         else:
             op("G", lambda: g.iota(out, pat, base, cm), [], wr, 0.13 + 2 * n * CY)
 
-    dma("S", "ldZ", T.zb[:], T.z[:], [], ["zb", "~S"], 2 ** 15)
-    dma("S", "ldM", T.msi[:], T.ms[:], [], ["msi", "~S"], 2 ** 16)
-    dma("S", "ldC", T.cj[:], T.cp[:], [], ["cj", "~S"], 2 ** 12)
-    dma("Y", "ldX", T.X[:], T.tx[:], ["~S"], ["X", "~Y"], 2 ** 20 + 2 ** 17)
-    dma("Y", "ldK", T.kti[:], T.kt[:], [], ["kti", "~Y"], 2 ** 18)
+    dma("Y", "ldZ", T.zb[:], T.z[:], [], ["zb", "~Y"], 2 ** 12)
+    dma("S", "ldM", T.msi[:], T.ms[:], [], ["msi", "~S"], 2 ** 18)
+    dma("S", "ldC", T.cj[:], T.cp[:], [], ["cj", "~S"], 2 ** 18)
+    dma("S", "ldX2", T.X[:, 2048:4096], T.tx[:, 2048:4096], [], ["Xb", "~S"], 2 ** 20 + 2 ** 17)
+    dma("Y", "ldX", T.X[:, 0:2048], T.tx[:, 0:2048], [], ["X", "~Y"], 2 ** 20 + 2 ** 17)
+    dma("S", "ldK", T.kti[:], T.kt[:], [], ["kti", "~S"], 2 ** 20 + 2 ** 17 + 2 ** 18)
 
     iota(T.tmpi[:, 0:128], [[-1, 128]], 0, 1, ["tmpi", "~G"], 128)
     iota(T.tmpj[:, 0:128], [[-16, 8], [0, 16]], 0, 1, ["tmpj", "~G"], 128)
@@ -319,7 +321,7 @@ def rank_program(g, core, T, topo):
     for gi in range(8):
         act(T.UL[:, 16 * gi:16 * gi + 129 * 15 + 1:129], T.Uw[:, 16 * gi:16 * gi + 16], ["Uw", "UL"], ["UL%d" % gi])
     ULall = ["UL%d" % gi for gi in range(8)]
-    cp(T.Mu[:], T.msi[:], ["msi"], ["Mu"], 128)
+    cp(T.Mu[:], T.msi[:], ["msi"], ["Mu0", "Mu1", "Mu2"], 128)
     ts(T.Mf[:], T.msi[:], -OFF, None, ALU.add, None, ["msi"], ["Mf"], 128)
     cp(T.Kw[:, 0:512], T.kti[:], ["kti", "Kwd"], ["Kw"], 512)
 
@@ -350,6 +352,7 @@ def rank_program(g, core, T, topo):
         base = 2048 if t == "m" else 0
         out = T.xm[:, base + 16 * s0:base + 16 * (s0 + n)]
         src = T.X[:].indirect(lst[:, s0:s0 + n])
+        lname = lname + ["Xb"]
         if e == "S":
             act(out, src, ["X"] + lname, tags(t, s0, n) + ["~g"], 16 * n, "g", scale=0.5)
         else:
@@ -371,13 +374,15 @@ def rank_program(g, core, T, topo):
         nlz = ["lz%d" % r, "lz%dr" % r]
         Mf, nMf = (lz[:, 0:384:3], nlz) if r else (T.Mf[:], ["Mf"])
         if r:
-            ts(T.Mu[:], Mf, OFF, None, ALU.add, None, nMf, ["Mu"], 128)
+            ts(T.Mu[:, 16:32], lz[:, ZW:2 * ZW:3], OFF, None, ALU.add, None, nlz[:1], ["Mu1"], 16)
+            ts(T.Mu[:, 32:128], lz[:, 2 * ZW:384:3], OFF, None, ALU.add, None, nlz, ["Mu2"], 96)
+            ts(T.Mu[:, 0:16], lz[:, 0:ZW:3], OFF, None, ALU.add, None, nlz, ["Mu0"], 16)
             if ZB_ON == "S":
                 act(T.zb[:], lz[:, 1:384:3], nlz, ["zb"], 128)
             else:
                 cp(T.zb[:], lz[:, 1:384:3], nlz, ["zb"], 128)
         for e, s0, n in G_M[r]:
-            gather(e, "m", T.Mu, ["Mu"], s0, n)
+            gather(e, "m", T.Mu, ["Mu%d" % j for j in range(min(s0 // 16, 2), min((s0 + n - 1) // 16, 2) + 1)], s0, n)
         mm(T.PA[:, 0:128], T.zb[:], T.Ib[:], True, True, ["zb", "Ib"], ["PA"])
         cp(T.zT[:], T.PA[:, 0:128], ["PA"], ["zT"], 128)
         if r:
@@ -409,7 +414,7 @@ def rank_program(g, core, T, topo):
         if r == 0:
             ms(T.sc[:], 0.0, ["sc"], 32)
             cp(T.sc[:, 0:32:4], T.c2m[:], ["c2m"], ["sc"])
-            send(lambda h: T.sc[:, 4 * h:4 * h + 4], lambda s: T.lc[:, 4 * s:4 * s + 4], "arC", ["sc", "kti", "X"], ["lcr"])
+            send(lambda h: T.sc[:, 4 * h:4 * h + 4], lambda s: T.lc[:, 4 * s:4 * s + 4], "arC", ["sc", "kti", "X", "Xb"], ["lcr"])
             act(T.lc[:, 4:8], T.sc[:, 0:4], ["sc"], ["lc"])
         for lo, hi in ((0, 128), (256, 384)):
             mm(T.PA[:, lo:hi], T.Uw[:], T.zb[:], True, False, ["Uw", "zb"], ["PA"])
@@ -523,7 +528,7 @@ def rank_program(g, core, T, topo):
                 tt(T.xa[:, cols], win.indirect(off), T.nzb[:, cols], ALU.add, ["X", "vu", "nzb"], ["xa%d" % j], 64, "g")
                 ts(T.xb[:, cols], T.xa[:, cols], 1, None, ALU.arith_shift_right, None, ["xa%d" % j], ["xb%d" % j], 64)
                 cp(win.indirect(off), T.xb[:, cols], ["vu", "xb%d" % j], [xj, "~X"], 64, "s")
-                dma("Y", ("stX", "stX2")[j], T.ytx[:, 2048 * j:2048 * j + 2048], win, [xj], [], 2 ** 19)
+                dma("YS"[j], ("stX", "stX2")[j], T.ytx[:, 2048 * j:2048 * j + 2048], win, [xj], [], 2 ** (19 + j))
         else:
             tt(T.vi[:], T.uj[:], T.S32[:], ALU.add, ["uj", "S32"], ["vi"])
             cp(T.vu[:], T.vi[:], ["vi"], ["vu"])

@@ -2,14 +2,16 @@ from concourse.bass import DstId, RemoteDMATransfer
 from concourse.mybir import AluOpType as ALU, ActivationFunctionType as ACT
 
 RO = 3
-ZW = 48
 BIG = float(2 ** 26)
-MAGIC = float(3 * 2 ** 22)
+HUGE = float(2 ** 30)
 MAGIC4 = float(3 * 2 ** 34)
-KBASE = -4081 * 4096
+MAGIC32 = float(3 * 2 ** 27)
+ZO = 1536.0
+BO = 1280.0
 OFF = 2047.5
+YC, YA, YW = 2048, 2176, 3200
 
-F, B, I, U = "float32", "bfloat16", "int32", "uint16"
+F, B, I, U, H = "float32", "bfloat16", "int32", "uint16", "float16"
 SCRATCH = {}
 
 
@@ -18,39 +20,41 @@ def _sb(dtype, **kw):
         SCRATCH[name] = ("sbuf", [128] + list(shape), dtype)
 
 
-_sb(B, X=[4096], xm=[4096], mn=[4096], E=[2048], UL=[2048], zb=[128], zT=[128], nzb=[128],
-    Ib=[128], I37=[128], Inh=[128], Inq=[128], Uw=[128], Kcol=[128], ones=[128], ZX=[512], ZM=[384],
-    WR=[4, 32], WN=[4, 32], masks=[256], eq=[16, 128], kap=[8], ny=[128], y2=[128], ohA=[128], TRm=[128])
-_sb(F, Kw=[640], If=[128], nIf=[128], I16=[128], BD=[128], KCX=[128], KCM=[128], D0S=[256], D8=[128], D16=[128],
-    DA=[128], DM=[256], TRI=[128], tabA=[16], tabN=[640], pm=[8], SL=[8], S32=[8], D512=[8],
-    lz1=[8 * ZW], lz2=[8 * ZW], sz0=[8 * ZW], sz1=[8 * ZW],
-    Mf=[128], Mn=[128], kc=[128], DD=[256], cmpv=[256], mmin=[128], msum=[256], aTD=[8], thr=[8],
-    thrT=[16], A8=[8], rs=[256], xmin=[128], amax=[128], q=[16], qm=[8], rmin=[8], nrm=[8], PSI=[24], L1=[128],
-    L2=[256], Wm=[256], Wz=[256], ag=[8], lo=[8], s1=[8], cu=[8], yy=[128],
-
-    w=[8], nk=[8], tL=[8], old=[128], oM=[128], o1=[8], cnt=[32], s2=[8], s3=[8], tq=[8], S32h=[8], sc=[32], lc=[32])
-_sb(I, kti=[512], msi=[128], tmpi=[256], tmpj=[256], ksi=[8], KS=[8], seli=[8],
-    bi=[8], c2m=[8], ci=[8], cj=[8], ui=[8], uj=[8], vi=[8], xa=[128], xb=[128], ai=[8], P2=[16])
-_sb(U, Mu=[128], kcu=[128], cu16=[8], EX=[16], EX3=[16], selu=[8],
-    szu=[8], eu=[8], au=[8], tu=[8], vu=[8], ou=[16])
-BANKS = ("ZE0", "ZE1", "ZE2", "ZE3", "PX", "PM", "PA", "PB")
+_sb(B, X=[4096], yw=[YW], xm=[2048], mnm=[2048], mnx=[2048], UL=[2048], DM=[2048], CH=[8, 128], E=[1024], BT=[512],
+    zb=[128], zT=[256], Ib=[128], I37=[128], Inh=[128], I8k=[128], In1k=[128], Uw=[128], Kcol=[128], ones=[128],
+    e8=[128], TRI=[128], C30=[128], WX=[4, 32], WM=[4, 48], BDb=[128], nIb=[128], y2=[128], ya=[128], ny=[128],
+    mA=[128], mK=[128], nA=[128], cb=[16], val=[16], S32=[32], bits=[256], nzb=[128])
+_sb(F, Kw=[640], If=[128], nIf=[128], nBI=[128], BD=[128], CX=[16, 12], DX=[192], LX=[192], LQ=[192], CM=[24, 9],
+    D16=[128], DA=[128], D2s=[16], CC=[16], CG=[16], D512=[16], pm=[8], SL=[8], kc=[128], zz=[128], yy=[128],
+    DD=[384], Wm=[400], LMk=[128], LMs=[24], LXk=[128], mmin=[128], amax=[128], mkhi=[8], thr=[16], LE=[64],
+    LV=[64], L1=[128], nameN=[128], D1=[128], D2=[128], tq=[8], lo=[16], Mn=[128])
+_sb(H, lz0=[128, 4], lz1=[128, 4], lz2=[128, 4], sz0=[128, 4], sz1=[128, 4], sz2=[128, 4], sc0=[64], sc1=[64], sc2=[64],
+    lc0=[64], lc1=[64], ce=[8], oM=[128])
+_sb(I, kti=[512], msi=[128], tmpi=[256], tmpj=[256], BI=[256], ksi=[8], KS=[8], ci=[16], cj=[8], c8=[8], ui=[8],
+    xa=[128], xb=[128])
+_sb(U, Mu=[128], kcu=[128], cu16=[8], EX=[8], EXS=[8], EXA=[8], EXD=[2], selu=[8], szu=[8], eu=[16], vu=[8], ou=[16])
+BANKS = ("ZA", "ZB", "PX", "PM", "EA", "EB", "PA", "PB")
 for _n in BANKS:
-    SCRATCH[_n] = ("psum", [128, 512], F)
+    SCRATCH[_n] = ("psum", [128, 64, 16], B) if _n[0] == "Z" else \
+        ("psum", [128, 32, 16], F) if _n in ("PX", "PM") else ("psum", [128, 512], F)
 
 SEMAPHORES = ["cV", "cS", "cP", "cG", "ldX", "ldX2", "ldK", "ldM", "ldZ", "ldC", "stX", "stX2", "stK", "stM", "stZ",
-              "arC", "arZ0", "arZ1", "sent"]
+              "arC0", "arC1", "arA0", "arA1", "arB0", "arB1", "sent", "cpD"]
 
-CH_M = [(0, 32), (32, 32), (64, 32), (96, 32)]
-CH_X = [(0, 32), (32, 32), (64, 32), (96, 16), (112, 16)]
-_LATER = [("S", 16, 16), ("S", 0, 16), ("V", 32, 32), ("S", 64, 32), ("S", 96, 32)]
-G_M = [[("V", 0, 32), ("S", 32, 32), ("S", 64, 32), ("V", 96, 16), ("S", 112, 16)], _LATER, _LATER]
-G_X = [[("S", 0, 32), ("S", 32, 32), ("S", 64, 32), ("S", 96, 16), ("S", 112, 16)]] * RO
+CH_M = [(0, 64), (64, 64)]
+CH_X = [(0, 64), (64, 32), (96, 32)]
+G_M = [[("V", 0, 32), ("S", 32, 32), ("S", 64, 32), ("V", 96, 32)],
+       [("S", 0, 32), ("S", 32, 32), ("S", 64, 32), ("V", 96, 32)],
+       [("S", 0, 32), ("S", 32, 32), ("S", 64, 32), ("V", 96, 32)]]
+G_X = [[("S", 0, 32), ("V", 32, 32), ("S", 64, 32), ("S", 96, 16), ("V", 112, 16)]] * RO
 MM_X = [(0, 96), (96, 32)]
+CALL_A, CALL_B, CALL_C = ((7, 8), (1, 4), (2, 4)), ((3, 4), (4, 4), (5, 4), (6, 4)), \
+    ((1, 2), (2, 2), (3, 2), (4, 2), (5, 2), (6, 2), (7, 4))
 CY, GAT, SCA, PEC, WAKE, FIX, T_DMA, BW = 1.04e-3, 1.56, 3.8, 0.53e-3, 0.12, 0.03, 2.2, 250e3
-T_REM, T_FIRST = 4.4, 1.5
-KC_ON, ZB_ON, DEDUP = "S", "S", "VVS"
+T_A, T_B, T_C, T_FIRST = 2.4, 3.4, 3.9, 1.5
+KCU_GATHER = True
 BOOST = {"send": 6.0, "X0": 3.0}
-SEED, TRIES, HEAT = 3, 1500, 0.0
+SEED, TRIES, HEAT = 3, 1200, 0.0
 PLANS = {}
 
 
@@ -142,7 +146,7 @@ def plan(ops):
         while todo:
             i = todo.pop()
             for p in pred[i]:
-                if p not in seen and "rs" not in ops[i]["wr"] and ops[p]["round"] == ops[i]["round"] and ops[p]["tail"]:
+                if p not in seen and "LQ" not in ops[i]["wr"] and ops[p]["round"] == ops[i]["round"] and ops[p]["tail"]:
                     seen.add(p)
                     todo.append(p)
         for i in seen:
@@ -183,7 +187,8 @@ def rank_program(g, core, T, topo):
     where = [-1, False]
 
     def op(e, fn, rd, wr, hold, lat=0.0, sem=None, inc=1, remote=False):
-        ops.append(dict(round=where[0], tail=where[1], e=e, fn=fn, rd=list(rd), wr=list(wr), hold=hold, lat=lat, sem=sem or SEM[e], inc=inc, remote=remote))
+        ops.append(dict(round=where[0], tail=where[1], e=e, fn=fn, rd=list(rd), wr=list(wr), hold=hold, lat=lat,
+                        sem=sem or SEM[e], inc=inc, remote=remote))
 
     def cost(n, k):
         if k == "g":
@@ -208,8 +213,8 @@ def rank_program(g, core, T, topo):
         else:
             op("V", lambda: V.tensor_scalar(out, a, s1, s2, o0, o1), rd, wr, cost(n, k))
 
-    def scan(out, d0, d1, o0, o1, rd, wr, n):
-        op("V", lambda: V.tensor_tensor_scan(out, d0, d1, 0.0, o0, o1), rd, wr, cost(n, ""))
+    def scan(out, d0, d1, o0, o1, rd, wr, n, init=0.0):
+        op("V", lambda: V.tensor_tensor_scan(out, d0, d1, init, o0, o1), rd, wr, cost(n, ""))
 
     def ms(out, val, wr, n=8, k=""):
         op("V", lambda: V.memset(out, val), [], wr, cost(n, k))
@@ -219,7 +224,7 @@ def rank_program(g, core, T, topo):
 
     group = {}
 
-    def mm(out, l, r, st, sp, rd, wr, n=128, f32=False, m=128):
+    def mm(out, l, r, st, sp, rd, wr, n=128, f32=False, m=128, close=True):
         bank = wr[0]
         if st and not sp:
             group[bank] = []
@@ -228,14 +233,26 @@ def rank_program(g, core, T, topo):
             group[bank].append("~%s_%d" % (bank, len(group[bank])))
             rd, wr = rd + ["~" + bank], wr[1:] + group[bank][-1:]
         elif not st:
-            rd = rd + group[bank]
-        op("P", lambda: P.matmul(out, l, r, st, sp), rd, wr, max(min(64, m), n) * PEC * (4 if f32 else 1))
+            rd = rd + group.pop(bank, [])
+        op("P", lambda: P.matmul(out, l, r, st, sp and close), rd, wr, max(min(64, m), n) * PEC * (4 if f32 else 1))
+
+    def mms(bank, items, start=True, stop=True):
+        for j, (out, l, r, rd, n, f32) in enumerate(items):
+            end = j == len(items) - 1
+            if not start:
+                op("P", lambda out=out, l=l, r=r, end=end: P.matmul(out, l, r, False, end), rd, [bank],
+                   max(64, n) * PEC * (4 if f32 else 1))
+            else:
+                mm(out, l, r, j == 0, end, rd, [bank], n, f32, 128, stop)
+
+    def tr(out, in_, rd, bank):
+        op("P", lambda: P.transpose(out, in_, T.Ib[:]), rd + ["Ib"], [bank], 128 * PEC)
 
     def iota(out, pat, base, cm, wr, n, fl=False):
         if fl:
-            op("G", lambda: g.iota(out, pat, base, cm, allow_small_or_imprecise_dtypes=True), [], wr, 0.13 + 2 * n * CY)
+            op("G", lambda: g.iota(out, pat, base, cm, allow_small_or_imprecise_dtypes=True), [], wr + ["~G"], 0.13 + 2 * n * CY)
         else:
-            op("G", lambda: g.iota(out, pat, base, cm), [], wr, 0.13 + 2 * n * CY)
+            op("G", lambda: g.iota(out, pat, base, cm), [], wr + ["~G"], 0.13 + 2 * n * CY)
 
     dma("Y", "ldZ", T.zb[:], T.z[:], [], ["zb", "~Y"], 2 ** 12)
     dma("S", "ldM", T.msi[:], T.ms[:], [], ["msi", "~S"], 2 ** 18)
@@ -244,113 +261,144 @@ def rank_program(g, core, T, topo):
     dma("Y", "ldX", T.X[:, 0:2048], T.tx[:, 0:2048], [], ["X", "~Y"], 2 ** 20 + 2 ** 17)
     dma("S", "ldK", T.kti[:], T.kt[:], [], ["kti", "~S"], 2 ** 20 + 2 ** 17 + 2 ** 18)
 
-    iota(T.tmpi[:, 0:128], [[-1, 128]], 0, 1, ["tmpi", "~G"], 128)
-    iota(T.tmpj[:, 0:128], [[-16, 8], [0, 16]], 0, 1, ["tmpj", "~G"], 128)
-    iota(T.ui[:, 0:1], [[0, 1]], 0, 1, ["ui", "~G"], 1)
-    iota(T.tmpj[:, 160:176], [[1, 16]], 0, 0, ["J16", "~G"], 16)
-    iota(T.tmpj[:, 128:144], [[-1, 16]], 30, 0, ["tmpj2", "~G"], 16)
-    iota(T.Wm[:], [[0, 16], [1, 16]], 0, 0, ["Wm", "~G"], 256, True)
-    iota(T.KCM[:], [[0, 8], [1, 16]], KBASE + 2048, 16, ["KCM", "~G"], 128, True)
-    iota(T.KCX[:], [[0, 8], [1, 16]], KBASE, 16, ["KCX", "~G"], 128, True)
-    iota(T.Kw[:, 512:640], [[0, 128]], 0, 0, ["Kwd", "~G"], 128, True)
-    iota(T.sz0[:], [[0, 8 * ZW]], 0, 0, ["sz0", "~G"], 8 * ZW, True)
-    iota(T.sz1[:], [[0, 8 * ZW]], 0, 0, ["sz1", "~G"], 8 * ZW, True)
-    iota(T.TRI[:], [[1, 128]], 0, 0, ["TRI", "~G"], 128, True)
-    iota(T.tabN[:], [[256, 640]], 0, 0, ["tabN", "~G"], 640, True)
-    ms(T.UL[:], 0.0, ["UL"], 2048, "h")
-    ms(T.D0S[:], 1.0, ["D0S"], 256)
-    ms(T.D8[:], 0.0, ["D8"], 128)
-    ms(T.D16[:], 0.0, ["D16"], 128)
-    ms(T.DA[:], 2.0, ["DA"], 128)
-    J16 = T.tmpj[:, 160:176]
-    ms(T.ZX[:, 128:384], 0.0, ["ZX0"], 256, "h")
-    ms(T.ZM[:, 128:256], 0.0, ["ZM0"], 128, "h")
+    iota(T.tmpi[:, 0:128], [[-1, 128]], 0, 1, ["tmpi"], 128)
+    iota(T.tmpj[:, 0:128], [[-16, 8], [0, 16]], 0, 1, ["tmpj"], 128)
+    iota(T.ui[:, 0:1], [[0, 1]], 0, 1, ["ui"], 1)
+    iota(T.tmpj[:, 160:176], [[1, 16]], 0, 0, ["J16"], 16)
+    iota(T.Wm[:, 0:128], [[0, 8], [1, 16]], 0, 0, ["Wma"], 128, True)
+    iota(T.tmpj[:, 192:224:2], [[128, 2], [0, 8]], 0, 1, ["CIa"], 16)
+    iota(T.tmpj[:, 193:224:2], [[-128, 2], [0, 8]], 255, -1, ["CIb"], 16)
+    iota(T.CM[:, 16:24, :], [[0, 72]], 256, 16, ["CMa"], 72, True)
+    iota(T.CM[:, 0:16, 0:8], [[0, 8], [8, 2], [1, 8]], 0, 16, ["CMb"], 128, True)
+    iota(T.CX[:, :, 0:8], [[0, 8], [8, 2], [1, 8]], 0, 16, ["CXa"], 128, True)
+    iota(T.CX[:, :, 8], [[0, 16]], YC, 1, ["CXb"], 16, True)
+    iota(T.CX[:, 1:16:2, 10], [[0, 8]], 2 ** 24 - 4096 + YA, 8, ["CXc"], 8, True)
+    iota(T.C30[:], [[0, 8], [-2, 16]], 30, 0, ["C30"], 128, True)
+    iota(T.Kw[:, 512:640], [[0, 128]], 0, 0, ["Kwd"], 128, True)
+    iota(T.Wm[:, 256:272], [[0, 16]], 0, 0, ["Wmz"], 16, True)
+    iota(T.DX[:], [[0, 192]], 1, 0, ["DX"], 192, True)
+    iota(T.yw[:, YA:YW], [[0, YW - YA]], 0, 0, ["ya2"], YW - YA, True)
+    iota(T.UL[:], [[0, 2048]], 0, 0, ["UL"], 2048, True)
     ms(T.ones[:], 1.0, ["ones"], 128, "h")
-    ms(T.A8[:], 0.0, ["A8"])
-    ms(T.WR[:, 2:4, 24:32], 0.0, ["WR0"])
-    ms(T.D0S[:, 0:256:16], 0.0, ["D0S"])
-    ms(T.D8[:, 0:128:8], BIG, ["D8"])
-    ms(T.D16[:, 0:128:16], BIG, ["D16"])
-    ms(T.DA[:, 0:128:16], -BIG, ["DA"])
+
+    def fill(out, val, wr, n=8, rd=()):
+        act(out, T.ones[:, 0:n], ["ones"] + list(rd), wr, n, scale=val)
+    for nm in ("sz0", "sz1"):
+        cp(T[nm][:, :, 2], T.ones[:], ["ones"], [nm], 128, "h")
+    for nm in ("sc0", "sc1"):
+        cp(T[nm][:], T.ones[:, 0:64], ["ones"], [nm], 64, "h")
+    ms(T.D16[:], 0.0, ["D16"], 128)
+    ms(T.D16[:, 0:128:16], HUGE, ["D16"])
+    act(T.DA[:], T.D16[:], ["D16"], ["DA"], 128, scale=-1.0)
+    fill(T.e8[:], 8.0, ["e8"], 128)
+    fill(T.DX[:, 8:192:12], -1.0, ["DXa"], 16, ["DX"])
+    fill(T.DX[:, 9:192:12], -1.0, ["DXb"], 16, ["DX"])
+    fill(T.DX[:, 10:192:24], -1.0, ["DXc"], 8, ["DX"])
+    fill(T.DX[:, 23:192:24], -1.0, ["DXd"], 8, ["DX"])
+    DXall = ["DX" + x for x in "abcd"]
+    act(T.D2s[:], T.D16[:, 0:128:8], ["D16"], ["D2s"])
+    ms(T.CM[:, 0:16, 8], 0.0, ["CMc"])
+    ms(T.CX[:, 0:16:2, 9], BIG / 2, ["CXd"])
+    ms(T.CX[:, 1:16:2, 9], -BIG / 2, ["CXe"])
+    fill(T.CX[:, 0:16:2, 10], -HUGE, ["CXf"])
+    fill(T.CX[:, 0:16:2, 11], HUGE, ["CXg"])
+    fill(T.CX[:, 1:16:2, 11], -HUGE, ["CXh"])
+    CXall = ["CX" + x for x in "abcdefgh"]
+    fill(T.CG[:, 0:16:2], 1025.0, ["CGa"])
+    fill(T.CG[:, 1:16:2], 1024.0, ["CGb"])
+    fill(T.CC[:, 0:16:2], -256 * ZO, ["CCa"])
+    fill(T.S32[:, 0:32:2], -15.5, ["S32c"], 16)
+    ms(T.WX[:, 0:2, :], 0.0, ["WX"])
+    ms(T.WM[:, 0:2, :], 0.0, ["WM"])
     ts(T.Ib[:], T.tmpi[:, 0:128], 0.0, None, ALU.is_equal, None, ["tmpi"], ["Ib"], 128)
+    ts(T.TRI[:], T.tmpi[:, 0:128], 0.0, -16.0, ALU.is_ge, ALU.mult, ["tmpi"], ["TRI"], 128)
     ts(T.tmpi[:, 128:256], T.tmpj[:, 0:128], 4, None, ALU.arith_shift_right, None, ["tmpj"], ["tmpi2"], 128)
-    ts(T.uj[:, 0:1], T.ui[:, 0:1], 15, None, ALU.bitwise_and, None, ["ui"], ["uj"])
+    ts(T.c8[:, 0:1], T.ui[:, 0:1], 15, None, ALU.bitwise_and, None, ["ui"], ["c8"])
+    ts(T.c8[:, 1:2], T.ui[:, 0:1], 4, None, ALU.arith_shift_right, None, ["ui"], ["c8b"])
+    ts(T.c8[:, 2:3], T.ui[:, 0:1], 4, 1, ALU.arith_shift_right, ALU.bitwise_and, ["ui"], ["c8c"])
+    ts(T.c8[:, 3:4], T.ui[:, 0:1], 7, None, ALU.bitwise_and, None, ["ui"], ["c8d"])
     ts(T.BD[:], T.tmpi[:, 128:256], 0.0, None, ALU.is_equal, None, ["tmpi2"], ["BD"], 128)
-    cp(T.pm[:, 0:1], T.uj[:, 0:1], ["uj"], ["pm"])
-    for k in range(16):
-        ts(T.E[:, k:2048:16], T.Ib[:], 0.5, None, ALU.mult, None, ["Ib"], ["E%d" % k], 128, "h")
-    Eall = ["E%d" % k for k in range(16)]
-    Ih = T.E[:, 0:2048:16]
-    G8 = T.BD[:, 0:128:16]
-    for name, sc in (("If", 1.0), ("nIf", -1.0), ("I16", 1.0 / 16), ("I37", 37.0), ("Inh", -0.5), ("Inq", -0.25)):
-        act(T[name][:], T.Ib[:], ["Ib"], [name], 128, scale=sc)
-    act(T.ZX[:, 0:128], T.BD[:], ["BD"], ["ZX1"], 128, scale=4096.0)
-    act(T.ZX[:, 384:512], T.BD[:], ["BD"], ["ZX2"], 128, scale=-1.0)
-    act(T.ZM[:, 0:128], T.BD[:], ["BD"], ["ZM1"], 128, scale=4096.0)
-    act(T.ZM[:, 256:384], T.BD[:], ["BD"], ["ZM2"], 128)
-    act(T.WR[:, 0, 0:8], G8, ["BD"], ["Wa"], scale=8192.0)
-    act(T.WR[:, 0, 8:24:2], G8, ["BD"], ["Wb"], scale=2 * BIG)
-    act(T.WR[:, 0, 9:24:2], G8, ["BD"], ["Wc"], scale=-2 * BIG)
-    act(T.WR[:, 0, 24:32], G8, ["BD"], ["Wd"], scale=-2.0)
-    act(T.WR[:, 1, :], T.WR[:, 0, :], ["Wa", "Wb", "Wc", "Wd"], ["We"])
-    act(T.WR[:, 1, 8:24], T.WR[:, 0, 8:24], ["Wb", "Wc"], ["We"], scale=-1.0)
-    act(T.WR[:, 2:4, 0:8], T.WR[:, 0:2, 0:8], ["Wa", "We"], ["Wf"])
-    act(T.WR[:, 2, 8:16], G8, ["BD"], ["Wg"], scale=-2.0)
-    act(T.WR[:, 3, 8:16], G8, ["BD"], ["Wh"], scale=2.0)
-    act(T.WR[:, 2:4, 16:24], T.WR[:, 0:2, 24:32], ["Wd", "We"], ["Wi"], scale=-1.0)
-    WRall = ["W" + x for x in "abcdefghi"] + ["WR0"]
-    act(T.WN[:], T.WR[:], WRall, ["WN"], 128, scale=-2.0)
-    pm, pm2, pm3 = T.pm[:, 0:1], T.pm[:, 1:2], T.pm[:, 2:3]
-    ts(T.DM[:], T.Wm[:], pm, None, ALU.is_equal, None, ["Wm", "pm"], ["DM"], 256)
+    cp(T.pm[:, 0:4], T.c8[:, 0:4], ["c8", "c8b", "c8c", "c8d"], ["pm"])
+    pm, pg, podd, p8, pm2, h1, h0 = (T.pm[:, j:j + 1] for j in range(7))
     ts(pm2, pm, 2.0, 1.0, ALU.mult, ALU.add, ["pm"], ["pm2"])
-    ts(pm3, pm, 8.0, None, ALU.is_ge, None, ["pm"], ["pm3"])
+    ts(h1, pm, 8.0, None, ALU.is_ge, None, ["pm"], ["h1"])
+    ts(h0, pm, 8.0, None, ALU.is_lt, None, ["pm"], ["h0"])
+    ts(T.EXD[:, 0:1], p8, 8.0, pg, ALU.mult, ALU.add, ["pm"], ["EXD"])
+    G8 = T.BD[:, 0:128:16]
+    for name, sc in (("If", 1.0), ("nBI", -BIG), ("I37", 37.0), ("Inh", -0.5), ("I8k", 8192.0), ("In1k", -1024.0),
+                     ("nIb", -1.0)):
+        act(T[name][:], T.Ib[:], ["Ib"], [name], 128, scale=sc)
+    for half in range(2):
+        sg = 2 * half - 1
+        act(T.WX[:, half, 2 * half:32:4], G8, ["BD", "WX"], ["WXa%d" % half], scale=8192.0)
+        act(T.WX[:, half, 1:32:4], G8, ["BD", "WX"], ["WXb%d" % half], scale=2 * BIG * sg)
+        act(T.WX[:, half, 3:32:4], G8, ["BD", "WX"], ["WXc%d" % half], scale=-2 * BIG * sg)
+        act(T.WM[:, half, 2 * half:32:4], G8, ["BD", "WM"], ["WMa%d" % half], scale=8192.0)
+        act(T.WM[:, half, 1:32:4], G8, ["BD", "WM"], ["WMb%d" % half], scale=2.0 * sg)
+        act(T.WM[:, half, 3:32:4], G8, ["BD", "WM"], ["WMc%d" % half], scale=-2.0 * sg)
+        act(T.WM[:, half, 33:48:2], G8, ["BD", "WM"], ["WMd%d" % half], scale=512.0)
+    WXall = ["WX%s%d" % (x, j) for x in "abc" for j in range(2)]
+    WMall = ["WM%s%d" % (x, j) for x in "abcd" for j in range(2)]
+    act(T.WX[:, 2:4, :], T.WX[:, 0:2, :], WXall, ["WXn"], 64, scale=-2.0)
+    act(T.WM[:, 2:4, :], T.WM[:, 0:2, :], WMall, ["WMn"], 96, scale=-2.0)
+    ts(T.DM[:, 0:128], T.Wm[:, 0:128], pm, None, ALU.is_equal, None, ["Wma", "pm"], ["DM0"], 128)
+    for j in range(2):
+        cp(T.DM[:, 128 << j:256 << j], T.DM[:, 0:128 << j], ["DM%d" % i for i in range(j + 1)], ["DM%d" % (j + 1)], 128 << j, "h")
+    for j in range(1, 4):
+        dma("Y", "cpD", T.DM[:, 512 * j:512 * j + 512], T.DM[:, 0:512], ["DM0", "DM1", "DM2", "kti", "X"], ["DM%d" % (j + 2)], 2 ** 17)
+    DMall = ["DM%d" % j for j in range(6)]
+    for gi in range(8):
+        cp(T.CH[:, :, 16 * gi:16 * gi + 16], T.Ib[:], ["Ib"], ["CH%d" % gi], 128, "h")
+    CHall = ["CH%d" % gi for gi in range(8)]
     act(T.Kcol[:], T.ones[:], ["ones", "pm"], ["Kcol"], 128, scale=pm)
     ts(T.SL[:], T.tmpj[:, 160:168], 16.0, pm, ALU.mult, ALU.add, ["J16", "pm"], ["SL"])
-    cp(T.EX[:], J16, ["J16"], ["EX"])
+    cp(T.EX[:], T.tmpj[:, 160:168], ["J16"], ["EX"])
+    ts(T.EXS[:], T.tmpj[:, 160:168], 16.0, None, ALU.add, None, ["J16"], ["EXS"])
+    ts(T.EXA[:], T.tmpj[:, 160:168], 16.0, 15.0, ALU.mult, ALU.add, ["J16"], ["EXA"])
     act(T.Uw[:], T.BD[:], ["BD", "pm2"], ["Uw"], 128, scale=pm2)
-    if "V" in DEDUP:
-        ts(T.TRm[:], T.Wm[:, 0:128], pm, None, ALU.is_ge, None, ["Wm", "pm"], ["TRm"], 128)
-    act(T.S32[:], T.SL[:], ["SL"], ["S32"], scale=32.0)
-    act(T.S32h[:, 0:4], T.SL[:, 0:4], ["SL"], ["S32h"], scale=32.0)
-    act(T.S32h[:, 4:8], T.SL[:, 0:4], ["SL"], ["S32g"], scale=32.0)
-    act(T.D512[:], T.SL[:], ["SL"], ["D512"], bias=512.0)
-    ts(T.EX3[:, 0:8], T.tmpj[:, 160:168], 2.0, pm3, ALU.mult, ALU.add, ["J16", "pm3"], ["EX3a"])
-    ts(T.EX3[:, 8:16], T.tmpj[:, 168:176], 8.0, None, ALU.add, None, ["J16"], ["EX3b"])
-    ts(T.tmpj[:, 144:160], T.tmpj[:, 128:144], 15, None, ALU.bitwise_and, None, ["tmpj2"], ["tmpj3"])
-    ts(T.tabA[:], T.tmpj[:, 144:160], pm, None, ALU.is_equal, None, ["tmpj3", "pm"], ["tabA"])
+    act(T.BDb[:], T.BD[:], ["BD"], ["BDb"], 128)
+    act(T.S32[:, 1:16:2], T.SL[:], ["SL"], ["S32a"], scale=32.0)
+    act(T.S32[:, 17:24:2], T.SL[:, 0:4], ["SL"], ["S32b"], scale=32.0)
+    act(T.S32[:, 25:32:2], T.SL[:, 0:4], ["SL"], ["S32d"], scale=32.0)
+    act(T.D512[:, 0:8], T.SL[:], ["SL"], ["D512a"], bias=512.0)
+    act(T.D512[:, 8:16], T.SL[:], ["SL"], ["D512b"], bias=512.0)
+    c0 = -8193.0 * BO - 16384.0
+    act(T.CC[:, 3:16:2], T.SL[:, 0:7], ["SL"], ["CCb"], scale=-16386.0, bias=c0)
+    act(T.CC[:, 1:2], T.SL[:, 7:8], ["SL"], ["CCc"], scale=-16386.0, bias=c0)
     for gi in range(8):
         act(T.UL[:, 16 * gi:16 * gi + 129 * 15 + 1:129], T.Uw[:, 16 * gi:16 * gi + 16], ["Uw", "UL"], ["UL%d" % gi])
     ULall = ["UL%d" % gi for gi in range(8)]
-    cp(T.Mu[:], T.msi[:], ["msi"], ["Mu0", "Mu1", "Mu2"], 128)
-    ts(T.Mf[:], T.msi[:], -OFF, None, ALU.add, None, ["msi"], ["Mf"], 128)
+    for b in range(8):
+        ts(T.BI[:, b:256:8], T.tmpj[:, 192:224], b, 1, ALU.arith_shift_right, ALU.bitwise_and, ["CIa", "CIb"], ["BI%d" % b], 32)
+    cp(T.bits[:], T.BI[:], ["BI%d" % b for b in range(8)], ["bits", "bits2"], 256)
+    mms("EA", [(T.EA[:, 128 * j:128 * j + 128], T.bits[:, 128 * j:128 * j + 128], T.Ib[:], ["bits", "bits2", "Ib"], 128, False)
+               for j in range(2)])
+    act(T.BT[:, 0:256], T.EA[:, 0:256], ["EA"], ["BTa"], 256)
+    cp(T.BT[:, 256:512], T.BT[:, 0:256], ["BTa"], ["BTb"], 256, "h")
+    cp(T.Mu[:], T.msi[:], ["msi"], ["MuA", "MuB"], 128)
+    ts(T.lz0[:, :, 0], T.msi[:], -2048.0, None, ALU.add, None, ["msi", "lz0"], ["lz0m"], 128)
+    ts(T.lz0[:, :, 1], T.zb[:], ZO, None, ALU.add, None, ["zb", "lz0"], ["lz0a"], 128, "h")
+    ts(T.lz0[:, :, 3], T.zb[:], ZO, None, ALU.add, None, ["zb", "lz0"], ["lz0b"], 128, "h")
     cp(T.Kw[:, 0:512], T.kti[:], ["kti", "Kwd"], ["Kw"], 512)
 
-    peers = []
-    taken = {True: 0, False: 0}
-    for h in range(1, N):
-        dst = T.cores[(rank + h) % N]
-        rid, pid, _ = topo.addr(dst)
-        eng = topo.engines(core, dst)
-        per = len(eng) // N
-        far = topo.die(dst) != topo.die(core)
-        mine = eng[int(far)::2][per * taken[far]:per * taken[far] + per]
-        taken[far] += 1
-        peers.append((DstId(rid=rid, pnc=pid), sum(1 << e for e in mine), per, h))
-    arrive = sum(p[2] for p in peers)
-
-    def send(src_of, dst_of, sem, rd, wr):
+    def send(call, src_of, dst_of, sem, rd, wr, lat, first=0.0):
+        trs, used = [], 0
+        for h, ne in call:
+            dst = T.cores[(rank + h) % N]
+            rid, pid, _ = topo.addr(dst)
+            mask = sum(1 << e for e in topo.engines(core, dst)[used:used + ne])
+            used += ne
+            trs.append((DstId(rid=rid, pnc=pid), mask, h))
         op("G", lambda: g.remote_dma_fused(
             [RemoteDMATransfer(dst_ids=[d], dma_engine_mask=m, remote_sem=T.sem[sem], src=src_of(h),
-                               dst=dst_of((h + 1) % N)) for d, m, _, h in peers], local_sem=T.sem.sent),
-           rd, wr + ["~R"], 0.5 + (T_FIRST if sem == "arC" else 0), T_REM - 0.5,
-           sem, arrive, True)
+                               dst=dst_of((h + 1) % N)) for d, m, h in trs], local_sem=T.sem.sent),
+           rd, wr + ["~R"], 0.5 + first, lat, sem, used, True)
 
     def tags(t, s0, n):
         return ["%s%d" % (t, b) for b in range(s0 // 8, (s0 + n) // 8)]
 
     def gather(e, t, lst, lname, s0, n):
-        base = 2048 if t == "m" else 0
-        out = T.xm[:, base + 16 * s0:base + 16 * (s0 + n)]
+        out = (T.xm if t == "m" else T.yw)[:, 16 * s0:16 * (s0 + n)]
         src = T.X[:].indirect(lst[:, s0:s0 + n])
         lname = lname + ["Xb"]
         if e == "S":
@@ -359,249 +407,210 @@ def rank_program(g, core, T, topo):
             ts(out, src, 0.5, None, ALU.mult, None, ["X"] + lname, tags(t, s0, n), 16 * n, "g")
 
     def mins(t, s0, n):
-        base = 2048 if t == "m" else 0
-        bank = "ZE%d" % (s0 // 32)
-        o = 16 * (s0 % 32)
-        tt(T.mn[:, base + 16 * s0:base + 16 * (s0 + n)], T.xm[:, base + 16 * s0:base + 16 * (s0 + n)],
-           T[bank][:, o:o + 16 * n], ALU.min, tags(t, s0, n) + [bank], tags("n" + t, s0, n) + ["~n"], 16 * n, "")
+        src, out = (T.xm, T.mnm) if t == "m" else (T.yw, T.mnx)
+        bank, o = ("ZA", "ZB")[s0 // 64], s0 % 64
+        tt(out[:, 16 * s0:16 * (s0 + n)], src[:, 16 * s0:16 * (s0 + n)], T[bank][:, o:o + n, :], ALU.min,
+           tags(t, s0, n) + [bank], tags("n" + t, s0, n) + ["~n"], 16 * n, "h")
+
+    def to_list(bank, val, rd):
+        return [(T[bank][:, 8 * h:8 * h + 8], T.CH[:, h, :], val, CHall + rd, 8, False) for h in range(8)]
 
     XM, XX = tags("m", 0, 128), tags("x", 0, 128)
 
     for r in range(RO):
         last = r == RO - 1
         where[0], where[1] = r, False
-        lz, sz = T["lz%d" % max(r, 1)], T["sz%d" % min(r, 1)]
-        nlz = ["lz%d" % r, "lz%dr" % r]
-        Mf, nMf = (lz[:, 0:384:3], nlz) if r else (T.Mf[:], ["Mf"])
+        lz, sz, sc = T["lz%d" % r], T["sz%d" % r], T["sc%d" % r]
+        nA = ["lz0m", "lz0a", "lz0b"] if r == 0 else ["lz%do" % r, "lz%dA" % r]
+        nB = nA if r == 0 else ["lz%dB" % r]
+        nz = nA + nB
+        M1, z1 = lz[:, :, 0], lz[:, :, 1]
         if r:
-            ts(T.Mu[:, 16:32], lz[:, ZW:2 * ZW:3], OFF, None, ALU.add, None, nlz[:1], ["Mu1"], 16)
-            ts(T.Mu[:, 32:128], lz[:, 2 * ZW:384:3], OFF, None, ALU.add, None, nlz, ["Mu2"], 96)
-            ts(T.Mu[:, 0:16], lz[:, 0:ZW:3], OFF, None, ALU.add, None, nlz, ["Mu0"], 16)
-            if ZB_ON == "S":
-                act(T.zb[:], lz[:, 1:384:3], nlz, ["zb"], 128)
-            else:
-                cp(T.zb[:], lz[:, 1:384:3], nlz, ["zb"], 128)
+            ts(T.Mu[:, 0:64], lz[:, 0:64, 0], 2048.0, None, ALU.add, None, nA, ["MuA"], 64, "h")
+            ts(T.Mu[:, 64:128], lz[:, 64:128, 0], 2048.0, None, ALU.add, None, nB, ["MuB"], 64, "h")
         for e, s0, n in G_M[r]:
-            gather(e, "m", T.Mu, ["Mu%d" % j for j in range(min(s0 // 16, 2), min((s0 + n - 1) // 16, 2) + 1)], s0, n)
-        mm(T.PA[:, 0:128], T.zb[:], T.Ib[:], True, True, ["zb", "Ib"], ["PA"])
-        cp(T.zT[:], T.PA[:, 0:128], ["PA"], ["zT"], 128)
+            gather(e, "m", T.Mu, ["MuA" if s0 < 64 else "MuB"], s0, n)
+        for j, (src, bank) in enumerate((("EA", "ZA"), ("EB", "ZB"))):
+            mms(src, [(T[src][:, 0:128], lz[:, 64 * j:64 * j + 64, 1:4:2], T.Ib[:], (nA, nB)[j] + ["Ib"], 128, False)])
+            act(T.zT[:, 128 * j:128 * j + 128], T[src][:, 0:128], [src], ["zT%d" % j], 128, scale=0.5, bias=-ZO / 2)
+            for k in range(0, 16, 2):
+                tr(T[bank][:, :, k:k + 2], T.zT[:, 128 * j:128 * j + 128], ["zT%d" % j], bank)
         if r:
-            for il in range(16):
-                mm(T.PA[:, 384:392], T.UL[:, 128 * il:128 * il + 128], T.zb[:, il:128:16], il == 0, il == 15,
-                   ULall + ["zb"], ["PA"], 8)
-            nxt, nn = lz[:, 2:384:ZW], nlz
-            if r == 1:
-                tt(T.s3[:], nxt, T.lc[:, 0:32:4], ALU.add, nlz + ["lc", "lcr"], ["s3"])
-                nxt, nn = T.s3[:], nlz + ["s3"]
-            tt(T.s2[:], T.PA[:, 384:392], nxt, ALU.subtract, ["PA"] + nn, ["s2"])
-            tt(T.cu[:], T.s2[:], lz[:, 5:384:ZW], ALU.mult, ["s2"] + nlz, ["cu"])
-            tt(T.ci[:], T.cu[:], nxt, ALU.add, ["cu"] + nn, ["ci"])
-            ts(T.cj[:], T.ci[:], 511, None, ALU.bitwise_and, None, ["ci"], ["cj"])
-        for b4 in range(4):
-            mm(T["ZE%d" % b4][:], T.zT[:], T.E[:, 512 * b4:512 * b4 + 512], True, True, ["zT"] + Eall, ["ZE%d" % b4], 512)
+            lc, sp, beta = T["lc%d" % (r - 1)], T["sc%d" % (r - 1)], lz[:, 0:128:16, 2]
+            mms("PA", [(T.PA[:, 384:400], T.If[:], T.CC[:], ["If", "CCa", "CCb", "CCc"], 16, True),
+                       (T.PA[:, 385:386], T.Ib[:], lc[:, 0:1], ["Ib", "lc%d" % (r - 1)], 8, False),
+                       (T.PA[:, 387:388], T.Ib[:], sp[:, 0:1], ["Ib", "sc%d" % (r - 1)], 8, False),
+                       (T.PA[:, 389:400:2], T.Ib[:], lc[:, 16:64:8], ["Ib", "lc%d" % (r - 1)], 8, False),
+                       (T.PA[:, 385:400:2], T.Ib[:], beta, ["Ib"] + nz, 8, False),
+                       (T.PA[:, 385:400:2], T.I8k[:], beta, ["I8k"] + nz, 8, False)] +
+                [(T.PA[:, 384:400:2], T.UL[:, 128 * il:128 * il + 128], lz[:, il:128:16, 1], ULall + nz, 8, False)
+                 for il in range(16)])
+            scan(T.ci[:], T.D2s[:], T.PA[:, 384:400], ALU.add, ALU.min, ["D2s", "PA"], ["ci"], 16)
+            ts(T.cj[:], T.ci[:, 1:16:2], 511, None, ALU.bitwise_and, None, ["ci"], ["cj"])
         cp(T.cu16[:], T.cj[:], ["cj"], ["cu16"])
         if r == 0:
-            ts(T.kc[:], T.kti[:].indirect(T.cu16[:]), -OFF, None, ALU.add, None, ["kti", "cu16"], ["kc"], 128, "g")
-        elif KC_ON == "S":
+            cp(T.kcu[:], T.kti[:].indirect(T.cu16[:]), ["kti", "cu16"], ["kcu"], 128, "g")
+            ts(T.kc[:], T.kcu[:], -OFF, None, ALU.add, None, ["kcu"], ["kc"], 128)
+        elif KCU_GATHER:
+            cp(T.kcu[:], T.Kw[:].indirect(T.cu16[:]), ["Kw", "cu16"], ["kcu"], 128, "g")
             act(T.kc[:], T.Kw[:].indirect(T.cu16[:]), ["Kw", "cu16"], ["kc"], 128, "g", bias=-OFF)
         else:
-            ts(T.kc[:], T.Kw[:].indirect(T.cu16[:]), -OFF, None, ALU.add, None, ["Kw", "cu16"], ["kc"], 128, "g")
-        ts(T.kcu[:], T.kc[:], OFF, None, ALU.add, None, ["kc"], ["kcu"], 128)
+            act(T.kc[:], T.Kw[:].indirect(T.cu16[:]), ["Kw", "cu16"], ["kc"], 128, "g", bias=-OFF)
+            ts(T.kcu[:], T.kc[:], OFF, None, ALU.add, None, ["kc"], ["kcu"], 128)
         for e, s0, n in G_X[r]:
             gather(e, "x", T.kcu, ["kcu"], s0, n)
-        ts(T.ci[:], T.cj[:], 2.0, None, ALU.mult, None, ["cj"], ["ci"])
-        ts(T.c2m[:], T.ci[:], 511, None, ALU.bitwise_and, None, ["ci"], ["c2m"])
-        if r == 0:
-            ms(T.sc[:], 0.0, ["sc"], 32)
-            cp(T.sc[:, 0:32:4], T.c2m[:], ["c2m"], ["sc"])
-            send(lambda h: T.sc[:, 4 * h:4 * h + 4], lambda s: T.lc[:, 4 * s:4 * s + 4], "arC", ["sc", "kti", "X", "Xb"], ["lcr"])
-            act(T.lc[:, 4:8], T.sc[:, 0:4], ["sc"], ["lc"])
-        for lo, hi in ((0, 128), (256, 384)):
-            mm(T.PA[:, lo:hi], T.Uw[:], T.zb[:], True, False, ["Uw", "zb"], ["PA"])
-            mm(T.PA[:, lo:hi], T.I37[:], T.Kcol[:], False, False, ["I37", "Kcol"], ["PA"])
-            mm(T.PA[:, lo:hi], T.If[:], T.kc[:], False, not lo, ["If", "kc"], ["PA"], 128, True)
-            if not lo:
-                act(T.yy[:], T.PA[:, 0:128], ["PA"], ["yy"], 128, bias=MAGIC4)
-                act(T.ny[:], T.yy[:], ["yy"], ["ny"], 128, bias=MAGIC4, scale=-1.0)
-                mm(T.PA[:, 128:256], T.If[:], T.kc[:], True, False, ["If", "kc"], ["PA"], 128, True)
-                mm(T.PA[:, 128:256], T.nIf[:], Mf, False, True, ["nIf"] + nMf, ["PA"], 128, True)
-        mm(T.PA[:, 256:384], T.nIf[:], Mf, False, False, ["nIf"] + nMf, ["PA"], 128, True)
-        mm(T.PA[:, 256:384], T.Ib[:], T.ny[:], False, True, ["Ib", "ny"], ["PA"])
-        act(T.DD[:], T.PA[:, 128:384], ["PA"], ["DD"], 256)
-        mm(T.PM[:, 0:384], T.zb[:], T.ZM[:], True, False, ["zb", "ZM0", "ZM1", "ZM2"], ["PM"], 384)
-        mm(T.PM[:, 0:128], T.If[:], T.KCM[:], False, False, ["If", "KCM"], ["PM"], 128, True)
+        ts(T.c8[:], T.cj[:], 255, None, ALU.bitwise_and, None, ["cj", "pm"], ["c8"])
+        c2m = sc[:, 0:64:8]
+        ts(c2m, T.c8[:], 2.0, None, ALU.mult, None, ["c8"], ["sc%d" % r])
+        if not last:
+            send(CALL_C, lambda h, a=sc: a[:, 8 * h:8 * h + 8], lambda s, a=T["lc%d" % r]: a[:, 8 * s:8 * s + 8], "arC%d" % r,
+                 ["sc%d" % r] + (["kti", "X", "Xb"] if r == 0 else []), ["lc%d" % r], T_C, T_FIRST if r == 0 else 0.0)
+        mm(T.PM[:, 0:24, 0:9], T.If[:], T.CM[:], True, False, ["If", "CMa", "CMb", "CMc"], ["PM"], 216, True)
+        if r:
+            for j in range(2):
+                for b in range(2):
+                    mm(T.PM[:, j:16:2, 8], T.e8[:], T.cb[:, b:16:2], False, False, ["e8", "cb"], ["PM"], 8)
         for s0, n in CH_M:
             mins("m", s0, n)
         for k in range(16):
-            mm(T.PM[:, k:384:16], T.xm[:, 2048 + k:4096:16], T.WR[:, 2 + k // 8, 0:24], False, False, XM + WRall,
-               ["PM", "~rm%d" % k], 24)
+            mm(T.PM[:, 0:24, k % 8:9:8 - k % 8], T.xm[:, k:2048:16], T.WM[:, k // 8, :], False, False, XM + WMall,
+               ["PM", "~rm%d" % k], 48)
         for k in range(16):
-            mm(T.PM[:, k:384:16], T.mn[:, 2048 + k:4096:16], T.WN[:, 2 + k // 8, 0:24], False, k == 15,
-               ["n" + x for x in XM] + ["WN", "~rm%d" % k], ["PM"], 24)
-        scan(T.msum[:], T.D0S[:], T.PM[:, 128:384], ALU.mult, ALU.add, ["D0S", "PM"], ["msum"], 256)
-        scan(T.mmin[:], T.D16[:], T.PM[:, 0:128], ALU.add, ALU.min, ["D16", "PM"], ["mmin"], 128)
-        act(T.cmpv[:, 128:256], T.PM[:, 256:384], ["PM"], ["cmpb"], 128, scale=16.0)
-        TD, TS, mk = T.msum[:, 15:128:16], T.msum[:, 143:256:16], T.mmin[:, 15:128:16]
-        act(T.aTD[:], TD, ["msum"], ["aTD"], func=ACT.Abs)
-        tt(T.thr[:], T.aTD[:], T.A8[:], ALU.add, ["aTD", "A8"], ["thr"])
-        act(T.thrT[:, 0:16:2], T.thr[:], ["thr"], ["thrTa"], bias=-0.5 * BIG, scale=BIG)
-        act(T.thrT[:, 1:16:2], T.thr[:], ["thr"], ["thrTb"], func=ACT.Relu, bias=-BIG, scale=BIG)
-        mm(T.PX[:], T.zb[:], T.ZX[:], True, False, ["zb", "ZX0", "ZX1", "ZX2"], ["PX"], 512)
-        mm(T.PX[:, 0:128], T.If[:], T.KCX[:], False, False, ["If", "KCX"], ["PX"], 128, True)
-        mm(T.PX[:, 384:512], T.I16[:], T.cmpv[:, 128:256], False, False, ["I16", "cmpb"], ["PX"], 128, True)
-        mm(T.PX[:, 128:384:16], T.If[:], T.thrT[:], False, False, ["If", "thrTa", "thrTb"], ["PX"], 16, True)
+            mm(T.PM[:, 0:24, k % 8:9:8 - k % 8], T.mnm[:, k:2048:16], T.WM[:, 2 + k // 8, :], False, k == 15,
+               ["n" + x for x in XM] + ["WMn", "~rm%d" % k], ["PM"], 48)
+        LMk, nLM = T.LMk[:], ["LMk"]
+        act(LMk, T.PM[:, 0:16, 0:8], ["PM"], nLM, 128)
+        act(T.LMs[:], T.PM[:, 0:24, 8], ["PM"], ["LMs"], 24)
+        scan(T.mmin[:], T.D16[:], LMk, ALU.add, ALU.min, ["D16"] + nLM, ["mmin"], 128)
+        mk = T.mmin[:, 15:128:16]
+        ts(T.mkhi[:], mk, MAGIC4, MAGIC4, ALU.add, ALU.subtract, ["mmin"], ["mkhi"])
+        tt(T.thr[:, 0:16:2], T.LMs[:, 0:16:2], T.LMs[:, 1:16:2], ALU.max, ["LMs"], ["thra"])
+        act(T.thr[:, 1:16:2], T.thr[:, 0:16:2], ["thra"], ["thrb"], func=ACT.Relu, bias=-1.0)
+        tt(T.ce[:], mk, T.mkhi[:], ALU.subtract, ["mmin", "mkhi"], ["ce"])
+        mms("PB", to_list("PB", T.ce[:], ["ce"]))
+        act(T.LE[:], T.PB[:, 0:64], ["PB"], ["LE"], 64)
+        cp(T.eu[:], T.LE[:].indirect(T.EXD[:, 0:1]), ["LE", "EXD"], ["eu"], 16, "g")
+        act(T.y2[:], T.xm[:].indirect(T.eu[:, 0:8]), XM + ["eu"], ["y2"], 128, "g")
+        mms("PB", [(T.PB[:, 0:128], T.Inh[:], z1, ["Inh"] + nz, 128, False),
+                   (T.PB[:, 0:128], T.Ib[:], T.y2[:], ["Ib", "y2"], 128, False)])
+        act(T.ya[:], T.PB[:, 0:128], ["PB"], ["ya"], 128, func=ACT.Abs, scale=2.0, bias=ZO)
+        mms("PB", [(T.PB[:, 0:128], T.Inh[:], z1, ["Inh"] + nz, 128, False),
+                   (T.PB[:, 0:128], T.Ib[:], T.ya[:], ["Ib", "ya"], 128, False)])
+        act(T.yw[:, YC:YC + 128], T.PB[:, 0:128], ["PB"], ["yc"], 128, bias=ZO / 2 + 0.25)
+        act(T.yw[:, YA:YW:8], T.PB[:, 0:128], ["PB"], ["ya2"], 128, bias=ZO / 2 + 0.25)
+        fresh = [(T.Uw[:], z1, ["Uw"] + nz, False), (T.I37[:], T.Kcol[:], ["I37", "Kcol"], False), (T.If[:], T.kc[:], ["If", "kc"], True)]
+        mms("PA", [(T.PA[:, 0:128], l, x, rd, 128, f) for l, x, rd, f in fresh])
+        act(T.yy[:], T.PA[:, 0:128], ["PA"], ["yy"], 128, bias=MAGIC4)
+        act(T.ny[:], T.yy[:], ["yy"], ["ny"], 128, bias=MAGIC4, scale=-1.0)
+        mms("PA", [(T.PA[:, 0:128], T.If[:], T.kc[:], ["If", "kc"], 128, True),
+                   (T.PA[:, 0:128], T.nIb[:], M1, ["nIb"] + nz, 128, False),
+                   (T.PA[:, 0:128], T.Inh[:], T.ones[:], ["Inh", "ones"], 128, False),
+                   (T.PA[:, 256:384], T.Inh[:], z1, ["Inh"] + nz, 128, False)] +
+            [(T.PA[:, 128:256], l, x, rd, 128, f) for l, x, rd, f in fresh] +
+            [(T.PA[:, 128:256], T.nIb[:], M1, ["nIb"] + nz, 128, False),
+             (T.PA[:, 128:256], T.Ib[:], T.ny[:], ["Ib", "ny"], 128, False)])
+        act(T.DD[:, 0:256:2], T.PA[:, 0:128], ["PA", "h0"], ["DDa"], 128, scale=h0)
+        act(T.DD[:, 1:256:2], T.PA[:, 0:128], ["PA", "h1"], ["DDb"], 128, scale=h1)
+        act(T.DD[:, 256:384], T.PA[:, 128:256], ["PA"], ["DDc"], 128, bias=-0.5)
+        act(T.zz[:], T.PA[:, 256:384], ["PA"], ["zz"], 128, scale=-1.0, bias=ZO / 2 - 0.25)
+        tt(T.mA[:], T.LMs[:].indirect(T.EXS[:]), LMk, ALU.is_le, ["LMs", "EXS"] + nLM, ["mA"], 128, "g")
+        mms("PB", [(T.PB[:, 0:128], T.mA[:], T.Ib[:], ["mA", "Ib"], 128, False)])
+        tt(T.Wm[:, 272:400], T.PB[:, 0:128], T.DD[:, 256:384], ALU.mult, ["PB", "DDc"], ["Wmc"], 128, "")
+        act(T.bits[:, 0:128], T.BT[:].indirect(T.cu16[:]), ["BTa", "BTb", "cu16"], ["bits"], 128, "g")
+        act(T.bits[:, 128:256], T.bits[:, 0:128], ["bits", "pm"], ["bits2"], 128, scale=podd)
+        for j, bank in enumerate(("EA", "EB")):
+            for q in range(4):
+                mm(T[bank][:, 128 * q:128 * q + 128], T.Ib[:], T.TRI[:], q == 0, False, ["Ib", "TRI"], [bank])
+            for q in range(4):
+                p0, o = 64 * j + 32 * (q // 2), T[bank][:, 128 * q:128 * q + 128]
+                rd, wr = (["Et0", "Et1"], []) if q > 1 else ([], ["Et%d" % q])
+                if q % 2:
+                    mm(o, T.bits[p0:p0 + 32, 128:256], T.bits[p0:p0 + 32, 0:128], False, q == 3, ["bits", "bits2"] + rd, [bank] + wr)
+                else:
+                    mm(o, T.bits[p0:p0 + 16, 0:128], T.bits[p0:p0 + 16, 0:128], False, False, ["bits"] + rd, [bank] + wr)
+            act(T.E[:, 512 * j:512 * j + 512], T[bank][:], [bank], ["E%d" % j], 512, func=ACT.Relu, scale=1024.0, bias=-7168.0)
+        mm(T.PX[:, 0:16, 0:12], T.If[:], T.CX[:], True, False, ["If"] + CXall, ["PX"], 192, True)
+        for j in range(2):
+            mm(T.PX[:, j:16:2, 8], T.If[:], T.mkhi[:], False, False, ["If", "mkhi"], ["PX"], 8, True)
+        mm(T.PX[:, 0:16, 9], T.nBI[:], T.thr[:], False, False, ["nBI", "thra", "thrb"], ["PX"], 16, True)
         for s0, n in CH_X:
             mins("x", s0, n)
         for s0, n in MM_X:
-            for buf, wt, t, dep in ((T.xm, T.WR, "x", WRall), (T.mn, T.WN, "nx", ["WN"])):
+            for buf, wo, t, dep in ((T.yw, 0, "x", WXall), (T.mnx, 2, "nx", ["WXn"])):
                 for k in range(15 if t == "nx" else 16):
-                    mm(T.PX[s0:s0 + n, k:512:16], buf[:, 16 * s0 + k:16 * (s0 + n):16], wt[:, k // 8, :], False,
-                       False, tags(t, s0, n) + dep + ["~rx%d_%d" % (s0, k)] * (t == "nx"),
+                    mm(T.PX[s0:s0 + n, 0:16, k % 8:10:9 - k % 8], buf[:, 16 * s0 + k:16 * (s0 + n):16], T.WX[:, wo + k // 8, :],
+                       False, False, tags(t, s0, n) + dep + ["~rx%d_%d" % (s0, k)] * (t == "nx"),
                        ["PX"] + ["~rx%d_%d" % (s0, k)] * (t == "x"), 32, False, n)
-        mm(T.PX[:, 15:512:16], T.mn[:, 15:2048:16], T.WN[:, 1, :], False, True, tags("nx", 0, 128) + ["WN"], ["PX"], 32)
+        mm(T.PX[:, 0:16, 7:10:2], T.mnx[:, 15:2048:16], T.WX[:, 3, :], False, True, tags("nx", 0, 128) + ["WXn"], ["PX"], 32)
         where[1] = True
-        scan(T.rs[:], T.D0S[:], T.PX[:, 128:384], ALU.mult, ALU.add, ["D0S", "PX"], ["rs"], 256)
-        scan(T.xmin[:], T.D8[:], T.PX[:, 0:128], ALU.add, ALU.min, ["D8", "PX"], ["xmin"], 128)
-        act(T.cmpv[:, 0:128], T.PX[:, 384:512], ["PX"], ["cmpa"], 128)
-        R, R0, R1 = T.rs[:, 15:256:16], T.rs[:, 15:256:32], T.rs[:, 31:256:32]
-        tt(T.q[:], T.xmin[:, 7:128:8], R, ALU.max, ["xmin", "rs"], ["q"], 16)
-        tt(T.qm[:], T.q[:, 0:16:2], T.q[:, 1:16:2], ALU.min, ["q"], ["qm"])
-        tt(T.ksi[:], T.qm[:], mk, ALU.min, ["qm", "mmin"], ["ksi"])
+        act(T.LX[:], T.PX[:, 0:16, 0:12], ["PX"], ["LX", "~LX"], 192)
+        scan(T.LQ[:], T.LX[:], T.DX[:], ALU.min, ALU.mult, DXall + ["LX"], ["LQ"], 192, HUGE)
+        tt(T.ksi[:], T.LQ[:, 9:192:24], T.LQ[:, 22:192:24], ALU.min, ["LQ"], ["ksi"])
         ts(T.KS[:], T.ksi[:], 4095, None, ALU.bitwise_and, None, ["ksi"], ["KS"])
-        tt(T.L1[:], T.KS[:].indirect(T.EX[:, 0:8]), T.DM[:, 0:128], ALU.mult, ["KS", "EX", "DM"], ["L1"], 128, "g")
-        mm(T.PB[:, 0:8], T.L1[:], G8, True, True, ["L1", "BD"], ["PB"], 8, True)
+        tt(T.L1[:], T.KS[:].indirect(T.EX[:]), T.DM[:, 0:128], ALU.mult, ["KS", "EX", "DM0"], ["L1"], 128, "g")
+        tt(T.mK[:], T.PX[:, 0:16, 0:8], LMk, ALU.is_lt, ["PX", "~LX"] + nLM, ["mK"], 128, "")
+        tt(T.cb[:], T.LX[:, 8:192:12], T.LQ[:, 9:192:12], ALU.is_equal, ["LX", "LQ"], ["cb"], 16)
+        mms("PB", [(T.PB[:, 0:8], T.L1[:], G8, ["L1", "BD"], 8, True)])
         cp(T.selu[:], T.PB[:, 0:8], ["PB"], ["selu"])
-        ts(T.szu[:], T.PB[:, 0:8], 1.0 / 16, -15.0 / 32, ALU.mult, ALU.add, ["PB"], ["szu"])
-        cp(T.seli[:], T.PB[:, 0:8], ["PB"], ["seli"])
-        tt(T.rmin[:], R0, R1, ALU.min, ["rs"], ["rmin"])
-        act(T.PSI[:, 0:16], R, ["rs"], ["PSIa"], func=ACT.Relu, bias=BIG / 4)
-        act(T.nrm[:], T.rmin[:], ["rmin"], ["nrm"], func=ACT.Relu, scale=-1.0)
-        tt(T.PSI[:, 16:24], T.nrm[:], TS, ALU.max, ["nrm", "msum"], ["PSIb"])
-        tt(T.masks[:], T.PSI[:].indirect(T.EX3[:]), T.cmpv[:], ALU.is_lt,
-           ["PSIa", "PSIb", "EX3a", "EX3b", "cmpa", "cmpb"], ["masks"], 256, "g")
-        mm(T.ZE2[:, 0:128], T.masks[:, 0:128], T.Ib[:], True, True, ["masks", "Ib"], ["ZE2"])
-        mm(T.ZE2[:, 128:256], T.masks[:, 128:256], T.Ib[:], True, True, ["masks", "Ib"], ["ZE2"])
-        tt(T.Wm[:], T.ZE2[:, 0:256], T.DD[:], ALU.mult, ["ZE2", "DD"], ["Wm"], 256, "")
+        ts(T.szu[:], T.PB[:, 0:8], 0.125, -7.0 / 16, ALU.mult, ALU.add, ["PB"], ["szu"])
+        mms("PA", [(T.PA[:, j:256:2], T.mK[:], T.Ib[:], ["mK", "Ib"], 128, False) for j in range(2)])
+        tt(T.Wm[:, 0:256], T.PA[:, 0:256], T.DD[:, 0:256], ALU.mult, ["PA", "DDa", "DDb"], ["Wma"], 256, "")
+        nW = ["Wma", "Wmz", "Wmc", "szu"] + nz
+        ns = "sz%d" % r
+        tt(sz[:, :, 1], T.yw[:].indirect(T.selu[:]), T.zz[:], ALU.add, XX + ["yc", "ya2", "selu", "zz", ns], [ns + "a"], 128, "g")
+        cp(sz[:, :, 3], sz[:, :, 1], [ns + "a"], [ns + "c"], 128, "h")
         if last:
-            tt(T.Mn[:], T.Wm[:].indirect(T.szu[:]), Mf, ALU.add, ["Wm", "szu"] + nMf, ["Mn"], 128, "g")
-        else:
-            tt(sz[:, 0:384:3], T.Wm[:].indirect(T.szu[:]), Mf, ALU.add, ["Wm", "szu", "sz%d" % r] + nMf,
-               ["sz%dd" % r], 128, "g")
-        mm(T.ZE0[:, 0:128], Ih, T.zb[:], True, False, ["E0", "zb"], ["ZE0"])
-        mm(T.ZE0[:, 0:128], T.Inq[:], T.ones[:], False, False, ["Inq", "ones"], ["ZE0"])
-        mm(T.ZE1[:, 0:128], T.Inh[:], T.zb[:], True, False, ["Inh", "zb"], ["ZE1"])
-        act(T.y2[:], T.xm[:].indirect(T.selu[:]), XM + XX + ["selu"], ["y2"], 128, "g")
-        mm(T.ZE0[:, 0:128], T.Ib[:], T.y2[:], False, True, ["Ib", "y2"], ["ZE0"])
-        mm(T.ZE1[:, 0:128], T.Ib[:], T.y2[:], False, True, ["Ib", "y2"], ["ZE1"])
-        ts(T.Wz[:, 0:128], T.ZE0[:, 0:128], MAGIC, MAGIC, ALU.add, ALU.subtract, ["ZE0"], ["Wza"], 128)
-        act(T.Wz[:, 128:256], T.ZE1[:, 0:128], ["ZE1"], ["Wzb"], 128, func=ACT.Abs, scale=2.0)
-        act(T.nzb[:], T.Wz[:].indirect(T.szu[:]), ["Wza", "Wzb", "szu"], ["nzb"], 128, "g")
-        for il in range(16):
-            mm(T.ZE3[:, 128:136], T.UL[:, 128 * il:128 * il + 128], T.nzb[:, il:128:16], il == 0, il == 15,
-               ULall + ["nzb"], ["ZE3"], 8)
-        cp(T.ui[:], T.ZE3[:, 128:136], ["ZE3"], ["ui"])
-        if last:
-            act(T.yy[:], T.Mn[:], ["Mn"], ["yy"], 128, bias=OFF)
+            tt(T.Mn[:], T.Wm[:].indirect(T.szu[:]), M1, ALU.add, nW, ["Mn"], 128, "g")
+            act(T.yy[:], T.Mn[:], ["Mn"], ["yy"], 128, bias=2048.0)
+            ts(T.nzb[:], sz[:, :, 1], -ZO, None, ALU.add, None, [ns + "a"], ["nzb"], 128, "h")
             dma("Y", "stZ", T.yz[:], T.nzb[:], ["nzb"], [], 2 ** 15)
             dma("Y", "stM", T.yms[:], T.yy[:], ["yy"], [], 2 ** 16)
         else:
             lz2 = T["lz%d" % (r + 1)]
-            act(sz[:, 1:384:3], T.Wz[:].indirect(T.szu[:]), ["Wza", "Wzb", "szu", "sz%d" % r], ["sz%da" % r], 128, "g")
-            ts(T.bi[:], T.seli[:], 3, 1, ALU.arith_shift_right, ALU.bitwise_and, ["seli"], ["bi"])
-            act(T.s1[:], T.PB[:, 0:8], ["PB"], ["s1"], func=ACT.Sign, bias=-OFF)
-            act(sz[:, 5:384:ZW], T.s1[:], ["s1", "sz%d" % r], ["sz%dc" % r], func=ACT.Relu)
-            if r:
-                tt(sz[:, 2:384:ZW], T.bi[:], T.c2m[:], ALU.add, ["bi", "c2m", "sz%d" % r], ["sz%db" % r])
-            else:
-                cp(sz[:, 2:384:ZW], T.bi[:], ["bi", "sz%d" % r], ["sz%db" % r])
-            nsz = ["sz%d%s" % (r, x) for x in "abcd"]
-            send(lambda h, a=sz: a[:, ZW * h:ZW * h + ZW], lambda s, a=lz2: a[:, ZW * s:ZW * s + ZW], "arZ%d" % r, nsz,
-                 ["lz%dr" % (r + 1)])
-            act(lz2[:, ZW:2 * ZW], sz[:, 0:ZW], nsz, ["lz%d" % (r + 1)], ZW)
-        ts(T.uj[:], T.ui[:], 31, None, ALU.bitwise_and, None, ["ui"], ["uj"])
-        if last:
-            tt(T.vi[:], T.uj[:], T.S32h[:], ALU.add, ["uj", "S32h", "S32g"], ["vi"])
-            cp(T.vu[:], T.vi[:], ["vi"], ["vu"])
-            for j in range(2):
-                win, cols, xj = T.X[:, 2048 * j:2048 * j + 2048], slice(64 * j, 64 * j + 64), "X%d" % j
-                off = T.vu[:, 4 * j:4 * j + 4]
-                tt(T.xa[:, cols], win.indirect(off), T.nzb[:, cols], ALU.add, ["X", "vu", "nzb"], ["xa%d" % j], 64, "g")
-                ts(T.xb[:, cols], T.xa[:, cols], 1, None, ALU.arith_shift_right, None, ["xa%d" % j], ["xb%d" % j], 64)
-                cp(win.indirect(off), T.xb[:, cols], ["vu", "xb%d" % j], [xj, "~X"], 64, "s")
-                dma("YS"[j], ("stX", "stX2")[j], T.ytx[:, 2048 * j:2048 * j + 2048], win, [xj], [], 2 ** (19 + j))
-        else:
-            tt(T.vi[:], T.uj[:], T.S32[:], ALU.add, ["uj", "S32"], ["vi"])
-            cp(T.vu[:], T.vi[:], ["vi"], ["vu"])
-            mm(T.ZE3[:, 0:128], Ih, T.nzb[:], True, False, ["E0", "nzb"], ["ZE3"])
-            mm(T.ZE3[:, 0:128], T.Inq[:], T.ones[:], False, False, ["Inq", "ones"], ["ZE3"])
-            act(T.y2[:], T.X[:].indirect(T.vu[:]), ["X", "vu"], ["y2"], 128, "g", scale=0.5)
-            mm(T.ZE3[:, 0:128], T.Ib[:], T.y2[:], False, True, ["Ib", "y2"], ["ZE3"])
-            act(T.yy[:], T.ZE3[:, 0:128], ["ZE3"], ["yy"], 128, bias=MAGIC)
-            act(T.ny[:], T.yy[:], ["yy"], ["ny"], 128, bias=-MAGIC)
-            cp(T.X[:].indirect(T.vu[:]), T.ny[:], ["vu", "ny"], ["X"], 128, "s")
-        scan(T.amax[:], T.DA[:], T.PX[:, 0:128], ALU.add, ALU.max, ["DA", "PX"], ["amax"], 128)
-        cp(T.ai[:], T.amax[:, 15:128:16], ["amax"], ["ai"])
-        ts(T.P2[:, 0:8], T.ai[:], 15, None, ALU.bitwise_and, None, ["ai"], ["P2a"])
-        tt(T.aTD[:], mk, T.qm[:], ALU.subtract, ["mmin", "qm"], ["aTD"])
-        tt(T.w[:], T.aTD[:], T.rmin[:], ALU.max, ["aTD", "rmin"], ["w"])
-        act(T.nk[:], T.w[:], ["w"], ["nk"], bias=1024.0, scale=1024.0)
-        act(T.o1[:], R1, ["rs"], ["o1"], func=ACT.Sign, bias=1.0)
-        act(T.thr[:], T.o1[:], ["o1"], ["thr"], func=ACT.Relu)
-        tt(T.tq[:], T.nk[:], T.thr[:], ALU.max, ["nk", "thr"], ["P2b"])
-        if not last:
-            act(T.kap[:], T.w[:], ["w"], ["kap"], func=ACT.Sign, bias=0.5)
-            mm(T.PB[:, 32:40], T.ones[:], T.kap[:], True, True, ["ones", "kap"], ["PB"], 8)
-            act(T.A8[:], T.PB[:, 32:40], ["PB"], ["A8"], bias=512.0, scale=-4.0)
-        ts(T.bi[:], T.seli[:], 15, None, ALU.bitwise_and, None, ["seli"], ["bi"])
-        cp(T.eu[:], T.bi[:], ["bi"], ["eu"])
-        tt(T.oM[:], T.DM[:, 0:16].indirect(T.eu[:]), Mf, ALU.mult, ["DM", "eu"] + nMf, ["oM"], 128, "g")
-        tt(T.L2[:, 128:256], T.tq[:].indirect(T.EX[:, 0:8]), T.DM[:, 0:128], ALU.mult, ["P2b", "EX", "DM"],
-           ["L2b"], 128, "g")
-        mm(T.PM[:, 24:32], T.L2[:, 128:256], G8, True, True, ["L2b", "BD"], ["PM"], 8, True)
-        tt(T.o1[:], T.PM[:, 24:32], T.c2m[:], ALU.add, ["PM", "c2m"], ["o1"])
-        tt(T.L2[:, 0:128], T.P2[:, 0:8].indirect(T.EX[:, 0:8]), T.DM[:, 0:128], ALU.mult, ["P2a", "EX", "DM"],
-           ["L2a"], 128, "g")
-        mm(T.PB[:, 16:24], T.L2[:, 0:128], G8, True, True, ["L2a", "BD"], ["PB"], 8, True)
-        cp(T.au[:], T.PB[:, 16:24], ["PB"], ["au"])
-        tt(T.tL[:], T.o1[:], T.D512[:], ALU.min, ["o1", "D512"], ["tL"])
-        cp(T.tu[:], T.tL[:], ["tL"], ["tu"])
-        act(T.old[:], T.Kw[:].indirect(T.tu[:]), ["Kw", "tu"], ["old"], 128, "g", bias=-OFF)
-        act(T.ohA[:], T.tabA[:].indirect(T.au[:]), ["tabA", "au"], ["ohA"], 128, "g")
-        mm(T.PB[:, 128:256], T.BD[:], T.oM[:], True, False, ["BD", "oM"], ["PB"], 128, True)
-        mm(T.PB[:, 128:256], T.nIf[:], T.old[:], False, True, ["nIf", "old"], ["PB"], 128, True)
-        tt(T.oM[:], T.PB[:, 128:256], T.ohA[:], ALU.mult, ["PB", "ohA"], ["oM"], 128, "")
-        mm(T.PB[:, 256:384], T.If[:], T.old[:], True, False, ["If", "old"], ["PB"], 128, True)
-        mm(T.PB[:, 256:384], T.If[:], T.oM[:], False, True, ["If", "oM"], ["PB"], 128, True)
-        act(T.old[:], T.PB[:, 256:384], ["PB"], ["old"], 128, bias=OFF)
-        if DEDUP[r] == "V":
-            tt(T.L1[:], T.tabN[:].indirect(T.tu[:]), T.TRm[:], ALU.add, ["tabN", "tu", "TRm"], ["L1"], 128, "g")
-            act(T.nk[:], T.tL[:], ["tL"], ["nk"], scale=256.0)
-            tt(T.eq[:, 0, :], T.nk[:].indirect(T.EX[:, 0:8]), T.L1[:], ALU.is_equal, ["nk", "EX", "L1"], ["eq"], 128, "g")
-            scan(T.amax[:], T.D0S[:, 0:128], T.eq[:, 0, :], ALU.mult, ALU.max, ["D0S", "eq"], ["amax"], 128)
-            tt(T.ag[:], T.amax[:, 15:128:16], T.D512[:], ALU.mult, ["amax", "D512"], ["ag"])
-            tt(T.lo[:], T.ag[:], T.tL[:], ALU.max, ["ag", "tL"], ["lo"])
-            cp(T.ou[:, 0:16:2], T.lo[:], ["lo"], ["ou"])
-            for h in range(7, -1, -1):
-                cp(T.Kw[:].indirect(T.ou[:, 2 * h:2 * h + 1]), T.old[:, 16 * h:16 * h + 16], ["ou", "old"], ["Kw"], 16, "s")
+            ts(sz[:, 0:128:16, 2], T.PB[:, 0:8], 0.125, BO - 7.0 / 16, ALU.mult, ALU.add, ["PB", ns], [ns + "b"])
+            tt(sz[:, :, 0], T.Wm[:].indirect(T.szu[:]), M1, ALU.add, nW + [ns], [ns + "d"], 128, "g")
+            nsz = [ns + x for x in "abcd"]
+            for call, nm, lat in ((CALL_A, "A", T_A), (CALL_B, "B", T_B)):
+                send(call, lambda h, a=sz: a[:, 16 * h:16 * h + 16, :], lambda s, a=lz2: a[:, 16 * s:16 * s + 16, :],
+                     "ar%s%d" % (nm, r), nsz, ["lz%d%s" % (r + 1, nm)], lat)
+            cp(lz2[:, 16:32, :], sz[:, 0:16, :], nsz, ["lz%do" % (r + 1)], 64, "h")
+        Wv = T.PM[:, 24, 0:16]
+        mms("PM", [(Wv, T.Ib[:], T.S32[:, 16 * last:16 * last + 16], ["Ib", "S32a", "S32b", "S32c", "S32d"], 16, False)] +
+            [(Wv, T.UL[:, 128 * il:128 * il + 128], sz[:, il:128:16, 1:4:2], ULall + [ns + "a", ns + "c"], 16, False)
+             for il in range(16)])
+        ts(T.tq[:], T.PM[:, 24, 0:16:2], MAGIC32, MAGIC32, ALU.add, ALU.subtract, ["PM"], ["tq"])
+        tt(T.ui[:], T.PM[:, 24, 1:16:2], T.tq[:], ALU.subtract, ["PM", "tq", "pm"], ["ui"], 8, "")
+        cp(T.vu[:], T.ui[:], ["ui"], ["vu"])
+        for j, (c0, w) in enumerate(((0, 64), (64, 64)) if last else ((0, 128),)):
+            win, off = T.X[:, 32 * c0:32 * (c0 + w)], T.vu[:, c0 // 16:(c0 + w) // 16]
+            xj = "X%d" % j if last else "X"
+            tt(T.xa[:, c0:c0 + w], win.indirect(off), sz[:, c0:c0 + w, 1], ALU.add, ["X", "vu", ns + "a"], ["xa%d" % j], w, "g")
+            ts(T.xb[:, c0:c0 + w], T.xa[:, c0:c0 + w], 1, 255, ALU.arith_shift_right, ALU.bitwise_and, ["xa%d" % j], ["xb%d" % j], w)
+            cp(win.indirect(off), T.xb[:, c0:c0 + w], ["vu", "xb%d" % j], [xj] + ["~X"] * last, w, "s")
             if last:
-                dma("Y", "stK", T.ykt[:], T.Kw[:, 0:512], ["Kw"], [], 2 ** 18)
-            continue
-        tt(T.L1[:], T.tabN[:].indirect(T.tu[:]), T.TRI[:], ALU.add, ["tabN", "tu", "TRI"], ["L1"], 128, "g")
-        key, k0, nkey = T.L1, 0, "L1"
-        act(T.nk[:], T.tL[:], ["tL"], ["nk"], bias=0.5, scale=-256.0)
-        tt(T.cnt[:, 16:24], T.nk[:], T.SL[:], ALU.subtract, ["nk", "SL"], ["b0"])
-        act(T.cnt[:, 24:32], T.cnt[:, 16:24], ["b0"], ["b1"], bias=128.0)
-        for h in range(8):
-            for j in range(2):
-                op("S", lambda h=h, j=j: S.activation(T.eq[:, 8 * j + h, 0:16 * h + 16], key[:, k0:k0 + 16 * h + 16], ACT.Sign,
-                                                      bias=T.cnt[:, 16 + 8 * j + h:17 + 8 * j + h], scale=1.0,
-                                                      accum_out=T.cnt[:, 8 * j + h:8 * j + h + 1]),
-                   [nkey, "b%d" % j], ["cnt%d" % (8 * j + h), "~g"], cost(16 * h + 16, "") + 0.02)
-        tt(T.o1[:], T.cnt[:, 0:8], T.cnt[:, 8:16], ALU.not_equal, ["cnt%d" % j for j in range(16)], ["o1"])
-        tt(T.ag[:], T.o1[:], T.D512[:], ALU.mult, ["o1", "D512"], ["ag"])
-        tt(T.lo[:], T.ag[:], T.tL[:], ALU.max, ["ag", "tL"], ["lo"])
-        cp(T.ou[:, 0:8], T.lo[:], ["lo"], ["ou"])
-        cp(T.Kw[:].indirect(T.ou[:, 0:8]), T.old[:], ["ou", "old"], ["Kw"], 128, "s")
+                dma("YS"[j], ("stX", "stX2")[j], T.ytx[:, 2048 * j:2048 * j + 2048], win, [xj], [], 2 ** (19 + j))
+        tt(T.oM[:], T.DM[:].indirect(T.eu[:, 0:8]), M1, ALU.mult, DMall + ["eu"] + nz, ["oM"], 128, "g")
+        mms("EB", [(T.EB[:, 128:256], T.BDb[:], T.oM[:], ["BDb", "oM"], 128, False)])
+        act(T.nameN[:], T.EB[:, 128:256], ["EB"], ["nameN"], 128, bias=2048.0)
+        tt(T.LXk[:], T.PX[:, 0:16, 0:8], T.C30[:], ALU.add, ["PX", "C30", "~LX"], ["LXk"], 128, "")
+        scan(T.amax[:], T.DA[:], T.LXk[:], ALU.add, ALU.max, ["DA", "LXk"], ["amax"], 128)
+        tt(T.nA[:], T.amax[:].indirect(T.EXA[:]), T.LXk[:], ALU.not_equal, ["amax", "EXA", "LXk"], ["nA"], 128, "g")
+        tr(T.ZB[:, 0:8, :], T.nA[:], ["nA"], "ZB")
+        mms("EA", [(T.EA[:, 0:16], T.If[:], T.CG[:], ["If", "CGa", "CGb"], 16, True),
+                   (T.EA[:, 0:16], T.In1k[:], T.cb[:], ["In1k", "cb"], 16, False)] +
+            [(T.EA[:, 2 * gi:2 * gi + 2], T.E[:, 128 * gi:128 * gi + 128], T.cb[:, 2 * gi:2 * gi + 2], ["E%d" % (gi // 4), "cb"], 2, False)
+             for gi in range(8)])
+        scan(T.val[:], T.D2s[:], T.EA[:, 0:16], ALU.add, ALU.min, ["D2s", "EA"], ["val"], 16)
+        for gi in range(8):
+            mm(T.EB[:, gi:64:8], T.Ib[:], c2m, gi == 0, False, ["Ib", "sc%d" % r], ["EB", "~c2m%d" % gi], 8)
+        for h, (out, l, x, rd, n, f32) in enumerate(to_list("EB", T.val[:, 1:16:2], ["val"])):
+            mm(out, l, x, False, h == 7, rd + ["~c2m%d" % gi for gi in range(8)], ["EB"], n)
+        act(T.LV[:], T.EB[:, 0:64], ["EB"], ["LV"], 64)
+        tt(T.lo[:], T.LV[:].indirect(T.EXD[:, 0:1]), T.D512[:], ALU.min, ["LV", "EXD", "D512a", "D512b"], ["lo"], 16, "g")
+        cp(T.ou[:, 0:8], T.lo[:, 0:8], ["lo"], ["ou"])
+        tt(T.D1[:], T.Kw[:].indirect(T.ou[:, 0:8]), T.nameN[:], ALU.subtract, ["Kw", "ou", "nameN"], ["D1"], 128, "g")
+        tt(T.D2[:], T.ZB[:, 0:8, :], T.D1[:], ALU.mult, ["ZB", "D1"], ["D2"], 128, "")
+        tt(T.Kw[:].indirect(T.ou[:, 0:8]), T.nameN[:], T.D2[:], ALU.add, ["ou", "nameN", "D2"], ["Kw"], 128, "s")
         if last:
             dma("Y", "stK", T.ykt[:], T.Kw[:, 0:512], ["Kw"], [], 2 ** 18)
 

@@ -21,15 +21,15 @@ def _sb(dtype, **kw):
 
 
 _sb(B, X=[4096], yw=[YW], xm=[2048], mnm=[2048], mnx=[2048], UL=[2048], DM=[2048], CH=[8, 128], E=[1024], BT=[512],
-    zb=[128], zT=[256], Ib=[128], I37=[128], Inh=[128], I8k=[128], In1k=[128], Uw=[128], Kcol=[128], ones=[128],
+    zb=[128], zT=[256], Ib=[128], Inh=[128], I8k=[128], In1k=[128], Uw=[128], ones=[128],
     e8=[128], TRI=[128], C30=[128], WX=[4, 32], WM=[4, 48], BDb=[128], nIb=[128], y2=[128], ya=[128], ny=[128],
     mA=[128], mK=[128], nA=[128], cb=[16], val=[16], S32=[32], bits=[256], nzb=[128])
 _sb(F, Kw=[640], If=[128], nIf=[128], nBI=[128], BD=[128], CX=[16, 12], DX=[192], LX=[192], LQ=[192], CM=[24, 9],
-    D16=[128], DA=[128], D2s=[16], CC=[16], CG=[16], D512=[16], pm=[8], SL=[8], kc=[128], zz=[128], yy=[128],
+    D16=[128], DA=[128], D2s=[16], CC=[16], CG=[16], D512=[16], pm=[8], SL=[8], zz=[128], yy=[128],
     DD=[384], Wm=[400], LMk=[128], LMs=[24], LXk=[128], mmin=[128], amax=[128], mkhi=[8], thr=[16], LE=[64],
     LV=[64], L1=[128], nameN=[128], D1=[128], D2=[128], tq=[8], lo=[16], Mn=[128])
 _sb(H, lz0=[128, 4], lz1=[128, 4], lz2=[128, 4], sz0=[128, 4], sz1=[128, 4], sz2=[128, 4], sc0=[64], sc1=[64], sc2=[64],
-    lc0=[64], lc1=[64], ce=[8], oM=[128])
+    lc0=[64], lc1=[64], ce=[8], kc=[128], K37=[128], oM=[128])
 _sb(I, kti=[512], msi=[128], tmpi=[256], tmpj=[256], BI=[256], ksi=[8], KS=[8], ci=[16], cj=[8], c8=[8], ui=[8],
     xa=[128], xb=[128])
 _sb(U, Mu=[128], kcu=[128], cu16=[8], EX=[8], EXS=[8], EXA=[8], EXD=[2], selu=[8], szu=[8], eu=[16], vu=[8], ou=[16])
@@ -39,22 +39,20 @@ for _n in BANKS:
         ("psum", [128, 32, 16], F) if _n in ("PX", "PM") else ("psum", [128, 512], F)
 
 SEMAPHORES = ["cV", "cS", "cP", "cG", "ldX", "ldX2", "ldK", "ldM", "ldZ", "ldC", "stX", "stX2", "stK", "stM", "stZ",
-              "arC0", "arC1", "arA0", "arA1", "arB0", "arB1", "sent", "cpD"]
+              "arC0", "arC1", "arA0", "arA1", "arB0", "arB1", "arD0", "arD1", "sent", "cpD"]
 
 CH_M = [(0, 64), (64, 64)]
 CH_X = [(0, 64), (64, 32), (96, 32)]
-G_M = [[("V", 0, 32), ("S", 32, 32), ("S", 64, 32), ("V", 96, 32)],
-       [("S", 0, 32), ("S", 32, 32), ("S", 64, 32), ("V", 96, 32)],
-       [("S", 0, 32), ("S", 32, 32), ("S", 64, 32), ("V", 96, 32)]]
+_LATER = [("S", 0, 48), ("V", 48, 32), ("S", 80, 48)]
+G_M = [[("V", 0, 32), ("S", 32, 32), ("S", 64, 32), ("V", 96, 32)], _LATER, _LATER]
 G_X = [[("S", 0, 32), ("V", 32, 32), ("S", 64, 32), ("S", 96, 16), ("V", 112, 16)]] * RO
 MM_X = [(0, 96), (96, 32)]
-CALL_A, CALL_B, CALL_C = ((7, 8), (1, 4), (2, 4)), ((3, 4), (4, 4), (5, 4), (6, 4)), \
-    ((1, 2), (2, 2), (3, 2), (4, 2), (5, 2), (6, 2), (7, 4))
+CALLS = {"A": ((7, 4), (1, 4), (2, 4), (3, 4)), "B": ((4, 8), (5, 8)), "D": ((6, 16),)}
+CALL_C = ((1, 2), (2, 2), (3, 2), (4, 2), (5, 2), (6, 2), (7, 4))
+FIRST = 80
 CY, GAT, SCA, PEC, WAKE, FIX, T_DMA, BW = 1.04e-3, 1.56, 3.8, 0.53e-3, 0.12, 0.03, 2.2, 250e3
-T_A, T_B, T_C, T_FIRST = 2.4, 3.4, 3.9, 1.5
-KCU_GATHER = True
-BOOST = {"send": 6.0, "X0": 3.0}
-SEED, TRIES, HEAT = 3, 1200, 0.0
+T_CALL, T_C, T_FIRST = {"A": 2.4, "B": 2.65, "D": 2.5}, 3.9, 1.5
+SEED, TRIES, HEAT = 3, 6000, 0.15
 PLANS = {}
 
 
@@ -67,7 +65,7 @@ def plan(ops):
         for r in o["rd"] + o["wr"]:
             if r in writer:
                 pred[i].add(writer[r])
-                if r[0] == "~":
+                if r[0] == "~" and r != "~LX":
                     soft.add((writer[r], i))
         for w in o["wr"]:
             pred[i].update(readers.get(w, []))
@@ -77,102 +75,107 @@ def plan(ops):
             writer[w] = i
             readers[w] = []
         pred[i].discard(i)
-    succ = [[] for _ in ops]
-    for i in range(n):
-        for p in pred[i]:
-            succ[p].append(i)
+    eng = ["VSPGY".index(o["e"]) for o in ops]
+    hold = [o["hold"] for o in ops]
+    lat = [o["lat"] for o in ops]
 
     def gap(p, i):
         if (p, i) in soft:
-            return -ops[p]["lat"]
-        return 0.0 if ops[p]["e"] == "P" and ops[i]["e"] == "P" else WAKE
-    prio = [0.0] * n
-    for i in range(n - 1, -1, -1):
-        prio[i] = ops[i]["hold"] + ops[i]["lat"] + max([prio[s] + gap(i, s) for s in succ[i]] + [0.0])
-    eng = [o["e"] for o in ops]
-    hold = [o["hold"] for o in ops]
-    lat = [o["lat"] for o in ops]
-    rb = [[r for r in o["rd"] if r in BANKS] for o in ops]
-    ab = [[r for r in o["rd"] + o["wr"] if r in BANKS] for o in ops]
-    sg = [[(s, gap(i, s)) for s in succ[i]] for i in range(n)]
+            return 0.0
+        return lat[p] + (0.0 if eng[p] == 2 and eng[i] == 2 else WAKE)
+    before = [[(p, gap(p, i)) for p in sorted(pred[i])] for i in range(n)]
+    after = [[] for _ in ops]
+    for i in range(n):
+        for p, gp in before[i]:
+            after[p].append((i, gp))
 
-    def schedule(prio):
-        left = [len(p) for p in pred]
-        ready = {e: [] for e in "VSPGY"}
-        for i in range(n):
-            if not left[i]:
-                ready[eng[i]].append(i)
-        at = [0.0] * n
-        free = {e: 0.0 for e in ready}
-        bank = {b: ("", 0.0) for b in BANKS}
-        out, end = [], 0.0
-        for _ in range(n):
-            t0, e0, st0 = 1e9, None, None
-            for e, rl in ready.items():
-                if not rl or free[e] >= t0:
-                    continue
-                st = []
-                for i in rl:
-                    t = at[i] if at[i] > free[e] else free[e]
-                    for r in rb[i]:
-                        if bank[r][0] != e and bank[r][1] + WAKE > t:
-                            t = bank[r][1] + WAKE
-                    st.append(t)
-                if min(st) < t0:
-                    t0, e0, st0 = min(st), e, st
-            rl = ready[e0]
-            top = max(range(len(rl)), key=lambda j: prio[rl[j]])
-            j = max((j for j in range(len(rl)) if st0[j] <= t0 + 0.02), key=lambda j: prio[rl[j]])
-            if j != top and st0[top] - st0[j] < 0.4 * hold[rl[j]]:
-                j = top
-            i = rl.pop(j)
-            free[e0] = st0[j] + hold[i]
-            fin = free[e0] + lat[i]
-            end = max(end, fin)
-            for r in ab[i]:
-                bank[r] = (e0, fin)
-            out.append(i)
-            for s, gp in sg[i]:
-                if fin + gp > at[s]:
-                    at[s] = fin + gp
-                left[s] -= 1
-                if not left[s]:
-                    ready[eng[s]].append(s)
-        return end, out
+    def ranked(key, need):
+        key = list(key)
+        for i in (range(n) if need is before else range(n - 1, -1, -1)):
+            for p, _ in need[i]:
+                if key[p] >= key[i]:
+                    key[i] = key[p] + 1e-6
+        return sorted(range(n), key=lambda i: key[i])
 
-    for kind, boost in BOOST.items():
-        todo = [i for i, o in enumerate(ops) if kind in o["wr"] or (kind == "send" and o["remote"])]
-        seen = set(todo)
-        while todo:
-            i = todo.pop()
-            for p in pred[i]:
-                if p not in seen and "LQ" not in ops[i]["wr"] and ops[p]["round"] == ops[i]["round"] and ops[p]["tail"]:
-                    seen.add(p)
-                    todo.append(p)
-        for i in seen:
-            prio[i] += boost
-    best, out = schedule(prio)
+    def place(key, need, first):
+        start = [0.0] * n
+        used = [([], []) for _ in range(5)]
+        for i in ranked(key, need):
+            t = first[i]
+            for p, gp in need[i]:
+                if start[p] + hold[p] + gp > t:
+                    t = start[p] + hold[p] + gp
+            a, b = used[eng[i]]
+            lo, hi = 0, len(b)
+            while lo < hi:
+                mid = (lo + hi) // 2
+                if b[mid] <= t:
+                    lo = mid + 1
+                else:
+                    hi = mid
+            while lo < len(a) and a[lo] < t + hold[i] - 1e-9:
+                t = max(t, b[lo])
+                lo += 1
+            a.insert(lo, t)
+            b.insert(lo, t + hold[i])
+            start[i] = t
+        return start
+
+    zero = [0.0] * n
+
+    def forward(key):
+        fw = place(key, before, zero)
+        return max(fw[i] + hold[i] + lat[i] for i in range(n)), fw
+
+    def both(key):
+        end, fw = forward(key)
+        bw = place([end - fw[i] - hold[i] for i in range(n)], after, lat)
+        end = max(bw[i] + hold[i] for i in range(n))
+        return forward([end - bw[i] - hold[i] for i in range(n)])
+
     seed = [SEED]
 
     def rnd():
         seed[0] = (seed[0] * 1103515245 + 12345) % 2 ** 31
         return seed[0] / 2 ** 31
-    cur = best
-    movable = [i for i in range(n) if eng[i] != "P"]
+    tail = [0.0] * n
+    for i in range(n - 1, -1, -1):
+        tail[i] = hold[i] + max([tail[s] + gp for s, gp in after[i]] + [lat[i]])
+    cur, fw = both([-t for t in tail])
+    best, out = cur, fw
+    busy = [i for i in range(n) if eng[i] < 2 and ops[i]["round"] >= 0]
+    twin = [{} for _ in range(RO)]
+    for i, o in enumerate(ops):
+        if o["round"] >= 0:
+            w = (o["wr"] + [""])[0]
+            s = [o["e"], w[:2] + w[3:] if w[:2] in ("sz", "lz", "sc", "lc") else w, 0]
+            while tuple(s) in twin[o["round"]]:
+                s[2] += 1
+            twin[o["round"]][tuple(s)] = i
     for it in range(TRIES):
-        chain = {movable[int(rnd() * len(movable))]}
-        link = pred if rnd() < 0.7 else succ
-        for _d in range(int(rnd() * 10)):
-            chain |= {p for i in chain for p in link[i] if ops[p]["round"] == ops[i]["round"] and rnd() < 0.8}
-        d = (6 * rnd() - 3) * (1 if rnd() < 0.7 else 0.3)
-        trial = [p + d if i in chain else p for i, p in enumerate(prio)]
-        end, o2 = schedule(trial)
-        if end <= cur + HEAT * (1 - it / TRIES) * rnd() ** 3:
-            cur, prio = end, trial
+        if it % 100 == 99:
+            a, b = int(rnd() * RO), int(rnd() * RO)
+            d = fw[twin[a][("S", "LX", 0)]] - fw[twin[b][("S", "LX", 0)]]
+            trial = list(fw)
+            part = rnd()
+            for s, i in twin[a].items():
+                if s in twin[b] and (part < 0.4 or ops[i]["tail"] == (part < 0.7)):
+                    trial[i] = fw[twin[b][s]] + d
+            end, f2 = forward(trial)
+        else:
+            chain = {busy[int(rnd() * len(busy))] if rnd() < 0.8 else int(rnd() * n)}
+            link = before if rnd() < 0.6 else after
+            for _d in range(int(rnd() * 8)):
+                chain |= {p for i in chain for p, _ in link[i] if abs(fw[p] - fw[i]) < 4 and rnd() < 0.8}
+            d = (0.2 + 2.5 * rnd() ** 2) * (-1 if link is before else 1)
+            trial = [fw[i] + d if i in chain else fw[i] for i in range(n)]
+            end, f2 = forward(trial) if rnd() < 0.6 else both(trial)
+        if end <= cur + HEAT * (1 - it / TRIES) * rnd() ** 2:
+            cur, fw = end, f2
             if end < best:
-                best, out = end, o2
+                best, out = end, f2
     PLANS["t"] = best
-    return out
+    return ranked(out, before)
 
 
 def rank_program(g, core, T, topo):
@@ -325,7 +328,7 @@ def rank_program(g, core, T, topo):
     ts(h0, pm, 8.0, None, ALU.is_lt, None, ["pm"], ["h0"])
     ts(T.EXD[:, 0:1], p8, 8.0, pg, ALU.mult, ALU.add, ["pm"], ["EXD"])
     G8 = T.BD[:, 0:128:16]
-    for name, sc in (("If", 1.0), ("nBI", -BIG), ("I37", 37.0), ("Inh", -0.5), ("I8k", 8192.0), ("In1k", -1024.0),
+    for name, sc in (("If", 1.0), ("nBI", -BIG), ("Inh", -0.5), ("I8k", 8192.0), ("In1k", -1024.0),
                      ("nIb", -1.0)):
         act(T[name][:], T.Ib[:], ["Ib"], [name], 128, scale=sc)
     for half in range(2):
@@ -350,7 +353,8 @@ def rank_program(g, core, T, topo):
     for gi in range(8):
         cp(T.CH[:, :, 16 * gi:16 * gi + 16], T.Ib[:], ["Ib"], ["CH%d" % gi], 128, "h")
     CHall = ["CH%d" % gi for gi in range(8)]
-    act(T.Kcol[:], T.ones[:], ["ones", "pm"], ["Kcol"], 128, scale=pm)
+    ts(T.pm[:, 7:8], pm, 37.0, 0.5, ALU.mult, ALU.add, ["pm"], ["p37"])
+    ts(T.K37[:], T.ones[:], T.pm[:, 7:8], None, ALU.mult, None, ["ones", "p37"], ["K37"], 128, "h")
     ts(T.SL[:], T.tmpj[:, 160:168], 16.0, pm, ALU.mult, ALU.add, ["J16", "pm"], ["SL"])
     cp(T.EX[:], T.tmpj[:, 160:168], ["J16"], ["EX"])
     ts(T.EXS[:], T.tmpj[:, 160:168], 16.0, None, ALU.add, None, ["J16"], ["EXS"])
@@ -422,16 +426,16 @@ def rank_program(g, core, T, topo):
         where[0], where[1] = r, False
         lz, sz, sc = T["lz%d" % r], T["sz%d" % r], T["sc%d" % r]
         nA = ["lz0m", "lz0a", "lz0b"] if r == 0 else ["lz%do" % r, "lz%dA" % r]
-        nB = nA if r == 0 else ["lz%dB" % r]
+        nB = nA if r == 0 else ["lz%dB" % r, "lz%dD" % r]
         nz = nA + nB
         M1, z1 = lz[:, :, 0], lz[:, :, 1]
         if r:
-            ts(T.Mu[:, 0:64], lz[:, 0:64, 0], 2048.0, None, ALU.add, None, nA, ["MuA"], 64, "h")
-            ts(T.Mu[:, 64:128], lz[:, 64:128, 0], 2048.0, None, ALU.add, None, nB, ["MuB"], 64, "h")
+            ts(T.Mu[:, 0:FIRST], lz[:, 0:FIRST, 0], 2048.0, None, ALU.add, None, nA, ["MuA"], 64, "h")
+            ts(T.Mu[:, FIRST:128], lz[:, FIRST:128, 0], 2048.0, None, ALU.add, None, nB, ["MuB"], 64, "h")
         for e, s0, n in G_M[r]:
-            gather(e, "m", T.Mu, ["MuA" if s0 < 64 else "MuB"], s0, n)
+            gather(e, "m", T.Mu, ["MuA"] * (s0 < FIRST) + ["MuB"] * (s0 + n > FIRST), s0, n)
         for j, (src, bank) in enumerate((("EA", "ZA"), ("EB", "ZB"))):
-            mms(src, [(T[src][:, 0:128], lz[:, 64 * j:64 * j + 64, 1:4:2], T.Ib[:], (nA, nB)[j] + ["Ib"], 128, False)])
+            mms(src, [(T[src][:, 0:128], lz[:, 64 * j:64 * j + 64, 1:4:2], T.Ib[:], (nA, nz)[j] + ["Ib"], 128, False)])
             act(T.zT[:, 128 * j:128 * j + 128], T[src][:, 0:128], [src], ["zT%d" % j], 128, scale=0.5, bias=-ZO / 2)
             for k in range(0, 16, 2):
                 tr(T[bank][:, :, k:k + 2], T.zT[:, 128 * j:128 * j + 128], ["zT%d" % j], bank)
@@ -448,15 +452,8 @@ def rank_program(g, core, T, topo):
             scan(T.ci[:], T.D2s[:], T.PA[:, 384:400], ALU.add, ALU.min, ["D2s", "PA"], ["ci"], 16)
             ts(T.cj[:], T.ci[:, 1:16:2], 511, None, ALU.bitwise_and, None, ["ci"], ["cj"])
         cp(T.cu16[:], T.cj[:], ["cj"], ["cu16"])
-        if r == 0:
-            cp(T.kcu[:], T.kti[:].indirect(T.cu16[:]), ["kti", "cu16"], ["kcu"], 128, "g")
-            ts(T.kc[:], T.kcu[:], -OFF, None, ALU.add, None, ["kcu"], ["kc"], 128)
-        elif KCU_GATHER:
-            cp(T.kcu[:], T.Kw[:].indirect(T.cu16[:]), ["Kw", "cu16"], ["kcu"], 128, "g")
-            act(T.kc[:], T.Kw[:].indirect(T.cu16[:]), ["Kw", "cu16"], ["kc"], 128, "g", bias=-OFF)
-        else:
-            act(T.kc[:], T.Kw[:].indirect(T.cu16[:]), ["Kw", "cu16"], ["kc"], 128, "g", bias=-OFF)
-            ts(T.kcu[:], T.kc[:], OFF, None, ALU.add, None, ["kc"], ["kcu"], 128)
+        cp(T.kcu[:], (T.Kw if r else T.kti)[:].indirect(T.cu16[:]), ["Kw" if r else "kti", "cu16"], ["kcu"], 128, "g")
+        ts(T.kc[:], T.kcu[:], -2048.0, None, ALU.add, None, ["kcu"], ["kc"], 128, "h")
         for e, s0, n in G_X[r]:
             gather(e, "x", T.kcu, ["kcu"], s0, n)
         ts(T.c8[:], T.cj[:], 255, None, ALU.bitwise_and, None, ["cj", "pm"], ["c8"])
@@ -498,13 +495,12 @@ def rank_program(g, core, T, topo):
                    (T.PB[:, 0:128], T.Ib[:], T.ya[:], ["Ib", "ya"], 128, False)])
         act(T.yw[:, YC:YC + 128], T.PB[:, 0:128], ["PB"], ["yc"], 128, bias=ZO / 2 + 0.25)
         act(T.yw[:, YA:YW:8], T.PB[:, 0:128], ["PB"], ["ya2"], 128, bias=ZO / 2 + 0.25)
-        fresh = [(T.Uw[:], z1, ["Uw"] + nz, False), (T.I37[:], T.Kcol[:], ["I37", "Kcol"], False), (T.If[:], T.kc[:], ["If", "kc"], True)]
+        fresh = [(T.Uw[:], z1, ["Uw"] + nz, False), (T.Ib[:], T.K37[:], ["Ib", "K37"], False), (T.Ib[:], T.kc[:], ["Ib", "kc"], False)]
         mms("PA", [(T.PA[:, 0:128], l, x, rd, 128, f) for l, x, rd, f in fresh])
         act(T.yy[:], T.PA[:, 0:128], ["PA"], ["yy"], 128, bias=MAGIC4)
         act(T.ny[:], T.yy[:], ["yy"], ["ny"], 128, bias=MAGIC4, scale=-1.0)
-        mms("PA", [(T.PA[:, 0:128], T.If[:], T.kc[:], ["If", "kc"], 128, True),
+        mms("PA", [(T.PA[:, 0:128], T.Ib[:], T.kc[:], ["Ib", "kc"], 128, False),
                    (T.PA[:, 0:128], T.nIb[:], M1, ["nIb"] + nz, 128, False),
-                   (T.PA[:, 0:128], T.Inh[:], T.ones[:], ["Inh", "ones"], 128, False),
                    (T.PA[:, 256:384], T.Inh[:], z1, ["Inh"] + nz, 128, False)] +
             [(T.PA[:, 128:256], l, x, rd, 128, f) for l, x, rd, f in fresh] +
             [(T.PA[:, 128:256], T.nIb[:], M1, ["nIb"] + nz, 128, False),
@@ -514,8 +510,6 @@ def rank_program(g, core, T, topo):
         act(T.DD[:, 256:384], T.PA[:, 128:256], ["PA"], ["DDc"], 128, bias=-0.5)
         act(T.zz[:], T.PA[:, 256:384], ["PA"], ["zz"], 128, scale=-1.0, bias=ZO / 2 - 0.25)
         tt(T.mA[:], T.LMs[:].indirect(T.EXS[:]), LMk, ALU.is_le, ["LMs", "EXS"] + nLM, ["mA"], 128, "g")
-        mms("PB", [(T.PB[:, 0:128], T.mA[:], T.Ib[:], ["mA", "Ib"], 128, False)])
-        tt(T.Wm[:, 272:400], T.PB[:, 0:128], T.DD[:, 256:384], ALU.mult, ["PB", "DDc"], ["Wmc"], 128, "")
         act(T.bits[:, 0:128], T.BT[:].indirect(T.cu16[:]), ["BTa", "BTb", "cu16"], ["bits"], 128, "g")
         act(T.bits[:, 128:256], T.bits[:, 0:128], ["bits", "pm"], ["bits2"], 128, scale=podd)
         for j, bank in enumerate(("EA", "EB")):
@@ -542,6 +536,8 @@ def rank_program(g, core, T, topo):
                        False, False, tags(t, s0, n) + dep + ["~rx%d_%d" % (s0, k)] * (t == "nx"),
                        ["PX"] + ["~rx%d_%d" % (s0, k)] * (t == "x"), 32, False, n)
         mm(T.PX[:, 0:16, 7:10:2], T.mnx[:, 15:2048:16], T.WX[:, 3, :], False, True, tags("nx", 0, 128) + ["WXn"], ["PX"], 32)
+        tr(T.ZA[:, 0:8, :], T.mA[:], ["mA"], "ZA")
+        tt(T.Wm[:, 272:400], T.ZA[:, 0:8, :], T.DD[:, 256:384], ALU.mult, ["ZA", "DDc"], ["Wmc"], 128, "")
         where[1] = True
         act(T.LX[:], T.PX[:, 0:16, 0:12], ["PX"], ["LX", "~LX"], 192)
         scan(T.LQ[:], T.LX[:], T.DX[:], ALU.min, ALU.mult, DXall + ["LX"], ["LQ"], 192, HUGE)
@@ -550,9 +546,10 @@ def rank_program(g, core, T, topo):
         tt(T.L1[:], T.KS[:].indirect(T.EX[:]), T.DM[:, 0:128], ALU.mult, ["KS", "EX", "DM0"], ["L1"], 128, "g")
         tt(T.mK[:], T.PX[:, 0:16, 0:8], LMk, ALU.is_lt, ["PX", "~LX"] + nLM, ["mK"], 128, "")
         tt(T.cb[:], T.LX[:, 8:192:12], T.LQ[:, 9:192:12], ALU.is_equal, ["LX", "LQ"], ["cb"], 16)
-        mms("PB", [(T.PB[:, 0:8], T.L1[:], G8, ["L1", "BD"], 8, True)])
-        cp(T.selu[:], T.PB[:, 0:8], ["PB"], ["selu"])
-        ts(T.szu[:], T.PB[:, 0:8], 0.125, -7.0 / 16, ALU.mult, ALU.add, ["PB"], ["szu"])
+        code = T.PM[:, 25, 0:8]
+        mms("PM", [(code, T.L1[:], G8, ["L1", "BD"], 8, True)])
+        cp(T.selu[:], code, ["PM"], ["selu"])
+        ts(T.szu[:], code, 0.125, -7.0 / 16, ALU.mult, ALU.add, ["PM"], ["szu"])
         mms("PA", [(T.PA[:, j:256:2], T.mK[:], T.Ib[:], ["mK", "Ib"], 128, False) for j in range(2)])
         tt(T.Wm[:, 0:256], T.PA[:, 0:256], T.DD[:, 0:256], ALU.mult, ["PA", "DDa", "DDb"], ["Wma"], 256, "")
         nW = ["Wma", "Wmz", "Wmc", "szu"] + nz
@@ -567,12 +564,12 @@ def rank_program(g, core, T, topo):
             dma("Y", "stM", T.yms[:], T.yy[:], ["yy"], [], 2 ** 16)
         else:
             lz2 = T["lz%d" % (r + 1)]
-            ts(sz[:, 0:128:16, 2], T.PB[:, 0:8], 0.125, BO - 7.0 / 16, ALU.mult, ALU.add, ["PB", ns], [ns + "b"])
+            ts(sz[:, 0:128:16, 2], code, 0.125, BO - 7.0 / 16, ALU.mult, ALU.add, ["PM", ns], [ns + "b"])
             tt(sz[:, :, 0], T.Wm[:].indirect(T.szu[:]), M1, ALU.add, nW + [ns], [ns + "d"], 128, "g")
             nsz = [ns + x for x in "abcd"]
-            for call, nm, lat in ((CALL_A, "A", T_A), (CALL_B, "B", T_B)):
+            for nm, call in CALLS.items():
                 send(call, lambda h, a=sz: a[:, 16 * h:16 * h + 16, :], lambda s, a=lz2: a[:, 16 * s:16 * s + 16, :],
-                     "ar%s%d" % (nm, r), nsz, ["lz%d%s" % (r + 1, nm)], lat)
+                     "ar%s%d" % (nm, r), nsz, ["lz%d%s" % (r + 1, nm)], T_CALL[nm])
             cp(lz2[:, 16:32, :], sz[:, 0:16, :], nsz, ["lz%do" % (r + 1)], 64, "h")
         Wv = T.PM[:, 24, 0:16]
         mms("PM", [(Wv, T.Ib[:], T.S32[:, 16 * last:16 * last + 16], ["Ib", "S32a", "S32b", "S32c", "S32d"], 16, False)] +

@@ -9,7 +9,7 @@ MAGIC32 = float(3 * 2 ** 27)
 ZO = 1536.0
 BO = 1280.0
 OFF = 2047.5
-YC, YA, YW = 2048, 2176, 3200
+YC, YA, YW = 2048, 2304, 3328
 
 F, B, I, U, H = "float32", "bfloat16", "int32", "uint16", "float16"
 SCRATCH = {}
@@ -22,14 +22,14 @@ def _sb(dtype, **kw):
 
 _sb(B, X=[4096], yw=[YW], xm=[2048], mnm=[2048], mnx=[2048], UL=[2048], DM=[2048], CH=[8, 128], E=[1024], BT=[512],
     zb=[128], zT=[256], Ib=[128], Inh=[128], I8k=[128], In1k=[128], Uw=[128], ones=[128],
-    e8=[128], TRI=[128], C30=[128], WX=[4, 32], WM=[4, 48], BDb=[128], nIb=[128], y2=[128], ya=[128], ny=[128],
-    mA=[128], mK=[128], nA=[128], cb=[16], val=[16], S32=[32], bits=[256], nzb=[128])
-_sb(F, Kw=[640], If=[128], nIf=[128], nBI=[128], BD=[128], CX=[16, 12], DX=[192], LX=[192], LQ=[192], CM=[24, 9],
-    D16=[128], DA=[128], D2s=[16], CC=[16], CG=[16], D512=[16], pm=[8], SL=[8], zz=[128], yy=[128],
-    DD=[384], Wm=[400], LMk=[128], LMs=[24], LXk=[128], mmin=[128], amax=[128], mkhi=[8], thr=[16], LE=[64],
-    LV=[64], L1=[128], nameN=[128], D1=[128], D2=[128], tq=[8], lo=[16], Mn=[128])
+    e8=[128], two=[128], TRI=[128], C30=[128], WX=[4, 32], WM=[4, 48], BDb=[128], nIb=[128], y2=[128], ya=[128], ny=[128],
+    mA=[128], mK=[128], nA=[128], cb=[16], val=[16], S32=[96], bits=[256], nzb=[128])
+_sb(F, Kw=[640], If=[128], nIf=[128], BD=[128], CX=[16, 12], DX=[192], LX=[192], LM2=[192], LQ=[192], CM=[24, 9],
+    D16=[128], DA=[128], D2s=[16], DV=[48], CC=[16], D512=[16], pm=[8], SL=[8], zz=[128], yy=[128],
+    DD=[384], Wm=[416], LMk=[128], LMs=[24], LXk=[128], mmin=[128], amax=[128], LE=[64],
+    LV=[64], old=[128], D2=[128], tq=[48], lo=[16], Mn=[128])
 _sb(H, lz0=[128, 4], lz1=[128, 4], lz2=[128, 4], sz0=[128, 4], sz1=[128, 4], sz2=[128, 4], sc0=[64], sc1=[64], sc2=[64],
-    lc0=[64], lc1=[64], ce=[8], kc=[128], K37=[128], oM=[128])
+    lc0=[64], lc1=[64], ce=[8], L1=[128], CG=[16], CMh=[216], kc=[128], K37=[128], oM=[128])
 _sb(I, kti=[512], msi=[128], tmpi=[256], tmpj=[256], BI=[256], ksi=[8], KS=[8], ci=[16], cj=[8], c8=[8], ui=[8],
     xa=[128], xb=[128])
 _sb(U, Mu=[128], kcu=[128], cu16=[8], EX=[8], EXS=[8], EXA=[8], EXD=[2], selu=[8], szu=[8], eu=[16], vu=[8], ou=[16])
@@ -39,20 +39,20 @@ for _n in BANKS:
         ("psum", [128, 32, 16], F) if _n in ("PX", "PM") else ("psum", [128, 512], F)
 
 SEMAPHORES = ["cV", "cS", "cP", "cG", "ldX", "ldX2", "ldK", "ldM", "ldZ", "ldC", "stX", "stX2", "stK", "stM", "stZ",
-              "arC0", "arC1", "arA0", "arA1", "arB0", "arB1", "arD0", "arD1", "sent", "cpD"]
+              "arC0", "arC1", "arA0", "arA1", "arB0", "arB1", "arD0", "arD1", "sent", "cpD", "cpU"]
 
 CH_M = [(0, 64), (64, 64)]
 CH_X = [(0, 64), (64, 32), (96, 32)]
 _LATER = [("S", 0, 48), ("V", 48, 32), ("S", 80, 48)]
 G_M = [[("V", 0, 32), ("S", 32, 32), ("S", 64, 32), ("V", 96, 32)], _LATER, _LATER]
 G_X = [[("S", 0, 32), ("V", 32, 32), ("S", 64, 32), ("S", 96, 16), ("V", 112, 16)]] * RO
-MM_X = [(0, 96), (96, 32)]
+MM_M, MM_X = [(0, 128)], [(0, 96), (96, 32)]
 CALLS = {"A": ((7, 4), (1, 4), (2, 4), (3, 4)), "B": ((4, 8), (5, 8)), "D": ((6, 16),)}
 CALL_C = ((1, 2), (2, 2), (3, 2), (4, 2), (5, 2), (6, 2), (7, 4))
 FIRST = 80
-CY, GAT, SCA, PEC, WAKE, FIX, T_DMA, BW = 1.04e-3, 1.56, 3.8, 0.53e-3, 0.12, 0.03, 2.2, 250e3
-T_CALL, T_C, T_FIRST = {"A": 2.4, "B": 2.65, "D": 2.5}, 3.9, 1.5
-SEED, TRIES, HEAT = 3, 6000, 0.15
+CY, GAT, SCA, PEC, WAKE, WAKE_OWN, FIX, T_DMA, BW = 0.95e-3, 1.6, 3.8, 0.48e-3, 0.16, 0.17, 0.015, 1.9, 300e3
+T_CALL, T_C, T_FIRST = {"A": 1.7, "B": 2.0, "D": 1.9}, 4.0, 1.5
+SEED, TRIES, HEAT = 2, 20000, 0.15
 PLANS = {}
 
 
@@ -65,7 +65,7 @@ def plan(ops):
         for r in o["rd"] + o["wr"]:
             if r in writer:
                 pred[i].add(writer[r])
-                if r[0] == "~" and r != "~LX":
+                if r[0] == "~" and r not in ("~LX", "~szu"):
                     soft.add((writer[r], i))
         for w in o["wr"]:
             pred[i].update(readers.get(w, []))
@@ -82,7 +82,7 @@ def plan(ops):
     def gap(p, i):
         if (p, i) in soft:
             return 0.0
-        return lat[p] + (0.0 if eng[p] == 2 and eng[i] == 2 else WAKE)
+        return lat[p] + (WAKE if eng[p] != eng[i] else 0.0 if eng[i] == 2 else WAKE_OWN)
     before = [[(p, gap(p, i)) for p in sorted(pred[i])] for i in range(n)]
     after = [[] for _ in ops]
     for i in range(n):
@@ -155,7 +155,7 @@ def plan(ops):
     for it in range(TRIES):
         if it % 100 == 99:
             a, b = int(rnd() * RO), int(rnd() * RO)
-            d = fw[twin[a][("S", "LX", 0)]] - fw[twin[b][("S", "LX", 0)]]
+            d = fw[twin[a][("V", "LQ", 0)]] - fw[twin[b][("V", "LQ", 0)]]
             trial = list(fw)
             part = rnd()
             for s, i in twin[a].items():
@@ -227,8 +227,14 @@ def rank_program(g, core, T, topo):
 
     group = {}
 
-    def mm(out, l, r, st, sp, rd, wr, n=128, f32=False, m=128, close=True):
+    def mm(items, st, sp, wr, m=128, rd=()):
         bank = wr[0]
+        rd = sorted({x for it in items for x in it[3]}) + list(rd)
+
+        def fn():
+            for j, it in enumerate(items):
+                ins = P.matmul(it[0], it[1], it[2], st and j == 0, sp and j == len(items) - 1)
+            return ins
         if st and not sp:
             group[bank] = []
             wr = wr + ["~" + bank]
@@ -237,19 +243,14 @@ def rank_program(g, core, T, topo):
             rd, wr = rd + ["~" + bank], wr[1:] + group[bank][-1:]
         elif not st:
             rd = rd + group.pop(bank, [])
-        op("P", lambda: P.matmul(out, l, r, st, sp and close), rd, wr, max(min(64, m), n) * PEC * (4 if f32 else 1))
+        op("P", fn, rd, wr, sum(max(min(64, m), it[4]) * PEC * (4 if it[5] else 1) for it in items))
 
-    def mms(bank, items, start=True, stop=True):
-        for j, (out, l, r, rd, n, f32) in enumerate(items):
-            end = j == len(items) - 1
-            if not start:
-                op("P", lambda out=out, l=l, r=r, end=end: P.matmul(out, l, r, False, end), rd, [bank],
-                   max(64, n) * PEC * (4 if f32 else 1))
-            else:
-                mm(out, l, r, j == 0, end, rd, [bank], n, f32, 128, stop)
+    def mms(bank, *parts):
+        for j, items in enumerate(parts):
+            mm(items, j == 0, j == len(parts) - 1, [bank])
 
-    def tr(out, in_, rd, bank):
-        op("P", lambda: P.transpose(out, in_, T.Ib[:]), rd + ["Ib"], [bank], 128 * PEC)
+    def tr(outs, in_, rd, bank):
+        op("P", lambda: [P.transpose(o, in_, T.Ib[:]) for o in outs][-1], rd + ["Ib"], [bank], 128 * PEC * len(outs))
 
     def iota(out, pat, base, cm, wr, n, fl=False):
         if fl:
@@ -274,14 +275,15 @@ def rank_program(g, core, T, topo):
     iota(T.CM[:, 16:24, :], [[0, 72]], 256, 16, ["CMa"], 72, True)
     iota(T.CM[:, 0:16, 0:8], [[0, 8], [8, 2], [1, 8]], 0, 16, ["CMb"], 128, True)
     iota(T.CX[:, :, 0:8], [[0, 8], [8, 2], [1, 8]], 0, 16, ["CXa"], 128, True)
-    iota(T.CX[:, :, 8], [[0, 16]], YC, 1, ["CXb"], 16, True)
+    iota(T.CX[:, :, 8], [[0, 16]], YC, 2, ["CXb"], 16, True)
     iota(T.CX[:, 1:16:2, 10], [[0, 8]], 2 ** 24 - 4096 + YA, 8, ["CXc"], 8, True)
     iota(T.C30[:], [[0, 8], [-2, 16]], 30, 0, ["C30"], 128, True)
     iota(T.Kw[:, 512:640], [[0, 128]], 0, 0, ["Kwd"], 128, True)
-    iota(T.Wm[:, 256:272], [[0, 16]], 0, 0, ["Wmz"], 16, True)
+    iota(T.Wm[:, 256:288], [[0, 32]], 0, 0, ["Wmz"], 32, True)
     iota(T.DX[:], [[0, 192]], 1, 0, ["DX"], 192, True)
-    iota(T.yw[:, YA:YW], [[0, YW - YA]], 0, 0, ["ya2"], YW - YA, True)
-    iota(T.UL[:], [[0, 2048]], 0, 0, ["UL"], 2048, True)
+    iota(T.yw[:, YC:YW], [[0, YW - YC]], 0, 0, ["yc", "ya2"], YW - YC, True)
+    for j in range(2):
+        dma("Y", "cpU", T.UL[:, 1024 * j:1024 * j + 1024], T.yw[:, YA:YW], ["ya2", "kti", "X"], ["ULz%d" % j], 2 ** 18)
     ms(T.ones[:], 1.0, ["ones"], 128, "h")
 
     def fill(out, val, wr, n=8, rd=()):
@@ -293,7 +295,9 @@ def rank_program(g, core, T, topo):
     ms(T.D16[:], 0.0, ["D16"], 128)
     ms(T.D16[:, 0:128:16], HUGE, ["D16"])
     act(T.DA[:], T.D16[:], ["D16"], ["DA"], 128, scale=-1.0)
-    fill(T.e8[:], 8.0, ["e8"], 128)
+    fill(T.e8[:], -8 * BIG, ["e8"], 128)
+    fill(T.two[:], -2.0, ["two"], 128)
+    ms(T.LM2[:], 0.0, ["LM2"], 192)
     fill(T.DX[:, 8:192:12], -1.0, ["DXa"], 16, ["DX"])
     fill(T.DX[:, 9:192:12], -1.0, ["DXb"], 16, ["DX"])
     fill(T.DX[:, 10:192:24], -1.0, ["DXc"], 8, ["DX"])
@@ -301,6 +305,7 @@ def rank_program(g, core, T, topo):
     DXall = ["DX" + x for x in "abcd"]
     act(T.D2s[:], T.D16[:, 0:128:8], ["D16"], ["D2s"])
     ms(T.CM[:, 0:16, 8], 0.0, ["CMc"])
+    act(T.CMh[:], T.CM[:], ["CMa", "CMb", "CMc"], ["CMh"], 216)
     ms(T.CX[:, 0:16:2, 9], BIG / 2, ["CXd"])
     ms(T.CX[:, 1:16:2, 9], -BIG / 2, ["CXe"])
     fill(T.CX[:, 0:16:2, 10], -HUGE, ["CXf"])
@@ -310,7 +315,14 @@ def rank_program(g, core, T, topo):
     fill(T.CG[:, 0:16:2], 1025.0, ["CGa"])
     fill(T.CG[:, 1:16:2], 1024.0, ["CGb"])
     fill(T.CC[:, 0:16:2], -256 * ZO, ["CCa"])
-    fill(T.S32[:, 0:32:2], -15.5, ["S32c"], 16)
+    ms(T.S32[:], 0.0, ["S32"], 96, "h")
+    fill(T.S32[:, 0:96:6], -15.5, ["S32c"], 16, ["S32"])
+    fill(T.S32[:, 1:96:6], MAGIC32, ["S32e"], 16, ["S32"])
+    fill(T.S32[:, 2:96:6], -MAGIC32, ["S32f"], 16, ["S32"])
+    S32all = ["S32" + x for x in "abcdef"]
+    iota(T.DV[:], [[0, 48]], 1, 0, ["DV"], 48, True)
+    fill(T.DV[:, 0:48:6], 0.0, ["DVa"], 8, ["DV"])
+    fill(T.DV[:, 3:48:6], -1.0, ["DVb"], 8, ["DV"])
     ms(T.WX[:, 0:2, :], 0.0, ["WX"])
     ms(T.WM[:, 0:2, :], 0.0, ["WM"])
     ts(T.Ib[:], T.tmpi[:, 0:128], 0.0, None, ALU.is_equal, None, ["tmpi"], ["Ib"], 128)
@@ -328,7 +340,7 @@ def rank_program(g, core, T, topo):
     ts(h0, pm, 8.0, None, ALU.is_lt, None, ["pm"], ["h0"])
     ts(T.EXD[:, 0:1], p8, 8.0, pg, ALU.mult, ALU.add, ["pm"], ["EXD"])
     G8 = T.BD[:, 0:128:16]
-    for name, sc in (("If", 1.0), ("nBI", -BIG), ("Inh", -0.5), ("I8k", 8192.0), ("In1k", -1024.0),
+    for name, sc in (("If", 1.0), ("nIf", -1.0), ("Inh", -0.5), ("I8k", 8192.0), ("In1k", -1024.0),
                      ("nIb", -1.0)):
         act(T[name][:], T.Ib[:], ["Ib"], [name], 128, scale=sc)
     for half in range(2):
@@ -337,8 +349,8 @@ def rank_program(g, core, T, topo):
         act(T.WX[:, half, 1:32:4], G8, ["BD", "WX"], ["WXb%d" % half], scale=2 * BIG * sg)
         act(T.WX[:, half, 3:32:4], G8, ["BD", "WX"], ["WXc%d" % half], scale=-2 * BIG * sg)
         act(T.WM[:, half, 2 * half:32:4], G8, ["BD", "WM"], ["WMa%d" % half], scale=8192.0)
-        act(T.WM[:, half, 1:32:4], G8, ["BD", "WM"], ["WMb%d" % half], scale=2.0 * sg)
-        act(T.WM[:, half, 3:32:4], G8, ["BD", "WM"], ["WMc%d" % half], scale=-2.0 * sg)
+        act(T.WM[:, half, 1:32:4], G8, ["BD", "WM"], ["WMb%d" % half], scale=2 * BIG * sg)
+        act(T.WM[:, half, 3:32:4], G8, ["BD", "WM"], ["WMc%d" % half], scale=-2 * BIG * sg)
         act(T.WM[:, half, 33:48:2], G8, ["BD", "WM"], ["WMd%d" % half], scale=512.0)
     WXall = ["WX%s%d" % (x, j) for x in "abc" for j in range(2)]
     WMall = ["WM%s%d" % (x, j) for x in "abcd" for j in range(2)]
@@ -361,16 +373,16 @@ def rank_program(g, core, T, topo):
     ts(T.EXA[:], T.tmpj[:, 160:168], 16.0, 15.0, ALU.mult, ALU.add, ["J16"], ["EXA"])
     act(T.Uw[:], T.BD[:], ["BD", "pm2"], ["Uw"], 128, scale=pm2)
     act(T.BDb[:], T.BD[:], ["BD"], ["BDb"], 128)
-    act(T.S32[:, 1:16:2], T.SL[:], ["SL"], ["S32a"], scale=32.0)
-    act(T.S32[:, 17:24:2], T.SL[:, 0:4], ["SL"], ["S32b"], scale=32.0)
-    act(T.S32[:, 25:32:2], T.SL[:, 0:4], ["SL"], ["S32d"], scale=32.0)
+    act(T.S32[:, 3:48:6], T.SL[:], ["SL", "S32"], ["S32a"], scale=32.0)
+    act(T.S32[:, 51:72:6], T.SL[:, 0:4], ["SL", "S32"], ["S32b"], scale=32.0)
+    act(T.S32[:, 75:96:6], T.SL[:, 0:4], ["SL", "S32"], ["S32d"], scale=32.0)
     act(T.D512[:, 0:8], T.SL[:], ["SL"], ["D512a"], bias=512.0)
     act(T.D512[:, 8:16], T.SL[:], ["SL"], ["D512b"], bias=512.0)
     c0 = -8193.0 * BO - 16384.0
     act(T.CC[:, 3:16:2], T.SL[:, 0:7], ["SL"], ["CCb"], scale=-16386.0, bias=c0)
     act(T.CC[:, 1:2], T.SL[:, 7:8], ["SL"], ["CCc"], scale=-16386.0, bias=c0)
     for gi in range(8):
-        act(T.UL[:, 16 * gi:16 * gi + 129 * 15 + 1:129], T.Uw[:, 16 * gi:16 * gi + 16], ["Uw", "UL"], ["UL%d" % gi])
+        act(T.UL[:, 16 * gi:16 * gi + 129 * 15 + 1:129], T.Uw[:, 16 * gi:16 * gi + 16], ["Uw", "ULz0", "ULz1"], ["UL%d" % gi])
     ULall = ["UL%d" % gi for gi in range(8)]
     for b in range(8):
         ts(T.BI[:, b:256:8], T.tmpj[:, 192:224], b, 1, ALU.arith_shift_right, ALU.bitwise_and, ["CIa", "CIb"], ["BI%d" % b], 32)
@@ -437,16 +449,15 @@ def rank_program(g, core, T, topo):
         for j, (src, bank) in enumerate((("EA", "ZA"), ("EB", "ZB"))):
             mms(src, [(T[src][:, 0:128], lz[:, 64 * j:64 * j + 64, 1:4:2], T.Ib[:], (nA, nz)[j] + ["Ib"], 128, False)])
             act(T.zT[:, 128 * j:128 * j + 128], T[src][:, 0:128], [src], ["zT%d" % j], 128, scale=0.5, bias=-ZO / 2)
-            for k in range(0, 16, 2):
-                tr(T[bank][:, :, k:k + 2], T.zT[:, 128 * j:128 * j + 128], ["zT%d" % j], bank)
+            tr([T[bank][:, :, k:k + 2] for k in range(0, 16, 2)], T.zT[:, 128 * j:128 * j + 128], ["zT%d" % j], bank)
         if r:
             lc, sp, beta = T["lc%d" % (r - 1)], T["sc%d" % (r - 1)], lz[:, 0:128:16, 2]
             mms("PA", [(T.PA[:, 384:400], T.If[:], T.CC[:], ["If", "CCa", "CCb", "CCc"], 16, True),
                        (T.PA[:, 385:386], T.Ib[:], lc[:, 0:1], ["Ib", "lc%d" % (r - 1)], 8, False),
                        (T.PA[:, 387:388], T.Ib[:], sp[:, 0:1], ["Ib", "sc%d" % (r - 1)], 8, False),
-                       (T.PA[:, 389:400:2], T.Ib[:], lc[:, 16:64:8], ["Ib", "lc%d" % (r - 1)], 8, False),
-                       (T.PA[:, 385:400:2], T.Ib[:], beta, ["Ib"] + nz, 8, False),
-                       (T.PA[:, 385:400:2], T.I8k[:], beta, ["I8k"] + nz, 8, False)] +
+                       (T.PA[:, 389:400:2], T.Ib[:], lc[:, 16:64:8], ["Ib", "lc%d" % (r - 1)], 8, False)],
+                [(T.PA[:, 385:400:2], T.Ib[:], beta, ["Ib"] + nz, 8, False),
+                 (T.PA[:, 385:400:2], T.I8k[:], beta, ["I8k"] + nz, 8, False)] +
                 [(T.PA[:, 384:400:2], T.UL[:, 128 * il:128 * il + 128], lz[:, il:128:16, 1], ULall + nz, 8, False)
                  for il in range(16)])
             scan(T.ci[:], T.D2s[:], T.PA[:, 384:400], ALU.add, ALU.min, ["D2s", "PA"], ["ci"], 16)
@@ -462,28 +473,33 @@ def rank_program(g, core, T, topo):
         if not last:
             send(CALL_C, lambda h, a=sc: a[:, 8 * h:8 * h + 8], lambda s, a=T["lc%d" % r]: a[:, 8 * s:8 * s + 8], "arC%d" % r,
                  ["sc%d" % r] + (["kti", "X", "Xb"] if r == 0 else []), ["lc%d" % r], T_C, T_FIRST if r == 0 else 0.0)
-        mm(T.PM[:, 0:24, 0:9], T.If[:], T.CM[:], True, False, ["If", "CMa", "CMb", "CMc"], ["PM"], 216, True)
-        if r:
-            for j in range(2):
-                for b in range(2):
-                    mm(T.PM[:, j:16:2, 8], T.e8[:], T.cb[:, b:16:2], False, False, ["e8", "cb"], ["PM"], 8)
+        mm([(T.PM[:, 0:24, 0:9], T.Ib[:], T.CMh[:], ["Ib", "CMh"], 216, False)] +
+           [(T.PM[:, j:16:2, 8], T.e8[:], T.cb[:, b:16:2], ["e8", "cb"], 8, False) for j in range(2) for b in range(2) if r],
+           True, False, ["PM"])
         for s0, n in CH_M:
             mins("m", s0, n)
-        for k in range(16):
-            mm(T.PM[:, 0:24, k % 8:9:8 - k % 8], T.xm[:, k:2048:16], T.WM[:, k // 8, :], False, False, XM + WMall,
-               ["PM", "~rm%d" % k], 48)
-        for k in range(16):
-            mm(T.PM[:, 0:24, k % 8:9:8 - k % 8], T.mnm[:, k:2048:16], T.WM[:, 2 + k // 8, :], False, k == 15,
-               ["n" + x for x in XM] + ["WMn", "~rm%d" % k], ["PM"], 48)
+
+        def sums(bank, rows, col, chunks, tile, least, t, W, nW, nWn):
+            def part(buf, wo, s0, n, ks, rd):
+                return [(T[bank][s0:s0 + n, 0:rows, k % 8:col + 1:col - k % 8], buf[:, 16 * s0 + k:16 * (s0 + n):16],
+                         W[:, wo + k // 8, :], rd, 2 * rows, False) for k in ks]
+            for s0, n in chunks:
+                mm(part(tile, 0, s0, n, range(16), tags(t, s0, n) + nW), False, False, [bank, "~r%d" % s0], n)
+                if n < 128:
+                    mm(part(least, 2, s0, n, range(15), tags("n" + t, s0, n) + nWn), False, False, [bank], n, ["~r%d" % s0])
+            mm(part(least, 2, 0, 128, range(15 * (len(chunks) > 1), 16), tags("n" + t, 0, 128) + nWn), False, True, [bank])
+        sums("PM", 24, 8, MM_M, T.xm, T.mnm, "m", T.WM, WMall, ["WMn"])
         LMk, nLM = T.LMk[:], ["LMk"]
         act(LMk, T.PM[:, 0:16, 0:8], ["PM"], nLM, 128)
         act(T.LMs[:], T.PM[:, 0:24, 8], ["PM"], ["LMs"], 24)
         scan(T.mmin[:], T.D16[:], LMk, ALU.add, ALU.min, ["D16"] + nLM, ["mmin"], 128)
         mk = T.mmin[:, 15:128:16]
-        ts(T.mkhi[:], mk, MAGIC4, MAGIC4, ALU.add, ALU.subtract, ["mmin"], ["mkhi"])
-        tt(T.thr[:, 0:16:2], T.LMs[:, 0:16:2], T.LMs[:, 1:16:2], ALU.max, ["LMs"], ["thra"])
-        act(T.thr[:, 1:16:2], T.thr[:, 0:16:2], ["thra"], ["thrb"], func=ACT.Relu, bias=-1.0)
-        tt(T.ce[:], mk, T.mkhi[:], ALU.subtract, ["mmin", "mkhi"], ["ce"])
+        mkhi = T.LM2[:, 8:192:24]
+        ts(mkhi, mk, MAGIC4, MAGIC4, ALU.add, ALU.subtract, ["mmin", "LM2"], ["mkhi"])
+        act(T.LM2[:, 20:192:24], mkhi, ["mkhi"], ["mkhj"])
+        tt(T.LM2[:, 9:192:24], T.LMs[:, 0:16:2], T.LMs[:, 1:16:2], ALU.min, ["LMs", "LM2"], ["thra"])
+        ts(T.LM2[:, 21:192:24], T.LM2[:, 9:192:24], BIG, 0.0, ALU.add, ALU.min, ["thra"], ["thrb"])
+        tt(T.ce[:], mk, mkhi, ALU.subtract, ["mmin", "mkhi"], ["ce"])
         mms("PB", to_list("PB", T.ce[:], ["ce"]))
         act(T.LE[:], T.PB[:, 0:64], ["PB"], ["LE"], 64)
         cp(T.eu[:], T.LE[:].indirect(T.EXD[:, 0:1]), ["LE", "EXD"], ["eu"], 16, "g")
@@ -493,7 +509,7 @@ def rank_program(g, core, T, topo):
         act(T.ya[:], T.PB[:, 0:128], ["PB"], ["ya"], 128, func=ACT.Abs, scale=2.0, bias=ZO)
         mms("PB", [(T.PB[:, 0:128], T.Inh[:], z1, ["Inh"] + nz, 128, False),
                    (T.PB[:, 0:128], T.Ib[:], T.ya[:], ["Ib", "ya"], 128, False)])
-        act(T.yw[:, YC:YC + 128], T.PB[:, 0:128], ["PB"], ["yc"], 128, bias=ZO / 2 + 0.25)
+        act(T.yw[:, YC:YA:2], T.PB[:, 0:128], ["PB"], ["yc"], 128, bias=ZO / 2 + 0.25)
         act(T.yw[:, YA:YW:8], T.PB[:, 0:128], ["PB"], ["ya2"], 128, bias=ZO / 2 + 0.25)
         fresh = [(T.Uw[:], z1, ["Uw"] + nz, False), (T.Ib[:], T.K37[:], ["Ib", "K37"], False), (T.Ib[:], T.kc[:], ["Ib", "kc"], False)]
         mms("PA", [(T.PA[:, 0:128], l, x, rd, 128, f) for l, x, rd, f in fresh])
@@ -503,43 +519,31 @@ def rank_program(g, core, T, topo):
                    (T.PA[:, 0:128], T.nIb[:], M1, ["nIb"] + nz, 128, False),
                    (T.PA[:, 256:384], T.Inh[:], z1, ["Inh"] + nz, 128, False)] +
             [(T.PA[:, 128:256], l, x, rd, 128, f) for l, x, rd, f in fresh] +
-            [(T.PA[:, 128:256], T.nIb[:], M1, ["nIb"] + nz, 128, False),
-             (T.PA[:, 128:256], T.Ib[:], T.ny[:], ["Ib", "ny"], 128, False)])
-        act(T.DD[:, 0:256:2], T.PA[:, 0:128], ["PA", "h0"], ["DDa"], 128, scale=h0)
-        act(T.DD[:, 1:256:2], T.PA[:, 0:128], ["PA", "h1"], ["DDb"], 128, scale=h1)
+            [(T.PA[:, 128:256], T.nIb[:], M1, ["nIb"] + nz, 128, False)],
+            [(T.PA[:, 128:256], T.Ib[:], T.ny[:], ["Ib", "ny"], 128, False)])
+        act(T.DD[:, 0:128], T.PA[:, 0:128], ["PA"], ["DDa"], 128)
         act(T.DD[:, 256:384], T.PA[:, 128:256], ["PA"], ["DDc"], 128, bias=-0.5)
         act(T.zz[:], T.PA[:, 256:384], ["PA"], ["zz"], 128, scale=-1.0, bias=ZO / 2 - 0.25)
         tt(T.mA[:], T.LMs[:].indirect(T.EXS[:]), LMk, ALU.is_le, ["LMs", "EXS"] + nLM, ["mA"], 128, "g")
         act(T.bits[:, 0:128], T.BT[:].indirect(T.cu16[:]), ["BTa", "BTb", "cu16"], ["bits"], 128, "g")
         act(T.bits[:, 128:256], T.bits[:, 0:128], ["bits", "pm"], ["bits2"], 128, scale=podd)
         for j, bank in enumerate(("EA", "EB")):
-            for q in range(4):
-                mm(T[bank][:, 128 * q:128 * q + 128], T.Ib[:], T.TRI[:], q == 0, False, ["Ib", "TRI"], [bank])
-            for q in range(4):
-                p0, o = 64 * j + 32 * (q // 2), T[bank][:, 128 * q:128 * q + 128]
-                rd, wr = (["Et0", "Et1"], []) if q > 1 else ([], ["Et%d" % q])
-                if q % 2:
-                    mm(o, T.bits[p0:p0 + 32, 128:256], T.bits[p0:p0 + 32, 0:128], False, q == 3, ["bits", "bits2"] + rd, [bank] + wr)
-                else:
-                    mm(o, T.bits[p0:p0 + 16, 0:128], T.bits[p0:p0 + 16, 0:128], False, False, ["bits"] + rd, [bank] + wr)
+            mm([(T[bank][:, 128 * q:128 * q + 128], T.Ib[:], T.TRI[:], ["Ib", "TRI"], 128, False) for q in range(4)],
+               True, False, [bank])
+            for q in range(2):
+                p0, rd = 64 * j + 32 * q, ["bits", "bits2"] + ["Et"] * q
+                mm([(T[bank][:, 256 * q:256 * q + 128], T.bits[p0:p0 + 16, 0:128], T.bits[p0:p0 + 16, 0:128], rd, 128, False),
+                    (T[bank][:, 256 * q + 128:256 * q + 256], T.bits[p0:p0 + 32, 128:256], T.bits[p0:p0 + 32, 0:128], rd, 128, False)],
+                   False, q == 1, [bank] + ["Et"] * (1 - q))
             act(T.E[:, 512 * j:512 * j + 512], T[bank][:], [bank], ["E%d" % j], 512, func=ACT.Relu, scale=1024.0, bias=-7168.0)
-        mm(T.PX[:, 0:16, 0:12], T.If[:], T.CX[:], True, False, ["If"] + CXall, ["PX"], 192, True)
-        for j in range(2):
-            mm(T.PX[:, j:16:2, 8], T.If[:], T.mkhi[:], False, False, ["If", "mkhi"], ["PX"], 8, True)
-        mm(T.PX[:, 0:16, 9], T.nBI[:], T.thr[:], False, False, ["nBI", "thra", "thrb"], ["PX"], 16, True)
+        mm([(T.PX[:, 0:16, 0:12], T.If[:], T.CX[:], ["If"] + CXall, 192, True)], True, False, ["PX"])
         for s0, n in CH_X:
             mins("x", s0, n)
-        for s0, n in MM_X:
-            for buf, wo, t, dep in ((T.yw, 0, "x", WXall), (T.mnx, 2, "nx", ["WXn"])):
-                for k in range(15 if t == "nx" else 16):
-                    mm(T.PX[s0:s0 + n, 0:16, k % 8:10:9 - k % 8], buf[:, 16 * s0 + k:16 * (s0 + n):16], T.WX[:, wo + k // 8, :],
-                       False, False, tags(t, s0, n) + dep + ["~rx%d_%d" % (s0, k)] * (t == "nx"),
-                       ["PX"] + ["~rx%d_%d" % (s0, k)] * (t == "x"), 32, False, n)
-        mm(T.PX[:, 0:16, 7:10:2], T.mnx[:, 15:2048:16], T.WX[:, 3, :], False, True, tags("nx", 0, 128) + ["WXn"], ["PX"], 32)
-        tr(T.ZA[:, 0:8, :], T.mA[:], ["mA"], "ZA")
-        tt(T.Wm[:, 272:400], T.ZA[:, 0:8, :], T.DD[:, 256:384], ALU.mult, ["ZA", "DDc"], ["Wmc"], 128, "")
+        sums("PX", 16, 9, MM_X, T.yw, T.mnx, "x", T.WX, WXall, ["WXn"])
+        tr([T.ZA[:, 0:8, :]], T.mA[:], ["mA"], "ZA")
+        tt(T.Wm[:, 288:416], T.ZA[:, 0:8, :], T.DD[:, 256:384], ALU.mult, ["ZA", "DDc"], ["Wmc"], 128, "")
         where[1] = True
-        act(T.LX[:], T.PX[:, 0:16, 0:12], ["PX"], ["LX", "~LX"], 192)
+        tt(T.LX[:], T.PX[:, 0:16, 0:12], T.LM2[:], ALU.add, ["PX", "mkhi", "mkhj", "thra", "thrb"], ["LX", "~LX"], 192, "")
         scan(T.LQ[:], T.LX[:], T.DX[:], ALU.min, ALU.mult, DXall + ["LX"], ["LQ"], 192, HUGE)
         tt(T.ksi[:], T.LQ[:, 9:192:24], T.LQ[:, 22:192:24], ALU.min, ["LQ"], ["ksi"])
         ts(T.KS[:], T.ksi[:], 4095, None, ALU.bitwise_and, None, ["ksi"], ["KS"])
@@ -547,12 +551,14 @@ def rank_program(g, core, T, topo):
         tt(T.mK[:], T.PX[:, 0:16, 0:8], LMk, ALU.is_lt, ["PX", "~LX"] + nLM, ["mK"], 128, "")
         tt(T.cb[:], T.LX[:, 8:192:12], T.LQ[:, 9:192:12], ALU.is_equal, ["LX", "LQ"], ["cb"], 16)
         code = T.PM[:, 25, 0:8]
-        mms("PM", [(code, T.L1[:], G8, ["L1", "BD"], 8, True)])
+        mms("PM", [(code, T.L1[:], T.BDb[:, 0:128:16], ["L1", "BDb"], 8, False)])
         cp(T.selu[:], code, ["PM"], ["selu"])
-        ts(T.szu[:], code, 0.125, -7.0 / 16, ALU.mult, ALU.add, ["PM"], ["szu"])
-        mms("PA", [(T.PA[:, j:256:2], T.mK[:], T.Ib[:], ["mK", "Ib"], 128, False) for j in range(2)])
-        tt(T.Wm[:, 0:256], T.PA[:, 0:256], T.DD[:, 0:256], ALU.mult, ["PA", "DDa", "DDb"], ["Wma"], 256, "")
-        nW = ["Wma", "Wmz", "Wmc", "szu"] + nz
+        ts(T.szu[:], code, 0.125, -7.0 / 16, ALU.mult, ALU.add, ["PM", "selu"], ["szu", "~szu"])
+        mms("PA", [(T.PA[:, 0:128], T.mK[:], T.Ib[:], ["mK", "Ib"], 128, False)])
+        tt(T.DD[:, 128:256], T.PA[:, 0:128], T.DD[:, 0:128], ALU.mult, ["PA", "DDa"], ["DDb"], 128, "")
+        act(T.Wm[:, 0:256:2], T.DD[:, 128:256], ["DDb", "h0"], ["Wma"], 128, scale=h0)
+        act(T.Wm[:, 1:256:2], T.DD[:, 128:256], ["DDb", "h1", "DM0"], ["Wmb"], 128, scale=h1)
+        nW = ["Wma", "Wmb", "Wmz", "Wmc", "szu"] + nz
         ns = "sz%d" % r
         tt(sz[:, :, 1], T.yw[:].indirect(T.selu[:]), T.zz[:], ALU.add, XX + ["yc", "ya2", "selu", "zz", ns], [ns + "a"], 128, "g")
         cp(sz[:, :, 3], sz[:, :, 1], [ns + "a"], [ns + "c"], 128, "h")
@@ -564,20 +570,18 @@ def rank_program(g, core, T, topo):
             dma("Y", "stM", T.yms[:], T.yy[:], ["yy"], [], 2 ** 16)
         else:
             lz2 = T["lz%d" % (r + 1)]
-            ts(sz[:, 0:128:16, 2], code, 0.125, BO - 7.0 / 16, ALU.mult, ALU.add, ["PM", ns], [ns + "b"])
+            act(sz[:, 0:128:16, 2], code, ["PM", ns, "~szu"], [ns + "b"], scale=0.125, bias=BO - 7.0 / 16)
             tt(sz[:, :, 0], T.Wm[:].indirect(T.szu[:]), M1, ALU.add, nW + [ns], [ns + "d"], 128, "g")
             nsz = [ns + x for x in "abcd"]
             for nm, call in CALLS.items():
                 send(call, lambda h, a=sz: a[:, 16 * h:16 * h + 16, :], lambda s, a=lz2: a[:, 16 * s:16 * s + 16, :],
-                     "ar%s%d" % (nm, r), nsz, ["lz%d%s" % (r + 1, nm)], T_CALL[nm])
-            cp(lz2[:, 16:32, :], sz[:, 0:16, :], nsz, ["lz%do" % (r + 1)], 64, "h")
-        Wv = T.PM[:, 24, 0:16]
-        mms("PM", [(Wv, T.Ib[:], T.S32[:, 16 * last:16 * last + 16], ["Ib", "S32a", "S32b", "S32c", "S32d"], 16, False)] +
-            [(Wv, T.UL[:, 128 * il:128 * il + 128], sz[:, il:128:16, 1:4:2], ULall + [ns + "a", ns + "c"], 16, False)
+                     "ar%s%d" % (nm, r), nsz + ["lc%d" % r], ["lz%d%s" % (r + 1, nm)], T_CALL[nm])
+            act(lz2[:, 16:32, :], sz[:, 0:16, :], nsz, ["lz%do" % (r + 1)], 64)
+        mms("PB", [(T.PB[:, 0:48], T.Ib[:], T.S32[:, 48 * last:48 * last + 48], ["Ib"] + S32all, 48, False)],
+            [(T.PB[:, 0:48:3], T.UL[:, 128 * il:128 * il + 128], sz[:, il:128:16, 1:4:2], ULall + [ns + "a", ns + "c"], 16, False)
              for il in range(16)])
-        ts(T.tq[:], T.PM[:, 24, 0:16:2], MAGIC32, MAGIC32, ALU.add, ALU.subtract, ["PM"], ["tq"])
-        tt(T.ui[:], T.PM[:, 24, 1:16:2], T.tq[:], ALU.subtract, ["PM", "tq", "pm"], ["ui"], 8, "")
-        cp(T.vu[:], T.ui[:], ["ui"], ["vu"])
+        scan(T.tq[:], T.DV[:], T.PB[:, 0:48], ALU.mult, ALU.add, ["PB", "DVa", "DVb"], ["tq"], 48)
+        cp(T.vu[:], T.tq[:, 3:48:6], ["tq"], ["vu"])
         for j, (c0, w) in enumerate(((0, 64), (64, 64)) if last else ((0, 128),)):
             win, off = T.X[:, 32 * c0:32 * (c0 + w)], T.vu[:, c0 // 16:(c0 + w) // 16]
             xj = "X%d" % j if last else "X"
@@ -587,27 +591,27 @@ def rank_program(g, core, T, topo):
             if last:
                 dma("YS"[j], ("stX", "stX2")[j], T.ytx[:, 2048 * j:2048 * j + 2048], win, [xj], [], 2 ** (19 + j))
         tt(T.oM[:], T.DM[:].indirect(T.eu[:, 0:8]), M1, ALU.mult, DMall + ["eu"] + nz, ["oM"], 128, "g")
-        mms("EB", [(T.EB[:, 128:256], T.BDb[:], T.oM[:], ["BDb", "oM"], 128, False)])
-        act(T.nameN[:], T.EB[:, 128:256], ["EB"], ["nameN"], 128, bias=2048.0)
         tt(T.LXk[:], T.PX[:, 0:16, 0:8], T.C30[:], ALU.add, ["PX", "C30", "~LX"], ["LXk"], 128, "")
         scan(T.amax[:], T.DA[:], T.LXk[:], ALU.add, ALU.max, ["DA", "LXk"], ["amax"], 128)
-        tt(T.nA[:], T.amax[:].indirect(T.EXA[:]), T.LXk[:], ALU.not_equal, ["amax", "EXA", "LXk"], ["nA"], 128, "g")
-        tr(T.ZB[:, 0:8, :], T.nA[:], ["nA"], "ZB")
-        mms("EA", [(T.EA[:, 0:16], T.If[:], T.CG[:], ["If", "CGa", "CGb"], 16, True),
+        tt(T.nA[:], T.amax[:].indirect(T.EXA[:]), T.LXk[:], ALU.is_equal, ["amax", "EXA", "LXk"], ["nA"], 128, "g")
+        tr([T.ZB[:, 0:8, :]], T.nA[:], ["nA"], "ZB")
+        mms("EA", [(T.EA[:, 0:16], T.Ib[:], T.CG[:], ["Ib", "CGa", "CGb"], 16, False),
                    (T.EA[:, 0:16], T.In1k[:], T.cb[:], ["In1k", "cb"], 16, False)] +
             [(T.EA[:, 2 * gi:2 * gi + 2], T.E[:, 128 * gi:128 * gi + 128], T.cb[:, 2 * gi:2 * gi + 2], ["E%d" % (gi // 4), "cb"], 2, False)
              for gi in range(8)])
         scan(T.val[:], T.D2s[:], T.EA[:, 0:16], ALU.add, ALU.min, ["D2s", "EA"], ["val"], 16)
-        for gi in range(8):
-            mm(T.EB[:, gi:64:8], T.Ib[:], c2m, gi == 0, False, ["Ib", "sc%d" % r], ["EB", "~c2m%d" % gi], 8)
-        for h, (out, l, x, rd, n, f32) in enumerate(to_list("EB", T.val[:, 1:16:2], ["val"])):
-            mm(out, l, x, False, h == 7, rd + ["~c2m%d" % gi for gi in range(8)], ["EB"], n)
+        mms("EB", [(T.EB[:, gi:64:8], T.Ib[:], c2m, ["Ib", "sc%d" % r], 8, False) for gi in range(8)],
+            to_list("EB", T.val[:, 1:16:2], ["val"]))
         act(T.LV[:], T.EB[:, 0:64], ["EB"], ["LV"], 64)
         tt(T.lo[:], T.LV[:].indirect(T.EXD[:, 0:1]), T.D512[:], ALU.min, ["LV", "EXD", "D512a", "D512b"], ["lo"], 16, "g")
         cp(T.ou[:, 0:8], T.lo[:, 0:8], ["lo"], ["ou"])
-        tt(T.D1[:], T.Kw[:].indirect(T.ou[:, 0:8]), T.nameN[:], ALU.subtract, ["Kw", "ou", "nameN"], ["D1"], 128, "g")
-        tt(T.D2[:], T.ZB[:, 0:8, :], T.D1[:], ALU.mult, ["ZB", "D1"], ["D2"], 128, "")
-        tt(T.Kw[:].indirect(T.ou[:, 0:8]), T.nameN[:], T.D2[:], ALU.add, ["ou", "nameN", "D2"], ["Kw"], 128, "s")
+        act(T.mA[:], T.ZB[:, 0:8, :], ["ZB"], ["mA"], 128)
+        act(T.old[:], T.Kw[:].indirect(T.ou[:, 0:8]), ["Kw", "ou"], ["old"], 128, "g")
+        mms("PB", [(T.PB[:, 0:128], T.BDb[:], T.oM[:], ["BDb", "oM"], 128, False),
+                   (T.PB[:, 0:128], T.In1k[:], T.two[:], ["In1k", "two"], 128, False)],
+            [(T.PB[:, 0:128], T.nIf[:], T.old[:], ["nIf", "old"], 128, True)])
+        tt(T.D2[:], T.PB[:, 0:128], T.mA[:], ALU.mult, ["PB", "mA"], ["D2"], 128, "")
+        tt(T.Kw[:].indirect(T.ou[:, 0:8]), T.old[:], T.D2[:], ALU.add, ["ou", "old", "D2"], ["Kw"], 128, "s")
         if last:
             dma("Y", "stK", T.ykt[:], T.Kw[:, 0:512], ["Kw"], [], 2 ** 18)
 

@@ -21,7 +21,7 @@ def _sb(dtype, **kw):
 
 
 _sb(B, X=[4096], yw=[YW], xm=[2048], mnm=[2048], mnx=[2048], UL=[2048], DM=[2048], CH=[8, 128], E=[1024], BT=[512],
-    zb=[128], zT=[256], Ib=[128], Inh=[128], I8k=[128], In1k=[128], Uw=[128], ones=[128],
+    zb=[128], zT=[256], Ib=[128], I8k=[128], In1k=[128], Uw=[128], ones=[128],
     e8=[128], two=[128], TRI=[128], C30=[128], WX=[4, 32], WM=[4, 48], BDb=[128], nIb=[128], y2=[128], ya=[128], ny=[128],
     mA=[128], mK=[128], nA=[128], cb=[16], val=[16], S32=[96], bits=[256], nzb=[128])
 _sb(F, Kw=[640], If=[128], nIf=[128], BD=[128], CX=[16, 12], DX=[192], LX=[192], LM2=[192], LQ=[192], CM=[24, 9],
@@ -29,7 +29,7 @@ _sb(F, Kw=[640], If=[128], nIf=[128], BD=[128], CX=[16, 12], DX=[192], LX=[192],
     DD=[384], Wm=[416], LMk=[128], LMs=[24], LXk=[128], mmin=[128], amax=[128], LE=[64],
     LV=[64], old=[128], D2=[128], tq=[48], lo=[16], Mn=[128])
 _sb(H, lz0=[128, 4], lz1=[128, 4], lz2=[128, 4], sz0=[128, 4], sz1=[128, 4], sz2=[128, 4], sc0=[64], sc1=[64], sc2=[64],
-    lc0=[64], lc1=[64], ce=[8], L1=[128], CG=[16], CMh=[216], kc=[128], K37=[128], oM=[128])
+    lc0=[64], lc1=[64], ce=[8], zq=[128], L1=[128], CG=[16], CMh=[216], kc=[128], K37=[128], oM=[128])
 _sb(I, kti=[512], msi=[128], tmpi=[256], tmpj=[256], BI=[256], ksi=[8], KS=[8], ci=[16], cj=[8], c8=[8], ui=[8],
     xa=[128], xb=[128])
 _sb(U, Mu=[128], kcu=[128], cu16=[8], EX=[8], EXS=[8], EXA=[8], EXD=[2], selu=[8], szu=[8], eu=[16], vu=[8], ou=[16])
@@ -50,21 +50,25 @@ MM_M, MM_X = [(0, 128)], [(0, 96), (96, 32)]
 CALLS = {"A": ((7, 4), (1, 4), (2, 4), (3, 4)), "B": ((4, 8), (5, 8)), "D": ((6, 16),)}
 CALL_C = ((1, 2), (2, 2), (3, 2), (4, 2), (5, 2), (6, 2), (7, 4))
 FIRST = 80
-CY, GAT, SCA, PEC, WAKE, WAKE_OWN, FIX, T_DMA, BW = 0.95e-3, 1.6, 3.8, 0.48e-3, 0.16, 0.17, 0.015, 1.9, 300e3
-T_CALL, T_C, T_FIRST = {"A": 1.7, "B": 2.0, "D": 1.9}, 4.0, 1.5
-SEED, TRIES, HEAT = 2, 20000, 0.15
+PACE = [dict(cy=0.87e-3, gat=1.56, sca=3.8, wake=0.18, wakeP=0.25, dma=1.5, bw=400e3, rem=1.0),
+        dict(cy=1.12e-3, gat=1.75, sca=4.5, wake=0.20, wakeP=0.26, dma=1.8, bw=280e3, rem=1.8)]
+SLOW = 0.6
+T_CALL, T_C, T_FIRST = {"A": 0.0, "B": 0.25, "D": 0.15}, 2.5, 1.5
+SEED, TRIES, HEAT = 2, 12000, 0.2
 PLANS = {}
 
 
 def plan(ops):
     n = len(ops)
     pred = [set() for _ in ops]
-    soft = set()
+    soft, reads = set(), set()
     writer, readers = {}, {}
     for i, o in enumerate(ops):
         for r in o["rd"] + o["wr"]:
             if r in writer:
                 pred[i].add(writer[r])
+                if r in o["rd"] and r[0] != "~":
+                    reads.add((writer[r], i))
                 if r[0] == "~" and r not in ("~LX", "~szu"):
                     soft.add((writer[r], i))
         for w in o["wr"]:
@@ -76,14 +80,14 @@ def plan(ops):
             readers[w] = []
         pred[i].discard(i)
     eng = ["VSPGY".index(o["e"]) for o in ops]
-    hold = [o["hold"] for o in ops]
-    lat = [o["lat"] for o in ops]
+    hold, hold2 = ([o["hold"][m] for o in ops] for m in range(2))
+    lat, lat2 = ([o["lat"][m] for o in ops] for m in range(2))
 
-    def gap(p, i):
-        if (p, i) in soft:
+    def gap(p, i, m):
+        if (p, i) in soft or (eng[p] == eng[i] == 2 and (p, i) not in reads):
             return 0.0
-        return lat[p] + (WAKE if eng[p] != eng[i] else 0.0 if eng[i] == 2 else WAKE_OWN)
-    before = [[(p, gap(p, i)) for p in sorted(pred[i])] for i in range(n)]
+        return ops[p]["lat"][m] + PACE[m]["wakeP" if eng[p] == 2 else "wake"]
+    before, before2 = ([[(p, gap(p, i, m)) for p in sorted(pred[i])] for i in range(n)] for m in range(2))
     after = [[] for _ in ops]
     for i in range(n):
         for p, gp in before[i]:
@@ -123,13 +127,24 @@ def plan(ops):
 
     zero = [0.0] * n
 
+    def slow(fw):
+        start, free = [0.0] * n, [0.0] * 5
+        for i in ranked(fw, before):
+            t = free[eng[i]]
+            for p, gp in before2[i]:
+                if start[p] + hold2[p] + gp > t:
+                    t = start[p] + hold2[p] + gp
+            start[i] = t
+            free[eng[i]] = t + hold2[i]
+        return max(start[i] + hold2[i] + lat2[i] for i in range(n))
+
     def forward(key):
         fw = place(key, before, zero)
-        return max(fw[i] + hold[i] + lat[i] for i in range(n)), fw
+        return max(fw[i] + hold[i] + lat[i] for i in range(n)) + SLOW * slow(fw), fw
 
     def both(key):
-        end, fw = forward(key)
-        bw = place([end - fw[i] - hold[i] for i in range(n)], after, lat)
+        fw = place(key, before, zero)
+        bw = place([-fw[i] - hold[i] for i in range(n)], after, lat)
         end = max(bw[i] + hold[i] for i in range(n))
         return forward([end - bw[i] - hold[i] for i in range(n)])
 
@@ -174,7 +189,7 @@ def plan(ops):
             cur, fw = end, f2
             if end < best:
                 best, out = end, f2
-    PLANS["t"] = best
+    PLANS["t"] = (best - SLOW * slow(out), slow(out))
     return ranked(out, before)
 
 
@@ -189,20 +204,19 @@ def rank_program(g, core, T, topo):
     ops = []
     where = [-1, False]
 
-    def op(e, fn, rd, wr, hold, lat=0.0, sem=None, inc=1, remote=False):
+    def op(e, fn, rd, wr, hold, lat=(0.0, 0.0), sem=None, inc=1, remote=False):
         ops.append(dict(round=where[0], tail=where[1], e=e, fn=fn, rd=list(rd), wr=list(wr), hold=hold, lat=lat,
                         sem=sem or SEM[e], inc=inc, remote=remote))
 
     def cost(n, k):
-        if k == "g":
-            return 0.055 + n * GAT * CY
-        if k == "s":
-            return 0.05 + n * SCA * CY
-        return FIX + max(64, n * {"": 1, "h": 0.5, "2": 2}[k]) * CY
+        if k in ("g", "s"):
+            return [0.055 + n * m["gat" if k == "g" else "sca"] * m["cy"] for m in PACE]
+        return [0.01 + max(64, n * {"": 1, "h": 0.5, "2": 2}[k]) * m["cy"] for m in PACE]
 
     def dma(e, sem, out, in_, rd, wr, nbytes):
-        flow = nbytes / BW + 0.15
-        op(e, lambda: Q[e].dma_start(out, in_), rd, wr, flow if e == "Y" else 0.05, T_DMA + (0 if e == "Y" else flow), sem, 16)
+        flow = [nbytes / m["bw"] + 0.15 for m in PACE]
+        op(e, lambda: Q[e].dma_start(out, in_), rd, wr, flow if e == "Y" else [0.05] * 2,
+           [m["dma"] + (0 if e == "Y" else f) for m, f in zip(PACE, flow)], sem, 16)
 
     def cp(out, in_, rd, wr, n=8, k=""):
         op("V", lambda: V.tensor_copy(out, in_), rd, wr, cost(n, k))
@@ -243,20 +257,23 @@ def rank_program(g, core, T, topo):
             rd, wr = rd + ["~" + bank], wr[1:] + group[bank][-1:]
         elif not st:
             rd = rd + group.pop(bank, [])
-        op("P", fn, rd, wr, sum(max(min(64, m), it[4]) * PEC * (4 if it[5] else 1) for it in items))
+        cycles = sum(max(min(64, m), it[4]) * (4 if it[5] else 1) for it in items)
+        op("P", fn, rd, wr, [cycles * x["cy"] / 2 for x in PACE])
 
     def mms(bank, *parts):
         for j, items in enumerate(parts):
             mm(items, j == 0, j == len(parts) - 1, [bank])
 
     def tr(outs, in_, rd, bank):
-        op("P", lambda: [P.transpose(o, in_, T.Ib[:]) for o in outs][-1], rd + ["Ib"], [bank], 128 * PEC * len(outs))
+        op("P", lambda: [P.transpose(o, in_, T.Ib[:]) for o in outs][-1], rd + ["Ib"], [bank],
+           [64 * m["cy"] * len(outs) for m in PACE])
 
     def iota(out, pat, base, cm, wr, n, fl=False):
+        t = [0.13 + 2 * n * m["cy"] for m in PACE]
         if fl:
-            op("G", lambda: g.iota(out, pat, base, cm, allow_small_or_imprecise_dtypes=True), [], wr + ["~G"], 0.13 + 2 * n * CY)
+            op("G", lambda: g.iota(out, pat, base, cm, allow_small_or_imprecise_dtypes=True), [], wr + ["~G"], t)
         else:
-            op("G", lambda: g.iota(out, pat, base, cm), [], wr + ["~G"], 0.13 + 2 * n * CY)
+            op("G", lambda: g.iota(out, pat, base, cm), [], wr + ["~G"], t)
 
     dma("Y", "ldZ", T.zb[:], T.z[:], [], ["zb", "~Y"], 2 ** 12)
     dma("S", "ldM", T.msi[:], T.ms[:], [], ["msi", "~S"], 2 ** 18)
@@ -340,7 +357,7 @@ def rank_program(g, core, T, topo):
     ts(h0, pm, 8.0, None, ALU.is_lt, None, ["pm"], ["h0"])
     ts(T.EXD[:, 0:1], p8, 8.0, pg, ALU.mult, ALU.add, ["pm"], ["EXD"])
     G8 = T.BD[:, 0:128:16]
-    for name, sc in (("If", 1.0), ("nIf", -1.0), ("Inh", -0.5), ("I8k", 8192.0), ("In1k", -1024.0),
+    for name, sc in (("If", 1.0), ("nIf", -1.0), ("I8k", 8192.0), ("In1k", -1024.0),
                      ("nIb", -1.0)):
         act(T[name][:], T.Ib[:], ["Ib"], [name], 128, scale=sc)
     for half in range(2):
@@ -408,7 +425,7 @@ def rank_program(g, core, T, topo):
         op("G", lambda: g.remote_dma_fused(
             [RemoteDMATransfer(dst_ids=[d], dma_engine_mask=m, remote_sem=T.sem[sem], src=src_of(h),
                                dst=dst_of((h + 1) % N)) for d, m, h in trs], local_sem=T.sem.sent),
-           rd, wr + ["~R"], 0.5 + first, lat, sem, used, True)
+           rd, wr + ["~R"], [0.5 + first] * 2, [lat + m["rem"] for m in PACE], sem, used, True)
 
     def tags(t, s0, n):
         return ["%s%d" % (t, b) for b in range(s0 // 8, (s0 + n) // 8)]
@@ -496,34 +513,31 @@ def rank_program(g, core, T, topo):
         mk = T.mmin[:, 15:128:16]
         mkhi = T.LM2[:, 8:192:24]
         ts(mkhi, mk, MAGIC4, MAGIC4, ALU.add, ALU.subtract, ["mmin", "LM2"], ["mkhi"])
-        act(T.LM2[:, 20:192:24], mkhi, ["mkhi"], ["mkhj"])
+        ts(T.LM2[:, 20:192:24], mk, MAGIC4, MAGIC4, ALU.add, ALU.subtract, ["mmin", "LM2"], ["mkhj"])
         tt(T.LM2[:, 9:192:24], T.LMs[:, 0:16:2], T.LMs[:, 1:16:2], ALU.min, ["LMs", "LM2"], ["thra"])
         ts(T.LM2[:, 21:192:24], T.LM2[:, 9:192:24], BIG, 0.0, ALU.add, ALU.min, ["thra"], ["thrb"])
         tt(T.ce[:], mk, mkhi, ALU.subtract, ["mmin", "mkhi"], ["ce"])
         mms("PB", to_list("PB", T.ce[:], ["ce"]))
         act(T.LE[:], T.PB[:, 0:64], ["PB"], ["LE"], 64)
         cp(T.eu[:], T.LE[:].indirect(T.EXD[:, 0:1]), ["LE", "EXD"], ["eu"], 16, "g")
-        act(T.y2[:], T.xm[:].indirect(T.eu[:, 0:8]), XM + ["eu"], ["y2"], 128, "g")
-        mms("PB", [(T.PB[:, 0:128], T.Inh[:], z1, ["Inh"] + nz, 128, False),
-                   (T.PB[:, 0:128], T.Ib[:], T.y2[:], ["Ib", "y2"], 128, False)])
-        act(T.ya[:], T.PB[:, 0:128], ["PB"], ["ya"], 128, func=ACT.Abs, scale=2.0, bias=ZO)
-        mms("PB", [(T.PB[:, 0:128], T.Inh[:], z1, ["Inh"] + nz, 128, False),
-                   (T.PB[:, 0:128], T.Ib[:], T.ya[:], ["Ib", "ya"], 128, False)])
-        act(T.yw[:, YC:YA:2], T.PB[:, 0:128], ["PB"], ["yc"], 128, bias=ZO / 2 + 0.25)
-        act(T.yw[:, YA:YW:8], T.PB[:, 0:128], ["PB"], ["ya2"], 128, bias=ZO / 2 + 0.25)
+        act(T.zb[:], z1, nz, ["zb"], 128, scale=0.5, bias=-ZO / 2)
+        act(T.zq[:], z1, nz, ["zq"], 128, scale=0.5, bias=-ZO / 2 - 0.25)
+        tt(T.y2[:], T.xm[:].indirect(T.eu[:, 0:8]), T.zb[:], ALU.subtract, XM + ["eu", "zb"], ["y2"], 128, "g")
+        act(T.ya[:], T.y2[:], ["y2"], ["ya"], 128, func=ACT.Abs, scale=2.0)
+        tt(T.yw[:, YC:YA:2], T.ya[:], T.zq[:], ALU.subtract, ["ya", "zq"], ["yc"], 128, "")
+        tt(T.yw[:, YA:YW:8], T.ya[:], T.zq[:], ALU.subtract, ["ya", "zq"], ["ya2"], 128, "")
         fresh = [(T.Uw[:], z1, ["Uw"] + nz, False), (T.Ib[:], T.K37[:], ["Ib", "K37"], False), (T.Ib[:], T.kc[:], ["Ib", "kc"], False)]
         mms("PA", [(T.PA[:, 0:128], l, x, rd, 128, f) for l, x, rd, f in fresh])
         act(T.yy[:], T.PA[:, 0:128], ["PA"], ["yy"], 128, bias=MAGIC4)
         act(T.ny[:], T.yy[:], ["yy"], ["ny"], 128, bias=MAGIC4, scale=-1.0)
         mms("PA", [(T.PA[:, 0:128], T.Ib[:], T.kc[:], ["Ib", "kc"], 128, False),
-                   (T.PA[:, 0:128], T.nIb[:], M1, ["nIb"] + nz, 128, False),
-                   (T.PA[:, 256:384], T.Inh[:], z1, ["Inh"] + nz, 128, False)] +
+                   (T.PA[:, 0:128], T.nIb[:], M1, ["nIb"] + nz, 128, False)] +
             [(T.PA[:, 128:256], l, x, rd, 128, f) for l, x, rd, f in fresh] +
             [(T.PA[:, 128:256], T.nIb[:], M1, ["nIb"] + nz, 128, False)],
             [(T.PA[:, 128:256], T.Ib[:], T.ny[:], ["Ib", "ny"], 128, False)])
         act(T.DD[:, 0:128], T.PA[:, 0:128], ["PA"], ["DDa"], 128)
         act(T.DD[:, 256:384], T.PA[:, 128:256], ["PA"], ["DDc"], 128, bias=-0.5)
-        act(T.zz[:], T.PA[:, 256:384], ["PA"], ["zz"], 128, scale=-1.0, bias=ZO / 2 - 0.25)
+        act(T.zz[:], z1, nz, ["zz"], 128, scale=0.5, bias=ZO / 2 - 0.25)
         tt(T.mA[:], T.LMs[:].indirect(T.EXS[:]), LMk, ALU.is_le, ["LMs", "EXS"] + nLM, ["mA"], 128, "g")
         act(T.bits[:, 0:128], T.BT[:].indirect(T.cu16[:]), ["BTa", "BTb", "cu16"], ["bits"], 128, "g")
         act(T.bits[:, 128:256], T.bits[:, 0:128], ["bits", "pm"], ["bits2"], 128, scale=podd)
@@ -552,8 +566,8 @@ def rank_program(g, core, T, topo):
         tt(T.cb[:], T.LX[:, 8:192:12], T.LQ[:, 9:192:12], ALU.is_equal, ["LX", "LQ"], ["cb"], 16)
         code = T.PM[:, 25, 0:8]
         mms("PM", [(code, T.L1[:], T.BDb[:, 0:128:16], ["L1", "BDb"], 8, False)])
-        cp(T.selu[:], code, ["PM"], ["selu"])
-        ts(T.szu[:], code, 0.125, -7.0 / 16, ALU.mult, ALU.add, ["PM", "selu"], ["szu", "~szu"])
+        cp(T.selu[:], code, ["PM"], ["selu", "~selu"])
+        ts(T.szu[:], code, 0.125, -7.0 / 16, ALU.mult, ALU.add, ["PM", "~selu"], ["szu", "~szu"])
         mms("PA", [(T.PA[:, 0:128], T.mK[:], T.Ib[:], ["mK", "Ib"], 128, False)])
         tt(T.DD[:, 128:256], T.PA[:, 0:128], T.DD[:, 0:128], ALU.mult, ["PA", "DDa"], ["DDb"], 128, "")
         act(T.Wm[:, 0:256:2], T.DD[:, 128:256], ["DDb", "h0"], ["Wma"], 128, scale=h0)

@@ -4,11 +4,11 @@ from concourse.mybir import AluOpType as ALU, ActivationFunctionType as ACT
 RO = 3
 BIG = float(2 ** 26)
 HUGE = float(2 ** 30)
+VAST = float(2 ** 60)
 MAGIC4 = float(3 * 2 ** 34)
 MAGIC32 = float(3 * 2 ** 27)
+MAGIC512 = float(3 * 2 ** 31)
 ZO = 1536.0
-BO = 1280.0
-OFF = 2047.5
 YC, YA, YW = 2048, 2304, 3328
 
 F, B, I, U, H = "float32", "bfloat16", "int32", "uint16", "float16"
@@ -20,41 +20,49 @@ def _sb(dtype, **kw):
         SCRATCH[name] = ("sbuf", [128] + list(shape), dtype)
 
 
-_sb(B, X=[4096], yw=[YW], xm=[2048], mnm=[2048], mnx=[2048], UL=[2048], DM=[2048], CH=[8, 128], E=[1024], BT=[512],
-    zb=[128], zT=[256], Ib=[128], I8k=[128], In1k=[128], Uw=[128], ones=[128],
-    e8=[128], two=[128], TRI=[128], C30=[128], WX=[4, 32], WM=[4, 48], BDb=[128], nIb=[128], y2=[128], ya=[128], ny=[128],
-    mA=[128], mK=[128], nA=[128], cb=[16], val=[16], S32=[96], bits=[256], nzb=[128])
-_sb(F, Kw=[640], If=[128], nIf=[128], BD=[128], CX=[16, 12], DX=[192], LX=[192], LM2=[192], LQ=[192], CM=[24, 9],
-    D16=[128], DA=[128], D2s=[16], DV=[48], CC=[16], D512=[16], pm=[8], SL=[8], zz=[128], yy=[128],
-    DD=[384], Wm=[416], LMk=[128], LMs=[24], LXk=[128], mmin=[128], amax=[128], LE=[64],
-    LV=[64], old=[128], D2=[128], tq=[48], lo=[16], Mn=[128])
-_sb(H, lz0=[128, 4], lz1=[128, 4], lz2=[128, 4], sz0=[128, 4], sz1=[128, 4], sz2=[128, 4], sc0=[64], sc1=[64], sc2=[64],
-    lc0=[64], lc1=[64], ce=[8], zq=[128], L1=[128], CG=[16], CMh=[216], kc=[128], K37=[128], oM=[128])
-_sb(I, kti=[512], msi=[128], tmpi=[256], tmpj=[256], BI=[256], ksi=[8], KS=[8], ci=[16], cj=[8], c8=[8], ui=[8],
+_sb(B, X=[4096], yw=[YW], xm=[2048], mnm=[2048], mnx=[2048], UL=[1024], DM=[2048], CH=[8, 128], E=[1024], BT=[512],
+    zb=[128], zT=[256], Ib=[128], In1k=[128], Uw=[128], ones=[128],
+    e8=[128], TRI=[256], C30=[128], WX=[4, 32], WM=[4, 64], BDb=[128], nIb=[128], ya=[128], qq=[128],
+    I2=[128], In4k=[128], TC=[24], CY=[48],
+    mA=[128], mK=[128], nA=[128], cb=[16], val=[16], SU=[64], BD3=[24], oS=[128], yS=[128], bits=[256], nzb=[128])
+_sb(F, Kw=[640], If=[128], BD=[128], DX=[192], LQ=[192], CM=[8, 4, 9],
+    D16=[128], DA=[128], D2s=[16], DV=[128], DC=[64], tc=[64], CE=[2, 32], LM2=[192],
+    LX=[192], LMs=[32], YL=[8],
+    D512=[16], pm=[16], SL=[8], zz=[128], yy=[128],
+    DD=[384], Wm=[416], LMk=[128], LXk=[128], mmin=[128], amax=[128], LE=[64],
+    LV=[64], old=[128], D2=[128], tq=[64], Mn=[128])
+_sb(H, lz0=[128, 4], lz1=[128, 4], lz2=[128, 4], sz0=[128, 4], sz1=[128, 4], sz2=[128, 4], sc=[64], lc=[64],
+    CX=[16, 12], hq=[8], c8=[8], y2=[128], ce=[8], zq=[128], L1=[128], CG=[16], CMh=[288], kc=[128], K37=[128], oM=[128])
+_sb(I, kti=[512], msi=[128], tmpi=[256], tmpj=[256], BI=[256], ksi=[8], KS=[8], cj=[8], pint=[8], ui=[8],
     xa=[128], xb=[128])
-_sb(U, Mu=[128], kcu=[128], cu16=[8], EX=[8], EXS=[8], EXA=[8], EXD=[2], selu=[8], szu=[8], eu=[16], vu=[8], ou=[16])
+_sb(U, Mu=[128], Mo=[32], kcu=[128], cu16=[8], EX=[8], EXS=[8], EXA=[8], EXD=[2], selu=[8], szu=[8], eu=[16], vu=[8], ou=[16])
 BANKS = ("ZA", "ZB", "PX", "PM", "EA", "EB", "PA", "PB")
 for _n in BANKS:
     SCRATCH[_n] = ("psum", [128, 64, 16], B) if _n[0] == "Z" else \
-        ("psum", [128, 32, 16], F) if _n in ("PX", "PM") else ("psum", [128, 512], F)
+        ("psum", {"PX": [128, 32, 16], "PM": [128, 8, 4, 16]}.get(_n, [128, 512]), F)
 
-SEMAPHORES = ["cV", "cS", "cP", "cG", "ldX", "ldX2", "ldK", "ldM", "ldZ", "ldC", "stX", "stX2", "stK", "stM", "stZ",
-              "arC0", "arC1", "arA0", "arA1", "arB0", "arB1", "arD0", "arD1", "sent", "cpD", "cpU"]
+SEMAPHORES = ["cV", "cS", "cP", "cG", "ldX", "ldX2", "ldK", "ldM", "ldZ", "ldC", "stX0", "stX1", "stX2", "stK", "stM", "stZ",
+              "arC", "arA0", "arA1", "arB0", "arB1", "arD0", "arD1", "sent", "cpD", "cpU"]
 
 CH_M = [(0, 64), (64, 64)]
-CH_X = [(0, 64), (64, 32), (96, 32)]
-_LATER = [("S", 0, 48), ("V", 48, 32), ("S", 80, 48)]
+CH_X = [(0, 32), (32, 32), (64, 32), (96, 16), (112, 16)]
+_LATER = [("S", 0, 48), ("V", 48, 32), ("S", 80, 32), ("V", 112, 16)]
 G_M = [[("V", 0, 32), ("S", 32, 32), ("S", 64, 32), ("V", 96, 32)], _LATER, _LATER]
-G_X = [[("S", 0, 32), ("V", 32, 32), ("S", 64, 32), ("S", 96, 16), ("V", 112, 16)]] * RO
+G_X = [[("S", 0, 32), ("V", 32, 32), ("S", 64, 32), ("S", 96, 16), ("S", 112, 16)]] * RO
 MM_M, MM_X = [(0, 128)], [(0, 96), (96, 32)]
 CALLS = {"A": ((7, 4), (1, 4), (2, 4), (3, 4)), "B": ((4, 8), (5, 8)), "D": ((6, 16),)}
 CALL_C = ((1, 2), (2, 2), (3, 2), (4, 2), (5, 2), (6, 2), (7, 4))
+PIECES = ((0, 32), (32, 32), (64, 64))
+STORES = ("stZ", "stM", "stX0", "stX1", "stX2", "stK")
 FIRST = 80
 PACE = [dict(cy=0.87e-3, gat=1.56, sca=3.8, wake=0.18, wakeP=0.25, dma=1.5, bw=400e3, rem=1.0),
-        dict(cy=1.12e-3, gat=1.75, sca=4.5, wake=0.20, wakeP=0.26, dma=1.8, bw=280e3, rem=1.8)]
-SLOW = 0.6
+        dict(cy=1.12e-3, gat=2.05, sca=5.0, wake=0.20, wakeP=0.26, dma=1.8, bw=280e3, rem=1.5),
+        dict(cy=0.85e-3, gat=1.1, sca=2.2, wake=0.17, wakeP=0.24, dma=1.4, bw=420e3, rem=0.9)]
+WEIGHT = (1.0, 0.7, 1.0)
+NP = len(PACE)
 T_CALL, T_C, T_FIRST = {"A": 0.0, "B": 0.25, "D": 0.15}, 2.5, 1.5
-SEED, TRIES, HEAT = 2, 12000, 0.2
+SEED, TRIES, PASSES, HEAT, SHAKE = 1, 150000, 10, 0.9, 1.2
+ON_S = {"MuA", "MuB", "cu2", "oM", "bits", "szc", "zT", "LX", "eu", "xb", "kc", "szu"}
 PLANS = {}
 
 
@@ -163,7 +171,7 @@ def plan(ops):
     for i, o in enumerate(ops):
         if o["round"] >= 0:
             w = (o["wr"] + [""])[0]
-            s = [o["e"], w[:2] + w[3:] if w[:2] in ("sz", "lz", "sc", "lc") else w, 0]
+            s = [o["e"], w[:2] + w[3:] if w[:2] in ("sz", "lz") else w, 0]
             while tuple(s) in twin[o["round"]]:
                 s[2] += 1
             twin[o["round"]][tuple(s)] = i
@@ -193,6 +201,181 @@ def plan(ops):
     return ranked(out, before)
 
 
+def plan(ops):
+    n = len(ops)
+    pred, succ = [set() for _ in ops], [set() for _ in ops]
+    soft, reads = set(), set()
+    writer, readers = {}, {}
+    for i, o in enumerate(ops):
+        for r in o["rd"] + o["wr"]:
+            if r in writer:
+                pred[i].add(writer[r])
+                if r[0] == "~":
+                    soft.add((writer[r], i))
+                elif r in o["rd"]:
+                    reads.add((writer[r], i))
+        for w in o["wr"]:
+            pred[i].update(readers.get(w, []))
+        for r in o["rd"]:
+            readers.setdefault(r, []).append(i)
+        for w in o["wr"]:
+            writer[w] = i
+            readers[w] = []
+        pred[i].discard(i)
+        for p in pred[i]:
+            succ[p].add(i)
+    eng = ["VSPGYD".index(o["e"]) for o in ops]
+    hold, lat = ([[o[k][m] for o in ops] for m in range(NP)] for k in ("hold", "lat"))
+
+    def gap(p, i, m):
+        if ((p, i) in soft and (p, i) not in reads) or (eng[p] == eng[i] == 2 and (p, i) not in reads):
+            return 0.0
+        return lat[m][p] + PACE[m]["wakeP" if eng[p] == 2 else "wake"]
+    before = [[[(p, hold[m][p] + gap(p, i, m)) for p in sorted(pred[i])] for i in range(n)] for m in range(NP)]
+    last = [i for i in range(n) if not succ[i]]
+
+    def run(order, m, k=0, known=None):
+        start, free, h, b = list(known) if k else [0.0] * n, [0.0] * 6, hold[m], before[m]
+        for i in order[:k]:
+            free[eng[i]] = i + 1
+        free = [start[i - 1] + h[i - 1] if i else 0.0 for i in free]
+        for i in order[k:]:
+            e = eng[i]
+            t = free[e]
+            for p, d in b[i]:
+                if start[p] + d > t:
+                    t = start[p] + d
+            start[i] = t
+            free[e] = t + h[i]
+        return max(start[i] + h[i] + lat[m][i] for i in last), start
+
+    def guess(order, m, k, known):
+        start, free, h, b = list(known), [0] * 6, hold[m], before[m]
+        for i in order[max(0, k - 120):k]:
+            free[eng[i]] = i + 1
+        free = [start[i - 1] + h[i - 1] if i else 0.0 for i in free]
+        same, shift = 0, 0.0
+        for i in order[k:]:
+            e = eng[i]
+            t = free[e]
+            for p, d in b[i]:
+                if start[p] + d > t:
+                    t = start[p] + d
+            if -1e-9 < t - start[i] - shift < 1e-9:
+                same += 1
+                if same > 40:
+                    return shift
+            else:
+                same, shift = 0, t - start[i]
+            start[i] = t
+            free[e] = t + h[i]
+        return max(start[i] + h[i] + lat[m][i] for i in last) - max(known[i] + h[i] + lat[m][i] for i in last)
+
+    seed = [SEED]
+
+    def rnd():
+        seed[0] = (seed[0] * 1103515245 + 12345) % 2 ** 31
+        return seed[0] / 2 ** 31
+
+    def chain(order, m, start):
+        prev, top = [None] * n, [None] * 6
+        for i in order:
+            prev[i], top[eng[i]] = top[eng[i]], i
+        i = max(last, key=lambda j: start[j] + hold[m][j] + lat[m][j])
+        pairs = []
+        while start[i] > 1e-9:
+            c, q = [p for p, d in before[m][i] if start[p] + d > start[i] - 1e-9], prev[i]
+            if c and (q is None or start[q] + hold[m][q] < start[i] - 1e-9 or rnd() < 0.3):
+                i = c[int(rnd() * len(c))]
+            else:
+                pairs.append((q, i))
+                i = q
+        return pairs, prev
+
+    def move(order, at, a, b, up):
+        seg = order[at[a]:at[b] + 1]
+        s, link = ({b}, succ) if up else ({a}, pred)
+        for x in (seg[::-1] if up else seg):
+            if link[x] & s:
+                s.add(x)
+        if a in s and b in s:
+            return None
+        return order[:at[a]] + [x for x in seg if (x in s) == up] + [x for x in seg if (x in s) != up] + order[at[b] + 1:]
+
+    tail = [0.0] * n
+    for i in range(n - 1, -1, -1):
+        tail[i] = hold[0][i] + max([tail[s] + gap(i, s, 0) for s in succ[i]] + [lat[0][i]])
+    order, ready, free = [], [0.0] * n, [0.0] * 6
+    left, todo = [len(p) for p in pred], {i for i in range(n) if not pred[i]}
+    while todo:
+        first = min(max(ready[i], free[eng[i]]) for i in todo)
+        i = max(sorted(j for j in todo if max(ready[j], free[eng[j]]) <= first + 0.1), key=lambda j: tail[j])
+        todo.remove(i)
+        order.append(i)
+        free[eng[i]] = max(ready[i], free[eng[i]]) + hold[0][i]
+        for s in succ[i]:
+            ready[s] = max(ready[s], free[eng[i]] + gap(i, s, 0))
+            left[s] -= 1
+            if not left[s]:
+                todo.add(s)
+    best, out = sum(w * run(order, m)[0] for m, w in enumerate(WEIGHT)), order
+    name, twin = [], {}
+    for i, o in enumerate(ops):
+        w = (o["wr"] + [""])[0]
+        s = [o["round"], o["e"], w[:2] + w[3:] if w[:2] in ("sz", "lz") else w, 0]
+        while tuple(s) in twin:
+            s[3] += 1
+        name.append(tuple(s))
+        twin[tuple(s)] = i
+    marks = [i for i, o in enumerate(ops) if o["wr"][:1] == ["LQ"]]
+    for tries, part in [(TRIES // 4, None)] + [(3 * TRIES // (16 * PASSES), x) for _ in range(PASSES) for x in range(RO + 1)]:
+        order, it = list(out), 0
+        if part is not None and rnd() < 0.7:
+            start = run(out, 0)[1]
+            key, cut = list(start), [4.0] + [start[i] for i in marks] + [1e9]
+            if part in (1, 2) and rnd() < 0.5:
+                d = 2 * part - 3
+                for i, s in enumerate(name):
+                    j = twin.get((s[0] - d,) + s[1:])
+                    if j is not None and cut[part - d] <= start[j] < cut[part - d + 1]:
+                        key[i] = start[j] + cut[part + 1] - cut[part - d + 1]
+            else:
+                key = [x + SHAKE * rnd() * (cut[part] <= x < cut[part + 1]) for x in key]
+            for i in range(n):
+                key[i] = max([key[i]] + [key[p] + 1e-6 for p in pred[i]])
+            order.sort(key=lambda j: key[j])
+        while it < tries:
+            m = int(rnd() * NP)
+            both = [run(order, x)[1] for x in range(NP)]
+            start = both[m]
+            order.sort(key=lambda j: start[j])
+            at = {x: k for k, x in enumerate(order)}
+            pairs, prev = chain(order, m, start)
+            if part is not None:
+                cut = [0.0] + [start[i] for i in marks] + [1e9]
+                pairs = [x for x in pairs if cut[part] <= start[x[1]] < cut[part + 1]] or pairs
+            nxt = {q: i for i, q in enumerate(prev) if q is not None}
+            for _ in range(30):
+                it += 1
+                a, b = pairs[int(rnd() * len(pairs))]
+                up, k = rnd() < 0.5, int(rnd() ** 2 * 8)
+                while k and up and prev[a] is not None:
+                    a, k = prev[a], k - 1
+                while k and not up and b in nxt:
+                    b, k = nxt[b], k - 1
+                new = move(order, at, a, b, up)
+                if new is not None:
+                    v = sum(w * guess(new, x, at[a], both[x]) for x, w in enumerate(WEIGHT))
+                    if v <= HEAT * (1 - it / tries) * rnd() ** 3:
+                        order, v = new, sum(w * run(new, x, at[a], both[x])[0] for x, w in enumerate(WEIGHT))
+                        if v < best:
+                            best, out = v, list(new)
+                        break
+    PLANS["t"] = [run(out, m)[0] for m in range(NP)]
+    PLANS["start"] = run(out, 0)[1]
+    return out
+
+
 def rank_program(g, core, T, topo):
     rank = T.rank_of(core)
     if rank is None:
@@ -204,7 +387,7 @@ def rank_program(g, core, T, topo):
     ops = []
     where = [-1, False]
 
-    def op(e, fn, rd, wr, hold, lat=(0.0, 0.0), sem=None, inc=1, remote=False):
+    def op(e, fn, rd, wr, hold, lat=(0.0,) * NP, sem=None, inc=1, remote=False):
         ops.append(dict(round=where[0], tail=where[1], e=e, fn=fn, rd=list(rd), wr=list(wr), hold=hold, lat=lat,
                         sem=sem or SEM[e], inc=inc, remote=remote))
 
@@ -215,8 +398,14 @@ def rank_program(g, core, T, topo):
 
     def dma(e, sem, out, in_, rd, wr, nbytes):
         flow = [nbytes / m["bw"] + 0.15 for m in PACE]
-        op(e, lambda: Q[e].dma_start(out, in_), rd, wr, flow if e == "Y" else [0.05] * 2,
+        op(e, lambda: Q[e].dma_start(out, in_), rd, wr, flow if e == "Y" else [0.05] * NP,
            [m["dma"] + (0 if e == "Y" else f) for m, f in zip(PACE, flow)], sem, 16)
+
+    stores = {}
+
+    def store(e, sem, out, in_, rd, nbytes):
+        op(e, lambda: Q[e].dma_start(out, in_), rd, ["~" + sem], [0.05] * NP, sem=sem, inc=16)
+        stores[sem] = ("D", None, ["~" + sem], ["~D"], [nbytes / m["bw"] for m in PACE], [m["dma"] + 0.15 for m in PACE], sem)
 
     def cp(out, in_, rd, wr, n=8, k=""):
         op("V", lambda: V.tensor_copy(out, in_), rd, wr, cost(n, k))
@@ -238,6 +427,12 @@ def rank_program(g, core, T, topo):
 
     def act(out, in_, rd, wr, n=8, k="", func=ACT.Identity, bias=0.0, scale=1.0):
         op("S", lambda: S.activation(out, in_, func, bias=bias, scale=scale), rd, wr, cost(n, k))
+
+    def lin(name, out, in_, rd, wr, n=8, k="", scale=1.0, bias=0.0):
+        if name in ON_S:
+            act(out, in_, rd, wr, n, k if k == "g" else "", scale=scale, bias=bias)
+        else:
+            ts(out, in_, scale, bias, ALU.mult, ALU.add, rd, wr, n, k)
 
     group = {}
 
@@ -289,75 +484,80 @@ def rank_program(g, core, T, topo):
     iota(T.Wm[:, 0:128], [[0, 8], [1, 16]], 0, 0, ["Wma"], 128, True)
     iota(T.tmpj[:, 192:224:2], [[128, 2], [0, 8]], 0, 1, ["CIa"], 16)
     iota(T.tmpj[:, 193:224:2], [[-128, 2], [0, 8]], 255, -1, ["CIb"], 16)
-    iota(T.CM[:, 16:24, :], [[0, 72]], 256, 16, ["CMa"], 72, True)
-    iota(T.CM[:, 0:16, 0:8], [[0, 8], [8, 2], [1, 8]], 0, 16, ["CMb"], 128, True)
+    iota(T.CM[:, :, 2, :], [[0, 72]], 256, 16, ["CMa"], 72, True)
+    iota(T.CM[:, :, 0:2, 0:8], [[0, 8], [8, 2], [1, 8]], 0, 16, ["CMb"], 128, True)
     iota(T.CX[:, :, 0:8], [[0, 8], [8, 2], [1, 8]], 0, 16, ["CXa"], 128, True)
     iota(T.CX[:, :, 8], [[0, 16]], YC, 2, ["CXb"], 16, True)
-    iota(T.CX[:, 1:16:2, 10], [[0, 8]], 2 ** 24 - 4096 + YA, 8, ["CXc"], 8, True)
+    iota(T.CX[:, :, 9:12], [[0, 48]], 0, 0, ["CXz"], 48, True)
+    iota(T.CX[:, 1:16:2, 10], [[0, 8]], YA - 4096, 8, ["CXz"], 8, True)
     iota(T.C30[:], [[0, 8], [-2, 16]], 30, 0, ["C30"], 128, True)
     iota(T.Kw[:, 512:640], [[0, 128]], 0, 0, ["Kwd"], 128, True)
     iota(T.Wm[:, 256:288], [[0, 32]], 0, 0, ["Wmz"], 32, True)
     iota(T.DX[:], [[0, 192]], 1, 0, ["DX"], 192, True)
     iota(T.yw[:, YC:YW], [[0, YW - YC]], 0, 0, ["yc", "ya2"], YW - YC, True)
-    for j in range(2):
-        dma("Y", "cpU", T.UL[:, 1024 * j:1024 * j + 1024], T.yw[:, YA:YW], ["ya2", "kti", "X"], ["ULz%d" % j], 2 ** 18)
+    dma("Y", "cpU", T.UL[:], T.yw[:, YA:YW], ["ya2", "kti", "X"], ["ULz"], 2 ** 18)
     ms(T.ones[:], 1.0, ["ones"], 128, "h")
 
     def fill(out, val, wr, n=8, rd=()):
         act(out, T.ones[:, 0:n], ["ones"] + list(rd), wr, n, scale=val)
+
+    def steps(buf, vals, step):
+        for j, x in enumerate(vals):
+            fill(T[buf][:, j:8 * step:step], x, ["%s%d" % (buf, j)])
+        return ["%s%d" % (buf, j) for j in range(len(vals))]
     for nm in ("sz0", "sz1"):
         cp(T[nm][:, :, 2], T.ones[:], ["ones"], [nm], 128, "h")
-    for nm in ("sc0", "sc1"):
-        cp(T[nm][:], T.ones[:, 0:64], ["ones"], [nm], 64, "h")
+    cp(T.sc[:], T.ones[:, 0:64], ["ones"], ["sc"], 64, "h")
     ms(T.D16[:], 0.0, ["D16"], 128)
     ms(T.D16[:, 0:128:16], HUGE, ["D16"])
     act(T.DA[:], T.D16[:], ["D16"], ["DA"], 128, scale=-1.0)
     fill(T.e8[:], -8 * BIG, ["e8"], 128)
-    fill(T.two[:], -2.0, ["two"], 128)
-    ms(T.LM2[:], 0.0, ["LM2"], 192)
     fill(T.DX[:, 8:192:12], -1.0, ["DXa"], 16, ["DX"])
     fill(T.DX[:, 9:192:12], -1.0, ["DXb"], 16, ["DX"])
     fill(T.DX[:, 10:192:24], -1.0, ["DXc"], 8, ["DX"])
     fill(T.DX[:, 23:192:24], -1.0, ["DXd"], 8, ["DX"])
     DXall = ["DX" + x for x in "abcd"]
     act(T.D2s[:], T.D16[:, 0:128:8], ["D16"], ["D2s"])
-    ms(T.CM[:, 0:16, 8], 0.0, ["CMc"])
-    act(T.CMh[:], T.CM[:], ["CMa", "CMb", "CMc"], ["CMh"], 216)
-    ms(T.CX[:, 0:16:2, 9], BIG / 2, ["CXd"])
-    ms(T.CX[:, 1:16:2, 9], -BIG / 2, ["CXe"])
-    fill(T.CX[:, 0:16:2, 10], -HUGE, ["CXf"])
-    fill(T.CX[:, 0:16:2, 11], HUGE, ["CXg"])
-    fill(T.CX[:, 1:16:2, 11], -HUGE, ["CXh"])
-    CXall = ["CX" + x for x in "abcdefgh"]
+    ms(T.CM[:, :, 0:2, 8], 0.0, ["CMc"])
+    ms(T.CM[:, :, 3, :], 0.0, ["CMd"], 72)
+    act(T.CMh[:], T.CM[:], ["CMa", "CMb", "CMc", "CMd"], ["CMh"], 288)
+    iota(T.LM2[:], [[0, 192]], 0, 0, ["LM2"], 192, True)
+    iota(T.DC[:], [[0, 64]], 0, 0, ["DC"], 64, True)
+    for j, x in ((0, VAST), (5, -255.5), (6, MAGIC512), (7, -MAGIC512)):
+        fill(T.DC[:, j:64:8], x, ["DC%d" % j], 8, ["DC"])
+    DCall = ["DC0", "DC5", "DC6", "DC7"]
+    iota(T.CE[:, 0, :], [[0, 16], [1, 2]], 0, 0, ["CEz", "CEy"], 32, True)
+    CYall = steps("CY", (BIG / 2, -HUGE, HUGE, -BIG / 2, 2.0 ** 24, -HUGE), 6)
+    CXall = ["CXa", "CXb", "CXz"]
     fill(T.CG[:, 0:16:2], 1025.0, ["CGa"])
     fill(T.CG[:, 1:16:2], 1024.0, ["CGb"])
-    fill(T.CC[:, 0:16:2], -256 * ZO, ["CCa"])
-    ms(T.S32[:], 0.0, ["S32"], 96, "h")
-    fill(T.S32[:, 0:96:6], -15.5, ["S32c"], 16, ["S32"])
-    fill(T.S32[:, 1:96:6], MAGIC32, ["S32e"], 16, ["S32"])
-    fill(T.S32[:, 2:96:6], -MAGIC32, ["S32f"], 16, ["S32"])
-    S32all = ["S32" + x for x in "abcdef"]
-    iota(T.DV[:], [[0, 48]], 1, 0, ["DV"], 48, True)
-    fill(T.DV[:, 0:48:6], 0.0, ["DVa"], 8, ["DV"])
-    fill(T.DV[:, 3:48:6], -1.0, ["DVb"], 8, ["DV"])
+    iota(T.DV[:], [[0, 128]], 0, 0, ["DV"], 128, True)
+    fill(T.DV[:, 0:128:8], VAST, ["DVa"], 16, ["DV"])
+    fill(T.DV[:, 5:128:8], -15.5, ["DVb"], 16, ["DV"])
+    fill(T.DV[:, 6:128:8], MAGIC32, ["DVc"], 16, ["DV"])
+    DVall = ["DV" + x for x in ("a", "b", "c", "d", "p0", "p1", "p2")]
     ms(T.WX[:, 0:2, :], 0.0, ["WX"])
-    ms(T.WM[:, 0:2, :], 0.0, ["WM"])
+    ms(T.WM[:, 0:2, :], 0.0, ["WM"], 128, "h")
     ts(T.Ib[:], T.tmpi[:, 0:128], 0.0, None, ALU.is_equal, None, ["tmpi"], ["Ib"], 128)
-    ts(T.TRI[:], T.tmpi[:, 0:128], 0.0, -16.0, ALU.is_ge, ALU.mult, ["tmpi"], ["TRI"], 128)
+    ts(T.TRI[:, 128:256], T.tmpi[:, 0:128], 0.0, -16.0, ALU.is_ge, ALU.mult, ["tmpi"], ["TRI"], 128)
+    act(T.TRI[:, 0:128], T.TRI[:, 128:256], ["TRI"], ["TRJ"], 128, bias=120.0)
     ts(T.tmpi[:, 128:256], T.tmpj[:, 0:128], 4, None, ALU.arith_shift_right, None, ["tmpj"], ["tmpi2"], 128)
-    ts(T.c8[:, 0:1], T.ui[:, 0:1], 15, None, ALU.bitwise_and, None, ["ui"], ["c8"])
-    ts(T.c8[:, 1:2], T.ui[:, 0:1], 4, None, ALU.arith_shift_right, None, ["ui"], ["c8b"])
-    ts(T.c8[:, 2:3], T.ui[:, 0:1], 4, 1, ALU.arith_shift_right, ALU.bitwise_and, ["ui"], ["c8c"])
-    ts(T.c8[:, 3:4], T.ui[:, 0:1], 7, None, ALU.bitwise_and, None, ["ui"], ["c8d"])
+    ts(T.pint[:, 0:1], T.ui[:, 0:1], 15, None, ALU.bitwise_and, None, ["ui"], ["pia"])
+    ts(T.pint[:, 1:2], T.ui[:, 0:1], 4, None, ALU.arith_shift_right, None, ["ui"], ["pib"])
+    ts(T.pint[:, 2:3], T.ui[:, 0:1], 4, 1, ALU.arith_shift_right, ALU.bitwise_and, ["ui"], ["pic"])
+    ts(T.pint[:, 3:4], T.ui[:, 0:1], 7, None, ALU.bitwise_and, None, ["ui"], ["pid"])
     ts(T.BD[:], T.tmpi[:, 128:256], 0.0, None, ALU.is_equal, None, ["tmpi2"], ["BD"], 128)
-    cp(T.pm[:, 0:4], T.c8[:, 0:4], ["c8", "c8b", "c8c", "c8d"], ["pm"])
-    pm, pg, podd, p8, pm2, h1, h0 = (T.pm[:, j:j + 1] for j in range(7))
+    cp(T.pm[:, 0:4], T.pint[:, 0:4], ["pia", "pib", "pic", "pid"], ["pm"])
+    pm, pg, podd, p8, pm2, h1, h0, p37, nhalf, u1, u0, p14 = (T.pm[:, j:j + 1] for j in range(12))
+    ts(u1, pm, 8.0, 2.0 ** 20, ALU.is_ge, ALU.mult, ["pm"], ["u1"])
+    ts(u0, pm, 8.0, 2.0 ** 20, ALU.is_lt, ALU.mult, ["pm"], ["u0"])
     ts(pm2, pm, 2.0, 1.0, ALU.mult, ALU.add, ["pm"], ["pm2"])
+    fill(nhalf, -0.5, ["nhalf"], 1)
     ts(h1, pm, 8.0, None, ALU.is_ge, None, ["pm"], ["h1"])
     ts(h0, pm, 8.0, None, ALU.is_lt, None, ["pm"], ["h0"])
     ts(T.EXD[:, 0:1], p8, 8.0, pg, ALU.mult, ALU.add, ["pm"], ["EXD"])
     G8 = T.BD[:, 0:128:16]
-    for name, sc in (("If", 1.0), ("nIf", -1.0), ("I8k", 8192.0), ("In1k", -1024.0),
+    for name, sc in (("If", 1.0), ("I2", 2.0), ("In1k", -1024.0), ("In4k", -4096.0),
                      ("nIb", -1.0)):
         act(T[name][:], T.Ib[:], ["Ib"], [name], 128, scale=sc)
     for half in range(2):
@@ -365,14 +565,14 @@ def rank_program(g, core, T, topo):
         act(T.WX[:, half, 2 * half:32:4], G8, ["BD", "WX"], ["WXa%d" % half], scale=8192.0)
         act(T.WX[:, half, 1:32:4], G8, ["BD", "WX"], ["WXb%d" % half], scale=2 * BIG * sg)
         act(T.WX[:, half, 3:32:4], G8, ["BD", "WX"], ["WXc%d" % half], scale=-2 * BIG * sg)
-        act(T.WM[:, half, 2 * half:32:4], G8, ["BD", "WM"], ["WMa%d" % half], scale=8192.0)
-        act(T.WM[:, half, 1:32:4], G8, ["BD", "WM"], ["WMb%d" % half], scale=2 * BIG * sg)
-        act(T.WM[:, half, 3:32:4], G8, ["BD", "WM"], ["WMc%d" % half], scale=-2 * BIG * sg)
-        act(T.WM[:, half, 33:48:2], G8, ["BD", "WM"], ["WMd%d" % half], scale=512.0)
+        act(T.WM[:, half, 2 * half:64:8], G8, ["BD", "WM"], ["WMa%d" % half], scale=8192.0)
+        act(T.WM[:, half, 1:64:8], G8, ["BD", "WM"], ["WMb%d" % half], scale=2 * BIG * sg)
+        act(T.WM[:, half, 3:64:8], G8, ["BD", "WM"], ["WMc%d" % half], scale=-2 * BIG * sg)
+        act(T.WM[:, half, 5:64:8], G8, ["BD", "WM"], ["WMd%d" % half], scale=512.0)
     WXall = ["WX%s%d" % (x, j) for x in "abc" for j in range(2)]
     WMall = ["WM%s%d" % (x, j) for x in "abcd" for j in range(2)]
     act(T.WX[:, 2:4, :], T.WX[:, 0:2, :], WXall, ["WXn"], 64, scale=-2.0)
-    act(T.WM[:, 2:4, :], T.WM[:, 0:2, :], WMall, ["WMn"], 96, scale=-2.0)
+    act(T.WM[:, 2:4, :], T.WM[:, 0:2, :], WMall, ["WMn"], 128, scale=-2.0)
     ts(T.DM[:, 0:128], T.Wm[:, 0:128], pm, None, ALU.is_equal, None, ["Wma", "pm"], ["DM0"], 128)
     for j in range(2):
         cp(T.DM[:, 128 << j:256 << j], T.DM[:, 0:128 << j], ["DM%d" % i for i in range(j + 1)], ["DM%d" % (j + 1)], 128 << j, "h")
@@ -382,31 +582,38 @@ def rank_program(g, core, T, topo):
     for gi in range(8):
         cp(T.CH[:, :, 16 * gi:16 * gi + 16], T.Ib[:], ["Ib"], ["CH%d" % gi], 128, "h")
     CHall = ["CH%d" % gi for gi in range(8)]
-    ts(T.pm[:, 7:8], pm, 37.0, 0.5, ALU.mult, ALU.add, ["pm"], ["p37"])
-    ts(T.K37[:], T.ones[:], T.pm[:, 7:8], None, ALU.mult, None, ["ones", "p37"], ["K37"], 128, "h")
+    ts(p37, pm, 37.0, 0.5, ALU.mult, ALU.add, ["pm"], ["p37"])
+    ts(T.K37[:], T.ones[:], p37, None, ALU.mult, None, ["ones", "p37"], ["K37"], 128, "h")
     ts(T.SL[:], T.tmpj[:, 160:168], 16.0, pm, ALU.mult, ALU.add, ["J16", "pm"], ["SL"])
     cp(T.EX[:], T.tmpj[:, 160:168], ["J16"], ["EX"])
-    ts(T.EXS[:], T.tmpj[:, 160:168], 16.0, None, ALU.add, None, ["J16"], ["EXS"])
+    ts(T.EXS[:], T.tmpj[:, 160:168], 4.0, 2.0, ALU.mult, ALU.add, ["J16"], ["EXS"])
     ts(T.EXA[:], T.tmpj[:, 160:168], 16.0, 15.0, ALU.mult, ALU.add, ["J16"], ["EXA"])
     act(T.Uw[:], T.BD[:], ["BD", "pm2"], ["Uw"], 128, scale=pm2)
     act(T.BDb[:], T.BD[:], ["BD"], ["BDb"], 128)
-    act(T.S32[:, 3:48:6], T.SL[:], ["SL", "S32"], ["S32a"], scale=32.0)
-    act(T.S32[:, 51:72:6], T.SL[:, 0:4], ["SL", "S32"], ["S32b"], scale=32.0)
-    act(T.S32[:, 75:96:6], T.SL[:, 0:4], ["SL", "S32"], ["S32d"], scale=32.0)
+    for j in range(3):
+        act(T.BD3[:, 8 * j:8 * j + 8], G8, ["BD"], ["BD%d" % j])
+    act(T.DV[:, 7:64:8], T.SL[:], ["SL", "DV"], ["DVd"], scale=-32.0, bias=-MAGIC32)
+    for j, (c0, w) in enumerate(PIECES):
+        act(T.DV[:, 71 + c0 // 2:64 + (c0 + w) // 2:8], T.SL[:, 0:w // 16], ["SL", "DV"], ["DVp%d" % j], scale=-32.0, bias=-MAGIC32)
+    fill(T.SU[:], VAST, ["SU"], 64)
+    act(T.SU[:, 0:64:8], T.ones[:, 0:8], ["SU", "u1"], ["SUa"], scale=u1)
+    act(T.SU[:, 4:64:8], T.ones[:, 0:8], ["SU", "u0"], ["SUb"], scale=u0)
     act(T.D512[:, 0:8], T.SL[:], ["SL"], ["D512a"], bias=512.0)
     act(T.D512[:, 8:16], T.SL[:], ["SL"], ["D512b"], bias=512.0)
-    c0 = -8193.0 * BO - 16384.0
-    act(T.CC[:, 3:16:2], T.SL[:, 0:7], ["SL"], ["CCb"], scale=-16386.0, bias=c0)
-    act(T.CC[:, 1:2], T.SL[:, 7:8], ["SL"], ["CCc"], scale=-16386.0, bias=c0)
-    for gi in range(8):
-        act(T.UL[:, 16 * gi:16 * gi + 129 * 15 + 1:129], T.Uw[:, 16 * gi:16 * gi + 16], ["Uw", "ULz0", "ULz1"], ["UL%d" % gi])
+    act(T.YL[:], T.SL[:], ["SL"], ["YL"], scale=2.0, bias=float(YC))
+    fill(T.TC[:, 0:8], 0.0, ["TCc"])
+    act(T.TC[:, 8:16], T.SL[:], ["SL"], ["TCa"], scale=-16.0, bias=-16.0)
+    act(T.TC[:, 16:24], T.SL[:], ["SL"], ["TCb"], scale=-16.0, bias=-8.0)
+    for j in range(8):
+        act(T.UL[:, 129 * j:128 * j + 128:8], T.Uw[:, j:128:8], ["Uw", "ULz"], ["UL%d" % j], 16)
     ULall = ["UL%d" % gi for gi in range(8)]
     for b in range(8):
         ts(T.BI[:, b:256:8], T.tmpj[:, 192:224], b, 1, ALU.arith_shift_right, ALU.bitwise_and, ["CIa", "CIb"], ["BI%d" % b], 32)
     cp(T.bits[:], T.BI[:], ["BI%d" % b for b in range(8)], ["bits", "bits2"], 256)
     mms("EA", [(T.EA[:, 128 * j:128 * j + 128], T.bits[:, 128 * j:128 * j + 128], T.Ib[:], ["bits", "bits2", "Ib"], 128, False)
                for j in range(2)])
-    act(T.BT[:, 0:256], T.EA[:, 0:256], ["EA"], ["BTa"], 256)
+    ts(p14, podd, 3.0, 1.0, ALU.mult, ALU.add, ["pm"], ["p14"])
+    act(T.BT[:, 0:256], T.EA[:, 0:256], ["EA", "p14"], ["BTa"], 256, scale=p14)
     cp(T.BT[:, 256:512], T.BT[:, 0:256], ["BTa"], ["BTb"], 256, "h")
     cp(T.Mu[:], T.msi[:], ["msi"], ["MuA", "MuB"], 128)
     ts(T.lz0[:, :, 0], T.msi[:], -2048.0, None, ALU.add, None, ["msi", "lz0"], ["lz0m"], 128)
@@ -425,7 +632,7 @@ def rank_program(g, core, T, topo):
         op("G", lambda: g.remote_dma_fused(
             [RemoteDMATransfer(dst_ids=[d], dma_engine_mask=m, remote_sem=T.sem[sem], src=src_of(h),
                                dst=dst_of((h + 1) % N)) for d, m, h in trs], local_sem=T.sem.sent),
-           rd, wr + ["~R"], [0.5 + first] * 2, [lat + m["rem"] for m in PACE], sem, used, True)
+           rd, wr + ["~R"], [0.5 + first] * NP, [lat + m["rem"] for m in PACE], sem, used, True)
 
     def tags(t, s0, n):
         return ["%s%d" % (t, b) for b in range(s0 // 8, (s0 + n) // 8)]
@@ -448,109 +655,119 @@ def rank_program(g, core, T, topo):
     def to_list(bank, val, rd):
         return [(T[bank][:, 8 * h:8 * h + 8], T.CH[:, h, :], val, CHall + rd, 8, False) for h in range(8)]
 
+    def mixed(z, rd, out, consts, nc, wr):
+        mms("PB", [(T.PB[:, 0:64], T.Ib[:], T.SU[:], ["Ib", "SUa", "SUb"], 64, False)],
+            [(T.PB[:, 0:64:4], T.UL[:, 128 * j:128 * j + 128], z(j), ULall + rd, 16, False) for j in range(8)])
+        scan(out, consts, T.PB[:, 0:64], ALU.add, ALU.min, ["PB"] + nc, wr, 64)
+
     XM, XX = tags("m", 0, 128), tags("x", 0, 128)
 
     for r in range(RO):
         last = r == RO - 1
         where[0], where[1] = r, False
-        lz, sz, sc = T["lz%d" % r], T["sz%d" % r], T["sc%d" % r]
+        lz, sz = T["lz%d" % r], T["sz%d" % r]
         nA = ["lz0m", "lz0a", "lz0b"] if r == 0 else ["lz%do" % r, "lz%dA" % r]
         nB = nA if r == 0 else ["lz%dB" % r, "lz%dD" % r]
         nz = nA + nB
         M1, z1 = lz[:, :, 0], lz[:, :, 1]
         if r:
-            ts(T.Mu[:, 0:FIRST], lz[:, 0:FIRST, 0], 2048.0, None, ALU.add, None, nA, ["MuA"], 64, "h")
-            ts(T.Mu[:, FIRST:128], lz[:, FIRST:128, 0], 2048.0, None, ALU.add, None, nB, ["MuB"], 64, "h")
+            lin("MuA", T.Mu[:, 0:FIRST], lz[:, 0:FIRST, 0], nA, ["MuA"], FIRST, "h", bias=2048.0)
+            lin("MuB", T.Mu[:, FIRST:128], lz[:, FIRST:128, 0], nB, ["MuB"], 64, "h", bias=2048.0)
         for e, s0, n in G_M[r]:
-            gather(e, "m", T.Mu, ["MuA"] * (s0 < FIRST) + ["MuB"] * (s0 + n > FIRST), s0, n)
+            if r and (s0, n) == (16, 16):
+                lin("MuO", T.Mo[:, 16:32], lz[:, 16:32, 0], nA[:1], ["MuO"], 16, bias=2048.0)
+                gather(e, "m", T.Mo, ["MuO"], s0, n)
+            else:
+                gather(e, "m", T.Mu, ["MuA"] * (s0 < FIRST) + ["MuB"] * (s0 + n > FIRST), s0, n)
         for j, (src, bank) in enumerate((("EA", "ZA"), ("EB", "ZB"))):
             mms(src, [(T[src][:, 0:128], lz[:, 64 * j:64 * j + 64, 1:4:2], T.Ib[:], (nA, nz)[j] + ["Ib"], 128, False)])
-            act(T.zT[:, 128 * j:128 * j + 128], T[src][:, 0:128], [src], ["zT%d" % j], 128, scale=0.5, bias=-ZO / 2)
+            lin("zT", T.zT[:, 128 * j:128 * j + 128], T[src][:, 0:128], [src], ["zT%d" % j], 128, scale=0.5, bias=-ZO / 2)
             tr([T[bank][:, :, k:k + 2] for k in range(0, 16, 2)], T.zT[:, 128 * j:128 * j + 128], ["zT%d" % j], bank)
-        if r:
-            lc, sp, beta = T["lc%d" % (r - 1)], T["sc%d" % (r - 1)], lz[:, 0:128:16, 2]
-            mms("PA", [(T.PA[:, 384:400], T.If[:], T.CC[:], ["If", "CCa", "CCb", "CCc"], 16, True),
-                       (T.PA[:, 385:386], T.Ib[:], lc[:, 0:1], ["Ib", "lc%d" % (r - 1)], 8, False),
-                       (T.PA[:, 387:388], T.Ib[:], sp[:, 0:1], ["Ib", "sc%d" % (r - 1)], 8, False),
-                       (T.PA[:, 389:400:2], T.Ib[:], lc[:, 16:64:8], ["Ib", "lc%d" % (r - 1)], 8, False)],
-                [(T.PA[:, 385:400:2], T.Ib[:], beta, ["Ib"] + nz, 8, False),
-                 (T.PA[:, 385:400:2], T.I8k[:], beta, ["I8k"] + nz, 8, False)] +
-                [(T.PA[:, 384:400:2], T.UL[:, 128 * il:128 * il + 128], lz[:, il:128:16, 1], ULall + nz, 8, False)
-                 for il in range(16)])
-            scan(T.ci[:], T.D2s[:], T.PA[:, 384:400], ALU.add, ALU.min, ["D2s", "PA"], ["ci"], 16)
-            ts(T.cj[:], T.ci[:, 1:16:2], 511, None, ALU.bitwise_and, None, ["ci"], ["cj"])
-        cp(T.cu16[:], T.cj[:], ["cj"], ["cu16"])
-        cp(T.kcu[:], (T.Kw if r else T.kti)[:].indirect(T.cu16[:]), ["Kw" if r else "kti", "cu16"], ["kcu"], 128, "g")
-        ts(T.kc[:], T.kcu[:], -2048.0, None, ALU.add, None, ["kcu"], ["kc"], 128, "h")
+        c, nc = (T.cj[:], ["cj"]) if r == 0 else (T.cu16[:], ["cu16"]) if r == 1 else (lz[:, 12:128:16, 2], nz)
+        if r == 1:
+            tt(T.cu16[:], lz[:, 12:128:16, 2], T.lc[:, 0:64:8], ALU.add, nz + ["lc", "lco"], ["cu16"])
+        else:
+            lin("cu%d" % r, T.cu16[:], c, nc, ["cu16"])
+        lin("kcu", T.kcu[:], (T.Kw if r else T.kti)[:].indirect(T.cu16[:]), ["Kw" if r else "kti", "cu16"], ["kcu"], 128, "g")
+        lin("kc", T.kc[:], T.kcu[:], ["kcu"], ["kc"], 128, "h", bias=-2048.0)
         for e, s0, n in G_X[r]:
             gather(e, "x", T.kcu, ["kcu"], s0, n)
-        ts(T.c8[:], T.cj[:], 255, None, ALU.bitwise_and, None, ["cj", "pm"], ["c8"])
-        c2m = sc[:, 0:64:8]
-        ts(c2m, T.c8[:], 2.0, None, ALU.mult, None, ["c8"], ["sc%d" % r])
-        if not last:
-            send(CALL_C, lambda h, a=sc: a[:, 8 * h:8 * h + 8], lambda s, a=T["lc%d" % r]: a[:, 8 * s:8 * s + 8], "arC%d" % r,
-                 ["sc%d" % r] + (["kti", "X", "Xb"] if r == 0 else []), ["lc%d" % r], T_C, T_FIRST if r == 0 else 0.0)
-        mm([(T.PM[:, 0:24, 0:9], T.Ib[:], T.CMh[:], ["Ib", "CMh"], 216, False)] +
-           [(T.PM[:, j:16:2, 8], T.e8[:], T.cb[:, b:16:2], ["e8", "cb"], 8, False) for j in range(2) for b in range(2) if r],
+        ts(T.hq[:], c, 256.0, -256.0, ALU.is_ge, ALU.mult, nc, ["hq"])
+        tt(T.c8[:], c, T.hq[:], ALU.add, nc + ["hq"], ["c8"])
+        if r == 0:
+            act(T.sc[:, 0:64:8], T.c8[:], ["c8", "sc"], ["sc"], scale=2.0)
+            act(T.lc[:, 8:9], T.c8[:, 0:1], ["c8"], ["lco"], 1, scale=2.0)
+            send(CALL_C, lambda h: T.sc[:, 8 * h:8 * h + 8], lambda s: T.lc[:, 8 * s:8 * s + 8], "arC",
+                 ["sc", "kti", "X", "Xb"], ["lc"], T_C, T_FIRST)
+        mm([(T.PM[:, :, :, 0:9], T.Ib[:], T.CMh[:], ["Ib", "CMh"], 288, False)] +
+           [(T.PM[:, :, j, 8], T.e8[:], T.cb[:, b:16:2], ["e8", "cb"], 8, False) for j in range(2) for b in range(2) if r],
            True, False, ["PM"])
         for s0, n in CH_M:
             mins("m", s0, n)
 
         def sums(bank, rows, col, chunks, tile, least, t, W, nW, nWn):
             def part(buf, wo, s0, n, ks, rd):
-                return [(T[bank][s0:s0 + n, 0:rows, k % 8:col + 1:col - k % 8], buf[:, 16 * s0 + k:16 * (s0 + n):16],
+                at = (slice(s0, s0 + n),) + ((slice(0, rows),) if t == "x" else (slice(0, 8), slice(0, 4)))
+                return [(T[bank][at + (slice(k % 8, col + 1, col - k % 8),)], buf[:, 16 * s0 + k:16 * (s0 + n):16],
                          W[:, wo + k // 8, :], rd, 2 * rows, False) for k in ks]
             for s0, n in chunks:
                 mm(part(tile, 0, s0, n, range(16), tags(t, s0, n) + nW), False, False, [bank, "~r%d" % s0], n)
                 if n < 128:
                     mm(part(least, 2, s0, n, range(15), tags("n" + t, s0, n) + nWn), False, False, [bank], n, ["~r%d" % s0])
             mm(part(least, 2, 0, 128, range(15 * (len(chunks) > 1), 16), tags("n" + t, 0, 128) + nWn), False, True, [bank])
-        sums("PM", 24, 8, MM_M, T.xm, T.mnm, "m", T.WM, WMall, ["WMn"])
+        sums("PM", 32, 8, MM_M, T.xm, T.mnm, "m", T.WM, WMall, ["WMn"])
         LMk, nLM = T.LMk[:], ["LMk"]
-        act(LMk, T.PM[:, 0:16, 0:8], ["PM"], nLM, 128)
-        act(T.LMs[:], T.PM[:, 0:24, 8], ["PM"], ["LMs"], 24)
+        act(LMk, T.PM[:, :, 0:2, 0:8], ["PM"], nLM, 128)
+        act(T.LMs[:], T.PM[:, :, :, 8], ["PM"], ["LMs"], 32)
         scan(T.mmin[:], T.D16[:], LMk, ALU.add, ALU.min, ["D16"] + nLM, ["mmin"], 128)
-        mk = T.mmin[:, 15:128:16]
-        mkhi = T.LM2[:, 8:192:24]
+        tt(T.LM2[:, 9:192:24], T.LMs[:, 0:32:4], T.LMs[:, 1:32:4], ALU.min, ["LMs", "LM2"], ["thra"])
+        ts(T.LM2[:, 21:192:24], T.LM2[:, 9:192:24], BIG, 0.0, ALU.add, ALU.min, ["thra"], ["thrb"])
+        mk, mkhi = T.mmin[:, 15:128:16], T.LM2[:, 8:192:24]
         ts(mkhi, mk, MAGIC4, MAGIC4, ALU.add, ALU.subtract, ["mmin", "LM2"], ["mkhi"])
         ts(T.LM2[:, 20:192:24], mk, MAGIC4, MAGIC4, ALU.add, ALU.subtract, ["mmin", "LM2"], ["mkhj"])
-        tt(T.LM2[:, 9:192:24], T.LMs[:, 0:16:2], T.LMs[:, 1:16:2], ALU.min, ["LMs", "LM2"], ["thra"])
-        ts(T.LM2[:, 21:192:24], T.LM2[:, 9:192:24], BIG, 0.0, ALU.add, ALU.min, ["thra"], ["thrb"])
         tt(T.ce[:], mk, mkhi, ALU.subtract, ["mmin", "mkhi"], ["ce"])
         mms("PB", to_list("PB", T.ce[:], ["ce"]))
         act(T.LE[:], T.PB[:, 0:64], ["PB"], ["LE"], 64)
-        cp(T.eu[:], T.LE[:].indirect(T.EXD[:, 0:1]), ["LE", "EXD"], ["eu"], 16, "g")
-        act(T.zb[:], z1, nz, ["zb"], 128, scale=0.5, bias=-ZO / 2)
+        lin("eu", T.eu[:], T.LE[:].indirect(T.EXD[:, 0:1]), ["LE", "EXD"], ["eu"], 16, "g")
         act(T.zq[:], z1, nz, ["zq"], 128, scale=0.5, bias=-ZO / 2 - 0.25)
-        tt(T.y2[:], T.xm[:].indirect(T.eu[:, 0:8]), T.zb[:], ALU.subtract, XM + ["eu", "zb"], ["y2"], 128, "g")
-        act(T.ya[:], T.y2[:], ["y2"], ["ya"], 128, func=ACT.Abs, scale=2.0)
+        if "y2" in ON_S:
+            act(T.yS[:], T.xm[:].indirect(T.eu[:, 0:8]), XM + ["eu"], ["yS"], 128, "g")
+            tt(T.y2[:], T.yS[:], T.zq[:], ALU.subtract, ["yS", "zq"], ["y2"], 128, "")
+        else:
+            tt(T.y2[:], T.xm[:].indirect(T.eu[:, 0:8]), T.zq[:], ALU.subtract, XM + ["eu", "zq"], ["y2"], 128, "g")
+        act(T.ya[:], T.y2[:], ["y2", "nhalf"], ["ya"], 128, func=ACT.Abs, scale=2.0, bias=nhalf)
         tt(T.yw[:, YC:YA:2], T.ya[:], T.zq[:], ALU.subtract, ["ya", "zq"], ["yc"], 128, "")
-        tt(T.yw[:, YA:YW:8], T.ya[:], T.zq[:], ALU.subtract, ["ya", "zq"], ["ya2"], 128, "")
+        if not last:
+            mixed(lambda j: T.ya[:, j:128:8], ["ya"], T.tc[:], T.DC[:], DCall, ["tc"])
+            tt(T.CE[:, 1, 0:32:4], T.tc[:, 4:64:8], T.tc[:, 7:64:8], ALU.subtract, ["tc"], ["CE"])
+            act(T.CE[:, 1, 1:32:4], T.c8[:], ["c8"], ["CEa"], scale=-2.0, bias=-1.0)
+            act(T.CE[:, 1, 3:32:4], T.c8[:], ["c8"], ["CEb"], scale=2.0 * r)
         fresh = [(T.Uw[:], z1, ["Uw"] + nz, False), (T.Ib[:], T.K37[:], ["Ib", "K37"], False), (T.Ib[:], T.kc[:], ["Ib", "kc"], False)]
         mms("PA", [(T.PA[:, 0:128], l, x, rd, 128, f) for l, x, rd, f in fresh])
-        act(T.yy[:], T.PA[:, 0:128], ["PA"], ["yy"], 128, bias=MAGIC4)
-        act(T.ny[:], T.yy[:], ["yy"], ["ny"], 128, bias=MAGIC4, scale=-1.0)
+        act(T.qq[:], T.PA[:, 0:128], ["PA"], ["qq"], 128, scale=1 / 4096, bias=64.0)
         mms("PA", [(T.PA[:, 0:128], T.Ib[:], T.kc[:], ["Ib", "kc"], 128, False),
                    (T.PA[:, 0:128], T.nIb[:], M1, ["nIb"] + nz, 128, False)] +
             [(T.PA[:, 128:256], l, x, rd, 128, f) for l, x, rd, f in fresh] +
             [(T.PA[:, 128:256], T.nIb[:], M1, ["nIb"] + nz, 128, False)],
-            [(T.PA[:, 128:256], T.Ib[:], T.ny[:], ["Ib", "ny"], 128, False)])
+            [(T.PA[:, 128:256], T.In4k[:], T.qq[:], ["In4k", "qq"], 128, False)])
         act(T.DD[:, 0:128], T.PA[:, 0:128], ["PA"], ["DDa"], 128)
-        act(T.DD[:, 256:384], T.PA[:, 128:256], ["PA"], ["DDc"], 128, bias=-0.5)
+        act(T.DD[:, 256:384], T.PA[:, 128:256], ["PA"], ["DDc"], 128, bias=64 * 4096 - 0.5)
         act(T.zz[:], z1, nz, ["zz"], 128, scale=0.5, bias=ZO / 2 - 0.25)
         tt(T.mA[:], T.LMs[:].indirect(T.EXS[:]), LMk, ALU.is_le, ["LMs", "EXS"] + nLM, ["mA"], 128, "g")
-        act(T.bits[:, 0:128], T.BT[:].indirect(T.cu16[:]), ["BTa", "BTb", "cu16"], ["bits"], 128, "g")
-        act(T.bits[:, 128:256], T.bits[:, 0:128], ["bits", "pm"], ["bits2"], 128, scale=podd)
+        lin("bits", T.bits[:, 0:128], T.BT[:].indirect(T.cu16[:]), ["BTa", "BTb", "cu16"], ["bits"], 128, "g")
         for j, bank in enumerate(("EA", "EB")):
-            mm([(T[bank][:, 128 * q:128 * q + 128], T.Ib[:], T.TRI[:], ["Ib", "TRI"], 128, False) for q in range(4)],
+            mm([(T[bank][:, 256 * q:256 * q + 256], T.Ib[:], T.TRI[:], ["Ib", "TRI", "TRJ"], 256, False) for q in range(2)],
                True, False, [bank])
             for q in range(2):
-                p0, rd = 64 * j + 32 * q, ["bits", "bits2"] + ["Et"] * q
-                mm([(T[bank][:, 256 * q:256 * q + 128], T.bits[p0:p0 + 16, 0:128], T.bits[p0:p0 + 16, 0:128], rd, 128, False),
-                    (T[bank][:, 256 * q + 128:256 * q + 256], T.bits[p0:p0 + 32, 128:256], T.bits[p0:p0 + 32, 0:128], rd, 128, False)],
+                p0, rd = 64 * j + 32 * q, ["bits"] + ["Et"] * q
+                mm([(T[bank][:, 256 * q + 128 * o:256 * q + 128 * o + 128], T.bits[p0:p0 + 16 + 16 * o, 0:128],
+                     T.bits[p0:p0 + 16 + 16 * o, 0:128], rd, 128, False) for o in range(2)],
                    False, q == 1, [bank] + ["Et"] * (1 - q))
-            act(T.E[:, 512 * j:512 * j + 512], T[bank][:], [bank], ["E%d" % j], 512, func=ACT.Relu, scale=1024.0, bias=-7168.0)
-        mm([(T.PX[:, 0:16, 0:12], T.If[:], T.CX[:], ["If"] + CXall, 192, True)], True, False, ["PX"])
+            for q in range(2):
+                act(T.E[:, 512 * j + 256 * q:512 * j + 256 * q + 256], T[bank][:, 256 * q:256 * q + 256], [bank],
+                    ["E%d" % (2 * j + q)], 256, func=ACT.Relu, scale=1024.0, bias=-127.0 * 1024)
+        mm([(T.PX[:, 0:16, 0:12], T.Ib[:], T.CX[:], ["Ib"] + CXall, 192, False),
+            (T.PX[:, 0:16, 9:12], T.Ib[:], T.CY[:], ["Ib"] + CYall, 48, False)], True, False, ["PX"])
         for s0, n in CH_X:
             mins("x", s0, n)
         sums("PX", 16, 9, MM_X, T.yw, T.mnx, "x", T.WX, WXall, ["WXn"])
@@ -564,70 +781,84 @@ def rank_program(g, core, T, topo):
         tt(T.L1[:], T.KS[:].indirect(T.EX[:]), T.DM[:, 0:128], ALU.mult, ["KS", "EX", "DM0"], ["L1"], 128, "g")
         tt(T.mK[:], T.PX[:, 0:16, 0:8], LMk, ALU.is_lt, ["PX", "~LX"] + nLM, ["mK"], 128, "")
         tt(T.cb[:], T.LX[:, 8:192:12], T.LQ[:, 9:192:12], ALU.is_equal, ["LX", "LQ"], ["cb"], 16)
-        code = T.PM[:, 25, 0:8]
-        mms("PM", [(code, T.L1[:], T.BDb[:, 0:128:16], ["L1", "BDb"], 8, False)])
-        cp(T.selu[:], code, ["PM"], ["selu", "~selu"])
-        ts(T.szu[:], code, 0.125, -7.0 / 16, ALU.mult, ALU.add, ["PM", "~selu"], ["szu", "~szu"])
+        code, past = T.PM[:, 0, 0, 0:8], T.PM[:, 0, 1:3, 0:8]
+        mms("PM", *[[(T.PM[:, 0, 0:3, 0:8], T.Ib[:], T.TC[:], ["Ib", "TCa", "TCb", "TCc"], 24, False)]] * (not last),
+            [(T.PM[:, 0, 0:3, 0:8], T.L1[:], T.BD3[:], ["L1", "BD0", "BD1", "BD2"], 24, False)])
+        tt(T.selu[:], code, T.YL[:], ALU.min, ["PM", "YL"], ["selu"])
+        lin("szu", T.szu[:], code, ["PM", "selu"], ["szu"], scale=0.125, bias=-7.0 / 16)
         mms("PA", [(T.PA[:, 0:128], T.mK[:], T.Ib[:], ["mK", "Ib"], 128, False)])
         tt(T.DD[:, 128:256], T.PA[:, 0:128], T.DD[:, 0:128], ALU.mult, ["PA", "DDa"], ["DDb"], 128, "")
         act(T.Wm[:, 0:256:2], T.DD[:, 128:256], ["DDb", "h0"], ["Wma"], 128, scale=h0)
         act(T.Wm[:, 1:256:2], T.DD[:, 128:256], ["DDb", "h1", "DM0"], ["Wmb"], 128, scale=h1)
         nW = ["Wma", "Wmb", "Wmz", "Wmc", "szu"] + nz
         ns = "sz%d" % r
-        tt(sz[:, :, 1], T.yw[:].indirect(T.selu[:]), T.zz[:], ALU.add, XX + ["yc", "ya2", "selu", "zz", ns], [ns + "a"], 128, "g")
-        cp(sz[:, :, 3], sz[:, :, 1], [ns + "a"], [ns + "c"], 128, "h")
+        tt(sz[:, :, 1], T.yw[:, 0:YA].indirect(T.selu[:]), T.zz[:], ALU.add, XX + ["yc", "selu", "zz", ns], [ns + "a"], 128, "g")
+        if not last:
+            lin("szc", sz[:, :, 3], sz[:, :, 1], [ns + "a"], [ns + "c"], 128, "h")
         if last:
             tt(T.Mn[:], T.Wm[:].indirect(T.szu[:]), M1, ALU.add, nW, ["Mn"], 128, "g")
             act(T.yy[:], T.Mn[:], ["Mn"], ["yy"], 128, bias=2048.0)
             ts(T.nzb[:], sz[:, :, 1], -ZO, None, ALU.add, None, [ns + "a"], ["nzb"], 128, "h")
-            dma("Y", "stZ", T.yz[:], T.nzb[:], ["nzb"], [], 2 ** 15)
-            dma("Y", "stM", T.yms[:], T.yy[:], ["yy"], [], 2 ** 16)
+            store("Y", "stZ", T.yz[:], T.nzb[:], ["nzb"], 2 ** 15)
+            store("Y", "stM", T.yms[:], T.yy[:], ["yy"], 2 ** 16)
         else:
             lz2 = T["lz%d" % (r + 1)]
-            act(sz[:, 0:128:16, 2], code, ["PM", ns, "~szu"], [ns + "b"], scale=0.125, bias=BO - 7.0 / 16)
+            ts(T.CE[:, :, 2:32:4], past, 0.0, None, ALU.is_ge, None, ["PM", "szu", "CEz"], ["FL"])
+            scan(sz[:, 0:128:4, 2], T.CE[:, 0, :], T.CE[:, 1, :], ALU.mult, ALU.add, ["FL", "CEa", "CEb", "CE", "CEy", ns],
+                 [ns + "b"], 32)
             tt(sz[:, :, 0], T.Wm[:].indirect(T.szu[:]), M1, ALU.add, nW + [ns], [ns + "d"], 128, "g")
             nsz = [ns + x for x in "abcd"]
             for nm, call in CALLS.items():
                 send(call, lambda h, a=sz: a[:, 16 * h:16 * h + 16, :], lambda s, a=lz2: a[:, 16 * s:16 * s + 16, :],
-                     "ar%s%d" % (nm, r), nsz + ["lc%d" % r], ["lz%d%s" % (r + 1, nm)], T_CALL[nm])
+                     "ar%s%d" % (nm, r), nsz + ["lc"], ["lz%d%s" % (r + 1, nm)], T_CALL[nm])
             act(lz2[:, 16:32, :], sz[:, 0:16, :], nsz, ["lz%do" % (r + 1)], 64)
-        mms("PB", [(T.PB[:, 0:48], T.Ib[:], T.S32[:, 48 * last:48 * last + 48], ["Ib"] + S32all, 48, False)],
-            [(T.PB[:, 0:48:3], T.UL[:, 128 * il:128 * il + 128], sz[:, il:128:16, 1:4:2], ULall + [ns + "a", ns + "c"], 16, False)
-             for il in range(16)])
-        scan(T.tq[:], T.DV[:], T.PB[:, 0:48], ALU.mult, ALU.add, ["PB", "DVa", "DVb"], ["tq"], 48)
-        cp(T.vu[:], T.tq[:, 3:48:6], ["tq"], ["vu"])
-        for j, (c0, w) in enumerate(((0, 64), (64, 64)) if last else ((0, 128),)):
+        mixed(lambda j, a=sz: a[:, j:128:8, 1], [ns + "a"], T.tq[:], T.DV[:, 64 * last:64 * last + 64], DVall, ["tq"])
+        tt(T.vu[:], T.tq[:, 4:64:8], T.tq[:, 7:64:8], ALU.subtract, ["tq"], ["vu"])
+        for j, (c0, w) in enumerate(PIECES if last else ((0, 128),)):
             win, off = T.X[:, 32 * c0:32 * (c0 + w)], T.vu[:, c0 // 16:(c0 + w) // 16]
             xj = "X%d" % j if last else "X"
             tt(T.xa[:, c0:c0 + w], win.indirect(off), sz[:, c0:c0 + w, 1], ALU.add, ["X", "vu", ns + "a"], ["xa%d" % j], w, "g")
-            ts(T.xb[:, c0:c0 + w], T.xa[:, c0:c0 + w], 1, 255, ALU.arith_shift_right, ALU.bitwise_and, ["xa%d" % j], ["xb%d" % j], w)
+            lin("xb", T.xb[:, c0:c0 + w], T.xa[:, c0:c0 + w], ["xa%d" % j], ["xb%d" % j], w, scale=0.5, bias=-ZO / 2 - 0.25)
             cp(win.indirect(off), T.xb[:, c0:c0 + w], ["vu", "xb%d" % j], [xj] + ["~X"] * last, w, "s")
             if last:
-                dma("YS"[j], ("stX", "stX2")[j], T.ytx[:, 2048 * j:2048 * j + 2048], win, [xj], [], 2 ** (19 + j))
-        tt(T.oM[:], T.DM[:].indirect(T.eu[:, 0:8]), M1, ALU.mult, DMall + ["eu"] + nz, ["oM"], 128, "g")
-        tt(T.LXk[:], T.PX[:, 0:16, 0:8], T.C30[:], ALU.add, ["PX", "C30", "~LX"], ["LXk"], 128, "")
-        scan(T.amax[:], T.DA[:], T.LXk[:], ALU.add, ALU.max, ["DA", "LXk"], ["amax"], 128)
-        tt(T.nA[:], T.amax[:].indirect(T.EXA[:]), T.LXk[:], ALU.is_equal, ["amax", "EXA", "LXk"], ["nA"], 128, "g")
+                store("YSY"[j], "stX%d" % j, T.ytx[:, 32 * c0:32 * (c0 + w)], win, [xj], 2 ** 13 * w)
+        if "oM" in ON_S:
+            act(T.oS[:], T.DM[:].indirect(T.eu[:, 0:8]), DMall + ["eu"], ["oS"], 128, "g")
+            tt(T.oM[:], T.oS[:], M1, ALU.mult, ["oS"] + nz, ["oM"], 128, "")
+        else:
+            tt(T.oM[:], T.DM[:].indirect(T.eu[:, 0:8]), M1, ALU.mult, DMall + ["eu"] + nz, ["oM"], 128, "g")
+        if "nA" in ON_S:
+            act(T.LXk[:], T.PX[:, 0:16, 0:8], ["PX", "LX"], ["LXk"], 128)
+            mms("PB", [(T.PB[:, 0:128], T.Ib[:], T.C30[:], ["Ib", "C30"], 128, False)],
+                [(T.PB[:, 0:128], T.If[:], T.LXk[:], ["If", "LXk"], 128, True)])
+            scan(T.amax[:], T.DA[:], T.PB[:, 0:128], ALU.add, ALU.max, ["DA", "PB"], ["amax"], 128)
+            act(T.LXk[:], T.amax[:].indirect(T.EXA[:]), ["amax", "EXA"], ["LXk"], 128, "g")
+            tt(T.nA[:], T.PB[:, 0:128], T.LXk[:], ALU.not_equal, ["PB", "LXk"], ["nA"], 128, "")
+        else:
+            tt(T.LXk[:], T.PX[:, 0:16, 0:8], T.C30[:], ALU.add, ["PX", "C30", "~LX"], ["LXk"], 128, "")
+            scan(T.amax[:], T.DA[:], T.LXk[:], ALU.add, ALU.max, ["DA", "LXk"], ["amax"], 128)
+            tt(T.nA[:], T.amax[:].indirect(T.EXA[:]), T.LXk[:], ALU.not_equal, ["amax", "EXA", "LXk"], ["nA"], 128, "g")
         tr([T.ZB[:, 0:8, :]], T.nA[:], ["nA"], "ZB")
         mms("EA", [(T.EA[:, 0:16], T.Ib[:], T.CG[:], ["Ib", "CGa", "CGb"], 16, False),
                    (T.EA[:, 0:16], T.In1k[:], T.cb[:], ["In1k", "cb"], 16, False)] +
-            [(T.EA[:, 2 * gi:2 * gi + 2], T.E[:, 128 * gi:128 * gi + 128], T.cb[:, 2 * gi:2 * gi + 2], ["E%d" % (gi // 4), "cb"], 2, False)
+            [(T.EA[:, 2 * gi:2 * gi + 2], T.E[:, 128 * gi:128 * gi + 128], T.cb[:, 2 * gi:2 * gi + 2], ["E%d" % (gi // 2), "cb"], 2, False)
              for gi in range(8)])
         scan(T.val[:], T.D2s[:], T.EA[:, 0:16], ALU.add, ALU.min, ["D2s", "EA"], ["val"], 16)
-        mms("EB", [(T.EB[:, gi:64:8], T.Ib[:], c2m, ["Ib", "sc%d" % r], 8, False) for gi in range(8)],
+        mms("EB", [(T.EB[:, gi:64:8], T.I2[:], T.c8[:], ["I2", "c8"], 8, False) for gi in range(8)],
             to_list("EB", T.val[:, 1:16:2], ["val"]))
         act(T.LV[:], T.EB[:, 0:64], ["EB"], ["LV"], 64)
-        tt(T.lo[:], T.LV[:].indirect(T.EXD[:, 0:1]), T.D512[:], ALU.min, ["LV", "EXD", "D512a", "D512b"], ["lo"], 16, "g")
-        cp(T.ou[:, 0:8], T.lo[:, 0:8], ["lo"], ["ou"])
+        tt(T.ou[:], T.LV[:].indirect(T.EXD[:, 0:1]), T.D512[:], ALU.min, ["LV", "EXD", "D512a", "D512b"], ["ou"], 16, "g")
         act(T.mA[:], T.ZB[:, 0:8, :], ["ZB"], ["mA"], 128)
-        act(T.old[:], T.Kw[:].indirect(T.ou[:, 0:8]), ["Kw", "ou"], ["old"], 128, "g")
-        mms("PB", [(T.PB[:, 0:128], T.BDb[:], T.oM[:], ["BDb", "oM"], 128, False),
-                   (T.PB[:, 0:128], T.In1k[:], T.two[:], ["In1k", "two"], 128, False)],
-            [(T.PB[:, 0:128], T.nIf[:], T.old[:], ["nIf", "old"], 128, True)])
-        tt(T.D2[:], T.PB[:, 0:128], T.mA[:], ALU.mult, ["PB", "mA"], ["D2"], 128, "")
-        tt(T.Kw[:].indirect(T.ou[:, 0:8]), T.old[:], T.D2[:], ALU.add, ["ou", "old", "D2"], ["Kw"], 128, "s")
+        mms("PA", [(T.PA[:, 0:128], T.BDb[:], T.oM[:], ["BDb", "oM"], 128, False),
+                   (T.PA[:, 0:128], T.nA[:], T.In4k[:], ["nA", "In4k"], 128, False)])
+        act(T.D2[:], T.PA[:, 0:128], ["PA"], ["D2"], 128, bias=2048.0)
+        tt(T.old[:], T.Kw[:].indirect(T.ou[:, 0:8]), T.mA[:], ALU.mult, ["Kw", "ou", "mA"], ["old"], 128, "g")
+        tt(T.Kw[:].indirect(T.ou[:, 0:8]), T.old[:], T.D2[:], ALU.max, ["ou", "old", "D2"], ["Kw"], 128, "s")
         if last:
-            dma("Y", "stK", T.ykt[:], T.Kw[:, 0:512], ["Kw"], [], 2 ** 18)
+            store("Y", "stK", T.ykt[:], T.Kw[:, 0:512], ["Kw"], 2 ** 18)
+
+    for sem in STORES:
+        op(*stores[sem])
 
     count = {}
     clock = {e: {} for e in Q}
@@ -649,6 +880,8 @@ def rank_program(g, core, T, topo):
     for i in PLANS["order"]:
         o = ops[i]
         e = o["e"]
+        if e == "D":
+            continue
         o["rd"] = [r for r in o["rd"] if r[0] != "~"]
         o["wr"] = [w for w in o["wr"] if w[0] != "~"]
         evs = []

from concourse.bass import DstId, RemoteDMATransfer
from concourse.mybir import AluOpType as ALU, ActivationFunctionType as ACT

RO = 3
BIG = float(2 ** 26)
HUGE = float(2 ** 30)
VAST = float(2 ** 60)
MAGIC4 = float(3 * 2 ** 34)
MAGIC32 = float(3 * 2 ** 27)
MAGIC512 = float(3 * 2 ** 31)
ZO = 1536.0
YC, YA, YW = 2048, 2304, 3328

F, B, I, U, H = "float32", "bfloat16", "int32", "uint16", "float16"
SCRATCH = {}


def _sb(dtype, **kw):
    for name, shape in kw.items():
        SCRATCH[name] = ("sbuf", [128] + list(shape), dtype)


_sb(B, X=[4096], yw=[YW], xm=[2048], mnm=[2048], mnx=[2048], UL=[1024], DM=[2048], CH=[8, 128], E=[1024], BT=[512],
    zb=[128], zT=[256], Ib=[128], In1k=[128], Uw=[128], ones=[128],
    e8=[128], TRI=[256], C30=[128], WX=[4, 32], WM=[4, 64], BDb=[128], nIb=[128], ya=[128], qq=[128],
    I2=[128], In4k=[128], TC=[24], CY=[48],
    mA=[128], mK=[128], nA=[128], cb=[16], val=[16], SU=[64], BD3=[24], oS=[128], yS=[128], bits=[256], nzb=[128])
_sb(F, Kw=[640], If=[128], BD=[128], DX=[192], LQ=[192], CM=[8, 4, 9],
    D16=[128], DA=[128], D2s=[16], DV=[128], DC=[64], tc=[64], CE=[2, 32], LM2=[192],
    LX=[192], LMs=[32], YL=[8],
    D512=[16], pm=[16], SL=[8], zz=[128], yy=[128],
    DD=[384], Wm=[416], LMk=[128], LXk=[128], mmin=[128], amax=[128], LE=[64],
    LV=[64], old=[128], D2=[128], tq=[64], Mn=[128])
_sb(H, lz0=[128, 4], lz1=[128, 4], lz2=[128, 4], sz0=[128, 4], sz1=[128, 4], sz2=[128, 4], sc=[64], lc=[64],
    CX=[16, 12], hq=[8], c8=[8], y2=[128], ce=[8], zq=[128], L1=[128], CG=[16], CMh=[288], kc=[128], K37=[128], oM=[128])
_sb(I, kti=[512], msi=[128], tmpi=[256], tmpj=[256], BI=[256], ksi=[8], KS=[8], cj=[8], pint=[8], ui=[8],
    xa=[128], xb=[128])
_sb(U, Mu=[128], Mo=[32], kcu=[128], cu16=[8], EX=[8], EXS=[8], EXA=[8], EXD=[2], selu=[8], szu=[8], eu=[16], vu=[8], ou=[16])
BANKS = ("ZA", "ZB", "PX", "PM", "EA", "EB", "PA", "PB")
for _n in BANKS:
    SCRATCH[_n] = ("psum", [128, 64, 16], B) if _n[0] == "Z" else \
        ("psum", {"PX": [128, 32, 16], "PM": [128, 8, 4, 16]}.get(_n, [128, 512]), F)

SEMAPHORES = ["cV", "cS", "cP", "cG", "ldX", "ldX2", "ldK", "ldM", "ldZ", "ldC", "stX0", "stX1", "stX2", "stK", "stM", "stZ",
              "arC", "arA0", "arA1", "arB0", "arB1", "arD0", "arD1", "sent", "cpD", "cpU"]

CH_M = [(0, 64), (64, 64)]
CH_X = [(0, 32), (32, 32), (64, 32), (96, 16), (112, 16)]
_LATER = [("S", 0, 48), ("V", 48, 32), ("S", 80, 32), ("V", 112, 16)]
G_M = [[("V", 0, 32), ("S", 32, 32), ("S", 64, 32), ("V", 96, 32)], _LATER, _LATER]
G_X = [[("S", 0, 32), ("V", 32, 32), ("S", 64, 32), ("S", 96, 16), ("S", 112, 16)]] * RO
MM_M, MM_X = [(0, 128)], [(0, 96), (96, 32)]
CALLS = {"A": ((7, 4), (1, 4), (2, 4), (3, 4)), "B": ((4, 8), (5, 8)), "D": ((6, 16),)}
CALL_C = ((1, 2), (2, 2), (3, 2), (4, 2), (5, 2), (6, 2), (7, 4))
PIECES = ((0, 32), (32, 32), (64, 64))
STORES = ("stZ", "stM", "stX0", "stX1", "stX2", "stK")
FIRST = 80
PACE = [dict(cy=0.87e-3, gat=1.56, sca=3.8, wake=0.18, wakeP=0.25, dma=1.5, bw=400e3, rem=1.0),
        dict(cy=1.12e-3, gat=2.05, sca=5.0, wake=0.20, wakeP=0.26, dma=1.8, bw=280e3, rem=1.5),
        dict(cy=0.85e-3, gat=1.1, sca=2.2, wake=0.17, wakeP=0.24, dma=1.4, bw=420e3, rem=0.9)]
WEIGHT = (1.0, 0.7, 1.0)
NP = len(PACE)
T_CALL, T_C, T_FIRST = {"A": 0.0, "B": 0.25, "D": 0.15}, 2.5, 1.5
SEED, TRIES, PASSES, HEAT, SHAKE = 1, 150000, 10, 0.9, 1.2
ON_S = {"MuA", "MuB", "cu2", "oM", "bits", "szc", "zT", "LX", "eu", "xb", "kc", "szu"}
PLANS = {}


def plan(ops):
    n = len(ops)
    pred = [set() for _ in ops]
    soft, reads = set(), set()
    writer, readers = {}, {}
    for i, o in enumerate(ops):
        for r in o["rd"] + o["wr"]:
            if r in writer:
                pred[i].add(writer[r])
                if r in o["rd"] and r[0] != "~":
                    reads.add((writer[r], i))
                if r[0] == "~" and r not in ("~LX", "~szu"):
                    soft.add((writer[r], i))
        for w in o["wr"]:
            pred[i].update(readers.get(w, []))
        for r in o["rd"]:
            readers.setdefault(r, []).append(i)
        for w in o["wr"]:
            writer[w] = i
            readers[w] = []
        pred[i].discard(i)
    eng = ["VSPGY".index(o["e"]) for o in ops]
    hold, hold2 = ([o["hold"][m] for o in ops] for m in range(2))
    lat, lat2 = ([o["lat"][m] for o in ops] for m in range(2))

    def gap(p, i, m):
        if (p, i) in soft or (eng[p] == eng[i] == 2 and (p, i) not in reads):
            return 0.0
        return ops[p]["lat"][m] + PACE[m]["wakeP" if eng[p] == 2 else "wake"]
    before, before2 = ([[(p, gap(p, i, m)) for p in sorted(pred[i])] for i in range(n)] for m in range(2))
    after = [[] for _ in ops]
    for i in range(n):
        for p, gp in before[i]:
            after[p].append((i, gp))

    def ranked(key, need):
        key = list(key)
        for i in (range(n) if need is before else range(n - 1, -1, -1)):
            for p, _ in need[i]:
                if key[p] >= key[i]:
                    key[i] = key[p] + 1e-6
        return sorted(range(n), key=lambda i: key[i])

    def place(key, need, first):
        start = [0.0] * n
        used = [([], []) for _ in range(5)]
        for i in ranked(key, need):
            t = first[i]
            for p, gp in need[i]:
                if start[p] + hold[p] + gp > t:
                    t = start[p] + hold[p] + gp
            a, b = used[eng[i]]
            lo, hi = 0, len(b)
            while lo < hi:
                mid = (lo + hi) // 2
                if b[mid] <= t:
                    lo = mid + 1
                else:
                    hi = mid
            while lo < len(a) and a[lo] < t + hold[i] - 1e-9:
                t = max(t, b[lo])
                lo += 1
            a.insert(lo, t)
            b.insert(lo, t + hold[i])
            start[i] = t
        return start

    zero = [0.0] * n

    def slow(fw):
        start, free = [0.0] * n, [0.0] * 5
        for i in ranked(fw, before):
            t = free[eng[i]]
            for p, gp in before2[i]:
                if start[p] + hold2[p] + gp > t:
                    t = start[p] + hold2[p] + gp
            start[i] = t
            free[eng[i]] = t + hold2[i]
        return max(start[i] + hold2[i] + lat2[i] for i in range(n))

    def forward(key):
        fw = place(key, before, zero)
        return max(fw[i] + hold[i] + lat[i] for i in range(n)) + SLOW * slow(fw), fw

    def both(key):
        fw = place(key, before, zero)
        bw = place([-fw[i] - hold[i] for i in range(n)], after, lat)
        end = max(bw[i] + hold[i] for i in range(n))
        return forward([end - bw[i] - hold[i] for i in range(n)])

    seed = [SEED]

    def rnd():
        seed[0] = (seed[0] * 1103515245 + 12345) % 2 ** 31
        return seed[0] / 2 ** 31
    tail = [0.0] * n
    for i in range(n - 1, -1, -1):
        tail[i] = hold[i] + max([tail[s] + gp for s, gp in after[i]] + [lat[i]])
    cur, fw = both([-t for t in tail])
    best, out = cur, fw
    busy = [i for i in range(n) if eng[i] < 2 and ops[i]["round"] >= 0]
    twin = [{} for _ in range(RO)]
    for i, o in enumerate(ops):
        if o["round"] >= 0:
            w = (o["wr"] + [""])[0]
            s = [o["e"], w[:2] + w[3:] if w[:2] in ("sz", "lz") else w, 0]
            while tuple(s) in twin[o["round"]]:
                s[2] += 1
            twin[o["round"]][tuple(s)] = i
    for it in range(TRIES):
        if it % 100 == 99:
            a, b = int(rnd() * RO), int(rnd() * RO)
            d = fw[twin[a][("V", "LQ", 0)]] - fw[twin[b][("V", "LQ", 0)]]
            trial = list(fw)
            part = rnd()
            for s, i in twin[a].items():
                if s in twin[b] and (part < 0.4 or ops[i]["tail"] == (part < 0.7)):
                    trial[i] = fw[twin[b][s]] + d
            end, f2 = forward(trial)
        else:
            chain = {busy[int(rnd() * len(busy))] if rnd() < 0.8 else int(rnd() * n)}
            link = before if rnd() < 0.6 else after
            for _d in range(int(rnd() * 8)):
                chain |= {p for i in chain for p, _ in link[i] if abs(fw[p] - fw[i]) < 4 and rnd() < 0.8}
            d = (0.2 + 2.5 * rnd() ** 2) * (-1 if link is before else 1)
            trial = [fw[i] + d if i in chain else fw[i] for i in range(n)]
            end, f2 = forward(trial) if rnd() < 0.6 else both(trial)
        if end <= cur + HEAT * (1 - it / TRIES) * rnd() ** 2:
            cur, fw = end, f2
            if end < best:
                best, out = end, f2
    PLANS["t"] = (best - SLOW * slow(out), slow(out))
    return ranked(out, before)


def plan(ops):
    n = len(ops)
    pred, succ = [set() for _ in ops], [set() for _ in ops]
    soft, reads = set(), set()
    writer, readers = {}, {}
    for i, o in enumerate(ops):
        for r in o["rd"] + o["wr"]:
            if r in writer:
                pred[i].add(writer[r])
                if r[0] == "~":
                    soft.add((writer[r], i))
                elif r in o["rd"]:
                    reads.add((writer[r], i))
        for w in o["wr"]:
            pred[i].update(readers.get(w, []))
        for r in o["rd"]:
            readers.setdefault(r, []).append(i)
        for w in o["wr"]:
            writer[w] = i
            readers[w] = []
        pred[i].discard(i)
        for p in pred[i]:
            succ[p].add(i)
    eng = ["VSPGYD".index(o["e"]) for o in ops]
    hold, lat = ([[o[k][m] for o in ops] for m in range(NP)] for k in ("hold", "lat"))

    def gap(p, i, m):
        if ((p, i) in soft and (p, i) not in reads) or (eng[p] == eng[i] == 2 and (p, i) not in reads):
            return 0.0
        return lat[m][p] + PACE[m]["wakeP" if eng[p] == 2 else "wake"]
    before = [[[(p, hold[m][p] + gap(p, i, m)) for p in sorted(pred[i])] for i in range(n)] for m in range(NP)]
    last = [i for i in range(n) if not succ[i]]

    def run(order, m, k=0, known=None):
        start, free, h, b = list(known) if k else [0.0] * n, [0.0] * 6, hold[m], before[m]
        for i in order[:k]:
            free[eng[i]] = i + 1
        free = [start[i - 1] + h[i - 1] if i else 0.0 for i in free]
        for i in order[k:]:
            e = eng[i]
            t = free[e]
            for p, d in b[i]:
                if start[p] + d > t:
                    t = start[p] + d
            start[i] = t
            free[e] = t + h[i]
        return max(start[i] + h[i] + lat[m][i] for i in last), start

    def guess(order, m, k, known):
        start, free, h, b = list(known), [0] * 6, hold[m], before[m]
        for i in order[max(0, k - 120):k]:
            free[eng[i]] = i + 1
        free = [start[i - 1] + h[i - 1] if i else 0.0 for i in free]
        same, shift = 0, 0.0
        for i in order[k:]:
            e = eng[i]
            t = free[e]
            for p, d in b[i]:
                if start[p] + d > t:
                    t = start[p] + d
            if -1e-9 < t - start[i] - shift < 1e-9:
                same += 1
                if same > 40:
                    return shift
            else:
                same, shift = 0, t - start[i]
            start[i] = t
            free[e] = t + h[i]
        return max(start[i] + h[i] + lat[m][i] for i in last) - max(known[i] + h[i] + lat[m][i] for i in last)

    seed = [SEED]

    def rnd():
        seed[0] = (seed[0] * 1103515245 + 12345) % 2 ** 31
        return seed[0] / 2 ** 31

    def chain(order, m, start):
        prev, top = [None] * n, [None] * 6
        for i in order:
            prev[i], top[eng[i]] = top[eng[i]], i
        i = max(last, key=lambda j: start[j] + hold[m][j] + lat[m][j])
        pairs = []
        while start[i] > 1e-9:
            c, q = [p for p, d in before[m][i] if start[p] + d > start[i] - 1e-9], prev[i]
            if c and (q is None or start[q] + hold[m][q] < start[i] - 1e-9 or rnd() < 0.3):
                i = c[int(rnd() * len(c))]
            else:
                pairs.append((q, i))
                i = q
        return pairs, prev

    def move(order, at, a, b, up):
        seg = order[at[a]:at[b] + 1]
        s, link = ({b}, succ) if up else ({a}, pred)
        for x in (seg[::-1] if up else seg):
            if link[x] & s:
                s.add(x)
        if a in s and b in s:
            return None
        return order[:at[a]] + [x for x in seg if (x in s) == up] + [x for x in seg if (x in s) != up] + order[at[b] + 1:]

    tail = [0.0] * n
    for i in range(n - 1, -1, -1):
        tail[i] = hold[0][i] + max([tail[s] + gap(i, s, 0) for s in succ[i]] + [lat[0][i]])
    order, ready, free = [], [0.0] * n, [0.0] * 6
    left, todo = [len(p) for p in pred], {i for i in range(n) if not pred[i]}
    while todo:
        first = min(max(ready[i], free[eng[i]]) for i in todo)
        i = max(sorted(j for j in todo if max(ready[j], free[eng[j]]) <= first + 0.1), key=lambda j: tail[j])
        todo.remove(i)
        order.append(i)
        free[eng[i]] = max(ready[i], free[eng[i]]) + hold[0][i]
        for s in succ[i]:
            ready[s] = max(ready[s], free[eng[i]] + gap(i, s, 0))
            left[s] -= 1
            if not left[s]:
                todo.add(s)
    best, out = sum(w * run(order, m)[0] for m, w in enumerate(WEIGHT)), order
    name, twin = [], {}
    for i, o in enumerate(ops):
        w = (o["wr"] + [""])[0]
        s = [o["round"], o["e"], w[:2] + w[3:] if w[:2] in ("sz", "lz") else w, 0]
        while tuple(s) in twin:
            s[3] += 1
        name.append(tuple(s))
        twin[tuple(s)] = i
    marks = [i for i, o in enumerate(ops) if o["wr"][:1] == ["LQ"]]
    for tries, part in [(TRIES // 4, None)] + [(3 * TRIES // (16 * PASSES), x) for _ in range(PASSES) for x in range(RO + 1)]:
        order, it = list(out), 0
        if part is not None and rnd() < 0.7:
            start = run(out, 0)[1]
            key, cut = list(start), [4.0] + [start[i] for i in marks] + [1e9]
            if part in (1, 2) and rnd() < 0.5:
                d = 2 * part - 3
                for i, s in enumerate(name):
                    j = twin.get((s[0] - d,) + s[1:])
                    if j is not None and cut[part - d] <= start[j] < cut[part - d + 1]:
                        key[i] = start[j] + cut[part + 1] - cut[part - d + 1]
            else:
                key = [x + SHAKE * rnd() * (cut[part] <= x < cut[part + 1]) for x in key]
            for i in range(n):
                key[i] = max([key[i]] + [key[p] + 1e-6 for p in pred[i]])
            order.sort(key=lambda j: key[j])
        while it < tries:
            m = int(rnd() * NP)
            both = [run(order, x)[1] for x in range(NP)]
            start = both[m]
            order.sort(key=lambda j: start[j])
            at = {x: k for k, x in enumerate(order)}
            pairs, prev = chain(order, m, start)
            if part is not None:
                cut = [0.0] + [start[i] for i in marks] + [1e9]
                pairs = [x for x in pairs if cut[part] <= start[x[1]] < cut[part + 1]] or pairs
            nxt = {q: i for i, q in enumerate(prev) if q is not None}
            for _ in range(30):
                it += 1
                a, b = pairs[int(rnd() * len(pairs))]
                up, k = rnd() < 0.5, int(rnd() ** 2 * 8)
                while k and up and prev[a] is not None:
                    a, k = prev[a], k - 1
                while k and not up and b in nxt:
                    b, k = nxt[b], k - 1
                new = move(order, at, a, b, up)
                if new is not None:
                    v = sum(w * guess(new, x, at[a], both[x]) for x, w in enumerate(WEIGHT))
                    if v <= HEAT * (1 - it / tries) * rnd() ** 3:
                        order, v = new, sum(w * run(new, x, at[a], both[x])[0] for x, w in enumerate(WEIGHT))
                        if v < best:
                            best, out = v, list(new)
                        break
    PLANS["t"] = [run(out, m)[0] for m in range(NP)]
    PLANS["start"] = run(out, 0)[1]
    return out


def rank_program(g, core, T, topo):
    rank = T.rank_of(core)
    if rank is None:
        return
    N = len(T.cores)
    Q = {"V": g.vector, "S": g.scalar, "P": g.tensor, "G": g, "Y": g.sync}
    SEM = {"V": "cV", "S": "cS", "P": "cP", "G": "cG"}
    V, S, P = g.vector, g.scalar, g.tensor
    ops = []
    where = [-1, False]

    def op(e, fn, rd, wr, hold, lat=(0.0,) * NP, sem=None, inc=1, remote=False):
        ops.append(dict(round=where[0], tail=where[1], e=e, fn=fn, rd=list(rd), wr=list(wr), hold=hold, lat=lat,
                        sem=sem or SEM[e], inc=inc, remote=remote))

    def cost(n, k):
        if k in ("g", "s"):
            return [0.055 + n * m["gat" if k == "g" else "sca"] * m["cy"] for m in PACE]
        return [0.01 + max(64, n * {"": 1, "h": 0.5, "2": 2}[k]) * m["cy"] for m in PACE]

    def dma(e, sem, out, in_, rd, wr, nbytes):
        flow = [nbytes / m["bw"] + 0.15 for m in PACE]
        op(e, lambda: Q[e].dma_start(out, in_), rd, wr, flow if e == "Y" else [0.05] * NP,
           [m["dma"] + (0 if e == "Y" else f) for m, f in zip(PACE, flow)], sem, 16)

    stores = {}

    def store(e, sem, out, in_, rd, nbytes):
        op(e, lambda: Q[e].dma_start(out, in_), rd, ["~" + sem], [0.05] * NP, sem=sem, inc=16)
        stores[sem] = ("D", None, ["~" + sem], ["~D"], [nbytes / m["bw"] for m in PACE], [m["dma"] + 0.15 for m in PACE], sem)

    def cp(out, in_, rd, wr, n=8, k=""):
        op("V", lambda: V.tensor_copy(out, in_), rd, wr, cost(n, k))

    def tt(out, a, b, o, rd, wr, n=8, k="2"):
        op("V", lambda: V.tensor_tensor(out, a, b, o), rd, wr, cost(n, k))

    def ts(out, a, s1, s2, o0, o1, rd, wr, n=8, k=""):
        if s2 is None:
            op("V", lambda: V.tensor_scalar(out, a, s1, None, o0), rd, wr, cost(n, k))
        else:
            op("V", lambda: V.tensor_scalar(out, a, s1, s2, o0, o1), rd, wr, cost(n, k))

    def scan(out, d0, d1, o0, o1, rd, wr, n, init=0.0):
        op("V", lambda: V.tensor_tensor_scan(out, d0, d1, init, o0, o1), rd, wr, cost(n, ""))

    def ms(out, val, wr, n=8, k=""):
        op("V", lambda: V.memset(out, val), [], wr, cost(n, k))

    def act(out, in_, rd, wr, n=8, k="", func=ACT.Identity, bias=0.0, scale=1.0):
        op("S", lambda: S.activation(out, in_, func, bias=bias, scale=scale), rd, wr, cost(n, k))

    def lin(name, out, in_, rd, wr, n=8, k="", scale=1.0, bias=0.0):
        if name in ON_S:
            act(out, in_, rd, wr, n, k if k == "g" else "", scale=scale, bias=bias)
        else:
            ts(out, in_, scale, bias, ALU.mult, ALU.add, rd, wr, n, k)

    group = {}

    def mm(items, st, sp, wr, m=128, rd=()):
        bank = wr[0]
        rd = sorted({x for it in items for x in it[3]}) + list(rd)

        def fn():
            for j, it in enumerate(items):
                ins = P.matmul(it[0], it[1], it[2], st and j == 0, sp and j == len(items) - 1)
            return ins
        if st and not sp:
            group[bank] = []
            wr = wr + ["~" + bank]
        elif not st and not sp:
            group[bank].append("~%s_%d" % (bank, len(group[bank])))
            rd, wr = rd + ["~" + bank], wr[1:] + group[bank][-1:]
        elif not st:
            rd = rd + group.pop(bank, [])
        cycles = sum(max(min(64, m), it[4]) * (4 if it[5] else 1) for it in items)
        op("P", fn, rd, wr, [cycles * x["cy"] / 2 for x in PACE])

    def mms(bank, *parts):
        for j, items in enumerate(parts):
            mm(items, j == 0, j == len(parts) - 1, [bank])

    def tr(outs, in_, rd, bank):
        op("P", lambda: [P.transpose(o, in_, T.Ib[:]) for o in outs][-1], rd + ["Ib"], [bank],
           [64 * m["cy"] * len(outs) for m in PACE])

    def iota(out, pat, base, cm, wr, n, fl=False):
        t = [0.13 + 2 * n * m["cy"] for m in PACE]
        if fl:
            op("G", lambda: g.iota(out, pat, base, cm, allow_small_or_imprecise_dtypes=True), [], wr + ["~G"], t)
        else:
            op("G", lambda: g.iota(out, pat, base, cm), [], wr + ["~G"], t)

    dma("Y", "ldZ", T.zb[:], T.z[:], [], ["zb", "~Y"], 2 ** 12)
    dma("S", "ldM", T.msi[:], T.ms[:], [], ["msi", "~S"], 2 ** 18)
    dma("S", "ldC", T.cj[:], T.cp[:], [], ["cj", "~S"], 2 ** 18)
    dma("S", "ldX2", T.X[:, 2048:4096], T.tx[:, 2048:4096], [], ["Xb", "~S"], 2 ** 20 + 2 ** 17)
    dma("Y", "ldX", T.X[:, 0:2048], T.tx[:, 0:2048], [], ["X", "~Y"], 2 ** 20 + 2 ** 17)
    dma("S", "ldK", T.kti[:], T.kt[:], [], ["kti", "~S"], 2 ** 20 + 2 ** 17 + 2 ** 18)

    iota(T.tmpi[:, 0:128], [[-1, 128]], 0, 1, ["tmpi"], 128)
    iota(T.tmpj[:, 0:128], [[-16, 8], [0, 16]], 0, 1, ["tmpj"], 128)
    iota(T.ui[:, 0:1], [[0, 1]], 0, 1, ["ui"], 1)
    iota(T.tmpj[:, 160:176], [[1, 16]], 0, 0, ["J16"], 16)
    iota(T.Wm[:, 0:128], [[0, 8], [1, 16]], 0, 0, ["Wma"], 128, True)
    iota(T.tmpj[:, 192:224:2], [[128, 2], [0, 8]], 0, 1, ["CIa"], 16)
    iota(T.tmpj[:, 193:224:2], [[-128, 2], [0, 8]], 255, -1, ["CIb"], 16)
    iota(T.CM[:, :, 2, :], [[0, 72]], 256, 16, ["CMa"], 72, True)
    iota(T.CM[:, :, 0:2, 0:8], [[0, 8], [8, 2], [1, 8]], 0, 16, ["CMb"], 128, True)
    iota(T.CX[:, :, 0:8], [[0, 8], [8, 2], [1, 8]], 0, 16, ["CXa"], 128, True)
    iota(T.CX[:, :, 8], [[0, 16]], YC, 2, ["CXb"], 16, True)
    iota(T.CX[:, :, 9:12], [[0, 48]], 0, 0, ["CXz"], 48, True)
    iota(T.CX[:, 1:16:2, 10], [[0, 8]], YA - 4096, 8, ["CXz"], 8, True)
    iota(T.C30[:], [[0, 8], [-2, 16]], 30, 0, ["C30"], 128, True)
    iota(T.Kw[:, 512:640], [[0, 128]], 0, 0, ["Kwd"], 128, True)
    iota(T.Wm[:, 256:288], [[0, 32]], 0, 0, ["Wmz"], 32, True)
    iota(T.DX[:], [[0, 192]], 1, 0, ["DX"], 192, True)
    iota(T.yw[:, YC:YW], [[0, YW - YC]], 0, 0, ["yc", "ya2"], YW - YC, True)
    dma("Y", "cpU", T.UL[:], T.yw[:, YA:YW], ["ya2", "kti", "X"], ["ULz"], 2 ** 18)
    ms(T.ones[:], 1.0, ["ones"], 128, "h")

    def fill(out, val, wr, n=8, rd=()):
        act(out, T.ones[:, 0:n], ["ones"] + list(rd), wr, n, scale=val)

    def steps(buf, vals, step):
        for j, x in enumerate(vals):
            fill(T[buf][:, j:8 * step:step], x, ["%s%d" % (buf, j)])
        return ["%s%d" % (buf, j) for j in range(len(vals))]
    for nm in ("sz0", "sz1"):
        cp(T[nm][:, :, 2], T.ones[:], ["ones"], [nm], 128, "h")
    cp(T.sc[:], T.ones[:, 0:64], ["ones"], ["sc"], 64, "h")
    ms(T.D16[:], 0.0, ["D16"], 128)
    ms(T.D16[:, 0:128:16], HUGE, ["D16"])
    act(T.DA[:], T.D16[:], ["D16"], ["DA"], 128, scale=-1.0)
    fill(T.e8[:], -8 * BIG, ["e8"], 128)
    fill(T.DX[:, 8:192:12], -1.0, ["DXa"], 16, ["DX"])
    fill(T.DX[:, 9:192:12], -1.0, ["DXb"], 16, ["DX"])
    fill(T.DX[:, 10:192:24], -1.0, ["DXc"], 8, ["DX"])
    fill(T.DX[:, 23:192:24], -1.0, ["DXd"], 8, ["DX"])
    DXall = ["DX" + x for x in "abcd"]
    act(T.D2s[:], T.D16[:, 0:128:8], ["D16"], ["D2s"])
    ms(T.CM[:, :, 0:2, 8], 0.0, ["CMc"])
    ms(T.CM[:, :, 3, :], 0.0, ["CMd"], 72)
    act(T.CMh[:], T.CM[:], ["CMa", "CMb", "CMc", "CMd"], ["CMh"], 288)
    iota(T.LM2[:], [[0, 192]], 0, 0, ["LM2"], 192, True)
    iota(T.DC[:], [[0, 64]], 0, 0, ["DC"], 64, True)
    for j, x in ((0, VAST), (5, -255.5), (6, MAGIC512), (7, -MAGIC512)):
        fill(T.DC[:, j:64:8], x, ["DC%d" % j], 8, ["DC"])
    DCall = ["DC0", "DC5", "DC6", "DC7"]
    iota(T.CE[:, 0, :], [[0, 16], [1, 2]], 0, 0, ["CEz", "CEy"], 32, True)
    CYall = steps("CY", (BIG / 2, -HUGE, HUGE, -BIG / 2, 2.0 ** 24, -HUGE), 6)
    CXall = ["CXa", "CXb", "CXz"]
    fill(T.CG[:, 0:16:2], 1025.0, ["CGa"])
    fill(T.CG[:, 1:16:2], 1024.0, ["CGb"])
    iota(T.DV[:], [[0, 128]], 0, 0, ["DV"], 128, True)
    fill(T.DV[:, 0:128:8], VAST, ["DVa"], 16, ["DV"])
    fill(T.DV[:, 5:128:8], -15.5, ["DVb"], 16, ["DV"])
    fill(T.DV[:, 6:128:8], MAGIC32, ["DVc"], 16, ["DV"])
    DVall = ["DV" + x for x in ("a", "b", "c", "d", "p0", "p1", "p2")]
    ms(T.WX[:, 0:2, :], 0.0, ["WX"])
    ms(T.WM[:, 0:2, :], 0.0, ["WM"], 128, "h")
    ts(T.Ib[:], T.tmpi[:, 0:128], 0.0, None, ALU.is_equal, None, ["tmpi"], ["Ib"], 128)
    ts(T.TRI[:, 128:256], T.tmpi[:, 0:128], 0.0, -16.0, ALU.is_ge, ALU.mult, ["tmpi"], ["TRI"], 128)
    act(T.TRI[:, 0:128], T.TRI[:, 128:256], ["TRI"], ["TRJ"], 128, bias=120.0)
    ts(T.tmpi[:, 128:256], T.tmpj[:, 0:128], 4, None, ALU.arith_shift_right, None, ["tmpj"], ["tmpi2"], 128)
    ts(T.pint[:, 0:1], T.ui[:, 0:1], 15, None, ALU.bitwise_and, None, ["ui"], ["pia"])
    ts(T.pint[:, 1:2], T.ui[:, 0:1], 4, None, ALU.arith_shift_right, None, ["ui"], ["pib"])
    ts(T.pint[:, 2:3], T.ui[:, 0:1], 4, 1, ALU.arith_shift_right, ALU.bitwise_and, ["ui"], ["pic"])
    ts(T.pint[:, 3:4], T.ui[:, 0:1], 7, None, ALU.bitwise_and, None, ["ui"], ["pid"])
    ts(T.BD[:], T.tmpi[:, 128:256], 0.0, None, ALU.is_equal, None, ["tmpi2"], ["BD"], 128)
    cp(T.pm[:, 0:4], T.pint[:, 0:4], ["pia", "pib", "pic", "pid"], ["pm"])
    pm, pg, podd, p8, pm2, h1, h0, p37, nhalf, u1, u0, p14 = (T.pm[:, j:j + 1] for j in range(12))
    ts(u1, pm, 8.0, 2.0 ** 20, ALU.is_ge, ALU.mult, ["pm"], ["u1"])
    ts(u0, pm, 8.0, 2.0 ** 20, ALU.is_lt, ALU.mult, ["pm"], ["u0"])
    ts(pm2, pm, 2.0, 1.0, ALU.mult, ALU.add, ["pm"], ["pm2"])
    fill(nhalf, -0.5, ["nhalf"], 1)
    ts(h1, pm, 8.0, None, ALU.is_ge, None, ["pm"], ["h1"])
    ts(h0, pm, 8.0, None, ALU.is_lt, None, ["pm"], ["h0"])
    ts(T.EXD[:, 0:1], p8, 8.0, pg, ALU.mult, ALU.add, ["pm"], ["EXD"])
    G8 = T.BD[:, 0:128:16]
    for name, sc in (("If", 1.0), ("I2", 2.0), ("In1k", -1024.0), ("In4k", -4096.0),
                     ("nIb", -1.0)):
        act(T[name][:], T.Ib[:], ["Ib"], [name], 128, scale=sc)
    for half in range(2):
        sg = 2 * half - 1
        act(T.WX[:, half, 2 * half:32:4], G8, ["BD", "WX"], ["WXa%d" % half], scale=8192.0)
        act(T.WX[:, half, 1:32:4], G8, ["BD", "WX"], ["WXb%d" % half], scale=2 * BIG * sg)
        act(T.WX[:, half, 3:32:4], G8, ["BD", "WX"], ["WXc%d" % half], scale=-2 * BIG * sg)
        act(T.WM[:, half, 2 * half:64:8], G8, ["BD", "WM"], ["WMa%d" % half], scale=8192.0)
        act(T.WM[:, half, 1:64:8], G8, ["BD", "WM"], ["WMb%d" % half], scale=2 * BIG * sg)
        act(T.WM[:, half, 3:64:8], G8, ["BD", "WM"], ["WMc%d" % half], scale=-2 * BIG * sg)
        act(T.WM[:, half, 5:64:8], G8, ["BD", "WM"], ["WMd%d" % half], scale=512.0)
    WXall = ["WX%s%d" % (x, j) for x in "abc" for j in range(2)]
    WMall = ["WM%s%d" % (x, j) for x in "abcd" for j in range(2)]
    act(T.WX[:, 2:4, :], T.WX[:, 0:2, :], WXall, ["WXn"], 64, scale=-2.0)
    act(T.WM[:, 2:4, :], T.WM[:, 0:2, :], WMall, ["WMn"], 128, scale=-2.0)
    ts(T.DM[:, 0:128], T.Wm[:, 0:128], pm, None, ALU.is_equal, None, ["Wma", "pm"], ["DM0"], 128)
    for j in range(2):
        cp(T.DM[:, 128 << j:256 << j], T.DM[:, 0:128 << j], ["DM%d" % i for i in range(j + 1)], ["DM%d" % (j + 1)], 128 << j, "h")
    for j in range(1, 4):
        dma("Y", "cpD", T.DM[:, 512 * j:512 * j + 512], T.DM[:, 0:512], ["DM0", "DM1", "DM2", "kti", "X"], ["DM%d" % (j + 2)], 2 ** 17)
    DMall = ["DM%d" % j for j in range(6)]
    for gi in range(8):
        cp(T.CH[:, :, 16 * gi:16 * gi + 16], T.Ib[:], ["Ib"], ["CH%d" % gi], 128, "h")
    CHall = ["CH%d" % gi for gi in range(8)]
    ts(p37, pm, 37.0, 0.5, ALU.mult, ALU.add, ["pm"], ["p37"])
    ts(T.K37[:], T.ones[:], p37, None, ALU.mult, None, ["ones", "p37"], ["K37"], 128, "h")
    ts(T.SL[:], T.tmpj[:, 160:168], 16.0, pm, ALU.mult, ALU.add, ["J16", "pm"], ["SL"])
    cp(T.EX[:], T.tmpj[:, 160:168], ["J16"], ["EX"])
    ts(T.EXS[:], T.tmpj[:, 160:168], 4.0, 2.0, ALU.mult, ALU.add, ["J16"], ["EXS"])
    ts(T.EXA[:], T.tmpj[:, 160:168], 16.0, 15.0, ALU.mult, ALU.add, ["J16"], ["EXA"])
    act(T.Uw[:], T.BD[:], ["BD", "pm2"], ["Uw"], 128, scale=pm2)
    act(T.BDb[:], T.BD[:], ["BD"], ["BDb"], 128)
    for j in range(3):
        act(T.BD3[:, 8 * j:8 * j + 8], G8, ["BD"], ["BD%d" % j])
    act(T.DV[:, 7:64:8], T.SL[:], ["SL", "DV"], ["DVd"], scale=-32.0, bias=-MAGIC32)
    for j, (c0, w) in enumerate(PIECES):
        act(T.DV[:, 71 + c0 // 2:64 + (c0 + w) // 2:8], T.SL[:, 0:w // 16], ["SL", "DV"], ["DVp%d" % j], scale=-32.0, bias=-MAGIC32)
    fill(T.SU[:], VAST, ["SU"], 64)
    act(T.SU[:, 0:64:8], T.ones[:, 0:8], ["SU", "u1"], ["SUa"], scale=u1)
    act(T.SU[:, 4:64:8], T.ones[:, 0:8], ["SU", "u0"], ["SUb"], scale=u0)
    act(T.D512[:, 0:8], T.SL[:], ["SL"], ["D512a"], bias=512.0)
    act(T.D512[:, 8:16], T.SL[:], ["SL"], ["D512b"], bias=512.0)
    act(T.YL[:], T.SL[:], ["SL"], ["YL"], scale=2.0, bias=float(YC))
    fill(T.TC[:, 0:8], 0.0, ["TCc"])
    act(T.TC[:, 8:16], T.SL[:], ["SL"], ["TCa"], scale=-16.0, bias=-16.0)
    act(T.TC[:, 16:24], T.SL[:], ["SL"], ["TCb"], scale=-16.0, bias=-8.0)
    for j in range(8):
        act(T.UL[:, 129 * j:128 * j + 128:8], T.Uw[:, j:128:8], ["Uw", "ULz"], ["UL%d" % j], 16)
    ULall = ["UL%d" % gi for gi in range(8)]
    for b in range(8):
        ts(T.BI[:, b:256:8], T.tmpj[:, 192:224], b, 1, ALU.arith_shift_right, ALU.bitwise_and, ["CIa", "CIb"], ["BI%d" % b], 32)
    cp(T.bits[:], T.BI[:], ["BI%d" % b for b in range(8)], ["bits", "bits2"], 256)
    mms("EA", [(T.EA[:, 128 * j:128 * j + 128], T.bits[:, 128 * j:128 * j + 128], T.Ib[:], ["bits", "bits2", "Ib"], 128, False)
               for j in range(2)])
    ts(p14, podd, 3.0, 1.0, ALU.mult, ALU.add, ["pm"], ["p14"])
    act(T.BT[:, 0:256], T.EA[:, 0:256], ["EA", "p14"], ["BTa"], 256, scale=p14)
    cp(T.BT[:, 256:512], T.BT[:, 0:256], ["BTa"], ["BTb"], 256, "h")
    cp(T.Mu[:], T.msi[:], ["msi"], ["MuA", "MuB"], 128)
    ts(T.lz0[:, :, 0], T.msi[:], -2048.0, None, ALU.add, None, ["msi", "lz0"], ["lz0m"], 128)
    ts(T.lz0[:, :, 1], T.zb[:], ZO, None, ALU.add, None, ["zb", "lz0"], ["lz0a"], 128, "h")
    ts(T.lz0[:, :, 3], T.zb[:], ZO, None, ALU.add, None, ["zb", "lz0"], ["lz0b"], 128, "h")
    cp(T.Kw[:, 0:512], T.kti[:], ["kti", "Kwd"], ["Kw"], 512)

    def send(call, src_of, dst_of, sem, rd, wr, lat, first=0.0):
        trs, used = [], 0
        for h, ne in call:
            dst = T.cores[(rank + h) % N]
            rid, pid, _ = topo.addr(dst)
            mask = sum(1 << e for e in topo.engines(core, dst)[used:used + ne])
            used += ne
            trs.append((DstId(rid=rid, pnc=pid), mask, h))
        op("G", lambda: g.remote_dma_fused(
            [RemoteDMATransfer(dst_ids=[d], dma_engine_mask=m, remote_sem=T.sem[sem], src=src_of(h),
                               dst=dst_of((h + 1) % N)) for d, m, h in trs], local_sem=T.sem.sent),
           rd, wr + ["~R"], [0.5 + first] * NP, [lat + m["rem"] for m in PACE], sem, used, True)

    def tags(t, s0, n):
        return ["%s%d" % (t, b) for b in range(s0 // 8, (s0 + n) // 8)]

    def gather(e, t, lst, lname, s0, n):
        out = (T.xm if t == "m" else T.yw)[:, 16 * s0:16 * (s0 + n)]
        src = T.X[:].indirect(lst[:, s0:s0 + n])
        lname = lname + ["Xb"]
        if e == "S":
            act(out, src, ["X"] + lname, tags(t, s0, n) + ["~g"], 16 * n, "g", scale=0.5)
        else:
            ts(out, src, 0.5, None, ALU.mult, None, ["X"] + lname, tags(t, s0, n), 16 * n, "g")

    def mins(t, s0, n):
        src, out = (T.xm, T.mnm) if t == "m" else (T.yw, T.mnx)
        bank, o = ("ZA", "ZB")[s0 // 64], s0 % 64
        tt(out[:, 16 * s0:16 * (s0 + n)], src[:, 16 * s0:16 * (s0 + n)], T[bank][:, o:o + n, :], ALU.min,
           tags(t, s0, n) + [bank], tags("n" + t, s0, n) + ["~n"], 16 * n, "h")

    def to_list(bank, val, rd):
        return [(T[bank][:, 8 * h:8 * h + 8], T.CH[:, h, :], val, CHall + rd, 8, False) for h in range(8)]

    def mixed(z, rd, out, consts, nc, wr):
        mms("PB", [(T.PB[:, 0:64], T.Ib[:], T.SU[:], ["Ib", "SUa", "SUb"], 64, False)],
            [(T.PB[:, 0:64:4], T.UL[:, 128 * j:128 * j + 128], z(j), ULall + rd, 16, False) for j in range(8)])
        scan(out, consts, T.PB[:, 0:64], ALU.add, ALU.min, ["PB"] + nc, wr, 64)

    XM, XX = tags("m", 0, 128), tags("x", 0, 128)

    for r in range(RO):
        last = r == RO - 1
        where[0], where[1] = r, False
        lz, sz = T["lz%d" % r], T["sz%d" % r]
        nA = ["lz0m", "lz0a", "lz0b"] if r == 0 else ["lz%do" % r, "lz%dA" % r]
        nB = nA if r == 0 else ["lz%dB" % r, "lz%dD" % r]
        nz = nA + nB
        M1, z1 = lz[:, :, 0], lz[:, :, 1]
        if r:
            lin("MuA", T.Mu[:, 0:FIRST], lz[:, 0:FIRST, 0], nA, ["MuA"], FIRST, "h", bias=2048.0)
            lin("MuB", T.Mu[:, FIRST:128], lz[:, FIRST:128, 0], nB, ["MuB"], 64, "h", bias=2048.0)
        for e, s0, n in G_M[r]:
            if r and (s0, n) == (16, 16):
                lin("MuO", T.Mo[:, 16:32], lz[:, 16:32, 0], nA[:1], ["MuO"], 16, bias=2048.0)
                gather(e, "m", T.Mo, ["MuO"], s0, n)
            else:
                gather(e, "m", T.Mu, ["MuA"] * (s0 < FIRST) + ["MuB"] * (s0 + n > FIRST), s0, n)
        for j, (src, bank) in enumerate((("EA", "ZA"), ("EB", "ZB"))):
            mms(src, [(T[src][:, 0:128], lz[:, 64 * j:64 * j + 64, 1:4:2], T.Ib[:], (nA, nz)[j] + ["Ib"], 128, False)])
            lin("zT", T.zT[:, 128 * j:128 * j + 128], T[src][:, 0:128], [src], ["zT%d" % j], 128, scale=0.5, bias=-ZO / 2)
            tr([T[bank][:, :, k:k + 2] for k in range(0, 16, 2)], T.zT[:, 128 * j:128 * j + 128], ["zT%d" % j], bank)
        c, nc = (T.cj[:], ["cj"]) if r == 0 else (T.cu16[:], ["cu16"]) if r == 1 else (lz[:, 12:128:16, 2], nz)
        if r == 1:
            tt(T.cu16[:], lz[:, 12:128:16, 2], T.lc[:, 0:64:8], ALU.add, nz + ["lc", "lco"], ["cu16"])
        else:
            lin("cu%d" % r, T.cu16[:], c, nc, ["cu16"])
        lin("kcu", T.kcu[:], (T.Kw if r else T.kti)[:].indirect(T.cu16[:]), ["Kw" if r else "kti", "cu16"], ["kcu"], 128, "g")
        lin("kc", T.kc[:], T.kcu[:], ["kcu"], ["kc"], 128, "h", bias=-2048.0)
        for e, s0, n in G_X[r]:
            gather(e, "x", T.kcu, ["kcu"], s0, n)
        ts(T.hq[:], c, 256.0, -256.0, ALU.is_ge, ALU.mult, nc, ["hq"])
        tt(T.c8[:], c, T.hq[:], ALU.add, nc + ["hq"], ["c8"])
        if r == 0:
            act(T.sc[:, 0:64:8], T.c8[:], ["c8", "sc"], ["sc"], scale=2.0)
            act(T.lc[:, 8:9], T.c8[:, 0:1], ["c8"], ["lco"], 1, scale=2.0)
            send(CALL_C, lambda h: T.sc[:, 8 * h:8 * h + 8], lambda s: T.lc[:, 8 * s:8 * s + 8], "arC",
                 ["sc", "kti", "X", "Xb"], ["lc"], T_C, T_FIRST)
        mm([(T.PM[:, :, :, 0:9], T.Ib[:], T.CMh[:], ["Ib", "CMh"], 288, False)] +
           [(T.PM[:, :, j, 8], T.e8[:], T.cb[:, b:16:2], ["e8", "cb"], 8, False) for j in range(2) for b in range(2) if r],
           True, False, ["PM"])
        for s0, n in CH_M:
            mins("m", s0, n)

        def sums(bank, rows, col, chunks, tile, least, t, W, nW, nWn):
            def part(buf, wo, s0, n, ks, rd):
                at = (slice(s0, s0 + n),) + ((slice(0, rows),) if t == "x" else (slice(0, 8), slice(0, 4)))
                return [(T[bank][at + (slice(k % 8, col + 1, col - k % 8),)], buf[:, 16 * s0 + k:16 * (s0 + n):16],
                         W[:, wo + k // 8, :], rd, 2 * rows, False) for k in ks]
            for s0, n in chunks:
                mm(part(tile, 0, s0, n, range(16), tags(t, s0, n) + nW), False, False, [bank, "~r%d" % s0], n)
                if n < 128:
                    mm(part(least, 2, s0, n, range(15), tags("n" + t, s0, n) + nWn), False, False, [bank], n, ["~r%d" % s0])
            mm(part(least, 2, 0, 128, range(15 * (len(chunks) > 1), 16), tags("n" + t, 0, 128) + nWn), False, True, [bank])
        sums("PM", 32, 8, MM_M, T.xm, T.mnm, "m", T.WM, WMall, ["WMn"])
        LMk, nLM = T.LMk[:], ["LMk"]
        act(LMk, T.PM[:, :, 0:2, 0:8], ["PM"], nLM, 128)
        act(T.LMs[:], T.PM[:, :, :, 8], ["PM"], ["LMs"], 32)
        scan(T.mmin[:], T.D16[:], LMk, ALU.add, ALU.min, ["D16"] + nLM, ["mmin"], 128)
        tt(T.LM2[:, 9:192:24], T.LMs[:, 0:32:4], T.LMs[:, 1:32:4], ALU.min, ["LMs", "LM2"], ["thra"])
        ts(T.LM2[:, 21:192:24], T.LM2[:, 9:192:24], BIG, 0.0, ALU.add, ALU.min, ["thra"], ["thrb"])
        mk, mkhi = T.mmin[:, 15:128:16], T.LM2[:, 8:192:24]
        ts(mkhi, mk, MAGIC4, MAGIC4, ALU.add, ALU.subtract, ["mmin", "LM2"], ["mkhi"])
        ts(T.LM2[:, 20:192:24], mk, MAGIC4, MAGIC4, ALU.add, ALU.subtract, ["mmin", "LM2"], ["mkhj"])
        tt(T.ce[:], mk, mkhi, ALU.subtract, ["mmin", "mkhi"], ["ce"])
        mms("PB", to_list("PB", T.ce[:], ["ce"]))
        act(T.LE[:], T.PB[:, 0:64], ["PB"], ["LE"], 64)
        lin("eu", T.eu[:], T.LE[:].indirect(T.EXD[:, 0:1]), ["LE", "EXD"], ["eu"], 16, "g")
        act(T.zq[:], z1, nz, ["zq"], 128, scale=0.5, bias=-ZO / 2 - 0.25)
        if "y2" in ON_S:
            act(T.yS[:], T.xm[:].indirect(T.eu[:, 0:8]), XM + ["eu"], ["yS"], 128, "g")
            tt(T.y2[:], T.yS[:], T.zq[:], ALU.subtract, ["yS", "zq"], ["y2"], 128, "")
        else:
            tt(T.y2[:], T.xm[:].indirect(T.eu[:, 0:8]), T.zq[:], ALU.subtract, XM + ["eu", "zq"], ["y2"], 128, "g")
        act(T.ya[:], T.y2[:], ["y2", "nhalf"], ["ya"], 128, func=ACT.Abs, scale=2.0, bias=nhalf)
        tt(T.yw[:, YC:YA:2], T.ya[:], T.zq[:], ALU.subtract, ["ya", "zq"], ["yc"], 128, "")
        if not last:
            mixed(lambda j: T.ya[:, j:128:8], ["ya"], T.tc[:], T.DC[:], DCall, ["tc"])
            tt(T.CE[:, 1, 0:32:4], T.tc[:, 4:64:8], T.tc[:, 7:64:8], ALU.subtract, ["tc"], ["CE"])
            act(T.CE[:, 1, 1:32:4], T.c8[:], ["c8"], ["CEa"], scale=-2.0, bias=-1.0)
            act(T.CE[:, 1, 3:32:4], T.c8[:], ["c8"], ["CEb"], scale=2.0 * r)
        fresh = [(T.Uw[:], z1, ["Uw"] + nz, False), (T.Ib[:], T.K37[:], ["Ib", "K37"], False), (T.Ib[:], T.kc[:], ["Ib", "kc"], False)]
        mms("PA", [(T.PA[:, 0:128], l, x, rd, 128, f) for l, x, rd, f in fresh])
        act(T.qq[:], T.PA[:, 0:128], ["PA"], ["qq"], 128, scale=1 / 4096, bias=64.0)
        mms("PA", [(T.PA[:, 0:128], T.Ib[:], T.kc[:], ["Ib", "kc"], 128, False),
                   (T.PA[:, 0:128], T.nIb[:], M1, ["nIb"] + nz, 128, False)] +
            [(T.PA[:, 128:256], l, x, rd, 128, f) for l, x, rd, f in fresh] +
            [(T.PA[:, 128:256], T.nIb[:], M1, ["nIb"] + nz, 128, False)],
            [(T.PA[:, 128:256], T.In4k[:], T.qq[:], ["In4k", "qq"], 128, False)])
        act(T.DD[:, 0:128], T.PA[:, 0:128], ["PA"], ["DDa"], 128)
        act(T.DD[:, 256:384], T.PA[:, 128:256], ["PA"], ["DDc"], 128, bias=64 * 4096 - 0.5)
        act(T.zz[:], z1, nz, ["zz"], 128, scale=0.5, bias=ZO / 2 - 0.25)
        tt(T.mA[:], T.LMs[:].indirect(T.EXS[:]), LMk, ALU.is_le, ["LMs", "EXS"] + nLM, ["mA"], 128, "g")
        lin("bits", T.bits[:, 0:128], T.BT[:].indirect(T.cu16[:]), ["BTa", "BTb", "cu16"], ["bits"], 128, "g")
        for j, bank in enumerate(("EA", "EB")):
            mm([(T[bank][:, 256 * q:256 * q + 256], T.Ib[:], T.TRI[:], ["Ib", "TRI", "TRJ"], 256, False) for q in range(2)],
               True, False, [bank])
            for q in range(2):
                p0, rd = 64 * j + 32 * q, ["bits"] + ["Et"] * q
                mm([(T[bank][:, 256 * q + 128 * o:256 * q + 128 * o + 128], T.bits[p0:p0 + 16 + 16 * o, 0:128],
                     T.bits[p0:p0 + 16 + 16 * o, 0:128], rd, 128, False) for o in range(2)],
                   False, q == 1, [bank] + ["Et"] * (1 - q))
            for q in range(2):
                act(T.E[:, 512 * j + 256 * q:512 * j + 256 * q + 256], T[bank][:, 256 * q:256 * q + 256], [bank],
                    ["E%d" % (2 * j + q)], 256, func=ACT.Relu, scale=1024.0, bias=-127.0 * 1024)
        mm([(T.PX[:, 0:16, 0:12], T.Ib[:], T.CX[:], ["Ib"] + CXall, 192, False),
            (T.PX[:, 0:16, 9:12], T.Ib[:], T.CY[:], ["Ib"] + CYall, 48, False)], True, False, ["PX"])
        for s0, n in CH_X:
            mins("x", s0, n)
        sums("PX", 16, 9, MM_X, T.yw, T.mnx, "x", T.WX, WXall, ["WXn"])
        tr([T.ZA[:, 0:8, :]], T.mA[:], ["mA"], "ZA")
        tt(T.Wm[:, 288:416], T.ZA[:, 0:8, :], T.DD[:, 256:384], ALU.mult, ["ZA", "DDc"], ["Wmc"], 128, "")
        where[1] = True
        tt(T.LX[:], T.PX[:, 0:16, 0:12], T.LM2[:], ALU.add, ["PX", "mkhi", "mkhj", "thra", "thrb"], ["LX", "~LX"], 192, "")
        scan(T.LQ[:], T.LX[:], T.DX[:], ALU.min, ALU.mult, DXall + ["LX"], ["LQ"], 192, HUGE)
        tt(T.ksi[:], T.LQ[:, 9:192:24], T.LQ[:, 22:192:24], ALU.min, ["LQ"], ["ksi"])
        ts(T.KS[:], T.ksi[:], 4095, None, ALU.bitwise_and, None, ["ksi"], ["KS"])
        tt(T.L1[:], T.KS[:].indirect(T.EX[:]), T.DM[:, 0:128], ALU.mult, ["KS", "EX", "DM0"], ["L1"], 128, "g")
        tt(T.mK[:], T.PX[:, 0:16, 0:8], LMk, ALU.is_lt, ["PX", "~LX"] + nLM, ["mK"], 128, "")
        tt(T.cb[:], T.LX[:, 8:192:12], T.LQ[:, 9:192:12], ALU.is_equal, ["LX", "LQ"], ["cb"], 16)
        code, past = T.PM[:, 0, 0, 0:8], T.PM[:, 0, 1:3, 0:8]
        mms("PM", *[[(T.PM[:, 0, 0:3, 0:8], T.Ib[:], T.TC[:], ["Ib", "TCa", "TCb", "TCc"], 24, False)]] * (not last),
            [(T.PM[:, 0, 0:3, 0:8], T.L1[:], T.BD3[:], ["L1", "BD0", "BD1", "BD2"], 24, False)])
        tt(T.selu[:], code, T.YL[:], ALU.min, ["PM", "YL"], ["selu"])
        lin("szu", T.szu[:], code, ["PM", "selu"], ["szu"], scale=0.125, bias=-7.0 / 16)
        mms("PA", [(T.PA[:, 0:128], T.mK[:], T.Ib[:], ["mK", "Ib"], 128, False)])
        tt(T.DD[:, 128:256], T.PA[:, 0:128], T.DD[:, 0:128], ALU.mult, ["PA", "DDa"], ["DDb"], 128, "")
        act(T.Wm[:, 0:256:2], T.DD[:, 128:256], ["DDb", "h0"], ["Wma"], 128, scale=h0)
        act(T.Wm[:, 1:256:2], T.DD[:, 128:256], ["DDb", "h1", "DM0"], ["Wmb"], 128, scale=h1)
        nW = ["Wma", "Wmb", "Wmz", "Wmc", "szu"] + nz
        ns = "sz%d" % r
        tt(sz[:, :, 1], T.yw[:, 0:YA].indirect(T.selu[:]), T.zz[:], ALU.add, XX + ["yc", "selu", "zz", ns], [ns + "a"], 128, "g")
        if not last:
            lin("szc", sz[:, :, 3], sz[:, :, 1], [ns + "a"], [ns + "c"], 128, "h")
        if last:
            tt(T.Mn[:], T.Wm[:].indirect(T.szu[:]), M1, ALU.add, nW, ["Mn"], 128, "g")
            act(T.yy[:], T.Mn[:], ["Mn"], ["yy"], 128, bias=2048.0)
            ts(T.nzb[:], sz[:, :, 1], -ZO, None, ALU.add, None, [ns + "a"], ["nzb"], 128, "h")
            store("Y", "stZ", T.yz[:], T.nzb[:], ["nzb"], 2 ** 15)
            store("Y", "stM", T.yms[:], T.yy[:], ["yy"], 2 ** 16)
        else:
            lz2 = T["lz%d" % (r + 1)]
            ts(T.CE[:, :, 2:32:4], past, 0.0, None, ALU.is_ge, None, ["PM", "szu", "CEz"], ["FL"])
            scan(sz[:, 0:128:4, 2], T.CE[:, 0, :], T.CE[:, 1, :], ALU.mult, ALU.add, ["FL", "CEa", "CEb", "CE", "CEy", ns],
                 [ns + "b"], 32)
            tt(sz[:, :, 0], T.Wm[:].indirect(T.szu[:]), M1, ALU.add, nW + [ns], [ns + "d"], 128, "g")
            nsz = [ns + x for x in "abcd"]
            for nm, call in CALLS.items():
                send(call, lambda h, a=sz: a[:, 16 * h:16 * h + 16, :], lambda s, a=lz2: a[:, 16 * s:16 * s + 16, :],
                     "ar%s%d" % (nm, r), nsz + ["lc"], ["lz%d%s" % (r + 1, nm)], T_CALL[nm])
            act(lz2[:, 16:32, :], sz[:, 0:16, :], nsz, ["lz%do" % (r + 1)], 64)
        mixed(lambda j, a=sz: a[:, j:128:8, 1], [ns + "a"], T.tq[:], T.DV[:, 64 * last:64 * last + 64], DVall, ["tq"])
        tt(T.vu[:], T.tq[:, 4:64:8], T.tq[:, 7:64:8], ALU.subtract, ["tq"], ["vu"])
        for j, (c0, w) in enumerate(PIECES if last else ((0, 128),)):
            win, off = T.X[:, 32 * c0:32 * (c0 + w)], T.vu[:, c0 // 16:(c0 + w) // 16]
            xj = "X%d" % j if last else "X"
            tt(T.xa[:, c0:c0 + w], win.indirect(off), sz[:, c0:c0 + w, 1], ALU.add, ["X", "vu", ns + "a"], ["xa%d" % j], w, "g")
            lin("xb", T.xb[:, c0:c0 + w], T.xa[:, c0:c0 + w], ["xa%d" % j], ["xb%d" % j], w, scale=0.5, bias=-ZO / 2 - 0.25)
            cp(win.indirect(off), T.xb[:, c0:c0 + w], ["vu", "xb%d" % j], [xj] + ["~X"] * last, w, "s")
            if last:
                store("YSY"[j], "stX%d" % j, T.ytx[:, 32 * c0:32 * (c0 + w)], win, [xj], 2 ** 13 * w)
        if "oM" in ON_S:
            act(T.oS[:], T.DM[:].indirect(T.eu[:, 0:8]), DMall + ["eu"], ["oS"], 128, "g")
            tt(T.oM[:], T.oS[:], M1, ALU.mult, ["oS"] + nz, ["oM"], 128, "")
        else:
            tt(T.oM[:], T.DM[:].indirect(T.eu[:, 0:8]), M1, ALU.mult, DMall + ["eu"] + nz, ["oM"], 128, "g")
        if "nA" in ON_S:
            act(T.LXk[:], T.PX[:, 0:16, 0:8], ["PX", "LX"], ["LXk"], 128)
            mms("PB", [(T.PB[:, 0:128], T.Ib[:], T.C30[:], ["Ib", "C30"], 128, False)],
                [(T.PB[:, 0:128], T.If[:], T.LXk[:], ["If", "LXk"], 128, True)])
            scan(T.amax[:], T.DA[:], T.PB[:, 0:128], ALU.add, ALU.max, ["DA", "PB"], ["amax"], 128)
            act(T.LXk[:], T.amax[:].indirect(T.EXA[:]), ["amax", "EXA"], ["LXk"], 128, "g")
            tt(T.nA[:], T.PB[:, 0:128], T.LXk[:], ALU.not_equal, ["PB", "LXk"], ["nA"], 128, "")
        else:
            tt(T.LXk[:], T.PX[:, 0:16, 0:8], T.C30[:], ALU.add, ["PX", "C30", "~LX"], ["LXk"], 128, "")
            scan(T.amax[:], T.DA[:], T.LXk[:], ALU.add, ALU.max, ["DA", "LXk"], ["amax"], 128)
            tt(T.nA[:], T.amax[:].indirect(T.EXA[:]), T.LXk[:], ALU.not_equal, ["amax", "EXA", "LXk"], ["nA"], 128, "g")
        tr([T.ZB[:, 0:8, :]], T.nA[:], ["nA"], "ZB")
        mms("EA", [(T.EA[:, 0:16], T.Ib[:], T.CG[:], ["Ib", "CGa", "CGb"], 16, False),
                   (T.EA[:, 0:16], T.In1k[:], T.cb[:], ["In1k", "cb"], 16, False)] +
            [(T.EA[:, 2 * gi:2 * gi + 2], T.E[:, 128 * gi:128 * gi + 128], T.cb[:, 2 * gi:2 * gi + 2], ["E%d" % (gi // 2), "cb"], 2, False)
             for gi in range(8)])
        scan(T.val[:], T.D2s[:], T.EA[:, 0:16], ALU.add, ALU.min, ["D2s", "EA"], ["val"], 16)
        mms("EB", [(T.EB[:, gi:64:8], T.I2[:], T.c8[:], ["I2", "c8"], 8, False) for gi in range(8)],
            to_list("EB", T.val[:, 1:16:2], ["val"]))
        act(T.LV[:], T.EB[:, 0:64], ["EB"], ["LV"], 64)
        tt(T.ou[:], T.LV[:].indirect(T.EXD[:, 0:1]), T.D512[:], ALU.min, ["LV", "EXD", "D512a", "D512b"], ["ou"], 16, "g")
        act(T.mA[:], T.ZB[:, 0:8, :], ["ZB"], ["mA"], 128)
        mms("PA", [(T.PA[:, 0:128], T.BDb[:], T.oM[:], ["BDb", "oM"], 128, False),
                   (T.PA[:, 0:128], T.nA[:], T.In4k[:], ["nA", "In4k"], 128, False)])
        act(T.D2[:], T.PA[:, 0:128], ["PA"], ["D2"], 128, bias=2048.0)
        tt(T.old[:], T.Kw[:].indirect(T.ou[:, 0:8]), T.mA[:], ALU.mult, ["Kw", "ou", "mA"], ["old"], 128, "g")
        tt(T.Kw[:].indirect(T.ou[:, 0:8]), T.old[:], T.D2[:], ALU.max, ["ou", "old", "D2"], ["Kw"], 128, "s")
        if last:
            store("Y", "stK", T.ykt[:], T.Kw[:, 0:512], ["Kw"], 2 ** 18)

    for sem in STORES:
        op(*stores[sem])

    count = {}
    clock = {e: {} for e in Q}
    snap = {}
    writer, readers = {}, {}

    def wait(e, ev):
        s, n = ev
        if clock[e].get(s, 0) >= n:
            return
        Q[e].wait_ge(T.sem[s], n)
        clock[e][s] = n
        for k, v in snap.get(ev, {}).items():
            if clock[e].get(k, 0) < v:
                clock[e][k] = v

    if "order" not in PLANS:
        PLANS["order"] = plan(ops)
    for i in PLANS["order"]:
        o = ops[i]
        e = o["e"]
        if e == "D":
            continue
        o["rd"] = [r for r in o["rd"] if r[0] != "~"]
        o["wr"] = [w for w in o["wr"] if w[0] != "~"]
        evs = []
        for r in o["rd"]:
            if r in writer:
                evs.append(writer[r])
            if r in BANKS:
                evs += [ev for ev in readers.get(r, []) if ev[0] != SEM[e]]
        for w in o["wr"]:
            if w in writer and not (e == "P" and writer[w][0] == "cP"):
                evs.append(writer[w])
            evs += readers.get(w, [])
        best = {}
        for s, n in evs:
            best[s] = max(best.get(s, 0), n)
        for s, n in best.items():
            wait(e, (s, n))
        ins = o["fn"]()
        count[o["sem"]] = count.get(o["sem"], 0) + o["inc"]
        ev = (o["sem"], count[o["sem"]])
        if o["remote"]:
            count["sent"] = count.get("sent", 0) + o["inc"]
        else:
            ins.then_inc(T.sem[o["sem"]], o["inc"])
            snap[ev] = dict(clock[e])
            for r in o["rd"]:
                readers.setdefault(r, []).append(ev)
        for w in o["wr"]:
            writer[w] = ev
            readers[w] = []

    for s, n in count.items():
        wait("G", (s, n))
